import numpy as np, ml_dtypes
CORES = [9,25,41,57]
N = 4
BF = ml_dtypes.bfloat16
def gentries(a):
    return np.ascontiguousarray(a.reshape(8, 16, -1).transpose(0, 2, 1)).reshape(8, -1)
def gtable(e):
    e = np.asarray(e); return np.ascontiguousarray(e.reshape(8, -1, 16).transpose(0, 2, 1)).reshape(128, -1).astype(np.int32)
P, L, J, RO, NEED = 512, 8192, 16, 4, 9
def parts(rng):
    share = rng.choice(np.array([0.03, 0.06, 0.12, 0.25, 0.4]), (N, 8, 1, 1))
    dic = np.where(rng.random((N, 8, 1, L)) < share, rng.integers(0, 6, (N, 8, 16, L), dtype=np.int8), rng.integers(6, 16, (N, 8, 16, L), dtype=np.int8))
    pup = (rng.random((N, 8, 16, P)) * rng.integers(2, 13, (N, 8, 1, P))).astype(np.int8)
    return dic, pup, np.argsort(rng.random((N, 8, P)), axis=-1), rng.integers(0, 4096, (N, 8, 16, 1))
def pack(dic, pup, seat, wt):
    return {"dic": dic.astype(np.float32).reshape(N, 128, L).astype(BF), "pup": pup.astype(np.float32).reshape(N, 128, P).astype(BF),
            "seat": np.stack([gtable(a) for a in seat]), "wt": np.ascontiguousarray(wt.reshape(N, 128, 1)).astype(np.int32)}
def setup_inputs(rng):
    return pack(*parts(rng))
def setup_inputs_spread(rng):
    hard = rng.choice(np.array([0.6, 0.85, 0.97]), (N, 8, 1, 1))
    a = np.where(rng.random((N, 8, 1, L)) < hard, 0.1, rng.choice(np.array([0.5, 1.0, 2.0, 6.0]), (N, 8, 1, L)))
    dic = np.minimum(16 * rng.random((N, 8, 16, L)) ** a, 15).astype(np.int8)
    pup = np.minimum(16 * rng.random((N, 8, 16, P)) ** rng.choice(np.array([0.3, 1.0, 2.0, 4.0, 8.0]), (N, 8, 1, P)), 15).astype(np.int8)
    wt = np.minimum(np.exp2(12 * rng.random((N, 8, 16, 1))) - 1, 4095).astype(np.int64)
    return pack(dic, pup, np.argsort(rng.random((N, 8, P)), axis=-1), wt)
def setup_inputs_ends(rng):
    kind = (7 - np.arange(8)[None, :] + N - 1 - np.arange(N)[:, None]) % 4; k4 = kind[:, :, None, None]
    hard = np.where(rng.random((N, 8, 1, L)) < np.where(k4 == 0, 0.6, 0.96), 0.95, 0.3)
    dic = 15 * (rng.random((N, 8, 16, L)) < hard)
    pup = 15 * (rng.random((N, 8, 16, P)) >= rng.choice(np.array([0.6, 0.9, 0.97, 1.0]), (N, 8, 1, P)))
    wt = 4095 * ((rng.random((N, 8, 16, 1)) < 0.6) | (k4 == 0)); wt[:, :, 0] = 4095; wt[:, :, 15] = np.where(kind == 0, 4095, 0)[:, :, None]
    shut = (k4 == 1) & (np.arange(16)[:, None] >= NEED - 1)
    dic = np.where(shut, 15, dic); pup = np.where(shut, 0, pup)
    half = np.arange(P // 2); z = np.stack([half, P - 1 - half], 1).reshape(-1)
    seat = np.stack([np.stack([np.roll(z[::int(rng.choice(np.array([-1, 1])))], int(rng.integers(0, P))) for g in range(8)]) for r in range(N)])
    for r in range(N):
        for g in range(8):
            a = seat[r, g]; one = a[np.array([0, 2, 5, P - J, P - 1])]
            pup[r, g][:, one] = 0; pup[r, g][0, one] = 1
            if kind[r, g] != 1: pup[r, g][:, a[np.array([4, P - 2])]] = 15
    return pack(dic, pup, seat, wt)
def setup_inputs_corners(rng):
    dic, pup, seat, wt = parts(rng); c = int(rng.integers(0, 8))
    for r in range(N):
        for g in range(8):
            k = (r + g + c) % 8
            if k == 0: dic[r, g] = 0
            if k == 1: pup[r, g] = 0; dic[r, g] = np.maximum(dic[r, g], 1)
            if k == 2: wt[r, g] = 0; dic[r, g][:, 111] = 0
            if k == 3: wt[r, g] = 4095
            if k == 4:
                m = np.where(rng.random(L) < 0.1, NEED, NEED - 1); low = np.argsort(rng.random((16, L)), axis=0) < m
                dic[r, g] = np.where(low, rng.integers(0, 8, (16, L)), 15); pup[r, g] = rng.integers(7, 15, (16, P))
            if k == 5: dic[r, g] = 15 - (rng.random((16, L)) < 0.1); pup[r, g] = 15 - np.where(rng.random((16, P)) < 0.35, 0, rng.integers(1, 4, (16, P)))
            if k == 6: dic[r, g] = 7 + (rng.random((16, L)) < 0.6); pup[r, g] = 7 + (rng.random((16, P)) < 0.2)
            if k == 7:
                dic[r, g] = 8; pup[r, g] = rng.integers(0, 3, (16, P)); e = seat[r, g][J - 1::J]
                pup[r, g][:, e] = rng.integers(8, 16, (16, P // J))
    return pack(dic, pup, seat, wt)
def wn(a, b, j=0, t=0):
    return ((a * b >> 5) + 37 * j + 11 * t) & (L - 1)
def hexed(rng, three, kk, lo, hi):
    x = rng.integers(lo, hi + 1, (16, P)); x[three] = (kk[None, :] >> np.array([[0], [4], [8]])) & 15
    return x
def rule(rng, three, hard):
    d = np.where(hard, 15, rng.integers(0, 6, (16, L))); d[three] = rng.integers(0, 16, (3, L))
    return d
def setup_inputs_full(rng):
    dic, pup, seat, wt = parts(rng); c = int(rng.integers(0, 8)); S = P // J
    K = np.arange(4096); V = (K * K >> 5) & (P - 1); W0 = wn(K, K); top = int(V[4095]); z = P - J + 1; every = np.arange(L)
    for g in range(8):
        k = (g + c) % 8; three = rng.permutation(16)[:3]; rest = np.setdiff1d(np.arange(16), three)
        if k < 5: wt[:, g] = 0; wt[:, g, three, 0] = np.array([1, 16, 256])
        if k < 4:
            h1 = wn(4095, 4094)
            sp = int(rng.choice(np.flatnonzero((z - V >= 0) & (z - V < J) & (W0 != h1) & (W0 != wn(4094, 4094))))); jz = z - int(V[sp])
            hs = np.array([h1, int(W0[sp])]); own = K[~np.isin(W0, hs)]; line = {}
            for r in range(N):
                if r % 2 == k % 2: continue
                kk = rng.choice(own, P); kk[top] = 4094; kk[P - 1] = sp
                kk[top + 1] = rng.choice(own[~np.isin(wn(4095, own, 1), hs)]); kk[0] = rng.choice(own[~np.isin(wn(181, own, 1), hs)])
                line[r] = kk; pup[r, g][:, seat[r, g]] = hexed(rng, three, kk, 6, 14); dic[r, g] = rule(rng, three, np.isin(every, hs))
            for r in range(N):
                if r % 2 != k % 2: continue
                kb = line[(r + 1) % N]
                s = K[~np.isin(V, np.array([0, P - 1, top, top + 1])) & ~np.isin(wn(K, kb[V]), hs) & (wn(sp, K, jz) != W0)]
                s = rng.permutation(s); s = rng.permutation(s[np.unique(V[s], return_index=True)[1]])
                more = [4095]
                if k >= 2: more = more + [181, int(rng.choice(np.flatnonzero((V == 0) & ~np.isin(wn(K, kb[0]), hs))))]
                kk = rng.integers(0, 4096, P); kk[0] = 4095
                kk[1::J] = np.concatenate([rng.permutation(np.concatenate([np.array(more), s[:S - 1 - len(more)]])), s[-1:]])
                x = hexed(rng, three, kk, 0, 13); x[:, 0] = 15; x[rest, z] = 14
                d = rule(rng, three, every >= 0); d[rest, wn(sp, int(kk[z]), jz)] = 14
                pup[r, g][:, seat[r, g]] = x; dic[r, g] = d
        if k == 4:
            sa = int(rng.choice(np.flatnonzero(V == P - 1))); ha = int(wn(sa, sa, 0, 1))
            sb = int(rng.choice(np.flatnonzero((K >= 64) & (V < P - J) & (W0 != W0[sa])))); hb = int(W0[sb]); u = int(V[sb])
            own = K[~np.isin(W0, np.array([ha, hb, ha - 11, hb - 11]) & (L - 1))]
            au = own[~np.isin(wn(sb, own), np.array([ha, hb])) & (wn(sa, own, 0, 1) != hb)]
            for r in range(N):
                kk = rng.choice(own, P); kk[u] = rng.choice(au); kk[P - 1] = sa if r < 2 else sb
                pup[r, g][:, seat[r, g]] = hexed(rng, three, kk, 6, 14); dic[r, g] = rule(rng, three, every == (ha if r < 2 else hb))
        if k == 5:
            for r in range(N):
                dic[r, g] = rng.integers(6, 12, (16, L))
                pup[r, g][:, seat[r, g]] = np.where((np.arange(P) + r) % 2 == 0, rng.integers(0, 6, (16, P)), rng.integers(12, 15, (16, P)))
        if k >= 6:
            wt[:, g] = rng.integers(4090, 4096, (N, 16, 1)) if k == 6 else 4095
            for r in range(N):
                x = 13 + (rng.random((16, P)) < 0.7) + (rng.random((16, P)) < 0.15)
                x = np.minimum(x, 15); x[:, np.array([P // 2, P - 1])] = 15
                pup[r, g][:, seat[r, g]] = x
                dic[r, g] = np.where(rng.random(L) < (0.7 if k == 6 else 0.9), 15, rng.integers(0, 14, (16, L)))
    return pack(dic, pup, seat, wt)
def check_inputs(d):
    bad = []
    for k, lo, hi in (("dic", 0, 15), ("pup", 0, 15), ("seat", 0, P - 1), ("wt", 0, 4095)):
        a = np.asarray(d[k]).astype(np.float64)
        if not (np.all(a >= lo) and np.all(a <= hi)): bad.append("range of " + k)
        elif not np.all(a == np.floor(a)): bad.append("whole numbers of " + k)
    for a in d["seat"]:
        if not np.all(np.sort(gentries(np.asarray(a)), axis=1) == np.arange(P)):
            bad.append("permutation of seat"); break
    return bad
def keys(x, o, w):
    xo = np.take_along_axis(x, o[:, None, :], 2)
    return xo, np.add.reduce(xo.astype(np.int64) * w, axis=1) & 4095
def reference(dic, pup, seat, wt):
    d = dic.astype(np.float32).astype(np.int16).reshape(N, 8, 16, L); x = pup.astype(np.float32).astype(np.int16).reshape(N, 8, 16, P)
    o = np.stack([gentries(a) for a in seat]).astype(np.int64); w = wt.astype(np.int64).reshape(N, 8, 16, 1)
    q = np.arange(P); jj = np.arange(J); pl = q[:, None] + jj; inside = pl < P; pc = np.minimum(pl, P - 1)
    for t in range(RO):
        away = []
        for r in range(N):
            xo, s = keys(x[r], o[r], w[r])
            ix = (((s[:, :, None] * s[:, pc]) >> 5) + 37 * jj + 11 * t) & (L - 1)
            D = np.take_along_axis(d[r], ix.reshape(8, 1, -1), 2)
            ok = inside & (np.add.reduce((xo[:, :, pc] >= D.reshape(8, 16, P, J)).astype(np.int16), axis=1) >= NEED)
            found = np.any(ok, axis=2); last = np.where(found, q + np.argmax(ok, axis=2), np.minimum(q + J - 1, P - 1))
            st = np.zeros((8, P), np.int64)
            for g in range(8):
                f = last[g].tolist(); p = 0
                while p < P:
                    st[g, p:f[p] + 1] = p; p = f[p] + 1
            fs = np.take_along_axis(found, st, 1); ls = np.take_along_axis(last, st, 1)
            D2 = np.take_along_axis(D, (st * J + q - st)[:, None, :], 2)
            xo = xo + ((fs & (q < ls))[:, None, :] & (D2 > xo))
            x[r] = np.take_along_axis(xo, np.argsort(o[r], axis=1)[:, None, :], 2)
            o[r] = np.take_along_axis(o[r], np.where(fs, np.where(q == st, ls, q - 1), q), 1)
            away.append((q == st) & ~fs)
        now = [keys(x[r], o[r], w[r]) for r in range(N)]; x0 = x.copy()
        for a in range(N):
            b = (a + 1 + t % (N - 1)) % N; xb, sb = now[b]
            for g in range(8):
                ps = np.flatnonzero(away[a][g])
                if len(ps) == 0: continue
                sv = now[a][1][g, ps]
                v = ((((sv * sv) >> 5) & (P - 1))[:, None] + jj) & (P - 1)
                D = d[b, g][:, (((sv[:, None] * sb[g, v]) >> 5) + 37 * jj + 11 * t) & (L - 1)]
                ok = (np.add.reduce((xb[g][:, v] >= D).astype(np.int16), axis=0) >= NEED) & ~away[b][g, v]
                h = np.flatnonzero(np.any(ok, axis=1))
                if len(h) == 0: continue
                u, i = np.unique(v[h, np.argmax(ok[h], axis=1)], return_index=True)
                pa = o[a][g, ps[h[i]]]; pb = o[b][g, u]
                x[a, g][:, pa] = x0[b, g][:, pb]; x[b, g][:, pb] = x0[a, g][:, pa]
    return {"ypup": x.reshape(N, 128, P).astype(np.float32).astype(BF), "yseat": o.astype(np.float32)}

@@ -1,0 +1,535 @@
+from concourse.mybir import AluOpType as OP, AxisListType as AX, ActivationFunctionType as AF
+
+RO = 4
+NS = 7
+NS0 = 6
+B0 = 48
+XW = 608
+DW = 8800
+TE, TC = 0, 768
+WDT = "float16"
+
+F, I, U, H = "float32", "int32", "uint16", "bfloat16"
+SB = {
+    "dicx": (DW, H), "pupb": (512, H), "seatb": (32, I), "wtb": (4, I), "seatu": (32, U),
+    "x0": (XW, H), "x1": (XW, H), "o0": (512, H), "o1": (512, H), "oio": (512, H), "x2": (752, H), "x2l": (48, U),
+    "lt": (17 * 1024, H), "d0": (512, H), "d1": (512, H), "d2": (512, H),
+    "ksi": (48, I), "ks": (48, I), "prod": (512, I), "prs": (512, I), "off": (512, U),
+    "pw": (512, H), "lns": (32, F), "nsi": (32, I), "roff": (64, U), "lnn": (32, F), "nni": (32, I),
+    "r32": (32, U), "nm": (32, F), "pz": (16, F), "pe": (16, F), "pu": (16, F), "pv": (16, F),
+    "tt": (3072, F), "cc": (768, F), "ch": (34 * 16, U),
+    "kni": (32, I), "kn": (32, I), "kn1": (32, F), "ksq": (32, I), "v0": (32, I), "v1": (32, F),
+    "nt": (32, F), "nu": (32, F), "nl": (32, F), "aw": (32, F), "st": (32, F), "apk": (64, WDT), "awq": (32, WDT),
+    "rf": (36, F), "rf2": (32, F), "yp": (32, I), "idx2": (32, U), "uu": (32, I), "e1": (32, F), "e2": (32, F),
+    "srcf": (32, F), "src": (32, U), "srof": (32, F), "sro": (32, U), "g2": (512, H),
+    "dm": (32, F), "avf": (4, F), "avl": (2, U), "avo": (2, U), "olf": (32, F), "olu": (32, U), "awo": (32, WDT),
+    "xv": (512, H), "sf": (32, F), "val": (32, F), "vi": (32, I), "vj": (32, I), "vk": (32, F), "vp": (32, F),
+    "khi": (32, I), "kh": (32, I), "hp": (32, I), "hs": (32, I), "hw": (32, U), "lt2": (512, H),
+    "ps2": (32, H), "fi": (32, F), "fv": (32, WDT), "cbm": (64, F), "eq": (64, F), "cl": (4, F), "cf": (4, F), "tgt": (2, U),
+    "xg": (B0 + 512, H), "lav": (2, U), "ypb": (544, H), "ysb": (512, F),
+    "zo": (144, H), "zw": (144, WDT), "zm": (144, H), "idn": (128, H), "nid": (128, H), "tri": (128, H), "g8": (8, H),
+    "dh": (128, H), "dl": (128, H), "ohi": (512, H), "olo": (512, H),
+    "blk": (128, F), "r15": (128, F), "io": (144, F), "mg": (128, F), "i16": (32, F), "iv": (768, F),
+    "ie": (256, F), "ia": (256, F), "t1": (256, F), "t2": (768, F), "t3": (768, F), "t4": (256, F), "blkb": (128, H),
+    "col": (32, F), "ci": (8, I), "q16": (32, F), "q32": (32, F), "qm1": (32, F), "dg": (32, F), "tm": (64, F),
+}
+for _t in range(RO):
+    SB["m1_%d" % _t] = (64, U); SB["l1_%d" % _t] = (64, U)
+    for _n in ("m2", "l2", "m3", "l3"):
+        SB["%s_%d" % (_n, _t)] = (32, H)
+PS = ["pc", "pa", "pb", "pk", "pm", "pn", "pp", "ph"]
+SCRATCH, HOME = {}, {}
+for _k, (_w, _d) in SB.items():
+    if _w > 64:
+        SCRATCH["b_" + _k] = ("sbuf", [128, _w], _d)
+        HOME[_k] = (_k, 0)
+    else:
+        _o = SCRATCH.get("b_pool" + _d, (0, [128, 0]))[1][1]
+        SCRATCH["b_pool" + _d] = ("sbuf", [128, _o + (_w + 15) // 16 * 16], _d)
+        HOME[_k] = ("pool" + _d, _o)
+SCRATCH.update({("b_" + k): ("psum", [128, 512], F) for k in PS})
+SEMAPHORES = ["qv", "qs", "qp", "qg", "sent", "zf", "a0", "out0", "out1"] + ["ld%d" % i for i in range(8)] + \
+             ["a%d_%d" % (m, t) for m in (1, 2, 3) for t in range(RO)]
+CP, CK, CG, CK16, CG15, CW, CM, CTH, CJ, CY, CHI0, CHI1, CC1, CC3, CE, C15, CX, CZ0, CZ1, CS, CQ, CT0 = range(22)
+CQ0, CTH0, CJ1, CES, CZ2 = 26, 27, 28, 29, 30
+CK32, CKM, CL = 25, 31, CC3
+CH = (CK, CK16, CK32)
+
+
+def a(name, lo=0, hi=None, step=1, ind=None, np_=128):
+    if hi is None:
+        hi = SB[name][0] if name in SB else 512
+    return (name, lo, hi, step, ind, np_)
+
+
+def c(j):
+    return a("col", j, j + 1)
+
+
+def rank_program(g, core, T, topo):
+    rank = T.rank_of(core)
+    if rank is None:
+        return
+    N = len(T.cores)
+    eng = {"v": g.vector, "s": g.scalar, "p": g.tensor, "g": g, "y": g.sync}
+    qsem = {"v": "qv", "s": "qs", "p": "qp", "g": "qg"}
+    count = {}
+    known = {q: {} for q in eng}
+    snap = {}
+    acc = {}
+
+    def ap(x):
+        if not isinstance(x, tuple):
+            return x
+        name, lo, hi, step, ind, np_ = x
+        home, base = HOME.get(name, (name, 0))
+        t, lo, hi = T["b_" + home], lo + base, hi + base
+        r = t[0:np_, lo:hi:step] if step != 1 else t[0:np_, lo:hi]
+        return r.indirect(ap(ind)) if ind is not None else r
+
+    def wait(q, s, v):
+        if known[q].get(s, 0) >= v:
+            return
+        eng[q].wait_ge(T.sem[s], v)
+        k = known[q]
+        for s2, v2 in snap.get((s, v), {s: v}).items():
+            if k.get(s2, 0) < v2:
+                k[s2] = v2
+
+    def order(q, rd, wr):
+        use = []
+        for w, xs in ((False, rd), (True, wr)):
+            for x in xs:
+                if isinstance(x, tuple):
+                    use.append((x[0], x[1], x[2], w))
+                    if x[4] is not None:
+                        use.append((x[4][0], x[4][1], x[4][2], False))
+        need = {}
+        for name, lo, hi, w in use:
+            for (l2, h2, w2, q2, s2, v2) in acc.get(name, []):
+                if name in PS and q2 != q:
+                    hit = True
+                elif name in PS and q == "p":
+                    hit = False
+                else:
+                    hit = (w or w2) and l2 < hi and lo < h2
+                if hit and need.get(s2, 0) < v2:
+                    need[s2] = v2
+        for s2 in sorted(need, key=lambda s: s == qsem.get(q)):
+            wait(q, s2, need[s2])
+        return use
+
+    def note(use, q, s, v):
+        sn = dict(known[q]) if q in known else {}
+        sn[s] = v
+        snap[(s, v)] = sn
+        for name, lo, hi, w in use:
+            lst = acc.setdefault(name, [])
+            if name in PS:
+                lst[:] = [e for e in lst if e[3] == q]
+            if w:
+                lst[:] = [e for e in lst if not (lo <= e[0] and e[1] <= hi)]
+            else:
+                lst[:] = [e for e in lst if not (e[4] == s and not e[2] and lo <= e[0] and e[1] <= hi)]
+            lst.append((lo, hi, w, q, s, v))
+
+    def op(q, rd, wr, fn):
+        use = order(q, rd, wr)
+        s = qsem[q]
+        count[s] = count.get(s, 0) + 1
+        fn().then_inc(T.sem[s], 1)
+        note(use, q, s, count[s])
+
+    def ts(o, i, s1, s2, o0, o1=None):
+        if o1 is None:
+            op("v", [i, s1], [o], lambda: g.vector.tensor_scalar(ap(o), ap(i), ap(s1), None, o0))
+        else:
+            op("v", [i, s1, s2], [o], lambda: g.vector.tensor_scalar(ap(o), ap(i), ap(s1), ap(s2), o0, o1))
+
+    def tt(o, i0, i1, o0):
+        op("v", [i0, i1], [o], lambda: g.vector.tensor_tensor(ap(o), ap(i0), ap(i1), o0))
+
+    def cp(o, i):
+        op("v", [i], [o], lambda: g.vector.tensor_copy(ap(o), ap(i)))
+
+    def red(o, i, o0):
+        op("v", [i], [o], lambda: g.vector.tensor_reduce(ap(o), ap(i), AX.X, o0))
+
+    def ms(o, v):
+        op("v", [], [o], lambda: g.vector.memset(ap(o), v))
+
+    def act(o, i, f, bias=None, scale=1.0):
+        if bias is None:
+            op("s", [i], [o], lambda: g.scalar.activation(ap(o), ap(i), f))
+        else:
+            op("s", [i, bias, scale], [o], lambda: g.scalar.activation(ap(o), ap(i), f, bias=ap(bias), scale=ap(scale)))
+
+    def aff(o, i, scale, bias):
+        act(o, i, AF.Identity, bias, scale)
+
+    def mm(o, l, r, st=True, sp=True):
+        op("p", [l, r], [o], lambda: g.tensor.matmul(ap(o), ap(l), ap(r), st, sp))
+
+    def iota(o, pat, base, cm=0):
+        if SB[o[0]][1] == I:
+            op("g", [], [o], lambda: g.iota(ap(o), pat, base, cm))
+        else:
+            op("g", [], [o], lambda: g.iota(ap(o), pat, base, cm, allow_small_or_imprecise_dtypes=True))
+
+    def dma(q, s, pairs):
+        use = []
+        for o, i in pairs:
+            use += order(q, [i], [o])
+        for o, i in pairs:
+            eng[q].dma_start(ap(o), ap(i)).then_inc(T.sem[s], 16)
+        count[s] = 16 * len(pairs)
+        note(use, q, s, count[s])
+
+    def send(src, dst, s, to, loc="sent"):
+        order("g", [src], [])
+        d = T.cores[to]
+        rid, pid, _ = topo.addr(d)
+        g.remote_dma(ap(dst), ap(src), T.sem[s], T.sem[loc], pid, rid, topo.mask(core, d))
+        count[loc] = count.get(loc, 0) + len(topo.engines(core, d))
+        if loc != "sent":
+            note([(src[0], src[1], src[2], False)], "remote", loc, count[loc])
+
+    def landed(dst, s, frm):
+        n = len(topo.engines(T.cores[frm], core))
+        count[s] = n
+        note([(dst, 0, SB[dst][0], True)], "remote", s, n)
+
+    def sel(z, i):
+        return a(z, 15 - i, 143 - i)
+
+    def conv(o, z, buf, lo, hi):
+        for i in range(16):
+            mm(o, sel(z, i), a(buf, lo + i, hi, 16), i == 0, i == 15)
+
+    dma("y", "ld0", [(a("pupb"), T.pup[:])])
+    dma("s", "ld1", [(a("seatb"), T.seat[:])])
+    dma("s", "ld2", [(a("wtb", 0, 1), T.wt[:])])
+    dma("y", "ld3", [(a("dicx", 0, 4096), T.dic[:, 0:4096])])
+    dma("s", "ld4", [(a("dicx", 4096, 8192), T.dic[:, 4096:8192])])
+    dma("y", "ld5", [(a("dicx", 8192, DW), T.dic[:, 0:DW - 8192])])
+
+    iota(a("ci", 0, 1), [[0, 1]], 0, 1)
+    iota(a("io"), [[1, 144]], 0)
+    iota(a("mg"), [[16, 8], [0, 16]], 0)
+    iota(a("i16"), [[0, 2], [1, 16]], 0)
+    iota(a("iv"), [[1040, 16], [256, 3], [1, 16]], 0)
+    iota(a("ie"), [[1, 16], [0, 16]], 0)
+    iota(a("ia"), [[16, 16], [1, 16]], 1)
+    ex = a("tt", TC + 768, TC + 1536)
+    iota(ex, [[48, 16], [0, 3], [1, 16]], TC + 16)
+    op("g", [ex], [ex], lambda: g.affine_select(ap(ex), ap(ex), [[0, 16], [1, 3], [0, 16]], OP.is_ge, 0.0, -2, 0))
+    for x in ("x0", "x1"):
+        ms(a(x, 0, B0), -1.0)
+        ms(a(x, B0 + 512, XW), -1.0)
+    ms(a("lt", 16 * 1024, 17 * 1024), 0.0)
+    cp(c(CP), a("ci", 0, 1))
+    ts(a("ci", 1, 2), a("ci", 0, 1), 15, None, OP.bitwise_and)
+    ts(a("ci", 2, 3), a("ci", 0, 1), 112, None, OP.bitwise_and)
+    ms(a("t1", 0, 16), 0.25)
+    ms(a("t1", 16, 32), 0.0)
+    cp(a("col", CK, CG + 1), a("ci", 1, 3))
+    op("v", [a("t1", 0, 32)], [a("t1", 32, 48)], lambda: g.vector.tensor_tensor_scan(
+        ap(a("t1", 32, 48)), ap(a("t1", 0, 16)), ap(a("t1", 16, 32)), 4.0 ** 16, OP.mult, OP.add))
+    ts(c(CG15), c(CG), 15.0, None, OP.add)
+    ts(c(CS), c(CK), 32.0, float(B0), OP.mult, OP.add)
+    ts(a("idn"), a("io", 0, 128), c(CP), None, OP.is_equal)
+    ts(a("zo"), a("io"), c(CG15), None, OP.is_equal)
+    ts(a("t1", 64, 112), a("io", 0, 48), c(CS), None, OP.add)
+    ts(a("nid"), a("io", 0, 128), c(CP), -1.0, OP.is_equal, OP.mult)
+    ts(a("t1", 112, 160), a("t1", 64, 112), B0 + 511.5, None, OP.is_le)
+    ts(a("t4", 0, 128), a("io", 0, 128), c(CP), None, OP.is_gt)
+    tt(a("t1", 160, 208), a("t1", 64, 112), a("t1", 112, 160), OP.mult)
+    ts(a("blk"), a("mg"), c(CG), None, OP.is_equal)
+    ts(a("x2l"), a("t1", 160, 208), 32.0, None, OP.max)
+    ts(a("dg"), a("i16"), c(CK), None, OP.is_equal)
+    ts(c(CQ), c(CK), NS - 0.5, -8.5, OP.is_le, OP.mult)
+    tt(a("t1", 48, 64), a("t1", 32, 48), a("dg", 0, 16), OP.mult)
+    red(c(CM), a("t1", 48, 64), OP.add)
+    for j, (m, b) in {CK16: (1, 16), CJ: (1, B0), CJ1: (1, B0 - 1), CK32: (1, 32), CKM: (1, -16), CY: (1024, 1024), CHI0: (1, 576), CHI1: (1, 592), CC1: (-1024, 15360),
+                      CT0: (37, 0), CT0 + 1: (37, 11), CT0 + 2: (37, 22), CT0 + 3: (37, 33)}.items():
+        aff(c(j), c(CK), float(m), float(b))
+    aff(c(CTH), c(CQ), 1.0, 7.5)
+    ts(c(CQ0), c(CK), NS0 - 0.5, -8.5, OP.is_le, OP.mult)
+    aff(c(CTH0), c(CQ0), 1.0, 7.5)
+    cp(a("seatu"), a("seatb"))
+    ts(c(CX), a("wtb", 0, 1), 2048.0, -4096.0, OP.is_ge, OP.mult)
+    ts(a("zm"), a("zo"), c(CM), None, OP.mult)
+    tt(c(CW), a("wtb", 0, 1), c(CX), OP.add)
+    cp(a("x0", B0, B0 + 512), a("pupb", ind=a("seatu")))
+    ts(a("zw"), a("zo"), c(CW), None, OP.mult)
+
+    def later_constants():
+        aff(a("t2"), a("iv"), 1.0, c(CC1))
+        aff(a("t3"), a("t2"), -65536.0, 2.0 ** 30)
+        tt(a("cc"), a("t2"), a("t3"), OP.min)
+        op("g", [a("cc")], [a("cc")], lambda: g.affine_select(
+            ap(a("cc")), ap(a("cc")), [[0, 16], [-1, 3], [0, 16]], OP.is_ge, 0.0, 1, 0))
+        iota(a("ohi"), [[16, 32], [0, 16]], 0)
+        iota(a("olo"), [[0, 32], [1, 16]], 0)
+        ts(c(CZ0), c(CK), 0.0, None, OP.is_equal)
+        ts(c(CZ1), c(CK), 1.0, None, OP.is_equal)
+        ts(c(CZ2), c(CK), 2.0, None, OP.is_equal)
+        ts(a("blkb"), a("mg"), c(CG), None, OP.is_equal)
+        ts(c(CES), c(CZ1), c(CZ2), 32.0, OP.add, OP.mult)
+        ts(c(CX), c(CZ2), 32.0, None, OP.mult)
+        ts(c(CE), c(CES), TC / 32.0, c(CX), OP.mult, OP.add)
+        aff(a("ie"), a("ie"), c(CES), c(CE))
+        tt(a("tt", TE + 512, TE + 768), a("ie"), a("ia"), OP.add)
+        wait("y", "ld3", 16); wait("y", "ld4", 16); wait("y", "ld5", 16)
+        dma("y", "zf", [(a("lt", 1024 * j + 512, 1024 * j + 1024), a("lt", 16 * 1024, 16 * 1024 + 512)) for j in range(16)])
+        ts(c(C15), c(CK), 15.0, None, OP.is_equal)
+        tt(a("t4", 128, 256), a("idn"), a("t4", 0, 128), OP.subtract)
+        ts(a("g8"), a("io", 0, 8), 16.0, c(CG), OP.mult, OP.is_equal)
+        ts(a("r15"), a("blk"), c(C15), None, OP.mult)
+        tt(a("tri"), a("t4", 128, 256), a("blk"), OP.mult)
+        ts(a("q16"), a("io", 0, 32), 16.0, c(CJ), OP.mult, OP.add)
+        ts(a("tm", 0, 32), a("io", 0, 32), c(CK), None, OP.is_lt)
+        ts(a("tm", 32, 64), a("io", 0, 32), c(CK16), None, OP.is_lt)
+        ts(a("q32"), a("q16"), 32.0, None, OP.add)
+        ts(a("qm1"), a("q16"), -1.0, None, OP.add)
+        act(c(CQ), a("t1", 0, 1), AF.Ln)
+        op("v", [c(CQ)], [c(CL)], lambda: g.vector.reciprocal(ap(c(CL)), ap(c(CQ))))
+        ms(a("rf", 0, 1), 0.0)
+        cp(a("ch", 0, 1), c(CE))
+        ms(a("ypb", 0, 32), 0.0)
+        aff(a("t2"), a("cc"), 1.0, 512.0)
+        tt(a("tt", TC + 1536, TC + 2304), a("t2"), ex, OP.max)
+
+    def first_numbers():
+        mm(a("pa"), a("dh"), a("ohi"), True, False)
+        mm(a("pa"), a("dl"), a("olo"), False, True)
+        act(a("oio"), a("pa"), AF.Copy)
+        act(a("o0"), a("oio", ind=a("seatu")), AF.Copy)
+
+    BIG = float(1 << 20)
+    for t in range(RO):
+        xo, xn = ("x0", "x1") if t % 2 == 0 else ("x1", "x0")
+        oo, on = ("o0", "o1") if t % 2 == 0 else ("o1", "o0")
+        host = (rank + 1 + t % (N - 1)) % N
+        guest = (rank - 1 - t % (N - 1)) % N
+        last = t == RO - 1
+        m1, l1, m2, l2, m3, l3 = ["%s_%d" % (n, t) for n in ("m1", "l1", "m2", "l2", "m3", "l3")]
+        for i in range(16):
+            mm(a("pk", 0, 47), sel("zw", i), a(xo, B0 + 32 * i, B0 + 32 * i + 47), i == 0, i == 15)
+        act(a("x2"), a(xo, ind=a("x2l", 0, 47)), AF.Copy)
+        ts(a("ksi", 0, 47), a("pk", 0, 47), BIG, None, OP.add)
+        conv(a("pn", 0, 32), "zw", xo, B0, B0 + 512)
+        ts(a("ks", 0, 47), a("ksi", 0, 47), 4095, None, OP.bitwise_and)
+
+        def mults(js):
+            for j in js:
+                tt(a("prod", 32 * j, 32 * j + 32), a("ks", 0, 32), a("ks", j, j + 32), OP.mult)
+
+        def shift(js):
+            ts(a("prs", 32 * js[0], 32 * js[-1] + 32), a("prod", 32 * js[0], 32 * js[-1] + 32), 5, 8191,
+               OP.logical_shift_right, OP.bitwise_and)
+
+        def adds(js):
+            for j in js:
+                ts(a("off", 32 * j, 32 * j + 32), a("prs", 32 * j, 32 * j + 32), float((37 * j + 11 * t) % 16), None, OP.add)
+
+        ch_ = [[0, 1], [2, 3, 4], [5, 6, 7, 8], [9, 10, 11, 12], [13, 14, 15]]
+        mults(ch_[0]); mults(ch_[1]); shift(ch_[0]); mults(ch_[2][:1]); adds(ch_[0]); shift(ch_[1]); mults(ch_[2][1:])
+        adds(ch_[1]); shift(ch_[2]); mults(ch_[3]); adds(ch_[2]); shift(ch_[3]); mults(ch_[4]); adds(ch_[3]); shift(ch_[4])
+        ts(a("kni"), a("pn", 0, 32), BIG, None, OP.add)
+        adds(ch_[4])
+        if t == 0:
+            later_constants()
+            wait("g", "ld3", 16); wait("g", "ld4", 16)
+            send(a(xo, 0, B0 + 512), a("xg"), "a0", host, "out0")
+            landed("xg", "a0", guest)
+
+        def word(j):
+            ws = (37 * j + 11 * t) // 16 * 16
+            return a("dicx", ws, ws + 8208, ind=a("off", 32 * j, 32 * j + 32))
+
+        def ltj(j):
+            return a("lt", 1024 * (15 - j), 1024 * (15 - j) + 512)
+
+        ev = []
+        ns = NS0 if t == 0 else NS
+        tv, tsc = (0.0 if t == 0 else 1.7), 0.0
+        for j in range(ns, 16):
+            ev.append((tv, "vg", j)); tv += 0.72; ev.append((tv + 0.6, "cnt", j))
+        for j in range(ns + 1):
+            if j < ns:
+                ev.append((tsc, "sg", j)); tsc += 0.73; ev.append((tsc, "sub", j))
+            if j > 0:
+                ev.append((tsc + 0.001, "sign", j - 1)); tsc += 0.48; ev.append((tsc + 0.3, "cnt", j - 1))
+        ev.sort()
+        ncnt = [0]
+        extra = [
+            lambda: ts(a("kn"), a("kni"), 4095, None, OP.bitwise_and),
+            lambda: (ts(a("kn1"), a("kn"), -2048.0, None, OP.add), tt(a("ksq"), a("kn"), a("kn"), OP.mult)),
+            lambda: ts(a("v0"), a("ksq"), 5, 511, OP.logical_shift_right, OP.bitwise_and),
+            lambda: ts(a("v1"), a("v0"), 1.0, None, OP.add),
+        ]
+        for _, kind, j in ev:
+            d, bank = a("d%d" % (j % 3)), a("pa" if j % 2 == 0 else "pb")
+            if kind == "vg":
+                tt(ltj(j), word(j), a("x2", 16 * j, 16 * j + 512), OP.is_gt)
+                if extra:
+                    extra.pop(0)()
+            elif kind == "sg":
+                act(d, word(j), AF.Copy)
+            elif kind == "sub":
+                mm(bank, a("idn"), d, True, False)
+                mm(bank, a("nid"), a("x2", 16 * j, 16 * j + 512), False, True)
+            elif kind == "sign":
+                act(ltj(j), bank, AF.Sign, -0.5)
+            else:
+                mm(a("pc"), sel("zo", j), ltj(j), ncnt[0] == 0, ncnt[0] == 15)
+                ncnt[0] += 1
+        ts(a("pw"), a("pc"), c(CTH0 if t == 0 else CTH), None, OP.is_le)
+        conv(a("pm", 0, 32), "zm", "pw", 0, 512)
+        for h in (0, 1):
+            for k in range(16):
+                mm(a("pn", 16 * h, 16 * h + 16), sel("zm", k), a("pw", 256 * h + 16 * k, 256 * h + 16 * k + 16), k == 0, k == 15)
+        act(a("lns"), a("pm", 0, 32), AF.Ln, 4.0 ** -16)
+        ts(a("nsi"), a("lns"), c(CL), 15.1, OP.mult, OP.add)
+        ts(a("nm"), a("nsi"), 15.0, 16.0, OP.min, OP.mult)
+        ts(a("pz"), a("nsi", 0, 32, 2), -1000.0, 16.0, OP.mult, OP.add)
+        for h in (0, 1, 2):
+            ts(a("roff", h, 64, 4), a("nsi", 16 * (h % 2), 16 * (h % 2) + 16), 48.0, c(CH[h]), OP.mult, OP.add)
+            if h == 0:
+                tt(a("pu"), a("pz"), a("nm", 1, 32, 2), OP.add)
+                ts(a("r32", 1, 32, 2), a("nm", 1, 32, 2), c(CK), None, OP.add)
+            if h == 1:
+                tt(a("pv"), a("pu"), a("nm", 0, 32, 2), OP.max)
+        ts(a("r32", 0, 32, 2), a("pv"), c(CKM), None, OP.add)
+        extra = {
+            13: lambda: act(a("lnn", 0, 32, 2), a("pn", 0, 16), AF.Ln, 4.0 ** -16),
+            12: lambda: act(a("lnn", 1, 32, 2), a("pn", 16, 32), AF.Ln, 4.0 ** -16),
+            9: lambda: ts(a("nni"), a("lnn"), c(CL), 16.1, OP.mult, OP.add),
+            7: lambda: ts(a("nt"), a("nni"), 20.0, None, OP.is_ge),
+            5: lambda: tt(a("nu"), a("nt"), a("q32"), OP.mult),
+            4: lambda: tt(a("nl"), a("nni"), a("nu"), OP.subtract),
+        }
+        if t == 0:
+            extra[3] = lambda: ts(a("dh"), a("idn"), c(CZ0), None, OP.mult)
+            extra[2] = lambda: ts(a("dl"), a("idn"), c(CZ1), None, OP.mult)
+        for k in range(15, -1, -1):
+            w = TE + 32 * (k + 1)
+            act(a("tt", w - 32, w), a("tt", w, w + 256, ind=a("r32", 2 * k, 2 * k + 2)), AF.Copy)
+            w = TC + 48 * (k + 1)
+            tt(a("tt", w - 48, w), a("tt", w, w + 1536, ind=a("roff", 4 * k, 4 * k + 3)), a("cc", 48 * k, 48 * k + 48), OP.max)
+            if k in extra:
+                extra[k]()
+        if t == 0:
+            first_numbers()
+        for i in range(17):
+            if i < 16:
+                o = 32 * i - 16 if i else 0
+                cp(a("ch", 32 * i + 16, 32 * i + 32), a("tt", 0, TC + 768, ind=a("ch", o, o + 1)))
+            if i > 0:
+                cp(a("ch", 32 * i, 32 * i + 16), a("tt", 0, TC + 768, ind=a("ch", 32 * i - 14, 32 * i - 13)))
+        A = a("ch", 17, 33 * 16, 16)
+        ts(a("aw"), A, 15872.0, None, OP.is_ge)
+        cp(a("rf", 1, 33), A)
+        tt(a("apk", 0, 32), a("aw"), a("v1"), OP.mult)
+        tt(a("apk", 32, 64), a("aw"), a("kn1"), OP.mult)
+        mm(a("pp", 0, 32), a("r15"), a("rf", 0, 32))
+        mm(a("ph", 0, 64), a("blkb"), a("apk"))
+        ts(a("rf2"), A, c(CY), None, OP.add)
+        ts(a("st"), A, 15360.0, None, OP.is_ge)
+        ts(a(m1, 0, 32), a("ph", 0, 32), c(CJ1), None, OP.add)
+        ts(a(m1, 32, 64), a("ph", 32, 64), 2048.0, None, OP.add)
+        send(a(m1), a(l1), "a1_%d" % t, host)
+        tt(a("yp"), a("pp", 0, 32), a("rf2"), OP.max)
+        ts(a("idx2"), a("yp"), c(CY), None, OP.subtract)
+        act(a("g2"), a("lt", 1024, 17 * 1024, ind=a("idx2")), AF.Relu)
+        tt(a("e1"), a("st"), a("nl"), OP.mult)
+        ts(a("uu"), a("yp"), 9, 1, OP.logical_shift_right, OP.bitwise_and)
+        tt(a("awq"), a("aw"), a("q16"), OP.mult)
+        tt(a("e2"), a("e1"), a("qm1"), OP.add)
+        mm(a("pp", 64, 96), a("blkb"), a("awq"))
+        tt(a("srcf"), a("e2"), a("uu"), OP.add)
+        tt(a("dm"), a("pp", 64, 96), a("dg"), OP.mult)
+        cp(a("src"), a("srcf"))
+        for h in (0, 1):
+            red(a("avf", h, h + 1), a("dm", 16 * h, 16 * h + 16), OP.max)
+        tt(a("srof"), a("srcf"), a("awq"), OP.max)
+        for h in (0, 1):
+            ts(a("avl", h, h + 1), a("avf", h, h + 1), c(CH[h]), None, OP.max)
+        ts(a("sro"), a("srof"), float(B0), None, OP.subtract)
+        tt(a(xn, B0, B0 + 512), a(xo, ind=a("src")), a("g2"), OP.add)
+        act(a(on), a(oo, ind=a("sro")), AF.Copy)
+        if t == 0:
+            send(a("avl"), a("lav"), "a2_0", host, "out1")
+        else:
+            cp(a(m2), a(xo, ind=a("avl")))
+            send(a(m2), a(l2), "a2_%d" % t, host)
+        cp(a(xn, B0 + 512, B0 + 528), a(xn, B0, B0 + 16))
+        landed(l1, "a1_%d" % t, guest)
+        landed(l2 if t else "lav", "a2_%d" % t, guest)
+        landed(l3, "a3_%d" % t, host)
+        cp(a("xv", 0, 256), a(xn, 0, 576, ind=a(l1, 0, 16)))
+        act(a("xv", 256, 512), a(xn, 0, 576, ind=a(l1, 16, 32)), AF.Copy)
+        conv(a("ph", 0, 32), "zw", "xv", 0, 512)
+        if last:
+            conv(a("pn", 0, 32), "zo", on, 0, 512)
+            mm(a("pa", np_=8), a("g8"), a(on))
+            act(a("ysb", np_=8), a("pa", np_=8), AF.Copy)
+            dma("s", "ld6", [(T.yseat[:], a("ysb", np_=8))])
+        if t == 0:
+            act(a(l2), a("xg", ind=a("lav")), AF.Copy)
+        act(a(xn, 576, XW), a(l2), AF.Copy)
+        ts(a("vi"), a(l1, 0, 32), float(B0), None, OP.subtract)
+        cp(a("sf"), a(l1, 32, 64))
+        ts(a("val"), a(l1, 0, 32), c(CJ), None, OP.is_ge)
+        ts(a("vj"), a("vi"), 511, None, OP.bitwise_and)
+        ts(a("khi"), a("ph", 0, 32), BIG, None, OP.add)
+        ts(a("kh"), a("khi"), 4095, None, OP.bitwise_and)
+        tt(a("hp"), a("kh"), a("sf"), OP.mult)
+        ts(a("hs"), a("hp"), 5, 8191, OP.logical_shift_right, OP.bitwise_and)
+        ts(a("hw"), a("hs"), c(CT0 + t), None, OP.add)
+        tt(a("lt2"), a("dicx", ind=a("hw")), a("xv"), OP.is_gt)
+        conv(a("pm", 0, 32), "zo", "lt2", 0, 512)
+        ts(a("vk"), a("vj"), float(B0), None, OP.add)
+        if last:
+            ts(a("olf"), a("pn", 0, 32), 32.0, None, OP.add)
+        tt(a("vp"), a("vk"), a("val"), OP.mult)
+        if last:
+            cp(a("olu"), a("olf"))
+            tt(a("awo"), a("aw"), a("olf"), OP.mult)
+        ts(a("ps2"), a("pm", 0, 32), 7.5, None, OP.is_le)
+        mm(a("ph", 0, 32), a("tri"), a("ps2"))
+        ts(a("fi"), a("ph", 0, 32), 0.5, None, OP.is_ge)
+        tt(a("fv"), a("fi"), a("vp"), OP.mult)
+        mm(a("pm", 0, 32), a("blkb"), a("fv"))
+        if last:
+            mm(a("pp", 64, 96), a("blkb"), a("awo"))
+        tt(a("dm"), a("pm", 0, 32), a("dg"), OP.mult)
+        tt(a("cbm", 0, 32), a("pm", 0, 32), a("tm", 0, 32), OP.mult)
+        for h in (0, 1):
+            red(a("cl", h, h + 1), a("dm", 16 * h, 16 * h + 16), OP.max)
+        tt(a("cbm", 32, 64), a("pm", 0, 32), a("tm", 32, 64), OP.mult)
+        for h in (0, 1):
+            ts(a("eq", 32 * h, 32 * h + 32), a("cbm", 32 * h, 32 * h + 32), a("cl", h, h + 1), c(CHI0 + h), OP.is_equal, OP.mult)
+        for h in (0, 1):
+            red(a("cf", h, h + 1), a("eq", 32 * h, 32 * h + 32), OP.max)
+        for h in (0, 1):
+            ts(a("tgt", h, h + 1), a("cf", h, h + 1), a("cl", h, h + 1), None, OP.max)
+        cp(a(m3), a(xn, ind=a("tgt")))
+        send(a(m3), a(l3), "a3_%d" % t, guest)
+        cp(a(xn, ind=a("tgt")), a(l2))
+        if not last:
+            cp(a(xn, ind=a("avl")), a(l3))
+        else:
+            tt(a("dm"), a("pp", 64, 96), a("dg"), OP.mult)
+            cp(a("ypb", ind=a("olu")), a(xn, B0, B0 + 512))
+            for h in (0, 1):
+                red(a("avf", h, h + 1), a("dm", 16 * h, 16 * h + 16), OP.max)
+            for h in (0, 1):
+                ts(a("avo", h, h + 1), a("avf", h, h + 1), c(CH[h]), None, OP.max)
+            cp(a("ypb", ind=a("avo")), a(l3))
+            dma("y", "ld7", [(T.ypup[:], a("ypb", 32, 544))])
+    for s in sorted(count):
+        if s != "ld7":
+            g.wait_ge(T.sem[s], count[s])
+    g.wait_ge(T.sem.ld7, 16)

@@ -4,9 +4,11 @@ RO = 4
 NS = 7
 NS0 = 6
 B0 = 48
+LAGV, LAGS = 0.2, 0.0
 XW = 608
 DW = 8800
 TE, TC = 0, 768
+TX = 3072
 WDT = "float16"
 
 F, I, U, H = "float32", "int32", "uint16", "bfloat16"
@@ -15,9 +17,10 @@ SB = {
     "x0": (XW, H), "x1": (XW, H), "o0": (512, H), "o1": (512, H), "oio": (512, H), "x2": (752, H), "x2l": (48, U),
     "lt": (17 * 1024, H), "d0": (512, H), "d1": (512, H), "d2": (512, H),
     "ksi": (48, I), "ks": (48, I), "prod": (512, I), "prs": (512, I), "off": (512, U),
-    "pw": (512, H), "lns": (32, F), "nsi": (32, I), "roff": (64, U), "lnn": (32, F), "nni": (32, I),
+    "pw": (512, H), "lns": (32, F), "nsi": (32, I), "roff": (32, U), "rofs": (32, U), "lnn": (32, F), "nni": (32, I),
     "r32": (32, U), "nm": (32, F), "pz": (16, F), "pe": (16, F), "pu": (16, F), "pv": (16, F),
-    "tt": (3072, F), "cc": (768, F), "ch": (34 * 16, U),
+    "pw0": (256, H), "pw1": (256, H), "ln2": (32, F), "neg": (256, H), "zo2": (144, H),
+    "tt": (5376, F), "mc": (64, H), "cc": (768, F), "ch": (34 * 16, U),
     "kni": (32, I), "kn": (32, I), "kn1": (32, F), "ksq": (32, I), "v0": (32, I), "v1": (32, F),
     "nt": (32, F), "nu": (32, F), "nl": (32, F), "aw": (32, F), "st": (32, F), "apk": (64, WDT), "awq": (32, WDT),
     "rf": (36, F), "rf2": (32, F), "yp": (32, I), "idx2": (32, U), "uu": (32, I), "e1": (32, F), "e2": (32, F),
@@ -25,13 +28,13 @@ SB = {
     "dm": (32, F), "avf": (4, F), "avl": (2, U), "avo": (2, U), "olf": (32, F), "olu": (32, U), "awo": (32, WDT),
     "xv": (512, H), "sf": (32, F), "val": (32, F), "vi": (32, I), "vj": (32, I), "vk": (32, F), "vp": (32, F),
     "khi": (32, I), "kh": (32, I), "hp": (32, I), "hs": (32, I), "hw": (32, U), "lt2": (512, H),
-    "ps2": (32, H), "fi": (32, F), "fv": (32, WDT), "cbm": (64, F), "eq": (64, F), "cl": (4, F), "cf": (4, F), "tgt": (2, U),
+    "ps2": (32, H), "fv": (48, WDT), "eq": (96, F), "cl": (4, F), "cf": (4, F), "tgt": (2, U),
     "xg": (B0 + 512, H), "lav": (2, U), "ypb": (544, H), "ysb": (512, F),
     "zo": (144, H), "zw": (144, WDT), "zm": (144, H), "idn": (128, H), "nid": (128, H), "tri": (128, H), "g8": (8, H),
     "dh": (128, H), "dl": (128, H), "ohi": (512, H), "olo": (512, H),
     "blk": (128, F), "r15": (128, F), "io": (144, F), "mg": (128, F), "i16": (32, F), "iv": (768, F),
     "ie": (256, F), "ia": (256, F), "t1": (256, F), "t2": (768, F), "t3": (768, F), "t4": (256, F), "blkb": (128, H),
-    "col": (32, F), "ci": (8, I), "q16": (32, F), "q32": (32, F), "qm1": (32, F), "dg": (32, F), "tm": (64, F),
+    "col": (32, F), "ci": (8, I), "q16": (32, F), "q32": (32, F), "qm1": (32, F), "dg": (32, F), "tm": (96, H), "dgm": (32, H), "vpm": (32, WDT),
 }
 for _t in range(RO):
     SB["m1_%d" % _t] = (64, U); SB["l1_%d" % _t] = (64, U)
@@ -52,7 +55,8 @@ SEMAPHORES = ["qv", "qs", "qp", "qg", "sent", "zf", "a0", "out0", "out1"] + ["ld
              ["a%d_%d" % (m, t) for m in (1, 2, 3) for t in range(RO)]
 CP, CK, CG, CK16, CG15, CW, CM, CTH, CJ, CY, CHI0, CHI1, CC1, CC3, CE, C15, CX, CZ0, CZ1, CS, CQ, CT0 = range(22)
 CQ0, CTH0, CJ1, CES, CZ2 = 26, 27, 28, 29, 30
-CK32, CKM, CL = 25, 31, CC3
+CK32, CL16, CL = 25, 31, CC3
+MAG = 1.5 * 2.0 ** 27
 CH = (CK, CK16, CK32)
 
 
@@ -220,9 +224,9 @@ def rank_program(g, core, T, topo):
     iota(a("iv"), [[1040, 16], [256, 3], [1, 16]], 0)
     iota(a("ie"), [[1, 16], [0, 16]], 0)
     iota(a("ia"), [[16, 16], [1, 16]], 1)
-    ex = a("tt", TC + 768, TC + 1536)
-    iota(ex, [[48, 16], [0, 3], [1, 16]], TC + 16)
-    op("g", [ex], [ex], lambda: g.affine_select(ap(ex), ap(ex), [[0, 16], [1, 3], [0, 16]], OP.is_ge, 0.0, -2, 0))
+    iota(a("tt", TC, TC + 1536), [[0, 1536]], 0)
+    for o in (768, 1536):
+        iota(a("tt", TX + o, TX + o + 768), [[48, 16], [0, 3], [1, 16]], TC + 16)
     for x in ("x0", "x1"):
         ms(a(x, 0, B0), -1.0)
         ms(a(x, B0 + 512, XW), -1.0)
@@ -250,7 +254,7 @@ def rank_program(g, core, T, topo):
     ts(c(CQ), c(CK), NS - 0.5, -8.5, OP.is_le, OP.mult)
     tt(a("t1", 48, 64), a("t1", 32, 48), a("dg", 0, 16), OP.mult)
     red(c(CM), a("t1", 48, 64), OP.add)
-    for j, (m, b) in {CK16: (1, 16), CJ: (1, B0), CJ1: (1, B0 - 1), CK32: (1, 32), CKM: (1, -16), CY: (1024, 1024), CHI0: (1, 576), CHI1: (1, 592), CC1: (-1024, 15360),
+    for j, (m, b) in {CK16: (1, 16), CJ: (1, B0), CJ1: (1, B0 - 1), CK32: (1, 32), CY: (1024, 1024), CHI0: (1, 576), CHI1: (1, 592), CC1: (-1024, 15360),
                       CT0: (37, 0), CT0 + 1: (37, 11), CT0 + 2: (37, 22), CT0 + 3: (37, 33)}.items():
         aff(c(j), c(CK), float(m), float(b))
     aff(c(CTH), c(CQ), 1.0, 7.5)
@@ -267,8 +271,6 @@ def rank_program(g, core, T, topo):
         aff(a("t2"), a("iv"), 1.0, c(CC1))
         aff(a("t3"), a("t2"), -65536.0, 2.0 ** 30)
         tt(a("cc"), a("t2"), a("t3"), OP.min)
-        op("g", [a("cc")], [a("cc")], lambda: g.affine_select(
-            ap(a("cc")), ap(a("cc")), [[0, 16], [-1, 3], [0, 16]], OP.is_ge, 0.0, 1, 0))
         iota(a("ohi"), [[16, 32], [0, 16]], 0)
         iota(a("olo"), [[0, 32], [1, 16]], 0)
         ts(c(CZ0), c(CK), 0.0, None, OP.is_equal)
@@ -276,7 +278,7 @@ def rank_program(g, core, T, topo):
         ts(c(CZ2), c(CK), 2.0, None, OP.is_equal)
         ts(a("blkb"), a("mg"), c(CG), None, OP.is_equal)
         ts(c(CES), c(CZ1), c(CZ2), 32.0, OP.add, OP.mult)
-        ts(c(CX), c(CZ2), 32.0, None, OP.mult)
+        ts(c(CX), c(CZ2), 32.0 + TX - TC, None, OP.mult)
         ts(c(CE), c(CES), TC / 32.0, c(CX), OP.mult, OP.add)
         aff(a("ie"), a("ie"), c(CES), c(CE))
         tt(a("tt", TE + 512, TE + 768), a("ie"), a("ia"), OP.add)
@@ -286,19 +288,27 @@ def rank_program(g, core, T, topo):
         tt(a("t4", 128, 256), a("idn"), a("t4", 0, 128), OP.subtract)
         ts(a("g8"), a("io", 0, 8), 16.0, c(CG), OP.mult, OP.is_equal)
         ts(a("r15"), a("blk"), c(C15), None, OP.mult)
-        tt(a("tri"), a("t4", 128, 256), a("blk"), OP.mult)
+        tt(a("t4", 0, 128), a("t4", 128, 256), a("blk"), OP.mult)
+        ts(a("tri"), a("t4", 0, 128), 1024.0, None, OP.mult)
         ts(a("q16"), a("io", 0, 32), 16.0, c(CJ), OP.mult, OP.add)
-        ts(a("tm", 0, 32), a("io", 0, 32), c(CK), None, OP.is_lt)
-        ts(a("tm", 32, 64), a("io", 0, 32), c(CK16), None, OP.is_lt)
+        ms(a("tm"), 0.0)
+        ts(a("fv"), a("io", 0, 48), 0.0, None, OP.mult)
+        ts(a("tm", 0, 32), a("io", 0, 32), c(CK), 2048.0, OP.is_ge, OP.mult)
+        ts(a("tm", 48, 80), a("io", 0, 32), c(CK16), 2048.0, OP.is_ge, OP.mult)
+        ts(a("dgm"), a("dg"), -2048.0, 2048.0, OP.mult, OP.add)
         ts(a("q32"), a("q16"), 32.0, None, OP.add)
         ts(a("qm1"), a("q16"), -1.0, None, OP.add)
         act(c(CQ), a("t1", 0, 1), AF.Ln)
         op("v", [c(CQ)], [c(CL)], lambda: g.vector.reciprocal(ap(c(CL)), ap(c(CQ))))
+        ms(a("neg"), -1.0)
+        ts(a("zo2"), a("zo"), 2.0, None, OP.mult)
+        ts(c(CL16), c(CL), 16.0, None, OP.mult)
         ms(a("rf", 0, 1), 0.0)
         cp(a("ch", 0, 1), c(CE))
         ms(a("ypb", 0, 32), 0.0)
-        aff(a("t2"), a("cc"), 1.0, 512.0)
-        tt(a("tt", TC + 1536, TC + 2304), a("t2"), ex, OP.max)
+        aff(a("tt", TC + 1536, TC + 2304), a("cc"), 1.0, 512.0)
+        ts(a("mc", 0, 32), a("io", 0, 32), 0.0, c(CJ1), OP.mult, OP.add)
+        ts(a("mc", 32, 64), a("io", 0, 32), 0.0, 2048.0, OP.mult, OP.add)
 
     def first_numbers():
         mm(a("pa"), a("dh"), a("ohi"), True, False)
@@ -318,7 +328,7 @@ def rank_program(g, core, T, topo):
             mm(a("pk", 0, 47), sel("zw", i), a(xo, B0 + 32 * i, B0 + 32 * i + 47), i == 0, i == 15)
         act(a("x2"), a(xo, ind=a("x2l", 0, 47)), AF.Copy)
         ts(a("ksi", 0, 47), a("pk", 0, 47), BIG, None, OP.add)
-        conv(a("pn", 0, 32), "zw", xo, B0, B0 + 512)
+        conv(a("pk", 64, 96), "zw", xo, B0, B0 + 512)
         ts(a("ks", 0, 47), a("ksi", 0, 47), 4095, None, OP.bitwise_and)
 
         def mults(js):
@@ -334,111 +344,127 @@ def rank_program(g, core, T, topo):
                 ts(a("off", 32 * j, 32 * j + 32), a("prs", 32 * j, 32 * j + 32), float((37 * j + 11 * t) % 16), None, OP.add)
 
         ch_ = [[0, 1], [2, 3, 4], [5, 6, 7, 8], [9, 10, 11, 12], [13, 14, 15]]
-        mults(ch_[0]); mults(ch_[1]); shift(ch_[0]); mults(ch_[2][:1]); adds(ch_[0]); shift(ch_[1]); mults(ch_[2][1:])
-        adds(ch_[1]); shift(ch_[2]); mults(ch_[3]); adds(ch_[2]); shift(ch_[3]); mults(ch_[4]); adds(ch_[3]); shift(ch_[4])
-        ts(a("kni"), a("pn", 0, 32), BIG, None, OP.add)
+        mults(ch_[0]); mults(ch_[1][:2]); shift(ch_[0]); mults(ch_[1][2:]); mults(ch_[2][:1]); adds(ch_[0]); shift(ch_[1])
+        mults(ch_[2][1:]); adds(ch_[1]); shift(ch_[2]); mults(ch_[3]); adds(ch_[2]); shift(ch_[3]); mults(ch_[4])
+        adds(ch_[3][:2]); shift(ch_[4]); adds(ch_[3][2:])
         adds(ch_[4])
         if t == 0:
             later_constants()
             wait("g", "ld3", 16); wait("g", "ld4", 16)
             send(a(xo, 0, B0 + 512), a("xg"), "a0", host, "out0")
             landed("xg", "a0", guest)
+            iota(a("tt", TX, TX + 768), [[0, 768]], 0)
 
-        def word(j):
+        def word(j, lo=0, hi=32):
             ws = (37 * j + 11 * t) // 16 * 16
-            return a("dicx", ws, ws + 8208, ind=a("off", 32 * j, 32 * j + 32))
+            return a("dicx", ws, ws + 8208, ind=a("off", 32 * j + lo, 32 * j + hi))
 
-        def ltj(j):
-            return a("lt", 1024 * (15 - j), 1024 * (15 - j) + 512)
+        def ltj(j, lo=0, hi=512):
+            return a("lt", 1024 * (15 - j) + lo, 1024 * (15 - j) + hi)
 
         ev = []
         ns = NS0 if t == 0 else NS
         tv, tsc = (0.0 if t == 0 else 1.7), 0.0
+        half = ns - 1
+        ev.append((tv, "vh", half)); tv += 0.38
         for j in range(ns, 16):
-            ev.append((tv, "vg", j)); tv += 0.72; ev.append((tv + 0.6, "cnt", j))
+            ev.append((tv, "vg", j)); tv += 0.72; ev.append((tv + LAGV, "cnt", j))
         for j in range(ns + 1):
             if j < ns:
                 ev.append((tsc, "sg", j)); tsc += 0.73; ev.append((tsc, "sub", j))
             if j > 0:
-                ev.append((tsc + 0.001, "sign", j - 1)); tsc += 0.48; ev.append((tsc + 0.3, "cnt", j - 1))
+                ev.append((tsc + 0.001, "sign", j - 1)); tsc += 0.48; ev.append((tsc + LAGS, "cnt", j - 1))
         ev.sort()
         ncnt = [0]
-        extra = [
-            lambda: ts(a("kn"), a("kni"), 4095, None, OP.bitwise_and),
-            lambda: (ts(a("kn1"), a("kn"), -2048.0, None, OP.add), tt(a("ksq"), a("kn"), a("kn"), OP.mult)),
-            lambda: ts(a("v0"), a("ksq"), 5, 511, OP.logical_shift_right, OP.bitwise_and),
-            lambda: ts(a("v1"), a("v0"), 1.0, None, OP.add),
-        ]
         for _, kind, j in ev:
-            d, bank = a("d%d" % (j % 3)), a("pa" if j % 2 == 0 else "pb")
+            n = 256 if j == half else 512
+            d, bank = a("d%d" % (j % 3), 0, n), a("pa" if j % 2 == 0 else "pb", 0, n)
             if kind == "vg":
                 tt(ltj(j), word(j), a("x2", 16 * j, 16 * j + 512), OP.is_gt)
-                if extra:
-                    extra.pop(0)()
+            elif kind == "vh":
+                tt(ltj(j, 256, 512), word(j, 16, 32), a("x2", 16 * j + 256, 16 * j + 512), OP.is_gt)
             elif kind == "sg":
-                act(d, word(j), AF.Copy)
+                act(d, word(j, 0, n // 16), AF.Copy)
             elif kind == "sub":
                 mm(bank, a("idn"), d, True, False)
-                mm(bank, a("nid"), a("x2", 16 * j, 16 * j + 512), False, True)
+                mm(bank, a("nid"), a("x2", 16 * j, 16 * j + n), False, True)
+                if j == half - 1:
+                    mm(a("pc", 256, 512), sel("zo2", half), ltj(half, 256, 512), False, False)
+                    mm(a("pc", 256, 512), sel("zo", half), a("neg"), False, False)
             elif kind == "sign":
-                act(ltj(j), bank, AF.Sign, -0.5)
+                act(ltj(j, 0, n), bank, AF.Sign, -0.5)
+            elif j == half:
+                mm(a("pc", 0, 256), sel("zo", j), ltj(j, 0, 256), False, ncnt[0] == 15)
+                ncnt[0] += 1
             else:
                 mm(a("pc"), sel("zo", j), ltj(j), ncnt[0] == 0, ncnt[0] == 15)
                 ncnt[0] += 1
+        for e in (0, 1):
+            ts(a("pw%d" % e), a("pc", e, 512, 2), c(CTH0 if t == 0 else CTH), None, OP.is_le)
+        for i in list(range(0, 16, 2)) + list(range(1, 16, 2)):
+            mm(a("pm", 0, 32), sel("zm", i), a("pw%d" % (i % 2), i // 2, 256, 8), i == 0, i == 15)
+        act(a("ln2"), a("pm", 0, 32), AF.Ln, 4.0 ** -0.1, 4.0 ** -0.1)
+        act(a("lns"), a("pm", 0, 32), AF.Ln, 4.0 ** -16)
         ts(a("pw"), a("pc"), c(CTH0 if t == 0 else CTH), None, OP.is_le)
-        conv(a("pm", 0, 32), "zm", "pw", 0, 512)
         for h in (0, 1):
             for k in range(16):
                 mm(a("pn", 16 * h, 16 * h + 16), sel("zm", k), a("pw", 256 * h + 16 * k, 256 * h + 16 * k + 16), k == 0, k == 15)
-        act(a("lns"), a("pm", 0, 32), AF.Ln, 4.0 ** -16)
+        ts(a("nm"), a("ln2"), c(CL16), MAG + 240.0, OP.mult, OP.add)
+        ts(a("pz"), a("ln2", 0, 32, 2), 20.1, -1024.0, OP.is_lt, OP.mult)
+        ts(a("pe"), a("ln2", 0, 32, 2), c(CL16), MAG + 224.0, OP.mult, OP.add)
         ts(a("nsi"), a("lns"), c(CL), 15.1, OP.mult, OP.add)
-        ts(a("nm"), a("nsi"), 15.0, 16.0, OP.min, OP.mult)
-        ts(a("pz"), a("nsi", 0, 32, 2), -1000.0, 16.0, OP.mult, OP.add)
-        for h in (0, 1, 2):
-            ts(a("roff", h, 64, 4), a("nsi", 16 * (h % 2), 16 * (h % 2) + 16), 48.0, c(CH[h]), OP.mult, OP.add)
-            if h == 0:
-                tt(a("pu"), a("pz"), a("nm", 1, 32, 2), OP.add)
-                ts(a("r32", 1, 32, 2), a("nm", 1, 32, 2), c(CK), None, OP.add)
-            if h == 1:
-                tt(a("pv"), a("pu"), a("nm", 0, 32, 2), OP.max)
-        ts(a("r32", 0, 32, 2), a("pv"), c(CKM), None, OP.add)
-        extra = {
-            13: lambda: act(a("lnn", 0, 32, 2), a("pn", 0, 16), AF.Ln, 4.0 ** -16),
-            12: lambda: act(a("lnn", 1, 32, 2), a("pn", 16, 32), AF.Ln, 4.0 ** -16),
-            9: lambda: ts(a("nni"), a("lnn"), c(CL), 16.1, OP.mult, OP.add),
-            7: lambda: ts(a("nt"), a("nni"), 20.0, None, OP.is_ge),
-            5: lambda: tt(a("nu"), a("nt"), a("q32"), OP.mult),
-            4: lambda: tt(a("nl"), a("nni"), a("nu"), OP.subtract),
-        }
+        tt(a("pu"), a("pz"), a("nm", 1, 32, 2), OP.add)
+        ts(a("r32", 1, 32, 2), a("nm", 1, 32, 2), MAG, c(CK), OP.subtract, OP.add)
+        ts(a("roff", 0, 32, 2), a("nsi", 0, 16), 48.0, c(CK), OP.mult, OP.add)
+        tt(a("pv"), a("pu"), a("pe"), OP.max)
+        ts(a("rofs", 0, 32, 2), a("nsi", 0, 16), 48.0, c(CK32), OP.mult, OP.add)
+        ts(a("roff", 1, 32, 2), a("nsi", 16, 32), 48.0, c(CK16), OP.mult, OP.add)
+        ts(a("r32", 0, 32, 2), a("pv"), MAG, c(CK), OP.subtract, OP.add)
+        extra = [
+            lambda: ts(a("kni"), a("pk", 64, 96), BIG, None, OP.add),
+            lambda: ts(a("nni"), a("lnn"), c(CL), 16.1, OP.mult, OP.add),
+            lambda: ts(a("kn"), a("kni"), 4095, None, OP.bitwise_and),
+            lambda: ts(a("nt"), a("nni"), 20.0, None, OP.is_ge),
+            lambda: tt(a("ksq"), a("kn"), a("kn"), OP.mult),
+            lambda: ts(a("kn1"), a("kn"), -2048.0, None, OP.add),
+            lambda: ts(a("v0"), a("ksq"), 5, 511, OP.logical_shift_right, OP.bitwise_and),
+            lambda: tt(a("nu"), a("nt"), a("q32"), OP.mult),
+            lambda: ts(a("v1"), a("v0"), 1.0, None, OP.add),
+            lambda: tt(a("nl"), a("nni"), a("nu"), OP.subtract),
+        ]
         if t == 0:
-            extra[3] = lambda: ts(a("dh"), a("idn"), c(CZ0), None, OP.mult)
-            extra[2] = lambda: ts(a("dl"), a("idn"), c(CZ1), None, OP.mult)
+            ts(a("dh"), a("idn"), c(CZ0), None, OP.mult)
+            ts(a("dl"), a("idn"), c(CZ1), None, OP.mult)
         for k in range(15, -1, -1):
+            w = TX + 48 * (k + 1)
+            act(a("tt", w - 16, w), a("tt", w, w + 1536, ind=a("rofs", 2 * k, 2 * k + 1)), AF.Copy)
             w = TE + 32 * (k + 1)
-            act(a("tt", w - 32, w), a("tt", w, w + 256, ind=a("r32", 2 * k, 2 * k + 2)), AF.Copy)
+            cp(a("tt", w - 32, w), a("tt", w, w + 256, ind=a("r32", 2 * k, 2 * k + 2)))
             w = TC + 48 * (k + 1)
-            tt(a("tt", w - 48, w), a("tt", w, w + 1536, ind=a("roff", 4 * k, 4 * k + 3)), a("cc", 48 * k, 48 * k + 48), OP.max)
-            if k in extra:
-                extra[k]()
+            tt(a("tt", w - 48, w - 16), a("tt", w, w + 1536, ind=a("roff", 2 * k, 2 * k + 2)), a("cc", 48 * k, 48 * k + 32), OP.max)
+            if k in (13, 12):
+                act(a("lnn", k % 2, 32, 2), a("pn", 16 * (k % 2), 16 * (k % 2) + 16), AF.Ln, 4.0 ** -16)
         if t == 0:
             first_numbers()
+        mm(a("ph", 0, 64), a("idn"), a("mc"), True, False)
         for i in range(17):
             if i < 16:
                 o = 32 * i - 16 if i else 0
-                cp(a("ch", 32 * i + 16, 32 * i + 32), a("tt", 0, TC + 768, ind=a("ch", o, o + 1)))
+                cp(a("ch", 32 * i + 16, 32 * i + 32), a("tt", 0, TX + 768, ind=a("ch", o, o + 1)))
             if i > 0:
-                cp(a("ch", 32 * i, 32 * i + 16), a("tt", 0, TC + 768, ind=a("ch", 32 * i - 14, 32 * i - 13)))
+                cp(a("ch", 32 * i, 32 * i + 16), a("tt", 0, TX + 768, ind=a("ch", 32 * i - 14, 32 * i - 13)))
+            if extra:
+                extra.pop(0)()
         A = a("ch", 17, 33 * 16, 16)
         ts(a("aw"), A, 15872.0, None, OP.is_ge)
         cp(a("rf", 1, 33), A)
         tt(a("apk", 0, 32), a("aw"), a("v1"), OP.mult)
         tt(a("apk", 32, 64), a("aw"), a("kn1"), OP.mult)
+        mm(a("ph", 0, 64), a("blkb"), a("apk"), False, True)
         mm(a("pp", 0, 32), a("r15"), a("rf", 0, 32))
-        mm(a("ph", 0, 64), a("blkb"), a("apk"))
         ts(a("rf2"), A, c(CY), None, OP.add)
         ts(a("st"), A, 15360.0, None, OP.is_ge)
-        ts(a(m1, 0, 32), a("ph", 0, 32), c(CJ1), None, OP.add)
-        ts(a(m1, 32, 64), a("ph", 32, 64), 2048.0, None, OP.add)
+        cp(a(m1), a("ph", 0, 64))
         send(a(m1), a(l1), "a1_%d" % t, host)
         tt(a("yp"), a("pp", 0, 32), a("rf2"), OP.max)
         ts(a("idx2"), a("yp"), c(CY), None, OP.subtract)
@@ -484,35 +510,37 @@ def rank_program(g, core, T, topo):
         ts(a("val"), a(l1, 0, 32), c(CJ), None, OP.is_ge)
         ts(a("vj"), a("vi"), 511, None, OP.bitwise_and)
         ts(a("khi"), a("ph", 0, 32), BIG, None, OP.add)
+        ts(a("vk"), a("vj"), float(B0), None, OP.add)
         ts(a("kh"), a("khi"), 4095, None, OP.bitwise_and)
+        tt(a("vp"), a("vk"), a("val"), OP.mult)
         tt(a("hp"), a("kh"), a("sf"), OP.mult)
+        ts(a("vpm"), a("vp"), -1024.0, None, OP.add)
         ts(a("hs"), a("hp"), 5, 8191, OP.logical_shift_right, OP.bitwise_and)
         ts(a("hw"), a("hs"), c(CT0 + t), None, OP.add)
+        mm(a("ph", 0, 32), a("idn"), a("vpm"), True, False)
+        mm(a("pc", 0, 32), a("idn"), a("dgm"), True, False)
+        mm(a("pa", 0, 33), a("idn"), a("tm", 0, 33), True, False)
+        mm(a("pb", 0, 33), a("idn"), a("tm", 48, 81), True, False)
         tt(a("lt2"), a("dicx", ind=a("hw")), a("xv"), OP.is_gt)
         conv(a("pm", 0, 32), "zo", "lt2", 0, 512)
-        ts(a("vk"), a("vj"), float(B0), None, OP.add)
         if last:
             ts(a("olf"), a("pn", 0, 32), 32.0, None, OP.add)
-        tt(a("vp"), a("vk"), a("val"), OP.mult)
-        if last:
             cp(a("olu"), a("olf"))
             tt(a("awo"), a("aw"), a("olf"), OP.mult)
         ts(a("ps2"), a("pm", 0, 32), 7.5, None, OP.is_le)
-        mm(a("ph", 0, 32), a("tri"), a("ps2"))
-        ts(a("fi"), a("ph", 0, 32), 0.5, None, OP.is_ge)
-        tt(a("fv"), a("fi"), a("vp"), OP.mult)
-        mm(a("pm", 0, 32), a("blkb"), a("fv"))
+        mm(a("ph", 0, 32), a("tri"), a("ps2"), False, True)
+        ts(a("fv", 0, 32), a("ph", 0, 32), 0.0, None, OP.max)
+        mm(a("pc", 0, 32), a("blkb"), a("fv", 0, 32), False, True)
+        mm(a("pa", 0, 33), a("blkb"), a("fv", 0, 33), False, True)
+        mm(a("pb", 0, 33), a("blkb"), a("fv", 0, 33), False, True)
         if last:
             mm(a("pp", 64, 96), a("blkb"), a("awo"))
-        tt(a("dm"), a("pm", 0, 32), a("dg"), OP.mult)
-        tt(a("cbm", 0, 32), a("pm", 0, 32), a("tm", 0, 32), OP.mult)
         for h in (0, 1):
-            red(a("cl", h, h + 1), a("dm", 16 * h, 16 * h + 16), OP.max)
-        tt(a("cbm", 32, 64), a("pm", 0, 32), a("tm", 32, 64), OP.mult)
+            red(a("cl", h, h + 1), a("pc", 16 * h, 16 * h + 16), OP.min)
         for h in (0, 1):
-            ts(a("eq", 32 * h, 32 * h + 32), a("cbm", 32 * h, 32 * h + 32), a("cl", h, h + 1), c(CHI0 + h), OP.is_equal, OP.mult)
+            ts(a("eq", 48 * h, 48 * h + 33), a("pb" if h else "pa", 0, 33), a("cl", h, h + 1), c(CHI0 + h), OP.is_equal, OP.mult)
         for h in (0, 1):
-            red(a("cf", h, h + 1), a("eq", 32 * h, 32 * h + 32), OP.max)
+            red(a("cf", h, h + 1), a("eq", 48 * h, 48 * h + 33), OP.max)
         for h in (0, 1):
             ts(a("tgt", h, h + 1), a("cf", h, h + 1), a("cl", h, h + 1), None, OP.max)
         cp(a(m3), a(xn, ind=a("tgt")))

@@ -1,3 +1,4 @@
+import math
 from concourse.mybir import AluOpType as OP, AxisListType as AX, ActivationFunctionType as AF
 
 RO = 4
@@ -5,36 +6,40 @@ NS = 7
 NS0 = 6
 B0 = 48
 LAGV, LAGS = 0.2, 0.0
-XW = 608
+QAT = 5
+XW = 576
 DW = 8800
-TE, TC = 0, 768
-TX = 3072
+RW = 3072
+E2, C2 = 768, 1536
+ZC = 8192
 WDT = "float16"
 
 F, I, U, H = "float32", "int32", "uint16", "bfloat16"
 SB = {
     "dicx": (DW, H), "pupb": (512, H), "seatb": (32, I), "wtb": (4, I), "seatu": (32, U),
     "x0": (XW, H), "x1": (XW, H), "o0": (512, H), "o1": (512, H), "oio": (512, H), "x2": (752, H), "x2l": (48, U),
-    "lt": (17 * 1024, H), "d0": (512, H), "d1": (512, H), "d2": (512, H),
+    "lt": (ZC + 16, H), "d0": (512, H), "d1": (512, H), "d2": (512, H),
     "ksi": (48, I), "ks": (48, I), "prod": (512, I), "prs": (512, I), "off": (512, U),
-    "pw": (512, H), "lns": (32, F), "nsi": (32, I), "roff": (32, U), "rofs": (32, U), "lnn": (32, F), "nni": (32, I),
-    "r32": (32, U), "nm": (32, F), "pz": (16, F), "pe": (16, F), "pu": (16, F), "pv": (16, F),
-    "pw0": (256, H), "pw1": (256, H), "ln2": (32, F), "neg": (256, H), "zo2": (144, H),
-    "tt": (5376, F), "mc": (64, H), "cc": (768, F), "ch": (34 * 16, U),
-    "kni": (32, I), "kn": (32, I), "kn1": (32, F), "ksq": (32, I), "v0": (32, I), "v1": (32, F),
-    "nt": (32, F), "nu": (32, F), "nl": (32, F), "aw": (32, F), "st": (32, F), "apk": (64, WDT), "awq": (32, WDT),
-    "rf": (36, F), "rf2": (32, F), "yp": (32, I), "idx2": (32, U), "uu": (32, I), "e1": (32, F), "e2": (32, F),
-    "srcf": (32, F), "src": (32, U), "srof": (32, F), "sro": (32, U), "g2": (512, H),
+    "pw": (512, H), "lns": (32, F), "nsi": (32, I), "roff": (32, U), "rof2": (32, U), "lnn": (32, F), "nni": (32, I),
+    "r32": (32, U), "pw0": (256, H), "pw1": (256, H), "ln2": (48, F), "neg": (256, H), "zo2": (144, H),
+    "pq": (112, F), "dq": (64, F), "zq": (32, F), "wq": (32, F), "tq": (48, F), "sq": (128, F), "st1": (32, F), "st2": (32, F),
+    "rq": (128, F), "sc": (128, F), "sd": (128, F), "n15": (32, F), "a15": (32, F), "n2": (32, F), "thn": (32, F),
+    "ex": (RW, F), "eb": (768, H), "cd": (RW, F), "cc": (512, F), "ce": (256, F), "le2": (8, U), "ch": (40, U), "w": (272, F),
+    "mc": (64, H), "kni": (32, I), "kn": (32, I), "kn1": (32, F), "ksq": (32, I), "v0": (32, I), "v1": (32, F),
+    "nt": (32, F), "nu": (32, F), "nl": (36, F), "aw": (32, F), "st": (36, F), "apk": (64, WDT), "awq": (32, WDT),
+    "yp": (36, F), "idx2": (34, U), "uu": (36, F), "e1": (36, F), "e2": (36, F),
+    "srcf": (36, F), "src": (34, U), "srof": (32, F), "sro": (32, U), "g2": (528, H),
     "dm": (32, F), "avf": (4, F), "avl": (2, U), "avo": (2, U), "olf": (32, F), "olu": (32, U), "awo": (32, WDT),
-    "xv": (512, H), "sf": (32, F), "val": (32, F), "vi": (32, I), "vj": (32, I), "vk": (32, F), "vp": (32, F),
+    "xv": (512, H), "sf": (32, F), "vb": (32, F), "vd": (32, F), "vh": (4, F), "vt": (32, F), "cs": (32, F),
     "khi": (32, I), "kh": (32, I), "hp": (32, I), "hs": (32, I), "hw": (32, U), "lt2": (512, H),
-    "ps2": (32, H), "fv": (48, WDT), "eq": (96, F), "cl": (4, F), "cf": (4, F), "tgt": (2, U),
+    "exd": (96, WDT), "exo": (224, WDT), "cf": (4, F), "tgt": (2, U), "tgf": (4, F), "tgw": (4, F), "tgc": (4, F), "tg2": (2, U),
     "xg": (B0 + 512, H), "lav": (2, U), "ypb": (544, H), "ysb": (512, F),
-    "zo": (144, H), "zw": (144, WDT), "zm": (144, H), "idn": (128, H), "nid": (128, H), "tri": (128, H), "g8": (8, H),
-    "dh": (128, H), "dl": (128, H), "ohi": (512, H), "olo": (512, H),
-    "blk": (128, F), "r15": (128, F), "io": (144, F), "mg": (128, F), "i16": (32, F), "iv": (768, F),
-    "ie": (256, F), "ia": (256, F), "t1": (256, F), "t2": (768, F), "t3": (768, F), "t4": (256, F), "blkb": (128, H),
-    "col": (32, F), "ci": (8, I), "q16": (32, F), "q32": (32, F), "qm1": (32, F), "dg": (32, F), "tm": (96, H), "dgm": (32, H), "vpm": (32, WDT),
+    "zo": (144, H), "zw": (144, WDT), "zm": (144, H), "zr": (144, H), "zk": (144, H), "idn": (128, H), "nid": (128, H),
+    "nidk": (128, H), "blkb": (128, H), "blkk": (128, H), "g8": (8, H), "dh": (128, H), "dl": (128, H), "ohi": (512, H), "olo": (512, H),
+    "io": (144, F), "mg": (128, F), "i16": (48, F), "i8": (32, F), "b32": (32, F),
+    "ie": (256, F), "ia": (256, F), "ic": (256, F), "t1": (256, F), "t2": (256, F), "t3": (256, F),
+    "col": (48, F), "ci": (8, I), "q16": (36, F), "qm1": (36, F), "dg": (48, F), "dg2": (32, F), "one": (112, WDT),
+    "tm": (232, H), "k7": (32, H), "nio": (16, F),
 }
 for _t in range(RO):
     SB["m1_%d" % _t] = (64, U); SB["l1_%d" % _t] = (64, U)
@@ -51,13 +56,13 @@ for _k, (_w, _d) in SB.items():
         SCRATCH["b_pool" + _d] = ("sbuf", [128, _o + (_w + 15) // 16 * 16], _d)
         HOME[_k] = ("pool" + _d, _o)
 SCRATCH.update({("b_" + k): ("psum", [128, 512], F) for k in PS})
-SEMAPHORES = ["qv", "qs", "qp", "qg", "sent", "zf", "a0", "out0", "out1"] + ["ld%d" % i for i in range(8)] + \
+SEMAPHORES = ["qv", "qs", "qp", "qg", "sent", "a0", "out0", "out1"] + ["ld%d" % i for i in range(8)] + \
              ["a%d_%d" % (m, t) for m in (1, 2, 3) for t in range(RO)]
-CP, CK, CG, CK16, CG15, CW, CM, CTH, CJ, CY, CHI0, CHI1, CC1, CC3, CE, C15, CX, CZ0, CZ1, CS, CQ, CT0 = range(22)
-CQ0, CTH0, CJ1, CES, CZ2 = 26, 27, 28, 29, 30
-CK32, CL16, CL = 25, 31, CC3
-MAG = 1.5 * 2.0 ** 27
-CH = (CK, CK16, CK32)
+(CP, CK, CG, CK16, CG15, CW, CM, CTH, CJ, CX, CS, CQ, CQ0, CTH0, CV, CZ0, CZ1, CA, CB, CD, CL, CL0, C34, CE, CY, CZ, CH0, CH1,
+ CT0) = range(29)
+MAG = 1.5 * 2.0 ** 23
+CH = (CK, CK16)
+NONE = 4096.0
 
 
 def a(name, lo=0, hi=None, step=1, ind=None, np_=128):
@@ -68,6 +73,13 @@ def a(name, lo=0, hi=None, step=1, ind=None, np_=128):
 
 def c(j):
     return a("col", j, j + 1)
+
+
+def bits(x):
+    lo, hi, step = x[1], x[2], x[3]
+    if step == 1:
+        return ((1 << (hi - lo)) - 1) << lo
+    return sum(1 << j for j in range(lo, hi, step))
 
 
 def rank_program(g, core, T, topo):
@@ -105,18 +117,18 @@ def rank_program(g, core, T, topo):
         for w, xs in ((False, rd), (True, wr)):
             for x in xs:
                 if isinstance(x, tuple):
-                    use.append((x[0], x[1], x[2], w))
+                    use.append((x[0], bits(x), w))
                     if x[4] is not None:
-                        use.append((x[4][0], x[4][1], x[4][2], False))
+                        use.append((x[4][0], bits(x[4]), False))
         need = {}
-        for name, lo, hi, w in use:
-            for (l2, h2, w2, q2, s2, v2) in acc.get(name, []):
+        for name, m, w in use:
+            for (m2, w2, q2, s2, v2) in acc.get(name, []):
                 if name in PS and q2 != q:
                     hit = True
                 elif name in PS and q == "p":
                     hit = False
                 else:
-                    hit = (w or w2) and l2 < hi and lo < h2
+                    hit = (w or w2) and (m & m2) != 0
                 if hit and need.get(s2, 0) < v2:
                     need[s2] = v2
         for s2 in sorted(need, key=lambda s: s == qsem.get(q)):
@@ -127,15 +139,15 @@ def rank_program(g, core, T, topo):
         sn = dict(known[q]) if q in known else {}
         sn[s] = v
         snap[(s, v)] = sn
-        for name, lo, hi, w in use:
+        for name, m, w in use:
             lst = acc.setdefault(name, [])
             if name in PS:
-                lst[:] = [e for e in lst if e[3] == q]
+                lst[:] = [e for e in lst if e[2] == q]
             if w:
-                lst[:] = [e for e in lst if not (lo <= e[0] and e[1] <= hi)]
+                lst[:] = [e for e in lst if e[0] & ~m]
             else:
-                lst[:] = [e for e in lst if not (e[4] == s and not e[2] and lo <= e[0] and e[1] <= hi)]
-            lst.append((lo, hi, w, q, s, v))
+                lst[:] = [e for e in lst if not (e[3] == s and not e[1] and not e[0] & ~m)]
+            lst.append((m, w, q, s, v))
 
     def op(q, rd, wr, fn):
         use = order(q, rd, wr)
@@ -156,8 +168,11 @@ def rank_program(g, core, T, topo):
     def cp(o, i):
         op("v", [i], [o], lambda: g.vector.tensor_copy(ap(o), ap(i)))
 
-    def red(o, i, o0):
-        op("v", [i], [o], lambda: g.vector.tensor_reduce(ap(o), ap(i), AX.X, o0))
+    def red(o, i, o0, **kw):
+        op("v", [i], [o], lambda: g.vector.tensor_reduce(ap(o), ap(i), AX.X, o0, **kw))
+
+    def scan(o, d0, d1, first, o0, o1):
+        op("v", [d0, d1], [o], lambda: g.vector.tensor_tensor_scan(ap(o), ap(d0), ap(d1), first, o0, o1))
 
     def ms(o, v):
         op("v", [], [o], lambda: g.vector.memset(ap(o), v))
@@ -196,12 +211,12 @@ def rank_program(g, core, T, topo):
         g.remote_dma(ap(dst), ap(src), T.sem[s], T.sem[loc], pid, rid, topo.mask(core, d))
         count[loc] = count.get(loc, 0) + len(topo.engines(core, d))
         if loc != "sent":
-            note([(src[0], src[1], src[2], False)], "remote", loc, count[loc])
+            note([(src[0], bits(src), False)], "remote", loc, count[loc])
 
     def landed(dst, s, frm):
         n = len(topo.engines(T.cores[frm], core))
         count[s] = n
-        note([(dst, 0, SB[dst][0], True)], "remote", s, n)
+        note([(dst, bits(a(dst)), True)], "remote", s, n)
 
     def sel(z, i):
         return a(z, 15 - i, 143 - i)
@@ -209,6 +224,9 @@ def rank_program(g, core, T, topo):
     def conv(o, z, buf, lo, hi):
         for i in range(16):
             mm(o, sel(z, i), a(buf, lo + i, hi, 16), i == 0, i == 15)
+
+    def row(r):
+        return a("dg", r, r + 1)
 
     dma("y", "ld0", [(a("pupb"), T.pup[:])])
     dma("s", "ld1", [(a("seatb"), T.seat[:])])
@@ -220,25 +238,27 @@ def rank_program(g, core, T, topo):
     iota(a("ci", 0, 1), [[0, 1]], 0, 1)
     iota(a("io"), [[1, 144]], 0)
     iota(a("mg"), [[16, 8], [0, 16]], 0)
-    iota(a("i16"), [[0, 2], [1, 16]], 0)
-    iota(a("iv"), [[1040, 16], [256, 3], [1, 16]], 0)
-    iota(a("ie"), [[1, 16], [0, 16]], 0)
-    iota(a("ia"), [[16, 16], [1, 16]], 1)
-    iota(a("tt", TC, TC + 1536), [[0, 1536]], 0)
-    for o in (768, 1536):
-        iota(a("tt", TX + o, TX + o + 768), [[48, 16], [0, 3], [1, 16]], TC + 16)
+    iota(a("i16"), [[0, 3], [1, 16]], 0)
+    iota(a("b32"), [[256, 2], [1, 16]], 0)
+    iota(a("ie"), [[0, 16], [1, 16]], 0)
+    iota(a("ia"), [[1, 16], [0, 16]], 0)
+    iota(a("ic"), [[32, 16], [1, 16]], 16)
+    iota(a("i8"), [[1, 16], [0, 2]], 0)
+    iota(a("sq", 0, 32), [[0, 8], [1, 4]], int(MAG) - 3)
+    iota(a("st1"), [[0, 8], [1, 4]], int(MAG) - 1026)
+    iota(a("st2"), [[0, 8], [1, 4]], int(MAG) - 1025)
+    iota(a("eb", 512, 768), [[1, 256]], 1)
+    iota(a("cd", 512, 1024), [[0, 512]], -1)
     for x in ("x0", "x1"):
         ms(a(x, 0, B0), -1.0)
         ms(a(x, B0 + 512, XW), -1.0)
-    ms(a("lt", 16 * 1024, 17 * 1024), 0.0)
     cp(c(CP), a("ci", 0, 1))
     ts(a("ci", 1, 2), a("ci", 0, 1), 15, None, OP.bitwise_and)
     ts(a("ci", 2, 3), a("ci", 0, 1), 112, None, OP.bitwise_and)
-    ms(a("t1", 0, 16), 0.25)
+    ms(a("t1", 0, 16), math.exp(-1.0))
     ms(a("t1", 16, 32), 0.0)
     cp(a("col", CK, CG + 1), a("ci", 1, 3))
-    op("v", [a("t1", 0, 32)], [a("t1", 32, 48)], lambda: g.vector.tensor_tensor_scan(
-        ap(a("t1", 32, 48)), ap(a("t1", 0, 16)), ap(a("t1", 16, 32)), 4.0 ** 16, OP.mult, OP.add))
+    scan(a("t1", 32, 48), a("t1", 0, 16), a("t1", 16, 32), math.e, OP.mult, OP.add)
     ts(c(CG15), c(CG), 15.0, None, OP.add)
     ts(c(CS), c(CK), 32.0, float(B0), OP.mult, OP.add)
     ts(a("idn"), a("io", 0, 128), c(CP), None, OP.is_equal)
@@ -246,69 +266,120 @@ def rank_program(g, core, T, topo):
     ts(a("t1", 64, 112), a("io", 0, 48), c(CS), None, OP.add)
     ts(a("nid"), a("io", 0, 128), c(CP), -1.0, OP.is_equal, OP.mult)
     ts(a("t1", 112, 160), a("t1", 64, 112), B0 + 511.5, None, OP.is_le)
-    ts(a("t4", 0, 128), a("io", 0, 128), c(CP), None, OP.is_gt)
-    tt(a("t1", 160, 208), a("t1", 64, 112), a("t1", 112, 160), OP.mult)
-    ts(a("blk"), a("mg"), c(CG), None, OP.is_equal)
-    ts(a("x2l"), a("t1", 160, 208), 32.0, None, OP.max)
     ts(a("dg"), a("i16"), c(CK), None, OP.is_equal)
+    tt(a("t1", 160, 208), a("t1", 64, 112), a("t1", 112, 160), OP.mult)
     ts(c(CQ), c(CK), NS - 0.5, -8.5, OP.is_le, OP.mult)
+    ts(a("x2l"), a("t1", 160, 208), 32.0, None, OP.max)
     tt(a("t1", 48, 64), a("t1", 32, 48), a("dg", 0, 16), OP.mult)
-    red(c(CM), a("t1", 48, 64), OP.add)
-    for j, (m, b) in {CK16: (1, 16), CJ: (1, B0), CJ1: (1, B0 - 1), CK32: (1, 32), CY: (1024, 1024), CHI0: (1, 576), CHI1: (1, 592), CC1: (-1024, 15360),
-                      CT0: (37, 0), CT0 + 1: (37, 11), CT0 + 2: (37, 22), CT0 + 3: (37, 33)}.items():
-        aff(c(j), c(CK), float(m), float(b))
-    aff(c(CTH), c(CQ), 1.0, 7.5)
     ts(c(CQ0), c(CK), NS0 - 0.5, -8.5, OP.is_le, OP.mult)
-    aff(c(CTH0), c(CQ0), 1.0, 7.5)
+    red(c(CM), a("t1", 48, 64), OP.add)
     cp(a("seatu"), a("seatb"))
     ts(c(CX), a("wtb", 0, 1), 2048.0, -4096.0, OP.is_ge, OP.mult)
-    ts(a("zm"), a("zo"), c(CM), None, OP.mult)
     tt(c(CW), a("wtb", 0, 1), c(CX), OP.add)
     cp(a("x0", B0, B0 + 512), a("pupb", ind=a("seatu")))
     ts(a("zw"), a("zo"), c(CW), None, OP.mult)
 
+    def scalar_constants():
+        for j, (m, b) in {CK16: (1, 16), CJ: (1, B0), CV: (-1, B0 - 1), CH0: (2, 0), CH1: (2, 1),
+                          CT0: (-37, 555), CT0 + 1: (-37, 566), CT0 + 2: (-37, 577), CT0 + 3: (-37, 588)}.items():
+            aff(c(j), c(CK), float(m), float(b))
+        aff(c(CTH), c(CQ), 1.0, 7.5)
+        aff(c(CTH0), c(CQ0), 1.0, 7.5)
+        aff(c(CY), row(11), 1.0, row(12))
+        aff(c(C34), row(3), 1.0, row(4))
+        aff(c(CL), row(1), float(E2), 0.0)
+        aff(c(CZ), c(CY), 32.0, row(1))
+        aff(c(CB), row(1), 8.0, c(CY))
+        aff(c(CL), row(12), float(C2), c(CL))
+        aff(c(CA), row(0), 16.0, c(CZ))
+        aff(c(CB), row(0), 1.0, c(CB))
+        aff(c(CD), c(C34), 60000.0, c(CL))
+        aff(c(CL0), c(C34), 512.0, c(CL))
+        aff(c(CE), c(C34), -60000.0, 60000.0)
+        aff(c(CD), c(CB), 1.0, c(CD))
+        aff(c(CE), row(4), float(C2), c(CE))
+        aff(a("t2"), a("ia"), c(CA), c(CD))
+        aff(a("t3"), a("ie"), c(CB), 0.0)
+        aff(a("ce"), a("ic"), c(C34), c(CE))
+
     def later_constants():
-        aff(a("t2"), a("iv"), 1.0, c(CC1))
-        aff(a("t3"), a("t2"), -65536.0, 2.0 ** 30)
-        tt(a("cc"), a("t2"), a("t3"), OP.min)
-        iota(a("ohi"), [[16, 32], [0, 16]], 0)
-        iota(a("olo"), [[0, 32], [1, 16]], 0)
-        ts(c(CZ0), c(CK), 0.0, None, OP.is_equal)
-        ts(c(CZ1), c(CK), 1.0, None, OP.is_equal)
-        ts(c(CZ2), c(CK), 2.0, None, OP.is_equal)
-        ts(a("blkb"), a("mg"), c(CG), None, OP.is_equal)
-        ts(c(CES), c(CZ1), c(CZ2), 32.0, OP.add, OP.mult)
-        ts(c(CX), c(CZ2), 32.0 + TX - TC, None, OP.mult)
-        ts(c(CE), c(CES), TC / 32.0, c(CX), OP.mult, OP.add)
-        aff(a("ie"), a("ie"), c(CES), c(CE))
-        tt(a("tt", TE + 512, TE + 768), a("ie"), a("ia"), OP.add)
-        wait("y", "ld3", 16); wait("y", "ld4", 16); wait("y", "ld5", 16)
-        dma("y", "zf", [(a("lt", 1024 * j + 512, 1024 * j + 1024), a("lt", 16 * 1024, 16 * 1024 + 512)) for j in range(16)])
-        ts(c(C15), c(CK), 15.0, None, OP.is_equal)
-        tt(a("t4", 128, 256), a("idn"), a("t4", 0, 128), OP.subtract)
-        ts(a("g8"), a("io", 0, 8), 16.0, c(CG), OP.mult, OP.is_equal)
-        ts(a("r15"), a("blk"), c(C15), None, OP.mult)
-        tt(a("t4", 0, 128), a("t4", 128, 256), a("blk"), OP.mult)
-        ts(a("tri"), a("t4", 0, 128), 1024.0, None, OP.mult)
-        ts(a("q16"), a("io", 0, 32), 16.0, c(CJ), OP.mult, OP.add)
-        ms(a("tm"), 0.0)
-        ts(a("fv"), a("io", 0, 48), 0.0, None, OP.mult)
-        ts(a("tm", 0, 32), a("io", 0, 32), c(CK), 2048.0, OP.is_ge, OP.mult)
-        ts(a("tm", 48, 80), a("io", 0, 32), c(CK16), 2048.0, OP.is_ge, OP.mult)
-        ts(a("dgm"), a("dg"), -2048.0, 2048.0, OP.mult, OP.add)
-        ts(a("q32"), a("q16"), 32.0, None, OP.add)
-        ts(a("qm1"), a("q16"), -1.0, None, OP.add)
-        act(c(CQ), a("t1", 0, 1), AF.Ln)
-        op("v", [c(CQ)], [c(CL)], lambda: g.vector.reciprocal(ap(c(CL)), ap(c(CQ))))
-        ms(a("neg"), -1.0)
+        tt(a("ex", 512, 768), a("t2"), a("t3"), OP.add)
+        J, gt, eq, lt, u = [a("t1", 64 + 16 * n, 80 + 16 * n) for n in range(5)]
+        add, uns, add2, uns2, v = [a("t1", 144 + 16 * n, 160 + 16 * n) for n in range(5)]
+        k0 = a("io", 0, 16)
+        ts(J, k0, -1.0, c(CK), OP.mult, OP.add)
+        ts(v, k0, 16.0, 7680.0, OP.mult, OP.add)
+        ts(gt, J, 0.5, None, OP.is_ge)
+        ts(u, J, -512.0, None, OP.mult)
+        ts(eq, J, 0.0, float(ZC + 2), OP.is_equal, OP.mult)
+        ts(lt, J, -0.5, None, OP.is_le)
+        tt(u, u, v, OP.add)
+        ts(uns, gt, float(ZC + 1), -1.0, OP.mult, OP.add)
+        ts(uns2, lt, float(ZC + 1), -1.0, OP.mult, OP.add)
+        ts(v, u, 1.0, None, OP.add)
+        ts(u, u, -8191.0, None, OP.add)
+        tt(add, v, gt, OP.mult)
+        tt(add2, u, lt, OP.mult)
+        tt(uns, uns, eq, OP.add)
+        tt(add, add, eq, OP.add)
+        ts(add2, add2, -1.0, None, OP.add)
+        ts(eq, eq, 1.0 / (ZC + 2), None, OP.mult)
+        ts(add, add, -1.0, None, OP.add)
+        tt(uns, uns, eq, OP.add)
+        for k in range(15, -1, -1):
+            def col(x):
+                return a("t1", x[1] + k, x[1] + k + 1)
+            aff(a("cc", 32 * k, 32 * k + 32), a("b32"), col(gt), col(add))
+            aff(a("cd", 1024 + 32 * k, 1056 + 32 * k), a("b32"), 0.0, col(uns))
+            aff(a("cd", C2 + 512 + 32 * k, C2 + 544 + 32 * k), a("b32"), col(lt), col(add2))
+            aff(a("cd", C2 + 1024 + 32 * k, C2 + 1056 + 32 * k), a("b32"), 0.0, col(uns2))
+        ms(a("lt", ZC, ZC + 16), 0.0)
+        ts(a("zm"), a("zo"), c(CM), None, OP.mult)
         ts(a("zo2"), a("zo"), 2.0, None, OP.mult)
-        ts(c(CL16), c(CL), 16.0, None, OP.mult)
-        ms(a("rf", 0, 1), 0.0)
-        cp(a("ch", 0, 1), c(CE))
-        ms(a("ypb", 0, 32), 0.0)
-        aff(a("tt", TC + 1536, TC + 2304), a("cc"), 1.0, 512.0)
-        ts(a("mc", 0, 32), a("io", 0, 32), 0.0, c(CJ1), OP.mult, OP.add)
-        ts(a("mc", 32, 64), a("io", 0, 32), 0.0, 2048.0, OP.mult, OP.add)
+        ms(a("neg"), -1.0)
+        ms(a("st1", 3, 32, 4), MAG - 8192)
+        ms(a("st2", 2, 32, 4), MAG - 8192)
+        ms(a("sq", 96, 128), MAG - 8192)
+        ms(a("pq", 96, 112), 0.0)
+        ms(a("st2", 3, 32, 4), MAG - 8192)
+        act(c(CQ), a("t1", 0, 1), AF.Ln)
+
+    def last_constants():
+        return [
+            lambda: ms(a("ln2", 32, 48), 0.0),
+            lambda: ms(a("sd"), 0.0),
+            lambda: ts(a("thn"), a("i16", 0, 32), -14.5, None, OP.add),
+            lambda: ms(a("sd", 3, 128, 4), -MAG),
+            lambda: ts(a("zr"), a("zo"), row(0), None, OP.mult),
+            lambda: cp(a("ch", 0, 1), c(CL0)),
+            lambda: ts(a("blkb"), a("mg"), c(CG), None, OP.is_equal),
+            lambda: ts(a("q16"), a("io", 0, 36), 16.0, c(CJ), OP.mult, OP.add),
+            lambda: ts(a("mc", 0, 32), a("io", 0, 32), 0.0, c(CV), OP.mult, OP.add),
+            lambda: cp(a("q16", 32, 33), c(CJ)),
+            lambda: ms(a("mc", 32, 64), 2048.0),
+            lambda: ts(a("qm1"), a("q16"), -1.0, None, OP.add),
+        ]
+
+    def visit_constants():
+        out = [
+            lambda: ts(a("dg2"), a("i8"), c(CK), None, OP.is_equal),
+            lambda: ts(a("zk"), a("zo"), NONE, None, OP.mult),
+            lambda: ms(a("k7"), -7 * NONE),
+            lambda: ts(a("nio"), a("io", 0, 16), -1.0, None, OP.mult),
+            lambda: ms(a("one"), 1.0),
+            lambda: ts(a("blkk"), a("mg"), c(CG), 1024.0, OP.is_equal, OP.mult),
+            lambda: ts(a("nidk"), a("io", 0, 128), c(CP), -1024.0, OP.is_equal, OP.mult),
+            lambda: ms(a("tm", 96, 128), 1024 * NONE),
+            lambda: ms(a("tm", 224, 232), 1024 * NONE),
+            lambda: ms(a("ypb", 0, 32), 0.0),
+            lambda: ts(a("g8"), a("io", 0, 8), 16.0, c(CG), OP.mult, OP.is_equal),
+        ]
+        for h in (0, 1):
+            out.append(lambda h=h: ts(a("tm", 128 * h, 128 * h + 32), a("io", 0, 32), c(CH0 + h), 2.0 ** 23, OP.is_ge, OP.mult))
+        for h in (0, 1):
+            for n, s in ((1, 2.0 ** 19), (2, -2.0 ** 19)):
+                out.append(lambda h=h, n=n, s=s: ts(a("tm", 128 * h + 32 * n, 128 * h + 32 * n + 32), a("tm", 128 * h, 128 * h + 32), s, None, OP.add))
+        return out
 
     def first_numbers():
         mm(a("pa"), a("dh"), a("ohi"), True, False)
@@ -316,6 +387,7 @@ def rank_program(g, core, T, topo):
         act(a("oio"), a("pa"), AF.Copy)
         act(a("o0"), a("oio", ind=a("seatu")), AF.Copy)
 
+    scalar_constants()
     BIG = float(1 << 20)
     for t in range(RO):
         xo, xn = ("x0", "x1") if t % 2 == 0 else ("x1", "x0")
@@ -350,32 +422,65 @@ def rank_program(g, core, T, topo):
         adds(ch_[4])
         if t == 0:
             later_constants()
+            for f in last_constants():
+                f()
+            iota(a("ex", E2 + 128, RW), [[0, RW - E2 - 128]], 0)
+            iota(a("ohi"), [[16, 32], [0, 16]], 0)
+            iota(a("olo"), [[0, 32], [1, 16]], 0)
             wait("g", "ld3", 16); wait("g", "ld4", 16)
             send(a(xo, 0, B0 + 512), a("xg"), "a0", host, "out0")
             landed("xg", "a0", guest)
-            iota(a("tt", TX, TX + 768), [[0, 768]], 0)
 
         def word(j, lo=0, hi=32):
             ws = (37 * j + 11 * t) // 16 * 16
             return a("dicx", ws, ws + 8208, ind=a("off", 32 * j + lo, 32 * j + hi))
 
         def ltj(j, lo=0, hi=512):
-            return a("lt", 1024 * (15 - j) + lo, 1024 * (15 - j) + hi)
+            w = 512 * ((14 - j) % 16)
+            return a("lt", w + lo, w + hi)
+
+        def quads():
+            p0 = lambda lo=0, step=1: a("pq", 64 + lo, 96 + lo if step == 1 else 96, step)
+            q = lambda n: a("tq", 8 * n, 8 * n + 8)
+            ts(a("pq", 0, 96), a("pp", 0, 96), -1.0, 1024.0, OP.is_le, OP.mult)
+            yield
+            tt(a("dq"), a("pq", 0, 64), a("pq", 32, 96), OP.subtract)
+            tt(a("zq"), p0(), p0(1), OP.min)
+            tt(a("sq", 32, 64), p0(), a("st1"), OP.add)
+            yield
+            tt(a("wq"), a("dq", 32, 64), a("zq"), OP.max)
+            tt(q(0), a("dq", 0, 32, 4), p0(0, 4), OP.subtract)
+            tt(q(1), a("dq", 32, 64, 4), p0(2, 4), OP.min)
+            yield
+            tt(q(2), p0(0, 4), a("wq", 1, 32, 4), OP.min)
+            tt(q(3), q(0), q(1), OP.max)
+            tt(a("sq", 64, 96), a("wq"), a("st2"), OP.add)
+            yield
+            tt(q(4), q(2), q(3), OP.max)
+            yield
+            ts(a("sq", 96, 128, 4), q(4), MAG - 1024, None, OP.add)
+            yield
 
         ev = []
         ns = NS0 if t == 0 else NS
         tv, tsc = (0.0 if t == 0 else 1.7), 0.0
         half = ns - 1
         ev.append((tv, "vh", half)); tv += 0.38
+        qat = QAT + (1 if t == 0 else 0)
         for j in range(ns, 16):
             ev.append((tv, "vg", j)); tv += 0.72; ev.append((tv + LAGV, "cnt", j))
+            if j - ns + 1 >= qat:
+                ev.append((tv - 0.01, "quad", j)); tv += 0.12
         for j in range(ns + 1):
             if j < ns:
                 ev.append((tsc, "sg", j)); tsc += 0.73; ev.append((tsc, "sub", j))
             if j > 0:
                 ev.append((tsc + 0.001, "sign", j - 1)); tsc += 0.48; ev.append((tsc + LAGS, "cnt", j - 1))
+                if j == 3:
+                    ev.append((tsc + LAGS + 0.001, "qcnt", j))
         ev.sort()
         ncnt = [0]
+        qs = quads()
         for _, kind, j in ev:
             n = 256 if j == half else 512
             d, bank = a("d%d" % (j % 3), 0, n), a("pa" if j % 2 == 0 else "pb", 0, n)
@@ -393,6 +498,10 @@ def rank_program(g, core, T, topo):
                     mm(a("pc", 256, 512), sel("zo", half), a("neg"), False, False)
             elif kind == "sign":
                 act(ltj(j, 0, n), bank, AF.Sign, -0.5)
+            elif kind == "qcnt":
+                conv(a("pp", 0, 96), "zo", "lt", 6144, 7680)
+            elif kind == "quad":
+                next(qs, None)
             elif j == half:
                 mm(a("pc", 0, 256), sel("zo", j), ltj(j, 0, 256), False, ncnt[0] == 15)
                 ncnt[0] += 1
@@ -403,100 +512,142 @@ def rank_program(g, core, T, topo):
             ts(a("pw%d" % e), a("pc", e, 512, 2), c(CTH0 if t == 0 else CTH), None, OP.is_le)
         for i in list(range(0, 16, 2)) + list(range(1, 16, 2)):
             mm(a("pm", 0, 32), sel("zm", i), a("pw%d" % (i % 2), i // 2, 256, 8), i == 0, i == 15)
-        act(a("ln2"), a("pm", 0, 32), AF.Ln, 4.0 ** -0.1, 4.0 ** -0.1)
-        act(a("lns"), a("pm", 0, 32), AF.Ln, 4.0 ** -16)
+        for _ in qs:
+            pass
+        act(a("ln2", 0, 32), a("pm", 0, 32), AF.Ln, math.exp(-15.4), math.exp(-0.2))
+        act(a("lns"), a("pm", 0, 32), AF.Ln, math.exp(-31.2), math.exp(-0.2))
         ts(a("pw"), a("pc"), c(CTH0 if t == 0 else CTH), None, OP.is_le)
         for h in (0, 1):
             for k in range(16):
                 mm(a("pn", 16 * h, 16 * h + 16), sel("zm", k), a("pw", 256 * h + 16 * k, 256 * h + 16 * k + 16), k == 0, k == 15)
-        ts(a("nm"), a("ln2"), c(CL16), MAG + 240.0, OP.mult, OP.add)
-        ts(a("pz"), a("ln2", 0, 32, 2), 20.1, -1024.0, OP.is_lt, OP.mult)
-        ts(a("pe"), a("ln2", 0, 32, 2), c(CL16), MAG + 224.0, OP.mult, OP.add)
-        ts(a("nsi"), a("lns"), c(CL), 15.1, OP.mult, OP.add)
-        tt(a("pu"), a("pz"), a("nm", 1, 32, 2), OP.add)
-        ts(a("r32", 1, 32, 2), a("nm", 1, 32, 2), MAG, c(CK), OP.subtract, OP.add)
-        ts(a("roff", 0, 32, 2), a("nsi", 0, 16), 48.0, c(CK), OP.mult, OP.add)
-        tt(a("pv"), a("pu"), a("pe"), OP.max)
-        ts(a("rofs", 0, 32, 2), a("nsi", 0, 16), 48.0, c(CK32), OP.mult, OP.add)
-        ts(a("roff", 1, 32, 2), a("nsi", 16, 32), 48.0, c(CK16), OP.mult, OP.add)
-        ts(a("r32", 0, 32, 2), a("pv"), MAG, c(CK), OP.subtract, OP.add)
+        for dl in range(4):
+            tt(a("rq", dl, 128, 4), a("sq", 32 * dl, 32 * dl + 32), a("ln2", dl, dl + 32), OP.subtract)
+        ts(a("nsi"), a("lns"), -1.0, None, OP.mult)
+        scan(a("sc"), a("rq"), a("sd"), 0.0, OP.max, OP.add)
+        tt(a("a15"), a("lns"), a("thn"), OP.is_le)
+        ts(a("roff", 0, 32, 2), a("nsi", 0, 16), 32.0, c(CK), OP.mult, OP.add)
+        ts(a("roff", 1, 32, 2), a("nsi", 16, 32), 32.0, c(CK16), OP.mult, OP.add)
+        ts(a("r32"), a("sc", 3, 128, 4), 16.0, c(CK), OP.mult, OP.add)
+        ts(a("n15"), a("nsi"), 1.0 / 15, None, OP.mult)
+
+        def codes(k):
+            w = 32 * (k + 1)
+            tt(a("cd", w - 32, w), a("cd", w, w + 1024, ind=a("roff", 2 * k, 2 * k + 2)), a("cc", 32 * k, 32 * k + 32), OP.max)
+
+        def codes2(k):
+            w = C2 + 32 * (k + 1)
+            act(a("cd", w - 32, w), a("cd", w, w + 1024, ind=a("rof2", 2 * k, 2 * k + 2)), AF.Copy)
+
+        def exits(q):
+            w = 64 * (q + 1)
+            src = a("ex", w, w + 256, ind=a("r32", 4 * q, 4 * q + 4))
+            if q >= 4:
+                tt(a("ex", w - 64, w), src, a("ce", w - 320, w - 256), OP.min)
+            else:
+                cp(a("ex", w - 64, w), src)
+            act(a("eb", w - 64, w), a("eb", w, w + 256, ind=a("r32", 4 * q, 4 * q + 4)), AF.Copy)
+            if q < 4:
+                for cc_ in range(4 * q + 3, 4 * q - 1, -1):
+                    mm(a("pp", 0, 8), sel("zr", cc_), a("eb", 16 * cc_, 16 * cc_ + 16, 2), cc_ == 15, cc_ == 0)
+
+        def chain(m):
+            cp(a("ch", 2 * m + 1, 2 * m + 17), a("ex", ind=a("ch", 2 * m, 2 * m + 1)))
+
         extra = [
             lambda: ts(a("kni"), a("pk", 64, 96), BIG, None, OP.add),
-            lambda: ts(a("nni"), a("lnn"), c(CL), 16.1, OP.mult, OP.add),
+            lambda: ts(a("nni"), a("lnn"), -1.0, 1.0, OP.mult, OP.add),
             lambda: ts(a("kn"), a("kni"), 4095, None, OP.bitwise_and),
             lambda: ts(a("nt"), a("nni"), 20.0, None, OP.is_ge),
             lambda: tt(a("ksq"), a("kn"), a("kn"), OP.mult),
-            lambda: ts(a("kn1"), a("kn"), -2048.0, None, OP.add),
+            lambda: tt(a("nu"), a("nt"), a("qm1", 0, 32), OP.mult),
             lambda: ts(a("v0"), a("ksq"), 5, 511, OP.logical_shift_right, OP.bitwise_and),
-            lambda: tt(a("nu"), a("nt"), a("q32"), OP.mult),
-            lambda: ts(a("v1"), a("v0"), 1.0, None, OP.add),
-            lambda: tt(a("nl"), a("nni"), a("nu"), OP.subtract),
+            lambda: tt(a("nl", 0, 32), a("nni"), a("nu"), OP.subtract),
+            lambda: ts(a("kn1"), a("kn"), -2048.0, None, OP.add),
+            lambda: cp(a("nl", 32, 33), a("nl", 0, 1)),
+            lambda: ts(a("v1"), a("v0"), 16.0, None, OP.add),
         ]
+        codes(15)
+        tt(a("n2"), a("n15"), a("a15"), OP.max)
+        exits(7)
+        codes(14)
+        ts(a("rof2", 0, 32, 2), a("n2", 0, 16), 480.0, c(CK), OP.mult, OP.add)
+        ts(a("rof2", 1, 32, 2), a("n2", 16, 32), 480.0, c(CK16), OP.mult, OP.add)
+        k1, k2 = 13, 15
+        for q in range(6, -1, -1):
+            exits(q)
+            codes(k1); k1 -= 1
+            codes2(k2); k2 -= 1
+            if q in (3, 2):
+                act(a("lnn", q % 2, 32, 2), a("pn", 16 * (q % 2), 16 * (q % 2) + 16), AF.Ln, math.exp(-31.2), math.exp(-0.2))
         if t == 0:
-            ts(a("dh"), a("idn"), c(CZ0), None, OP.mult)
-            ts(a("dl"), a("idn"), c(CZ1), None, OP.mult)
-        for k in range(15, -1, -1):
-            w = TX + 48 * (k + 1)
-            act(a("tt", w - 16, w), a("tt", w, w + 1536, ind=a("rofs", 2 * k, 2 * k + 1)), AF.Copy)
-            w = TE + 32 * (k + 1)
-            cp(a("tt", w - 32, w), a("tt", w, w + 256, ind=a("r32", 2 * k, 2 * k + 2)))
-            w = TC + 48 * (k + 1)
-            tt(a("tt", w - 48, w - 16), a("tt", w, w + 1536, ind=a("roff", 2 * k, 2 * k + 2)), a("cc", 48 * k, 48 * k + 32), OP.max)
-            if k in (13, 12):
-                act(a("lnn", k % 2, 32, 2), a("pn", 16 * (k % 2), 16 * (k % 2) + 16), AF.Ln, 4.0 ** -16)
-        if t == 0:
-            first_numbers()
+            ts(a("dh"), a("idn"), row(0), None, OP.mult)
+            ts(a("dl"), a("idn"), row(1), None, OP.mult)
+            extra = extra + visit_constants()
         mm(a("ph", 0, 64), a("idn"), a("mc"), True, False)
-        for i in range(17):
-            if i < 16:
-                o = 32 * i - 16 if i else 0
-                cp(a("ch", 32 * i + 16, 32 * i + 32), a("tt", 0, TX + 768, ind=a("ch", o, o + 1)))
-            if i > 0:
-                cp(a("ch", 32 * i, 32 * i + 16), a("tt", 0, TX + 768, ind=a("ch", 32 * i - 14, 32 * i - 13)))
-            if extra:
-                extra.pop(0)()
-        A = a("ch", 17, 33 * 16, 16)
-        ts(a("aw"), A, 15872.0, None, OP.is_ge)
-        cp(a("rf", 1, 33), A)
+        codes(k1); k1 -= 1
+        codes2(k2); k2 -= 1
+        extra.pop(0)()
+        cp(a("le2"), a("pp", 0, 8))
+        codes(k1); k1 -= 1
+        codes2(k2); k2 -= 1
+        extra.pop(0)()
+        cp(a("ex", E2, E2 + 128), a("ex", 0, E2, ind=a("le2")))
+        for m in range(8):
+            if k1 >= 0:
+                codes(k1); k1 -= 1
+            if k2 >= 0:
+                codes2(k2); k2 -= 1
+            for _ in range(1 if k1 >= 0 else 2):
+                if extra:
+                    extra.pop(0)()
+            chain(m)
+        act(a("w", 0, 160), a("cd", ind=a("ch", 0, 10)), AF.Copy)
+        cp(a("w", 160, 272), a("cd", ind=a("ch", 10, 17)))
+        A = a("w", 11, 267, 8)
+        ts(a("aw"), A, ZC + 1.5, None, OP.is_ge)
+        tt(a("yp", 0, 32), A, a("w", 4, 260, 8), OP.max)
+        cp(a("yp", 32, 33), a("w", 11, 12))
         tt(a("apk", 0, 32), a("aw"), a("v1"), OP.mult)
         tt(a("apk", 32, 64), a("aw"), a("kn1"), OP.mult)
+        cp(a("idx2", 0, 33), a("yp", 0, 33))
         mm(a("ph", 0, 64), a("blkb"), a("apk"), False, True)
-        mm(a("pp", 0, 32), a("r15"), a("rf", 0, 32))
-        ts(a("rf2"), A, c(CY), None, OP.add)
-        ts(a("st"), A, 15360.0, None, OP.is_ge)
+        act(a("g2", 0, 256), a("lt", ind=a("idx2", 0, 16)), AF.Relu)
+        act(a("g2", 256, 528), a("lt", ind=a("idx2", 16, 33)), AF.Relu)
+        ts(a("st", 0, 33), a("yp", 0, 33), ZC + 0.5, None, OP.is_ge)
+        ts(a("uu", 0, 33), a("yp", 0, 33), float(ZC), None, OP.is_equal)
+        tt(a("awq"), a("aw"), a("q16", 0, 32), OP.mult)
         cp(a(m1), a("ph", 0, 64))
         send(a(m1), a(l1), "a1_%d" % t, host)
-        tt(a("yp"), a("pp", 0, 32), a("rf2"), OP.max)
-        ts(a("idx2"), a("yp"), c(CY), None, OP.subtract)
-        act(a("g2"), a("lt", 1024, 17 * 1024, ind=a("idx2")), AF.Relu)
-        tt(a("e1"), a("st"), a("nl"), OP.mult)
-        ts(a("uu"), a("yp"), 9, 1, OP.logical_shift_right, OP.bitwise_and)
-        tt(a("awq"), a("aw"), a("q16"), OP.mult)
-        tt(a("e2"), a("e1"), a("qm1"), OP.add)
+        tt(a("e1", 0, 33), a("st", 0, 33), a("nl", 0, 33), OP.mult)
+        tt(a("e2", 0, 33), a("uu", 0, 33), a("qm1", 0, 33), OP.add)
         mm(a("pp", 64, 96), a("blkb"), a("awq"))
-        tt(a("srcf"), a("e2"), a("uu"), OP.add)
-        tt(a("dm"), a("pp", 64, 96), a("dg"), OP.mult)
-        cp(a("src"), a("srcf"))
+        tt(a("srcf", 0, 33), a("e1", 0, 33), a("e2", 0, 33), OP.add)
+        while extra:
+            extra.pop(0)()
+        tt(a("dm"), a("pp", 64, 96), a("dg2"), OP.mult)
+        cp(a("src", 0, 33), a("srcf", 0, 33))
         for h in (0, 1):
-            red(a("avf", h, h + 1), a("dm", 16 * h, 16 * h + 16), OP.max)
-        tt(a("srof"), a("srcf"), a("awq"), OP.max)
+            red(a("avf", h, h + 1), a("dm", h, 32, 2), OP.max)
+        tt(a(xn, B0, B0 + 256), a(xo, ind=a("src", 0, 16)), a("g2", 0, 256), OP.add)
+        tt(a(xn, B0 + 256, B0 + 528), a(xo, ind=a("src", 16, 33)), a("g2", 256, 528), OP.add)
         for h in (0, 1):
             ts(a("avl", h, h + 1), a("avf", h, h + 1), c(CH[h]), None, OP.max)
-        ts(a("sro"), a("srof"), float(B0), None, OP.subtract)
-        tt(a(xn, B0, B0 + 512), a(xo, ind=a("src")), a("g2"), OP.add)
-        act(a(on), a(oo, ind=a("sro")), AF.Copy)
+        tt(a("srof"), a("srcf", 0, 32), a("awq"), OP.max)
         if t == 0:
             send(a("avl"), a("lav"), "a2_0", host, "out1")
         else:
             cp(a(m2), a(xo, ind=a("avl")))
             send(a(m2), a(l2), "a2_%d" % t, host)
-        cp(a(xn, B0 + 512, B0 + 528), a(xn, B0, B0 + 16))
         landed(l1, "a1_%d" % t, guest)
         landed(l2 if t else "lav", "a2_%d" % t, guest)
         landed(l3, "a3_%d" % t, host)
-        cp(a("xv", 0, 256), a(xn, 0, 576, ind=a(l1, 0, 16)))
-        act(a("xv", 256, 512), a(xn, 0, 576, ind=a(l1, 16, 32)), AF.Copy)
+        cp(a("xv", 0, 256), a(xn, ind=a(l1, 0, 16)))
+        act(a("xv", 256, 512), a(xn, ind=a(l1, 16, 32)), AF.Copy)
         conv(a("ph", 0, 32), "zw", "xv", 0, 512)
+        ts(a("sro"), a("srof"), float(B0), None, OP.subtract)
+        if t == 0:
+            first_numbers()
+        act(a(on), a(oo, ind=a("sro")), AF.Copy)
         if last:
             conv(a("pn", 0, 32), "zo", on, 0, 512)
             mm(a("pa", np_=8), a("g8"), a(on))
@@ -504,57 +655,65 @@ def rank_program(g, core, T, topo):
             dma("s", "ld6", [(T.yseat[:], a("ysb", np_=8))])
         if t == 0:
             act(a(l2), a("xg", ind=a("lav")), AF.Copy)
-        act(a(xn, 576, XW), a(l2), AF.Copy)
-        ts(a("vi"), a(l1, 0, 32), float(B0), None, OP.subtract)
+        act(a(xn, 0, 32), a(l2), AF.Copy)
         cp(a("sf"), a(l1, 32, 64))
-        ts(a("val"), a(l1, 0, 32), c(CJ), None, OP.is_ge)
-        ts(a("vj"), a("vi"), 511, None, OP.bitwise_and)
+        ts(a("vb"), a(l1, 0, 32), c(CK), None, OP.add)
         ts(a("khi"), a("ph", 0, 32), BIG, None, OP.add)
-        ts(a("vk"), a("vj"), float(B0), None, OP.add)
+        tt(a("vd"), a("vb"), a("dg2"), OP.mult)
         ts(a("kh"), a("khi"), 4095, None, OP.bitwise_and)
-        tt(a("vp"), a("vk"), a("val"), OP.mult)
+        for h in (0, 1):
+            red(a("vh", h, h + 1), a("vd", h, 32, 2), OP.max)
         tt(a("hp"), a("kh"), a("sf"), OP.mult)
-        ts(a("vpm"), a("vp"), -1024.0, None, OP.add)
+        ts(a("vt", 0, 16), a("nio"), a("vh", 0, 1), None, OP.add)
         ts(a("hs"), a("hp"), 5, 8191, OP.logical_shift_right, OP.bitwise_and)
+        ts(a("vt", 16, 32), a("nio"), a("vh", 1, 2), None, OP.add)
         ts(a("hw"), a("hs"), c(CT0 + t), None, OP.add)
-        mm(a("ph", 0, 32), a("idn"), a("vpm"), True, False)
-        mm(a("pc", 0, 32), a("idn"), a("dgm"), True, False)
-        mm(a("pa", 0, 33), a("idn"), a("tm", 0, 33), True, False)
-        mm(a("pb", 0, 33), a("idn"), a("tm", 48, 81), True, False)
-        tt(a("lt2"), a("dicx", ind=a("hw")), a("xv"), OP.is_gt)
-        conv(a("pm", 0, 32), "zo", "lt2", 0, 512)
+        mm(a("pm", 0, 32), a("idn"), a("k7"), True, False)
+        mm(a("pb", 0, 225), a("idn"), a("tm", 0, 225), True, False)
+        for h in (0, 1):
+            tt(a("lt2", 256 * h, 256 * h + 256), a("dicx", ind=a("hw", 16 * h, 16 * h + 16)), a("xv", 256 * h, 256 * h + 256), OP.is_gt)
+        for i in range(16):
+            mm(a("pm", 0, 32), sel("zk", i), a("lt2", 32 * i, 32 * i + 32), False, i == 15)
         if last:
             ts(a("olf"), a("pn", 0, 32), 32.0, None, OP.add)
             cp(a("olu"), a("olf"))
             tt(a("awo"), a("aw"), a("olf"), OP.mult)
-        ts(a("ps2"), a("pm", 0, 32), 7.5, None, OP.is_le)
-        mm(a("ph", 0, 32), a("tri"), a("ps2"), False, True)
-        ts(a("fv", 0, 32), a("ph", 0, 32), 0.0, None, OP.max)
-        mm(a("pc", 0, 32), a("blkb"), a("fv", 0, 32), False, True)
-        mm(a("pa", 0, 33), a("blkb"), a("fv", 0, 33), False, True)
-        mm(a("pb", 0, 33), a("blkb"), a("fv", 0, 33), False, True)
+        for h in (0, 1):
+            scan(a("cs", 16 * h, 16 * h + 16), a("pm", 16 * h, 16 * h + 16), a("vt", 16 * h, 16 * h + 16), NONE, OP.min, OP.max)
+        cl = [a("cs", 15, 16), a("cs", 31, 32)]
+        for h in (0, 1):
+            ts(a("exd", h, 96, 2), a("dg"), cl[h], None, OP.mult)
+        for h in (0, 1):
+            ts(a("exo", 112 * h, 112 * h + 97), a("one", 0, 97), cl[h], None, OP.mult)
+        for h in (0, 1):
+            mm(a("pb", 128 * h, 128 * h + 96), a("blkk"), a("exd"), False, False)
+        for h in (0, 1):
+            mm(a("pb", 128 * h, 128 * h + 97), a("nidk"), a("exo", 112 * h, 112 * h + 97), False, h == 1)
         if last:
             mm(a("pp", 64, 96), a("blkb"), a("awo"))
         for h in (0, 1):
-            red(a("cl", h, h + 1), a("pc", 16 * h, 16 * h + 16), OP.min)
+            red(a("cf", h, h + 1), a("pb", 128 * h, 128 * h + 97), OP.min, apply_absolute_value=True)
         for h in (0, 1):
-            ts(a("eq", 48 * h, 48 * h + 33), a("pb" if h else "pa", 0, 33), a("cl", h, h + 1), c(CHI0 + h), OP.is_equal, OP.mult)
+            ts(a("tgt", h, h + 1), a("cf", h, h + 1), c(CH[h]), cl[h], OP.add, OP.min)
         for h in (0, 1):
-            red(a("cf", h, h + 1), a("eq", 48 * h, 48 * h + 33), OP.max)
-        for h in (0, 1):
-            ts(a("tgt", h, h + 1), a("cf", h, h + 1), a("cl", h, h + 1), None, OP.max)
+            ts(a("tgf", h, h + 1), a("cf", h, h + 1), c(CH[h]), cl[h], OP.add, OP.min)
         cp(a(m3), a(xn, ind=a("tgt")))
         send(a(m3), a(l3), "a3_%d" % t, guest)
-        cp(a(xn, ind=a("tgt")), a(l2))
+        ts(a("tgw", 0, 2), a("tgf", 0, 2), B0 + 511.5, -512.0, OP.is_ge, OP.mult)
+        if last:
+            tt(a("dm"), a("pp", 64, 96), a("dg2"), OP.mult)
+        tt(a("tgc", 0, 2), a("tgf", 0, 2), a("tgw", 0, 2), OP.add)
+        if last:
+            for h in (0, 1):
+                red(a("avf", h, h + 1), a("dm", h, 32, 2), OP.max)
+        cp(a("tg2"), a("tgc", 0, 2))
+        cp(a(xn, ind=a("tg2")), a(l2))
         if not last:
             cp(a(xn, ind=a("avl")), a(l3))
         else:
-            tt(a("dm"), a("pp", 64, 96), a("dg"), OP.mult)
-            cp(a("ypb", ind=a("olu")), a(xn, B0, B0 + 512))
-            for h in (0, 1):
-                red(a("avf", h, h + 1), a("dm", 16 * h, 16 * h + 16), OP.max)
             for h in (0, 1):
                 ts(a("avo", h, h + 1), a("avf", h, h + 1), c(CH[h]), None, OP.max)
+            cp(a("ypb", ind=a("olu")), a(xn, B0, B0 + 512))
             cp(a("ypb", ind=a("avo")), a(l3))
             dma("y", "ld7", [(T.ypup[:], a("ypb", 32, 544))])
     for s in sorted(count):

@@ -3,14 +3,15 @@ from concourse.mybir import AluOpType as OP, AxisListType as AX, ActivationFunct
 
 RO = 4
 NS = 7
-NS0 = 6
+NS0 = 7
 B0 = 48
 LAGV, LAGS = 0.2, 0.0
+HS, HS0 = 384, 128
 QAT = 5
 XW = 576
 DW = 8800
-RW = 3072
-E2, C2 = 768, 1536
+RW = 3216
+E2, C2 = 3072, 1536
 ZC = 8192
 WDT = "float16"
 
@@ -21,10 +22,10 @@ SB = {
     "lt": (ZC + 16, H), "d0": (512, H), "d1": (512, H), "d2": (512, H),
     "ksi": (48, I), "ks": (48, I), "prod": (512, I), "prs": (512, I), "off": (512, U),
     "pw": (512, H), "lns": (32, F), "nsi": (32, I), "roff": (32, U), "rof2": (32, U), "lnn": (32, F), "nni": (32, I),
-    "r32": (32, U), "pw0": (256, H), "pw1": (256, H), "ln2": (48, F), "neg": (256, H), "zo2": (144, H),
+    "r32": (32, U), "pw0": (256, H), "pw1": (256, H), "ln2": (48, F), "neg": (512, H), "zo2": (144, H),
     "pq": (112, F), "dq": (64, F), "zq": (32, F), "wq": (32, F), "tq": (48, F), "sq": (128, F), "st1": (32, F), "st2": (32, F),
     "rq": (128, F), "sc": (128, F), "sd": (128, F), "n15": (32, F), "a15": (32, F), "n2": (32, F), "thn": (32, F),
-    "ex": (RW, F), "eb": (768, H), "cd": (RW, F), "cc": (512, F), "ce": (256, F), "le2": (8, U), "ch": (40, U), "w": (272, F),
+    "ex": (RW, F), "eb": (768, H), "cd": (RW, F), "cc": (512, F), "ce": (256, F), "le2": (6, U), "ch": (40, U), "c1": (48, U), "w": (272, F),
     "mc": (64, H), "kni": (32, I), "kn": (32, I), "kn1": (32, F), "ksq": (32, I), "v0": (32, I), "v1": (32, F),
     "nt": (32, F), "nu": (32, F), "nl": (36, F), "aw": (32, F), "st": (36, F), "apk": (64, WDT), "awq": (32, WDT),
     "yp": (36, F), "idx2": (34, U), "uu": (36, F), "e1": (36, F), "e2": (36, F),
@@ -63,6 +64,9 @@ SEMAPHORES = ["qv", "qs", "qp", "qg", "sent", "a0", "out0", "out1"] + ["ld%d" % 
 MAG = 1.5 * 2.0 ** 23
 CH = (CK, CK16)
 NONE = 4096.0
+CYC, WAKE, HOP, SLACK, AHEAD = 0.92e-3, 0.2, 1.6, 0.1, 400
+ORDER = []
+LOADED = {"ld3": 5.0, "ld4": 8.5, "ld5": 9.0}
 
 
 def a(name, lo=0, hi=None, step=1, ind=None, np_=128):
@@ -80,6 +84,36 @@ def bits(x):
     if step == 1:
         return ((1 << (hi - lo)) - 1) << lo
     return sum(1 << j for j in range(lo, hi, step))
+
+
+def uses(rd, wr):
+    use = []
+    for w, xs in ((False, rd), (True, wr)):
+        for x in xs:
+            if isinstance(x, tuple):
+                use.append((x[0], bits(x), w))
+                if x[4] is not None:
+                    use.append((x[4][0], bits(x[4]), False))
+    return use
+
+
+def cost(q, rd, wr):
+    xs = [x for x in wr + rd if isinstance(x, tuple)]
+    n = len(range(*xs[0][1:4]))
+    if q == "p":
+        return max(64, n) * CYC / 2
+    if q == "g":
+        return 0.13 + 2 * n * CYC
+    for x in xs:
+        if x[4] is not None:
+            return 0.06 + 16 * len(range(*x[4][1:4])) * CYC * (3.8 if x is xs[0] else 1.56)
+    wide = [x for x in xs if len(range(*x[1:4])) > 1]
+    n = max(len(range(*x[1:4])) for x in xs)
+    if q == "v" and all(x[0] in SB and SB[x[0]][1] in (H, U, WDT) for x in wide):
+        n = n / 2
+    if q == "v" and len(wide) == 3 and all(x[0] in SB for x in wide[1:]):
+        n = 2 * n
+    return max(64, n) * CYC
 
 
 def rank_program(g, core, T, topo):
@@ -113,13 +147,7 @@ def rank_program(g, core, T, topo):
                 k[s2] = v2
 
     def order(q, rd, wr):
-        use = []
-        for w, xs in ((False, rd), (True, wr)):
-            for x in xs:
-                if isinstance(x, tuple):
-                    use.append((x[0], bits(x), w))
-                    if x[4] is not None:
-                        use.append((x[4][0], bits(x[4]), False))
+        use = uses(rd, wr)
         need = {}
         for name, m, w in use:
             for (m2, w2, q2, s2, v2) in acc.get(name, []):
@@ -149,12 +177,77 @@ def rank_program(g, core, T, topo):
                 lst[:] = [e for e in lst if not (e[3] == s and not e[1] and not e[0] & ~m)]
             lst.append((m, w, q, s, v))
 
+    calls = []
+    seen = {}
+    rows = {}
+    in_row = [None]
+
+    def record(q, rd, wr, busy, done, issue, after=()):
+        n, dep = len(calls), {m: WAKE for m in after}
+        use = uses(rd, wr)
+        for name, m, w in use:
+            for (m2, w2, q2, n2) in seen.get(name, []):
+                if name in PS and q == q2 == "p":
+                    dep.setdefault(n2, 0.0)
+                elif (name in PS and q2 != q) or ((w or w2) and m & m2):
+                    dep[n2] = WAKE
+        if in_row[0] is not None:
+            key = (in_row[0], q)
+            if key in rows:
+                dep.setdefault(rows[key], calls[rows[key]][1] - calls[rows[key]][2])
+            rows[key] = n
+        for name, m, w in use:
+            lst = seen.setdefault(name, [])
+            if name in PS and q == "p":
+                lst[:] = []
+            if w:
+                lst[:] = [e for e in lst if e[0] & ~m]
+            lst.append((m, w, q, n))
+        calls.append((q, busy, done, list(dep.items()), issue))
+        return n
+
     def op(q, rd, wr, fn):
-        use = order(q, rd, wr)
-        s = qsem[q]
-        count[s] = count.get(s, 0) + 1
-        fn().then_inc(T.sem[s], 1)
-        note(use, q, s, count[s])
+        def issue():
+            use = order(q, rd, wr)
+            s = qsem[q]
+            count[s] = count.get(s, 0) + 1
+            fn().then_inc(T.sem[s], 1)
+            note(use, q, s, count[s])
+        t = cost(q, rd, wr) + (1.3 if len(calls) < 9 and q == "s" else 0.0)
+        record(q, rd, wr, t, t, issue)
+
+    def issue_all():
+        if ORDER:
+            for i in ORDER:
+                calls[i][4]()
+            return
+        n = len(calls)
+        tail = [0.0] * n
+        for i in range(n - 1, -1, -1):
+            tail[i] += calls[i][2]
+            for m, w in calls[i][3]:
+                tail[m] = max(tail[m], w + tail[i])
+        end, free, todo = {}, {}, list(range(n))
+        while todo:
+            ahead, est, byq = todo[:AHEAD], {}, {}
+            for i in ahead:
+                est[i] = max([free.get(calls[i][0], 0.0)] + [(end[m] if m in end else est[m] + calls[m][2]) + w for m, w in calls[i][3]])
+                byq.setdefault(calls[i][0], []).append(i)
+            pick = None
+            for q, xs in byq.items():
+                xs.sort(key=lambda i: -tail[i])
+                for k, i in enumerate(xs):
+                    if all(m in end for m, _ in calls[i][3]) and all(
+                            est[i] + calls[i][1] + tail[m] <= est[m] + max(tail[m], calls[m][1] + tail[i]) + SLACK for m in xs[:k]):
+                        if pick is None or est[i] < est[pick]:
+                            pick = i
+            if pick is None:
+                pick = ahead[0]
+            end[pick] = est[pick] + calls[pick][2]
+            free[calls[pick][0]] = est[pick] + calls[pick][1]
+            todo.remove(pick)
+            ORDER.append(pick)
+            calls[pick][4]()
 
     def ts(o, i, s1, s2, o0, o1=None):
         if o1 is None:
@@ -196,27 +289,30 @@ def rank_program(g, core, T, topo):
             op("g", [], [o], lambda: g.iota(ap(o), pat, base, cm, allow_small_or_imprecise_dtypes=True))
 
     def dma(q, s, pairs):
-        use = []
-        for o, i in pairs:
-            use += order(q, [i], [o])
-        for o, i in pairs:
+        (o, i), = pairs
+
+        def issue():
+            use = order(q, [i], [o])
             eng[q].dma_start(ap(o), ap(i)).then_inc(T.sem[s], 16)
-        count[s] = 16 * len(pairs)
-        note(use, q, s, count[s])
+            count[s] = 16
+            note(use, q, s, 16)
+        record(q, [i], [o], 0.1, LOADED.get(s, 1.5), issue)
 
-    def send(src, dst, s, to, loc="sent"):
-        order("g", [src], [])
-        d = T.cores[to]
-        rid, pid, _ = topo.addr(d)
-        g.remote_dma(ap(dst), ap(src), T.sem[s], T.sem[loc], pid, rid, topo.mask(core, d))
-        count[loc] = count.get(loc, 0) + len(topo.engines(core, d))
-        if loc != "sent":
-            note([(src[0], bits(src), False)], "remote", loc, count[loc])
+    def send(src, dst, s, to, frm, loc="sent", also=()):
+        def issue():
+            order("g", [src] + list(also), [])
+            d = T.cores[to]
+            rid, pid, _ = topo.addr(d)
+            g.remote_dma(ap(dst), ap(src), T.sem[s], T.sem[loc], pid, rid, topo.mask(core, d))
+            count[loc] = count.get(loc, 0) + len(topo.engines(core, d))
+            if loc != "sent":
+                note([(src[0], bits(src), False)], "remote", loc, count[loc])
 
-    def landed(dst, s, frm):
-        n = len(topo.engines(T.cores[frm], core))
-        count[s] = n
-        note([(dst, bits(a(dst)), True)], "remote", s, n)
+        def landed():
+            count[s] = len(topo.engines(T.cores[frm], core))
+            note([(dst[0], bits(dst), True)], "remote", s, count[s])
+        n = record("g", [src] + list(also), [], 0.4, HOP, issue)
+        record("landing", [], [dst], 0.0, 0.0, landed, [n])
 
     def sel(z, i):
         return a(z, 15 - i, 143 - i)
@@ -228,12 +324,16 @@ def rank_program(g, core, T, topo):
     def row(r):
         return a("dg", r, r + 1)
 
+    in_row[0] = "loads"
     dma("y", "ld0", [(a("pupb"), T.pup[:])])
     dma("s", "ld1", [(a("seatb"), T.seat[:])])
     dma("s", "ld2", [(a("wtb", 0, 1), T.wt[:])])
     dma("y", "ld3", [(a("dicx", 0, 4096), T.dic[:, 0:4096])])
     dma("s", "ld4", [(a("dicx", 4096, 8192), T.dic[:, 4096:8192])])
     dma("y", "ld5", [(a("dicx", 8192, DW), T.dic[:, 0:DW - 8192])])
+    in_row[0] = None
+    ms(a("ln2"), 1.0)
+    act(a("lns", 0, 1), a("ln2", 0, 1), AF.Ln)
 
     iota(a("ci", 0, 1), [[0, 1]], 0, 1)
     iota(a("io"), [[1, 144]], 0)
@@ -294,7 +394,9 @@ def rank_program(g, core, T, topo):
         aff(c(CA), row(0), 16.0, c(CZ))
         aff(c(CB), row(0), 1.0, c(CB))
         aff(c(CD), c(C34), 60000.0, c(CL))
-        aff(c(CL0), c(C34), 512.0, c(CL))
+        aff(c(CZ0), row(1), -1.0, 1.0)
+        aff(c(CZ1), row(12), float(C2), 0.0)
+        aff(c(CL0), c(C34), 512.0, c(CZ1))
         aff(c(CE), c(C34), -60000.0, 60000.0)
         aff(c(CD), c(CB), 1.0, c(CD))
         aff(c(CE), row(4), float(C2), c(CE))
@@ -304,6 +406,8 @@ def rank_program(g, core, T, topo):
 
     def later_constants():
         tt(a("ex", 512, 768), a("t2"), a("t3"), OP.add)
+        for i in range(3):
+            ts(a("ex", 512 + i, 768, 16), a("ex", 512 + i, 768, 16), c(CZ0), None, OP.mult)
         J, gt, eq, lt, u = [a("t1", 64 + 16 * n, 80 + 16 * n) for n in range(5)]
         add, uns, add2, uns2, v = [a("t1", 144 + 16 * n, 160 + 16 * n) for n in range(5)]
         k0 = a("io", 0, 16)
@@ -342,11 +446,9 @@ def rank_program(g, core, T, topo):
         ms(a("sq", 96, 128), MAG - 8192)
         ms(a("pq", 96, 112), 0.0)
         ms(a("st2", 3, 32, 4), MAG - 8192)
-        act(c(CQ), a("t1", 0, 1), AF.Ln)
 
     def last_constants():
         return [
-            lambda: ms(a("ln2", 32, 48), 0.0),
             lambda: ms(a("sd"), 0.0),
             lambda: ts(a("thn"), a("i16", 0, 32), -14.5, None, OP.add),
             lambda: ms(a("sd", 3, 128, 4), -MAG),
@@ -415,21 +517,19 @@ def rank_program(g, core, T, topo):
             for j in js:
                 ts(a("off", 32 * j, 32 * j + 32), a("prs", 32 * j, 32 * j + 32), float((37 * j + 11 * t) % 16), None, OP.add)
 
-        ch_ = [[0, 1], [2, 3, 4], [5, 6, 7, 8], [9, 10, 11, 12], [13, 14, 15]]
-        mults(ch_[0]); mults(ch_[1][:2]); shift(ch_[0]); mults(ch_[1][2:]); mults(ch_[2][:1]); adds(ch_[0]); shift(ch_[1])
-        mults(ch_[2][1:]); adds(ch_[1]); shift(ch_[2]); mults(ch_[3]); adds(ch_[2]); shift(ch_[3]); mults(ch_[4])
-        adds(ch_[3][:2]); shift(ch_[4]); adds(ch_[3][2:])
-        adds(ch_[4])
+        for js in ([0, 1], [2, 3, 4, 5], [6, 7, 8, 9], [10, 11, 12], [13, 14, 15]):
+            mults(js); shift(js); adds(js)
         if t == 0:
             later_constants()
             for f in last_constants():
                 f()
+            send(a(xo, 0, B0 + 512), a("xg"), "a0", host, guest, "out0", [a("dicx", 0, 8192)])
+            for lo in range(768, E2, 584):
+                iota(a("ex", lo, lo + 584), [[0, 584]], 0)
             iota(a("ex", E2 + 128, RW), [[0, RW - E2 - 128]], 0)
+            iota(a("cd", E2, RW), [[0, RW - E2]], 0)
             iota(a("ohi"), [[16, 32], [0, 16]], 0)
             iota(a("olo"), [[0, 32], [1, 16]], 0)
-            wait("g", "ld3", 16); wait("g", "ld4", 16)
-            send(a(xo, 0, B0 + 512), a("xg"), "a0", host, "out0")
-            landed("xg", "a0", guest)
 
         def word(j, lo=0, hi=32):
             ws = (37 * j + 11 * t) // 16 * 16
@@ -465,11 +565,11 @@ def rank_program(g, core, T, topo):
         ns = NS0 if t == 0 else NS
         tv, tsc = (0.0 if t == 0 else 1.7), 0.0
         half = ns - 1
-        ev.append((tv, "vh", half)); tv += 0.38
-        qat = QAT + (1 if t == 0 else 0)
+        hs = HS0 if t == 0 else HS
+        ev.append((tv, "vh", half)); tv += 0.72 * (512 - hs) / 512
         for j in range(ns, 16):
             ev.append((tv, "vg", j)); tv += 0.72; ev.append((tv + LAGV, "cnt", j))
-            if j - ns + 1 >= qat:
+            if j >= 16 - QAT + (t == 0):
                 ev.append((tv - 0.01, "quad", j)); tv += 0.12
         for j in range(ns + 1):
             if j < ns:
@@ -477,46 +577,50 @@ def rank_program(g, core, T, topo):
             if j > 0:
                 ev.append((tsc + 0.001, "sign", j - 1)); tsc += 0.48; ev.append((tsc + LAGS, "cnt", j - 1))
                 if j == 3:
-                    ev.append((tsc + LAGS + 0.001, "qcnt", j))
+                    ev.append((tsc + LAGS + 0.001, "quads", j))
         ev.sort()
         ncnt = [0]
         qs = quads()
         for _, kind, j in ev:
-            n = 256 if j == half else 512
+            n = hs if j == half else 512
             d, bank = a("d%d" % (j % 3), 0, n), a("pa" if j % 2 == 0 else "pb", 0, n)
+            in_row[0] = t if kind in ("vg", "vh", "sg", "sign", "quad") else None
             if kind == "vg":
                 tt(ltj(j), word(j), a("x2", 16 * j, 16 * j + 512), OP.is_gt)
             elif kind == "vh":
-                tt(ltj(j, 256, 512), word(j, 16, 32), a("x2", 16 * j + 256, 16 * j + 512), OP.is_gt)
+                tt(ltj(j, hs, 512), word(j, hs // 16, 32), a("x2", 16 * j + hs, 16 * j + 512), OP.is_gt)
             elif kind == "sg":
                 act(d, word(j, 0, n // 16), AF.Copy)
             elif kind == "sub":
                 mm(bank, a("idn"), d, True, False)
                 mm(bank, a("nid"), a("x2", 16 * j, 16 * j + n), False, True)
                 if j == half - 1:
-                    mm(a("pc", 256, 512), sel("zo2", half), ltj(half, 256, 512), False, False)
-                    mm(a("pc", 256, 512), sel("zo", half), a("neg"), False, False)
+                    mm(a("pc", hs, 512), sel("zo2", half), ltj(half, hs, 512), False, False)
+                    mm(a("pc", hs, 512), sel("zo", half), a("neg", hs, 512), False, False)
             elif kind == "sign":
                 act(ltj(j, 0, n), bank, AF.Sign, -0.5)
-            elif kind == "qcnt":
+            elif kind == "quads":
                 conv(a("pp", 0, 96), "zo", "lt", 6144, 7680)
             elif kind == "quad":
                 next(qs, None)
             elif j == half:
-                mm(a("pc", 0, 256), sel("zo", j), ltj(j, 0, 256), False, ncnt[0] == 15)
+                mm(a("pc", 0, hs), sel("zo", j), ltj(j, 0, hs), False, ncnt[0] == 15)
                 ncnt[0] += 1
             else:
                 mm(a("pc"), sel("zo", j), ltj(j), ncnt[0] == 0, ncnt[0] == 15)
                 ncnt[0] += 1
+        in_row[0] = t
+        next(qs, None)
         for e in (0, 1):
             ts(a("pw%d" % e), a("pc", e, 512, 2), c(CTH0 if t == 0 else CTH), None, OP.is_le)
-        for i in list(range(0, 16, 2)) + list(range(1, 16, 2)):
-            mm(a("pm", 0, 32), sel("zm", i), a("pw%d" % (i % 2), i // 2, 256, 8), i == 0, i == 15)
         for _ in qs:
             pass
+        ts(a("pw"), a("pc"), c(CTH0 if t == 0 else CTH), None, OP.is_le)
+        in_row[0] = None
+        for i in list(range(0, 16, 2)) + list(range(1, 16, 2)):
+            mm(a("pm", 0, 32), sel("zm", i), a("pw%d" % (i % 2), i // 2, 256, 8), i == 0, i == 15)
         act(a("ln2", 0, 32), a("pm", 0, 32), AF.Ln, math.exp(-15.4), math.exp(-0.2))
         act(a("lns"), a("pm", 0, 32), AF.Ln, math.exp(-31.2), math.exp(-0.2))
-        ts(a("pw"), a("pc"), c(CTH0 if t == 0 else CTH), None, OP.is_le)
         for h in (0, 1):
             for k in range(16):
                 mm(a("pn", 16 * h, 16 * h + 16), sel("zm", k), a("pw", 256 * h + 16 * k, 256 * h + 16 * k + 16), k == 0, k == 15)
@@ -548,61 +652,49 @@ def rank_program(g, core, T, topo):
             act(a("eb", w - 64, w), a("eb", w, w + 256, ind=a("r32", 4 * q, 4 * q + 4)), AF.Copy)
             if q < 4:
                 for cc_ in range(4 * q + 3, 4 * q - 1, -1):
-                    mm(a("pp", 0, 8), sel("zr", cc_), a("eb", 16 * cc_, 16 * cc_ + 16, 2), cc_ == 15, cc_ == 0)
+                    mm(a("pp", 0, 6), sel("zr", cc_), a("eb", 16 * cc_ + 4, 16 * cc_ + 16, 2), cc_ == 15, cc_ == 0)
 
         def chain(m):
             cp(a("ch", 2 * m + 1, 2 * m + 17), a("ex", ind=a("ch", 2 * m, 2 * m + 1)))
 
-        extra = [
-            lambda: ts(a("kni"), a("pk", 64, 96), BIG, None, OP.add),
-            lambda: ts(a("nni"), a("lnn"), -1.0, 1.0, OP.mult, OP.add),
-            lambda: ts(a("kn"), a("kni"), 4095, None, OP.bitwise_and),
-            lambda: ts(a("nt"), a("nni"), 20.0, None, OP.is_ge),
-            lambda: tt(a("ksq"), a("kn"), a("kn"), OP.mult),
-            lambda: tt(a("nu"), a("nt"), a("qm1", 0, 32), OP.mult),
-            lambda: ts(a("v0"), a("ksq"), 5, 511, OP.logical_shift_right, OP.bitwise_and),
-            lambda: tt(a("nl", 0, 32), a("nni"), a("nu"), OP.subtract),
-            lambda: ts(a("kn1"), a("kn"), -2048.0, None, OP.add),
-            lambda: cp(a("nl", 32, 33), a("nl", 0, 1)),
-            lambda: ts(a("v1"), a("v0"), 16.0, None, OP.add),
-        ]
-        codes(15)
         tt(a("n2"), a("n15"), a("a15"), OP.max)
-        exits(7)
-        codes(14)
         ts(a("rof2", 0, 32, 2), a("n2", 0, 16), 480.0, c(CK), OP.mult, OP.add)
         ts(a("rof2", 1, 32, 2), a("n2", 16, 32), 480.0, c(CK16), OP.mult, OP.add)
-        k1, k2 = 13, 15
-        for q in range(6, -1, -1):
-            exits(q)
-            codes(k1); k1 -= 1
-            codes2(k2); k2 -= 1
-            if q in (3, 2):
-                act(a("lnn", q % 2, 32, 2), a("pn", 16 * (q % 2), 16 * (q % 2) + 16), AF.Ln, math.exp(-31.2), math.exp(-0.2))
+        for k in range(15, -1, -1):
+            if k >= 8:
+                exits(k - 8)
+            codes(k)
+            codes2(k)
+        cp(a("le2"), a("pp", 0, 6))
+        cp(a("ex", E2 + 32, E2 + 128), a("ex", 0, 768, ind=a("le2")))
+        for s in range(4):
+            cp(a("ch", 4, 20) if s == 3 else a("c1", 16 * s, 16 * s + 16),
+               a("ex", 0, E2, ind=a("c1", 16 * s - 16, 16 * s - 15) if s else a("ch", 0, 1)))
+        cp(a("ch", 1, 4), a("c1", 0, 48, 16))
+        for m in range(2, 8):
+            chain(m)
+        for h in (0, 1):
+            act(a("lnn", h, 32, 2), a("pn", 16 * h, 16 * h + 16), AF.Ln, math.exp(-31.2), math.exp(-0.2))
+        ts(a("kni"), a("pk", 64, 96), BIG, None, OP.add)
+        ts(a("nni"), a("lnn"), -1.0, 1.0, OP.mult, OP.add)
+        ts(a("kn"), a("kni"), 4095, None, OP.bitwise_and)
+        ts(a("nt"), a("nni"), 20.0, None, OP.is_ge)
+        tt(a("ksq"), a("kn"), a("kn"), OP.mult)
+        tt(a("nu"), a("nt"), a("qm1", 0, 32), OP.mult)
+        ts(a("v0"), a("ksq"), 5, 511, OP.logical_shift_right, OP.bitwise_and)
+        tt(a("nl", 0, 32), a("nni"), a("nu"), OP.subtract)
+        ts(a("kn1"), a("kn"), -2048.0, None, OP.add)
+        cp(a("nl", 32, 33), a("nl", 0, 1))
+        ts(a("v1"), a("v0"), 16.0, None, OP.add)
         if t == 0:
             ts(a("dh"), a("idn"), row(0), None, OP.mult)
             ts(a("dl"), a("idn"), row(1), None, OP.mult)
-            extra = extra + visit_constants()
+            for f in visit_constants():
+                f()
         mm(a("ph", 0, 64), a("idn"), a("mc"), True, False)
-        codes(k1); k1 -= 1
-        codes2(k2); k2 -= 1
-        extra.pop(0)()
-        cp(a("le2"), a("pp", 0, 8))
-        codes(k1); k1 -= 1
-        codes2(k2); k2 -= 1
-        extra.pop(0)()
-        cp(a("ex", E2, E2 + 128), a("ex", 0, E2, ind=a("le2")))
-        for m in range(8):
-            if k1 >= 0:
-                codes(k1); k1 -= 1
-            if k2 >= 0:
-                codes2(k2); k2 -= 1
-            for _ in range(1 if k1 >= 0 else 2):
-                if extra:
-                    extra.pop(0)()
-            chain(m)
-        act(a("w", 0, 160), a("cd", ind=a("ch", 0, 10)), AF.Copy)
-        cp(a("w", 160, 272), a("cd", ind=a("ch", 10, 17)))
+        act(a("w", 0, 128), a("cd", ind=a("ch", 0, 8)), AF.Copy)
+        cp(a("w", 128, 224), a("cd", ind=a("ch", 8, 14)))
+        cp(a("w", 224, 272), a("cd", ind=a("ch", 14, 17)))
         A = a("w", 11, 267, 8)
         ts(a("aw"), A, ZC + 1.5, None, OP.is_ge)
         tt(a("yp", 0, 32), A, a("w", 4, 260, 8), OP.max)
@@ -617,13 +709,11 @@ def rank_program(g, core, T, topo):
         ts(a("uu", 0, 33), a("yp", 0, 33), float(ZC), None, OP.is_equal)
         tt(a("awq"), a("aw"), a("q16", 0, 32), OP.mult)
         cp(a(m1), a("ph", 0, 64))
-        send(a(m1), a(l1), "a1_%d" % t, host)
+        send(a(m1), a(l1), "a1_%d" % t, host, guest)
         tt(a("e1", 0, 33), a("st", 0, 33), a("nl", 0, 33), OP.mult)
         tt(a("e2", 0, 33), a("uu", 0, 33), a("qm1", 0, 33), OP.add)
         mm(a("pp", 64, 96), a("blkb"), a("awq"))
         tt(a("srcf", 0, 33), a("e1", 0, 33), a("e2", 0, 33), OP.add)
-        while extra:
-            extra.pop(0)()
         tt(a("dm"), a("pp", 64, 96), a("dg2"), OP.mult)
         cp(a("src", 0, 33), a("srcf", 0, 33))
         for h in (0, 1):
@@ -634,13 +724,10 @@ def rank_program(g, core, T, topo):
             ts(a("avl", h, h + 1), a("avf", h, h + 1), c(CH[h]), None, OP.max)
         tt(a("srof"), a("srcf", 0, 32), a("awq"), OP.max)
         if t == 0:
-            send(a("avl"), a("lav"), "a2_0", host, "out1")
+            send(a("avl"), a("lav"), "a2_0", host, guest, "out1")
         else:
             cp(a(m2), a(xo, ind=a("avl")))
-            send(a(m2), a(l2), "a2_%d" % t, host)
-        landed(l1, "a1_%d" % t, guest)
-        landed(l2 if t else "lav", "a2_%d" % t, guest)
-        landed(l3, "a3_%d" % t, host)
+            send(a(m2), a(l2), "a2_%d" % t, host, guest)
         cp(a("xv", 0, 256), a(xn, ind=a(l1, 0, 16)))
         act(a("xv", 256, 512), a(xn, ind=a(l1, 16, 32)), AF.Copy)
         conv(a("ph", 0, 32), "zw", "xv", 0, 512)
@@ -698,7 +785,7 @@ def rank_program(g, core, T, topo):
         for h in (0, 1):
             ts(a("tgf", h, h + 1), a("cf", h, h + 1), c(CH[h]), cl[h], OP.add, OP.min)
         cp(a(m3), a(xn, ind=a("tgt")))
-        send(a(m3), a(l3), "a3_%d" % t, guest)
+        send(a(m3), a(l3), "a3_%d" % t, guest, host)
         ts(a("tgw", 0, 2), a("tgf", 0, 2), B0 + 511.5, -512.0, OP.is_ge, OP.mult)
         if last:
             tt(a("dm"), a("pp", 64, 96), a("dg2"), OP.mult)
@@ -716,6 +803,7 @@ def rank_program(g, core, T, topo):
             cp(a("ypb", ind=a("olu")), a(xn, B0, B0 + 512))
             cp(a("ypb", ind=a("avo")), a(l3))
             dma("y", "ld7", [(T.ypup[:], a("ypb", 32, 544))])
+    issue_all()
     for s in sorted(count):
         if s != "ld7":
             g.wait_ge(T.sem[s], count[s])

@@ -3,33 +3,35 @@ from concourse.mybir import AluOpType as OP, AxisListType as AX, ActivationFunct
 
 RO = 4
 NS = 7
-NS0 = 7
+NS0 = 6
 B0 = 48
 LAGV, LAGS = 0.2, 0.0
-HS, HS0 = 384, 128
-QAT = 5
+HS, HS0 = 128, 384
+QAT, QB = 2, 1
 XW = 576
 DW = 8800
-RW = 3216
-E2, C2 = 3072, 1536
+RW = 4240
+E2, C2 = 4096, 2048
 ZC = 8192
 WDT = "float16"
 
 F, I, U, H = "float32", "int32", "uint16", "bfloat16"
 SB = {
-    "dicx": (DW, H), "pupb": (512, H), "seatb": (32, I), "wtb": (4, I), "seatu": (32, U),
-    "x0": (XW, H), "x1": (XW, H), "o0": (512, H), "o1": (512, H), "oio": (512, H), "x2": (752, H), "x2l": (48, U),
+    "dicx": (DW, H), "dicy": (DW, H), "pupb": (512, H), "seatb": (32, I), "wtb": (4, I), "seatu": (32, U),
+    "x0": (XW, H), "x1": (XW, H), "o0": (B0 + 512, H), "o1": (B0 + 512, H), "oc": (32, H), "ocu": (2, U), "oio": (512, H), "x2": (752, H), "x2l": (48, U),
     "lt": (ZC + 16, H), "d0": (512, H), "d1": (512, H), "d2": (512, H),
     "ksi": (48, I), "ks": (48, I), "prod": (512, I), "prs": (512, I), "off": (512, U),
     "pw": (512, H), "lns": (32, F), "nsi": (32, I), "roff": (32, U), "rof2": (32, U), "lnn": (32, F), "nni": (32, I),
-    "r32": (32, U), "pw0": (256, H), "pw1": (256, H), "ln2": (48, F), "neg": (512, H), "zo2": (144, H),
+    "r32": (32, U), "pw0": (256, H), "pw1": (256, H), "ln2": (48, F),
     "pq": (112, F), "dq": (64, F), "zq": (32, F), "wq": (32, F), "tq": (48, F), "sq": (128, F), "st1": (32, F), "st2": (32, F),
     "rq": (128, F), "sc": (128, F), "sd": (128, F), "n15": (32, F), "a15": (32, F), "n2": (32, F), "thn": (32, F),
-    "ex": (RW, F), "eb": (768, H), "cd": (RW, F), "cc": (512, F), "ce": (256, F), "le2": (6, U), "ch": (40, U), "c1": (48, U), "w": (272, F),
+    "ex": (RW, F), "eb": (768, H), "cd": (RW, F), "cc": (512, F), "ce": (384, F), "mq": (32, F), "mq2": (32, F), "nq": (32, F), "nq2": (32, F),
+    "f15": (32, F), "m15": (32, F), "u15": (32, F), "nm": (32, F), "nnm": (32, F), "q32": (32, F), "s0": (168, F), "s1": (168, F),
+    "y1": (36, F), "y2": (36, F), "wa": (272, H), "v4": (136, WDT), "ap4": (136, WDT), "le2": (6, U), "ch": (40, U), "c1": (48, U), "w": (272, F),
     "mc": (64, H), "kni": (32, I), "kn": (32, I), "kn1": (32, F), "ksq": (32, I), "v0": (32, I), "v1": (32, F),
     "nt": (32, F), "nu": (32, F), "nl": (36, F), "aw": (32, F), "st": (36, F), "apk": (64, WDT), "awq": (32, WDT),
     "yp": (36, F), "idx2": (34, U), "uu": (36, F), "e1": (36, F), "e2": (36, F),
-    "srcf": (36, F), "src": (34, U), "srof": (32, F), "sro": (32, U), "g2": (528, H),
+    "srcf": (168, F), "src": (34, U), "srof": (32, F), "sro": (32, U), "g2": (528, H),
     "dm": (32, F), "avf": (4, F), "avl": (2, U), "avo": (2, U), "olf": (32, F), "olu": (32, U), "awo": (32, WDT),
     "xv": (512, H), "sf": (32, F), "vb": (32, F), "vd": (32, F), "vh": (4, F), "vt": (32, F), "cs": (32, F),
     "khi": (32, I), "kh": (32, I), "hp": (32, I), "hs": (32, I), "hw": (32, U), "lt2": (512, H),
@@ -38,7 +40,7 @@ SB = {
     "zo": (144, H), "zw": (144, WDT), "zm": (144, H), "zr": (144, H), "zk": (144, H), "idn": (128, H), "nid": (128, H),
     "nidk": (128, H), "blkb": (128, H), "blkk": (128, H), "g8": (8, H), "dh": (128, H), "dl": (128, H), "ohi": (512, H), "olo": (512, H),
     "io": (144, F), "mg": (128, F), "i16": (48, F), "i8": (32, F), "b32": (32, F),
-    "ie": (256, F), "ia": (256, F), "ic": (256, F), "t1": (256, F), "t2": (256, F), "t3": (256, F),
+    "ie": (256, F), "ia": (256, F), "ic": (384, F), "t1": (256, F), "t2": (256, F), "t3": (256, F),
     "col": (48, F), "ci": (8, I), "q16": (36, F), "qm1": (36, F), "dg": (48, F), "dg2": (32, F), "one": (112, WDT),
     "tm": (232, H), "k7": (32, H), "nio": (16, F),
 }
@@ -59,14 +61,19 @@ for _k, (_w, _d) in SB.items():
 SCRATCH.update({("b_" + k): ("psum", [128, 512], F) for k in PS})
 SEMAPHORES = ["qv", "qs", "qp", "qg", "sent", "a0", "out0", "out1"] + ["ld%d" % i for i in range(8)] + \
              ["a%d_%d" % (m, t) for m in (1, 2, 3) for t in range(RO)]
-(CP, CK, CG, CK16, CG15, CW, CM, CTH, CJ, CX, CS, CQ, CQ0, CTH0, CV, CZ0, CZ1, CA, CB, CD, CL, CL0, C34, CE, CY, CZ, CH0, CH1,
- CT0) = range(29)
+(CP, CK, CG, CK16, CG15, CW, CM, CJ, CX, CS, CQ, CV, CZ0, CA, CB, CD, CL0, C34, C67, CEF, C16, C24, CE, CY,
+ CH0, CH1, CT0) = range(27)
+CZ1 = CT0 + 4
+CTH = CZ1 + 3
 MAG = 1.5 * 2.0 ** 23
 CH = (CK, CK16)
 NONE = 4096.0
-CYC, WAKE, HOP, SLACK, AHEAD = 0.92e-3, 0.2, 1.6, 0.1, 400
+CYC, WAKE, HOP, SLACK, AHEAD = 0.92e-3, 0.2, 1.6, 0.03, 400
+PASSES = 2
+EARLY = 16
+SHORT = 0.1
 ORDER = []
-LOADED = {"ld3": 5.0, "ld4": 8.5, "ld5": 9.0}
+LOADED = {"ld3": 5.5, "ld4": 9.5, "ld5": 10.0}
 
 
 def a(name, lo=0, hi=None, step=1, ind=None, np_=128):
@@ -114,6 +121,33 @@ def cost(q, rd, wr):
     if q == "v" and len(wide) == 3 and all(x[0] in SB for x in wide[1:]):
         n = 2 * n
     return max(64, n) * CYC
+
+
+def lay_out(calls, deps, tail, todo, back):
+    end, free, out = [None] * len(calls), {}, []
+    lead = [x[2] - x[1] if back else 0.0 for x in calls]
+    while todo:
+        ahead, est, byq = todo[:AHEAD], {}, {}
+        for i in ahead:
+            e = free.get(calls[i][0], 0.0) - lead[i]
+            for m, w in deps[i]:
+                e = max(e, (est[m] + calls[m][2] if end[m] is None else end[m]) + w)
+            est[i] = e
+            byq.setdefault(calls[i][0], []).append(i)
+        pick = None
+        for xs in byq.values():
+            xs.sort(key=lambda i: -tail[i])
+            for k, i in enumerate(xs):
+                if (pick is None or est[i] + SHORT * calls[i][1] < est[pick] + SHORT * calls[pick][1]) and all(end[m] is not None for m, _ in deps[i]) and all(
+                        est[i] + calls[i][1] + tail[m] <= est[m] + max(tail[m], calls[m][1] + tail[i]) + SLACK for m in xs[:k]):
+                    pick = i
+        if pick is None:
+            pick = ahead[0]
+        end[pick] = est[pick] + calls[pick][2]
+        free[calls[pick][0]] = est[pick] + lead[pick] + calls[pick][1]
+        todo.remove(pick)
+        out.append(pick)
+    return out, end
 
 
 def rank_program(g, core, T, topo):
@@ -181,6 +215,7 @@ def rank_program(g, core, T, topo):
     seen = {}
     rows = {}
     in_row = [None]
+    in_sum, loose = [False], set()
 
     def record(q, rd, wr, busy, done, issue, after=()):
         n, dep = len(calls), {m: WAKE for m in after}
@@ -188,7 +223,8 @@ def rank_program(g, core, T, topo):
         for name, m, w in use:
             for (m2, w2, q2, n2) in seen.get(name, []):
                 if name in PS and q == q2 == "p":
-                    dep.setdefault(n2, 0.0)
+                    if n2 not in loose or not in_sum[0]:
+                        dep.setdefault(n2, 0.0)
                 elif (name in PS and q2 != q) or ((w or w2) and m & m2):
                     dep[n2] = WAKE
         if in_row[0] is not None:
@@ -198,9 +234,11 @@ def rank_program(g, core, T, topo):
             rows[key] = n
         for name, m, w in use:
             lst = seen.setdefault(name, [])
-            if name in PS and q == "p":
+            if name in PS and in_sum[0]:
+                loose.add(n)
+            elif name in PS and q == "p":
                 lst[:] = []
-            if w:
+            elif w:
                 lst[:] = [e for e in lst if e[0] & ~m]
             lst.append((m, w, q, n))
         calls.append((q, busy, done, list(dep.items()), issue))
@@ -217,37 +255,24 @@ def rank_program(g, core, T, topo):
         record(q, rd, wr, t, t, issue)
 
     def issue_all():
-        if ORDER:
-            for i in ORDER:
-                calls[i][4]()
-            return
-        n = len(calls)
-        tail = [0.0] * n
-        for i in range(n - 1, -1, -1):
-            tail[i] += calls[i][2]
-            for m, w in calls[i][3]:
-                tail[m] = max(tail[m], w + tail[i])
-        end, free, todo = {}, {}, list(range(n))
-        while todo:
-            ahead, est, byq = todo[:AHEAD], {}, {}
-            for i in ahead:
-                est[i] = max([free.get(calls[i][0], 0.0)] + [(end[m] if m in end else est[m] + calls[m][2]) + w for m, w in calls[i][3]])
-                byq.setdefault(calls[i][0], []).append(i)
-            pick = None
-            for q, xs in byq.items():
-                xs.sort(key=lambda i: -tail[i])
-                for k, i in enumerate(xs):
-                    if all(m in end for m, _ in calls[i][3]) and all(
-                            est[i] + calls[i][1] + tail[m] <= est[m] + max(tail[m], calls[m][1] + tail[i]) + SLACK for m in xs[:k]):
-                        if pick is None or est[i] < est[pick]:
-                            pick = i
-            if pick is None:
-                pick = ahead[0]
-            end[pick] = est[pick] + calls[pick][2]
-            free[calls[pick][0]] = est[pick] + calls[pick][1]
-            todo.remove(pick)
-            ORDER.append(pick)
-            calls[pick][4]()
+        if not ORDER:
+            n = len(calls)
+            before = [x[3] for x in calls]
+            behind = [[] for _ in calls]
+            tail = [0.0] * n
+            for i in range(n - 1, -1, -1):
+                tail[i] += calls[i][2]
+                for m, w in before[i]:
+                    tail[m] = max(tail[m], w + tail[i])
+                    behind[m].append((i, w))
+            best = None
+            for _ in range(PASSES):
+                order_, end = lay_out(calls, before, tail, list(range(n)), False)
+                if best is None or max(end) < best:
+                    best, ORDER[:] = max(end), order_
+                tail = lay_out(calls, behind, end, list(range(n - 1, -1, -1)), True)[1]
+        for i in ORDER:
+            calls[i][4]()
 
     def ts(o, i, s1, s2, o0, o1=None):
         if o1 is None:
@@ -282,21 +307,31 @@ def rank_program(g, core, T, topo):
     def mm(o, l, r, st=True, sp=True):
         op("p", [l, r], [o], lambda: g.tensor.matmul(ap(o), ap(l), ap(r), st, sp))
 
+    def add_mm(o, l, r, left):
+        def fn():
+            left[0] -= 1
+            return g.tensor.matmul(ap(o), ap(l), ap(r), False, left[0] == 0)
+        left[0] += 1
+        in_sum[0] = True
+        op("p", [l, r], [o], fn)
+        in_sum[0] = False
+
     def iota(o, pat, base, cm=0):
         if SB[o[0]][1] == I:
             op("g", [], [o], lambda: g.iota(ap(o), pat, base, cm))
         else:
             op("g", [], [o], lambda: g.iota(ap(o), pat, base, cm, allow_small_or_imprecise_dtypes=True))
 
-    def dma(q, s, pairs):
+    def dma(q, s, pairs, also=()):
         (o, i), = pairs
 
         def issue():
+            order(q, list(also), [])
             use = order(q, [i], [o])
             eng[q].dma_start(ap(o), ap(i)).then_inc(T.sem[s], 16)
             count[s] = 16
             note(use, q, s, 16)
-        record(q, [i], [o], 0.1, LOADED.get(s, 1.5), issue)
+        record(q, [i] + list(also), [o], 0.1, LOADED.get(s, 1.5), issue)
 
     def send(src, dst, s, to, frm, loc="sent", also=()):
         def issue():
@@ -330,8 +365,8 @@ def rank_program(g, core, T, topo):
     dma("s", "ld2", [(a("wtb", 0, 1), T.wt[:])])
     dma("y", "ld3", [(a("dicx", 0, 4096), T.dic[:, 0:4096])])
     dma("s", "ld4", [(a("dicx", 4096, 8192), T.dic[:, 4096:8192])])
-    dma("y", "ld5", [(a("dicx", 8192, DW), T.dic[:, 0:DW - 8192])])
     in_row[0] = None
+    cp(a("dicx", 8192, DW), a("dicx", 0, DW - 8192))
     ms(a("ln2"), 1.0)
     act(a("lns", 0, 1), a("ln2", 0, 1), AF.Ln)
 
@@ -342,13 +377,16 @@ def rank_program(g, core, T, topo):
     iota(a("b32"), [[256, 2], [1, 16]], 0)
     iota(a("ie"), [[0, 16], [1, 16]], 0)
     iota(a("ia"), [[1, 16], [0, 16]], 0)
-    iota(a("ic"), [[32, 16], [1, 16]], 16)
+    iota(a("ic"), [[64, 24], [1, 16]], 512)
+    iota(a("mq"), [[0, 8], [1, 4]], 0)
+    iota(a("thn"), [[1, 8], [0, 4]], 0)
     iota(a("i8"), [[1, 16], [0, 2]], 0)
     iota(a("sq", 0, 32), [[0, 8], [1, 4]], int(MAG) - 3)
     iota(a("st1"), [[0, 8], [1, 4]], int(MAG) - 1026)
     iota(a("st2"), [[0, 8], [1, 4]], int(MAG) - 1025)
     iota(a("eb", 512, 768), [[1, 256]], 1)
-    iota(a("cd", 512, 1024), [[0, 512]], -1)
+    for lo in (512, 1024, C2 + 512):
+        iota(a("cd", lo, lo + 512), [[0, 512]], -1)
     for x in ("x0", "x1"):
         ms(a(x, 0, B0), -1.0)
         ms(a(x, B0 + 512, XW), -1.0)
@@ -368,10 +406,8 @@ def rank_program(g, core, T, topo):
     ts(a("t1", 112, 160), a("t1", 64, 112), B0 + 511.5, None, OP.is_le)
     ts(a("dg"), a("i16"), c(CK), None, OP.is_equal)
     tt(a("t1", 160, 208), a("t1", 64, 112), a("t1", 112, 160), OP.mult)
-    ts(c(CQ), c(CK), NS - 0.5, -8.5, OP.is_le, OP.mult)
     ts(a("x2l"), a("t1", 160, 208), 32.0, None, OP.max)
     tt(a("t1", 48, 64), a("t1", 32, 48), a("dg", 0, 16), OP.mult)
-    ts(c(CQ0), c(CK), NS0 - 0.5, -8.5, OP.is_le, OP.mult)
     red(c(CM), a("t1", 48, 64), OP.add)
     cp(a("seatu"), a("seatb"))
     ts(c(CX), a("wtb", 0, 1), 2048.0, -4096.0, OP.is_ge, OP.mult)
@@ -383,26 +419,30 @@ def rank_program(g, core, T, topo):
         for j, (m, b) in {CK16: (1, 16), CJ: (1, B0), CV: (-1, B0 - 1), CH0: (2, 0), CH1: (2, 1),
                           CT0: (-37, 555), CT0 + 1: (-37, 566), CT0 + 2: (-37, 577), CT0 + 3: (-37, 588)}.items():
             aff(c(j), c(CK), float(m), float(b))
-        aff(c(CTH), c(CQ), 1.0, 7.5)
-        aff(c(CTH0), c(CQ0), 1.0, 7.5)
-        aff(c(CY), row(11), 1.0, row(12))
-        aff(c(C34), row(3), 1.0, row(4))
-        aff(c(CL), row(1), float(E2), 0.0)
-        aff(c(CZ), c(CY), 32.0, row(1))
-        aff(c(CB), row(1), 8.0, c(CY))
-        aff(c(CL), row(12), float(C2), c(CL))
-        aff(c(CA), row(0), 16.0, c(CZ))
-        aff(c(CB), row(0), 1.0, c(CB))
-        aff(c(CD), c(C34), 60000.0, c(CL))
+        for n in sorted({NS - 1, NS, NS0 - 1, NS0}):
+            ts(c(CQ), c(CK), n - 0.5, -8.5, OP.is_le, OP.mult)
+            aff(c(CTH + n), c(CQ), 1.0, 7.5)
+        def sums(j, first, *terms):
+            for f, x in terms:
+                aff(c(j), x, float(f), first)
+                first = c(j)
+        sums(C34, row(3), (1, row(4)))
+        sums(C67, row(6), (1, row(7)))
+        sums(CEF, row(14), (1, row(15)))
+        sums(CY, row(11), (1, row(12)), (1, c(CEF)))
+        sums(C16, c(C34), (1, c(C67)))
+        sums(C24, c(C16), (1, c(CEF)))
+        sums(CA, row(1), (64, c(CY)), (16, row(0)))
+        sums(CB, c(CY), (8, row(1)), (1, row(0)))
+        sums(CD, c(CB), (E2, row(1)), (559, c(CEF)), (C2, row(12)), (C2, row(14)), (60000, c(C16)))
+        sums(CL0, 0.0, (C2, row(12)), (512, c(C24)))
+        sums(CE, -60000.0, (-480, c(C67)), (-1008, c(C34)), (-1488, c(CEF)), (C2, row(4)), (C2, row(6)), (C2, row(14)))
         aff(c(CZ0), row(1), -1.0, 1.0)
-        aff(c(CZ1), row(12), float(C2), 0.0)
-        aff(c(CL0), c(C34), 512.0, c(CZ1))
-        aff(c(CE), c(C34), -60000.0, 60000.0)
-        aff(c(CD), c(CB), 1.0, c(CD))
-        aff(c(CE), row(4), float(C2), c(CE))
         aff(a("t2"), a("ia"), c(CA), c(CD))
         aff(a("t3"), a("ie"), c(CB), 0.0)
-        aff(a("ce"), a("ic"), c(C34), c(CE))
+        for n, j in enumerate((C67, C16, C24)):
+            aff(c(CZ1 + n), c(j), c(CE), 60000.0)
+            aff(a("ce", 128 * n, 128 * n + 128), a("ic", 128 * n, 128 * n + 128), c(j), c(CZ1 + n))
 
     def later_constants():
         tt(a("ex", 512, 768), a("t2"), a("t3"), OP.add)
@@ -431,16 +471,18 @@ def rank_program(g, core, T, topo):
         ts(add, add, -1.0, None, OP.add)
         tt(uns, uns, eq, OP.add)
         for k in range(15, -1, -1):
+            in_row[0] = 0 if k >= EARLY else None
             def col(x):
                 return a("t1", x[1] + k, x[1] + k + 1)
-            aff(a("cc", 32 * k, 32 * k + 32), a("b32"), col(gt), col(add))
-            aff(a("cd", 1024 + 32 * k, 1056 + 32 * k), a("b32"), 0.0, col(uns))
-            aff(a("cd", C2 + 512 + 32 * k, C2 + 544 + 32 * k), a("b32"), col(lt), col(add2))
-            aff(a("cd", C2 + 1024 + 32 * k, C2 + 1056 + 32 * k), a("b32"), 0.0, col(uns2))
+            w = 64 * (k % 8) + 32 * (k // 8)
+            aff(a("cc", w, w + 32), a("b32"), col(gt), col(add))
+            aff(a("cd", 1536 + w, 1568 + w), a("b32"), 0.0, col(uns))
+            aff(a("cd", C2 + 1024 + w, C2 + 1056 + w), a("b32"), col(lt), col(add2))
+            aff(a("cd", C2 + 1536 + w, C2 + 1568 + w), a("b32"), 0.0, col(uns2))
+        in_row[0] = None
         ms(a("lt", ZC, ZC + 16), 0.0)
-        ts(a("zm"), a("zo"), c(CM), None, OP.mult)
-        ts(a("zo2"), a("zo"), 2.0, None, OP.mult)
-        ms(a("neg"), -1.0)
+        ts(c(CX), c(CK), 14.5, c(CM), OP.is_le, OP.mult)
+        ts(a("zm"), a("zo"), c(CX), None, OP.mult)
         ms(a("st1", 3, 32, 4), MAG - 8192)
         ms(a("st2", 2, 32, 4), MAG - 8192)
         ms(a("sq", 96, 128), MAG - 8192)
@@ -450,7 +492,10 @@ def rank_program(g, core, T, topo):
     def last_constants():
         return [
             lambda: ms(a("sd"), 0.0),
-            lambda: ts(a("thn"), a("i16", 0, 32), -14.5, None, OP.add),
+            lambda: ts(a("thn"), a("thn"), -6.5, None, OP.add),
+            lambda: ts(a("mq2"), a("mq"), 1.0 / 60, None, OP.mult),
+            lambda: ts(a("mq"), a("mq"), 0.25, None, OP.mult),
+            lambda: ms(a("v4"), 0.0),
             lambda: ms(a("sd", 3, 128, 4), -MAG),
             lambda: ts(a("zr"), a("zo"), row(0), None, OP.mult),
             lambda: cp(a("ch", 0, 1), c(CL0)),
@@ -459,7 +504,11 @@ def rank_program(g, core, T, topo):
             lambda: ts(a("mc", 0, 32), a("io", 0, 32), 0.0, c(CV), OP.mult, OP.add),
             lambda: cp(a("q16", 32, 33), c(CJ)),
             lambda: ms(a("mc", 32, 64), 2048.0),
-            lambda: ts(a("qm1"), a("q16"), -1.0, None, OP.add),
+            lambda: ts(a("s1", 1, 165, 5), a("q16", 0, 33), -1.0, None, OP.add),
+            lambda: ts(a("q32"), a("q16", 0, 32), 1.0 / 32, None, OP.mult),
+            lambda: ms(a("s0"), 1.0),
+            lambda: ms(a("s0", 0, 165, 5), 0.0),
+            lambda: ms(a("y2", 32, 33), -1.0),
         ]
 
     def visit_constants():
@@ -467,7 +516,6 @@ def rank_program(g, core, T, topo):
             lambda: ts(a("dg2"), a("i8"), c(CK), None, OP.is_equal),
             lambda: ts(a("zk"), a("zo"), NONE, None, OP.mult),
             lambda: ms(a("k7"), -7 * NONE),
-            lambda: ts(a("nio"), a("io", 0, 16), -1.0, None, OP.mult),
             lambda: ms(a("one"), 1.0),
             lambda: ts(a("blkk"), a("mg"), c(CG), 1024.0, OP.is_equal, OP.mult),
             lambda: ts(a("nidk"), a("io", 0, 128), c(CP), -1024.0, OP.is_equal, OP.mult),
@@ -487,7 +535,9 @@ def rank_program(g, core, T, topo):
         mm(a("pa"), a("dh"), a("ohi"), True, False)
         mm(a("pa"), a("dl"), a("olo"), False, True)
         act(a("oio"), a("pa"), AF.Copy)
-        act(a("o0"), a("oio", ind=a("seatu")), AF.Copy)
+        act(a("o0", B0, B0 + 512), a("oio", ind=a("seatu")), AF.Copy)
+        for o in ("o0", "o1"):
+            ts(a(o, 0, B0), a("io", 0, B0), -32.0, row(0), OP.add, OP.mult)
 
     scalar_constants()
     BIG = float(1 << 20)
@@ -505,27 +555,30 @@ def rank_program(g, core, T, topo):
         conv(a("pk", 64, 96), "zw", xo, B0, B0 + 512)
         ts(a("ks", 0, 47), a("ksi", 0, 47), 4095, None, OP.bitwise_and)
 
-        def mults(js):
+        at = lambda j: 64 * (j % 8) + 32 * (j // 8)
+        for js in ([0], [1, 2], [3, 4, 5], [6, 7]):
             for j in js:
-                tt(a("prod", 32 * j, 32 * j + 32), a("ks", 0, 32), a("ks", j, j + 32), OP.mult)
-
-        def shift(js):
-            ts(a("prs", 32 * js[0], 32 * js[-1] + 32), a("prod", 32 * js[0], 32 * js[-1] + 32), 5, 8191,
-               OP.logical_shift_right, OP.bitwise_and)
-
-        def adds(js):
+                for j2 in (j, j + 8):
+                    tt(a("prod", at(j2), at(j2) + 32), a("ks", 0, 32), a("ks", j2, j2 + 32), OP.mult)
+            lo, hi = at(js[0]), at(js[-1]) + 64
+            ts(a("prs", lo, hi), a("prod", lo, hi), 5, 8191, OP.logical_shift_right, OP.bitwise_and)
+            in_row[0] = t
             for j in js:
-                ts(a("off", 32 * j, 32 * j + 32), a("prs", 32 * j, 32 * j + 32), float((37 * j + 11 * t) % 16), None, OP.add)
-
-        for js in ([0, 1], [2, 3, 4, 5], [6, 7, 8, 9], [10, 11, 12], [13, 14, 15]):
-            mults(js); shift(js); adds(js)
+                if t > 0:
+                    ts(a("off", at(j), at(j) + 64), a("prs", at(j), at(j) + 64), float((37 * j + 11 * t) % 8), None, OP.add)
+                else:
+                    for j2 in (j, j + 8):
+                        ts(a("off", at(j2), at(j2) + 32), a("prs", at(j2), at(j2) + 32), float(37 * j2 % 16), None, OP.add)
+            in_row[0] = None
         if t == 0:
             later_constants()
             for f in last_constants():
                 f()
             send(a(xo, 0, B0 + 512), a("xg"), "a0", host, guest, "out0", [a("dicx", 0, 8192)])
-            for lo in range(768, E2, 584):
-                iota(a("ex", lo, lo + 584), [[0, 584]], 0)
+            dma("y", "ld5", [(a("dicy", 0, DW - 8), a("dicx", 8, DW))])
+            ms(a("dicy", DW - 8, DW), 0.0)
+            for lo in range(768, E2, 560):
+                iota(a("ex", lo, lo + 560), [[0, 560]], 0)
             iota(a("ex", E2 + 128, RW), [[0, RW - E2 - 128]], 0)
             iota(a("cd", E2, RW), [[0, RW - E2]], 0)
             iota(a("ohi"), [[16, 32], [0, 16]], 0)
@@ -533,7 +586,8 @@ def rank_program(g, core, T, topo):
 
         def word(j, lo=0, hi=32):
             ws = (37 * j + 11 * t) // 16 * 16
-            return a("dicx", ws, ws + 8208, ind=a("off", 32 * j + lo, 32 * j + hi))
+            later = t > 0 and (37 * j + 11 * t) % 16 >= 8
+            return a("dicy" if later else "dicx", ws, ws + 8208, ind=a("off", at(j) + lo, at(j) + hi))
 
         def ltj(j, lo=0, hi=512):
             w = 512 * ((14 - j) % 16)
@@ -567,9 +621,9 @@ def rank_program(g, core, T, topo):
         half = ns - 1
         hs = HS0 if t == 0 else HS
         ev.append((tv, "vh", half)); tv += 0.72 * (512 - hs) / 512
-        for j in range(ns, 16):
+        for j in range(ns, 15):
             ev.append((tv, "vg", j)); tv += 0.72; ev.append((tv + LAGV, "cnt", j))
-            if j >= 16 - QAT + (t == 0):
+            if j >= 15 - QAT:
                 ev.append((tv - 0.01, "quad", j)); tv += 0.12
         for j in range(ns + 1):
             if j < ns:
@@ -579,11 +633,11 @@ def rank_program(g, core, T, topo):
                 if j == 3:
                     ev.append((tsc + LAGS + 0.001, "quads", j))
         ev.sort()
-        ncnt = [0]
-        qs = quads()
+        ncnt, opened = [0], False
+        qs = iter(())
         for _, kind, j in ev:
             n = hs if j == half else 512
-            d, bank = a("d%d" % (j % 3), 0, n), a("pa" if j % 2 == 0 else "pb", 0, n)
+            d, bank = a("d%d" % (j % 3), 0, n), a(("pa", "pb", "ph", "pn", "pm")[j % 5], 0, n)
             in_row[0] = t if kind in ("vg", "vh", "sg", "sign", "quad") else None
             if kind == "vg":
                 tt(ltj(j), word(j), a("x2", 16 * j, 16 * j + 512), OP.is_gt)
@@ -592,61 +646,83 @@ def rank_program(g, core, T, topo):
             elif kind == "sg":
                 act(d, word(j, 0, n // 16), AF.Copy)
             elif kind == "sub":
-                mm(bank, a("idn"), d, True, False)
-                mm(bank, a("nid"), a("x2", 16 * j, 16 * j + n), False, True)
+                mm(bank, a("nid"), a("x2", 16 * j, 16 * j + n), True, False)
+                mm(bank, a("idn"), d, False, True)
                 if j == half - 1:
-                    mm(a("pc", hs, 512), sel("zo2", half), ltj(half, hs, 512), False, False)
-                    mm(a("pc", hs, 512), sel("zo", half), a("neg", hs, 512), False, False)
+                    add_mm(a("pc", hs, 512), sel("zo", half), ltj(half, hs, 512), ncnt)
             elif kind == "sign":
                 act(ltj(j, 0, n), bank, AF.Sign, -0.5)
             elif kind == "quads":
                 conv(a("pp", 0, 96), "zo", "lt", 6144, 7680)
+                qs = quads()
             elif kind == "quad":
                 next(qs, None)
             elif j == half:
-                mm(a("pc", 0, hs), sel("zo", j), ltj(j, 0, hs), False, ncnt[0] == 15)
-                ncnt[0] += 1
+                add_mm(a("pc", 0, hs), sel("zo", j), ltj(j, 0, hs), ncnt)
+            elif opened:
+                add_mm(a("pc"), sel("zo", j), ltj(j), ncnt)
             else:
-                mm(a("pc"), sel("zo", j), ltj(j), ncnt[0] == 0, ncnt[0] == 15)
-                ncnt[0] += 1
+                mm(a("pc"), sel("zo", j), ltj(j), True, False)
+                opened = True
         in_row[0] = t
-        next(qs, None)
+        for _ in range(QB):
+            next(qs, None)
         for e in (0, 1):
-            ts(a("pw%d" % e), a("pc", e, 512, 2), c(CTH0 if t == 0 else CTH), None, OP.is_le)
+            for lo, hi in ((0, hs), (hs, 512)):
+                ts(a("pw%d" % e, lo // 2, hi // 2), a("pc", lo + e, hi, 2), c(CTH + ns - (lo > 0)), None, OP.is_le)
         for _ in qs:
             pass
-        ts(a("pw"), a("pc"), c(CTH0 if t == 0 else CTH), None, OP.is_le)
+        act(a("d1"), word(15), AF.Copy)
         in_row[0] = None
+        mm(a("ph"), a("nid"), a("x2", 240, 752), True, False)
+        mm(a("ph"), a("idn"), a("d1"), False, True)
+        act(ltj(15), a("ph"), AF.Sign, -0.5)
         for i in list(range(0, 16, 2)) + list(range(1, 16, 2)):
             mm(a("pm", 0, 32), sel("zm", i), a("pw%d" % (i % 2), i // 2, 256, 8), i == 0, i == 15)
-        act(a("ln2", 0, 32), a("pm", 0, 32), AF.Ln, math.exp(-15.4), math.exp(-0.2))
-        act(a("lns"), a("pm", 0, 32), AF.Ln, math.exp(-31.2), math.exp(-0.2))
+        LNB, LNS = math.exp(-15.2), math.exp(-0.2)
+        act(a("ln2", 0, 32), a("pm", 0, 32), AF.Ln, LNB, LNS)
+        halves = [(2 * u + h, 16 * h + 8 * u) for h in (0, 1) for u in (0, 1)]
+        for m, lo in halves:
+            act(a("lns", m, 32, 4), a("pm", lo, lo + 8), AF.Ln, LNB, LNS)
+        conv(a("pa", 0, 32), "zo", "lt", 7680, 8192)
+        for m, lo in halves:
+            act(a("f15", m, 32, 4), a("pa", lo, lo + 8), AF.Relu, 8.0, 8.0)
+        for lo in range(0, 512, 128):
+            act(a("d0", lo, lo + 128), a("pc", lo, lo + 128), AF.Sign, c(CTH + ns - (lo >= hs)), -1.0)
+            act(a("pw", lo, lo + 128), a("d0", lo, lo + 128), AF.Relu)
         for h in (0, 1):
             for k in range(16):
-                mm(a("pn", 16 * h, 16 * h + 16), sel("zm", k), a("pw", 256 * h + 16 * k, 256 * h + 16 * k + 16), k == 0, k == 15)
+                w = 256 * h + 16 * k
+                mm(a("pn", 16 * h, 16 * h + 16), sel("zm", k), a("pw", w, w + 16), k == 0, k == 15)
         for dl in range(4):
             tt(a("rq", dl, 128, 4), a("sq", 32 * dl, 32 * dl + 32), a("ln2", dl, dl + 32), OP.subtract)
-        ts(a("nsi"), a("lns"), -1.0, None, OP.mult)
         scan(a("sc"), a("rq"), a("sd"), 0.0, OP.max, OP.add)
-        tt(a("a15"), a("lns"), a("thn"), OP.is_le)
-        ts(a("roff", 0, 32, 2), a("nsi", 0, 16), 32.0, c(CK), OP.mult, OP.add)
-        ts(a("roff", 1, 32, 2), a("nsi", 16, 32), 32.0, c(CK16), OP.mult, OP.add)
         ts(a("r32"), a("sc", 3, 128, 4), 16.0, c(CK), OP.mult, OP.add)
-        ts(a("n15"), a("nsi"), 1.0 / 15, None, OP.mult)
+        ts(a("nsi"), a("lns"), -1.0, None, OP.mult)
+        ts(a("m15"), a("lns"), -14.6, 8.0, OP.is_le, OP.mult)
+        tt(a("a15"), a("lns"), a("thn"), OP.is_le)
+        tt(a("nm"), a("nsi"), a("mq"), OP.add)
+        tt(a("u15"), a("m15"), a("f15"), OP.min)
+        tt(a("nq2"), a("a15"), a("mq2"), OP.add)
+        tt(a("nq"), a("nm"), a("u15"), OP.add)
+        ts(a("roff"), a("nq"), 64.0, c(CK), OP.mult, OP.add)
+        aff(a("n15"), a("nq"), 1.0 / 15, 0.0)
+        tt(a("n2"), a("n15"), a("nq2"), OP.max)
+        ts(a("rof2"), a("n2"), 960.0, c(CK), OP.mult, OP.add)
 
         def codes(k):
-            w = 32 * (k + 1)
-            tt(a("cd", w - 32, w), a("cd", w, w + 1024, ind=a("roff", 2 * k, 2 * k + 2)), a("cc", 32 * k, 32 * k + 32), OP.max)
+            w = 64 * (k + 1)
+            tt(a("cd", w - 64, w), a("cd", w, w + 1536, ind=a("roff", 4 * k, 4 * k + 4)), a("cc", w - 64, w), OP.max)
 
         def codes2(k):
-            w = C2 + 32 * (k + 1)
-            act(a("cd", w - 32, w), a("cd", w, w + 1024, ind=a("rof2", 2 * k, 2 * k + 2)), AF.Copy)
+            w = C2 + 64 * (k + 1)
+            act(a("cd", w - 64, w), a("cd", w, w + 1536, ind=a("rof2", 4 * k, 4 * k + 4)), AF.Copy)
 
         def exits(q):
             w = 64 * (q + 1)
             src = a("ex", w, w + 256, ind=a("r32", 4 * q, 4 * q + 4))
-            if q >= 4:
-                tt(a("ex", w - 64, w), src, a("ce", w - 320, w - 256), OP.min)
+            if q >= 2:
+                tt(a("ex", w - 64, w), src, a("ce", w - 192, w - 128), OP.min)
             else:
                 cp(a("ex", w - 64, w), src)
             act(a("eb", w - 64, w), a("eb", w, w + 256, ind=a("r32", 4 * q, 4 * q + 4)), AF.Copy)
@@ -657,12 +733,9 @@ def rank_program(g, core, T, topo):
         def chain(m):
             cp(a("ch", 2 * m + 1, 2 * m + 17), a("ex", ind=a("ch", 2 * m, 2 * m + 1)))
 
-        tt(a("n2"), a("n15"), a("a15"), OP.max)
-        ts(a("rof2", 0, 32, 2), a("n2", 0, 16), 480.0, c(CK), OP.mult, OP.add)
-        ts(a("rof2", 1, 32, 2), a("n2", 16, 32), 480.0, c(CK16), OP.mult, OP.add)
-        for k in range(15, -1, -1):
-            if k >= 8:
-                exits(k - 8)
+        for k in range(7, -1, -1):
+            exits(k)
+        for k in range(7, -1, -1):
             codes(k)
             codes2(k)
         cp(a("le2"), a("pp", 0, 6))
@@ -674,70 +747,80 @@ def rank_program(g, core, T, topo):
         for m in range(2, 8):
             chain(m)
         for h in (0, 1):
-            act(a("lnn", h, 32, 2), a("pn", 16 * h, 16 * h + 16), AF.Ln, math.exp(-31.2), math.exp(-0.2))
+            act(a("lnn", h, 32, 2), a("pn", 16 * h, 16 * h + 16), AF.Ln, LNB, LNS)
+        aff(a("nnm"), a("lnn"), -1.0, MAG)
+        aff(a("s0", 1, 160, 5), a("nnm"), 1.0, 1.0 - MAG)
+        aff(a("s0", 161, 162), a("nnm", 0, 1), 1.0, 1.0 - MAG)
         ts(a("kni"), a("pk", 64, 96), BIG, None, OP.add)
-        ts(a("nni"), a("lnn"), -1.0, 1.0, OP.mult, OP.add)
         ts(a("kn"), a("kni"), 4095, None, OP.bitwise_and)
-        ts(a("nt"), a("nni"), 20.0, None, OP.is_ge)
         tt(a("ksq"), a("kn"), a("kn"), OP.mult)
-        tt(a("nu"), a("nt"), a("qm1", 0, 32), OP.mult)
         ts(a("v0"), a("ksq"), 5, 511, OP.logical_shift_right, OP.bitwise_and)
-        tt(a("nl", 0, 32), a("nni"), a("nu"), OP.subtract)
-        ts(a("kn1"), a("kn"), -2048.0, None, OP.add)
-        cp(a("nl", 32, 33), a("nl", 0, 1))
-        ts(a("v1"), a("v0"), 16.0, None, OP.add)
+        for lo in (0, 3):
+            ts(a("v4", lo, lo + 64, 2), a("v0"), 16.0, None, OP.add)
+            ts(a("v4", 68 + lo, 68 + lo + 64, 2), a("kn"), -2048.0, None, OP.add)
         if t == 0:
             ts(a("dh"), a("idn"), row(0), None, OP.mult)
             ts(a("dl"), a("idn"), row(1), None, OP.mult)
             for f in visit_constants():
                 f()
         mm(a("ph", 0, 64), a("idn"), a("mc"), True, False)
-        act(a("w", 0, 128), a("cd", ind=a("ch", 0, 8)), AF.Copy)
-        cp(a("w", 128, 224), a("cd", ind=a("ch", 8, 14)))
-        cp(a("w", 224, 272), a("cd", ind=a("ch", 14, 17)))
-        A = a("w", 11, 267, 8)
-        ts(a("aw"), A, ZC + 1.5, None, OP.is_ge)
-        tt(a("yp", 0, 32), A, a("w", 4, 260, 8), OP.max)
-        cp(a("yp", 32, 33), a("w", 11, 12))
-        tt(a("apk", 0, 32), a("aw"), a("v1"), OP.mult)
-        tt(a("apk", 32, 64), a("aw"), a("kn1"), OP.mult)
+        for lo, hi in ((0, 8), (8, 12), (12, 17)):
+            if hi < 17:
+                act(a("w", 16 * lo, 16 * hi), a("cd", ind=a("ch", lo, hi)), AF.Copy)
+            else:
+                cp(a("w", 16 * lo, 16 * hi), a("cd", ind=a("ch", lo, hi)))
+            act(a("wa", 16 * lo, 16 * hi), a("cd", ind=a("ch", lo, hi)), AF.Relu, -(ZC + 1.0))
+        tt(a("y1", 0, 32), a("w", 11, 267, 8), a("w", 23, 272, 8), OP.max)
+        tt(a("y1", 32, 33), a("w", 11, 12), a("w", 23, 24), OP.max)
+        tt(a("y2", 0, 32), a("w", 4, 260, 8), a("w", 14, 270, 8), OP.max)
+        for n in (0, 1):
+            tt(a("ap4", 68 * n, 68 * n + 66), a("wa", 11, 272, 4), a("v4", 68 * n, 68 * n + 66), OP.mult)
+        y1, y2 = a("y1", 0, 33), a("y2", 0, 33)
+        tt(a("yp", 0, 33), y1, y2, OP.max)
         cp(a("idx2", 0, 33), a("yp", 0, 33))
-        mm(a("ph", 0, 64), a("blkb"), a("apk"), False, True)
-        act(a("g2", 0, 256), a("lt", ind=a("idx2", 0, 16)), AF.Relu)
-        act(a("g2", 256, 528), a("lt", ind=a("idx2", 16, 33)), AF.Relu)
-        ts(a("st", 0, 33), a("yp", 0, 33), ZC + 0.5, None, OP.is_ge)
-        ts(a("uu", 0, 33), a("yp", 0, 33), float(ZC), None, OP.is_equal)
-        tt(a("awq"), a("aw"), a("q16", 0, 32), OP.mult)
+        for n in (0, 1):
+            for lo in (0, 3):
+                mm(a("ph", 32 * n, 32 * n + 32), a("blkb"), a("ap4", 68 * n + lo, 68 * n + lo + 63, 2), False, n == 1 and lo == 3)
         cp(a(m1), a("ph", 0, 64))
         send(a(m1), a(l1), "a1_%d" % t, host, guest)
-        tt(a("e1", 0, 33), a("st", 0, 33), a("nl", 0, 33), OP.mult)
-        tt(a("e2", 0, 33), a("uu", 0, 33), a("qm1", 0, 33), OP.add)
+        ts(a("s1", 0, 165, 5), y1, ZC + 0.5, None, OP.is_ge)
+        ts(a("s1", 2, 165, 5), y1, float(ZC), None, OP.is_equal)
+        ts(a("s1", 3, 165, 5), y2, float(ZC), None, OP.is_equal)
+        ts(a("s0", 4, 165, 5), y1, ZC + 1.5, None, OP.is_le)
+        ts(a("s1", 4, 165, 5), y1, ZC + 1.5, 32.0, OP.is_ge, OP.mult)
+        scan(a("srcf", 0, 165), a("s0", 0, 165), a("s1", 0, 165), 0.0, OP.mult, OP.add)
+        cp(a("src", 0, 33), a("srcf", 4, 165, 5))
+        aw = a("s1", 4, 160, 5)
+        tt(a("awq"), aw, a("q32"), OP.mult)
         mm(a("pp", 64, 96), a("blkb"), a("awq"))
-        tt(a("srcf", 0, 33), a("e1", 0, 33), a("e2", 0, 33), OP.add)
         tt(a("dm"), a("pp", 64, 96), a("dg2"), OP.mult)
-        cp(a("src", 0, 33), a("srcf", 0, 33))
         for h in (0, 1):
             red(a("avf", h, h + 1), a("dm", h, 32, 2), OP.max)
-        tt(a(xn, B0, B0 + 256), a(xo, ind=a("src", 0, 16)), a("g2", 0, 256), OP.add)
-        tt(a(xn, B0 + 256, B0 + 528), a(xo, ind=a("src", 16, 33)), a("g2", 256, 528), OP.add)
+        tt(a("srof"), a("srcf", 4, 160, 5), a("awq"), OP.max)
+        if t == 0:
+            first_numbers()
+        thirds = ((0, 10), (10, 22), (22, 33))
+        for lo, hi in thirds:
+            act(a("g2", 16 * lo, 16 * hi), a("lt", ind=a("idx2", lo, hi)), AF.Relu)
+        for lo, hi in thirds:
+            tt(a(xn, B0 + 16 * lo, B0 + 16 * hi), a(xo, ind=a("src", lo, hi)), a("g2", 16 * lo, 16 * hi), OP.add)
+            if lo == 0:
+                cp(a("sro"), a("srof"))
+        for h in (0, 1):
+            act(a(on, B0 + 256 * h, B0 + 256 * h + 256), a(oo, ind=a("sro", 16 * h, 16 * h + 16)), AF.Copy)
+        act(a("xv", 256, 512), a(xn, ind=a(l1, 16, 32)), AF.Copy)
         for h in (0, 1):
             ts(a("avl", h, h + 1), a("avf", h, h + 1), c(CH[h]), None, OP.max)
-        tt(a("srof"), a("srcf", 0, 32), a("awq"), OP.max)
         if t == 0:
             send(a("avl"), a("lav"), "a2_0", host, guest, "out1")
         else:
             cp(a(m2), a(xo, ind=a("avl")))
             send(a(m2), a(l2), "a2_%d" % t, host, guest)
         cp(a("xv", 0, 256), a(xn, ind=a(l1, 0, 16)))
-        act(a("xv", 256, 512), a(xn, ind=a(l1, 16, 32)), AF.Copy)
         conv(a("ph", 0, 32), "zw", "xv", 0, 512)
-        ts(a("sro"), a("srof"), float(B0), None, OP.subtract)
-        if t == 0:
-            first_numbers()
-        act(a(on), a(oo, ind=a("sro")), AF.Copy)
         if last:
-            conv(a("pn", 0, 32), "zo", on, 0, 512)
-            mm(a("pa", np_=8), a("g8"), a(on))
+            conv(a("pn", 0, 32), "zo", on, B0, B0 + 512)
+            mm(a("pa", np_=8), a("g8"), a(on, B0, B0 + 512))
             act(a("ysb", np_=8), a("pa", np_=8), AF.Copy)
             dma("s", "ld6", [(T.yseat[:], a("ysb", np_=8))])
         if t == 0:
@@ -751,9 +834,9 @@ def rank_program(g, core, T, topo):
         for h in (0, 1):
             red(a("vh", h, h + 1), a("vd", h, 32, 2), OP.max)
         tt(a("hp"), a("kh"), a("sf"), OP.mult)
-        ts(a("vt", 0, 16), a("nio"), a("vh", 0, 1), None, OP.add)
+        for h in (0, 1):
+            aff(a("vt", 16 * h, 16 * h + 16), a("io", 0, 16), -1.0, a("vh", h, h + 1))
         ts(a("hs"), a("hp"), 5, 8191, OP.logical_shift_right, OP.bitwise_and)
-        ts(a("vt", 16, 32), a("nio"), a("vh", 1, 2), None, OP.add)
         ts(a("hw"), a("hs"), c(CT0 + t), None, OP.add)
         mm(a("pm", 0, 32), a("idn"), a("k7"), True, False)
         mm(a("pb", 0, 225), a("idn"), a("tm", 0, 225), True, False)
@@ -762,9 +845,9 @@ def rank_program(g, core, T, topo):
         for i in range(16):
             mm(a("pm", 0, 32), sel("zk", i), a("lt2", 32 * i, 32 * i + 32), False, i == 15)
         if last:
-            ts(a("olf"), a("pn", 0, 32), 32.0, None, OP.add)
-            cp(a("olu"), a("olf"))
-            tt(a("awo"), a("aw"), a("olf"), OP.mult)
+            aff(a("olf"), a("pn", 0, 32), 1.0 / 32, 1.0)
+            ts(a("olu"), a("pn", 0, 32), 32.0, None, OP.add)
+            tt(a("awo"), aw, a("olf"), OP.mult)
         for h in (0, 1):
             scan(a("cs", 16 * h, 16 * h + 16), a("pm", 16 * h, 16 * h + 16), a("vt", 16 * h, 16 * h + 16), NONE, OP.min, OP.max)
         cl = [a("cs", 15, 16), a("cs", 31, 32)]
@@ -782,11 +865,10 @@ def rank_program(g, core, T, topo):
             red(a("cf", h, h + 1), a("pb", 128 * h, 128 * h + 97), OP.min, apply_absolute_value=True)
         for h in (0, 1):
             ts(a("tgt", h, h + 1), a("cf", h, h + 1), c(CH[h]), cl[h], OP.add, OP.min)
-        for h in (0, 1):
-            ts(a("tgf", h, h + 1), a("cf", h, h + 1), c(CH[h]), cl[h], OP.add, OP.min)
         cp(a(m3), a(xn, ind=a("tgt")))
         send(a(m3), a(l3), "a3_%d" % t, guest, host)
-        ts(a("tgw", 0, 2), a("tgf", 0, 2), B0 + 511.5, -512.0, OP.is_ge, OP.mult)
+        cp(a("tgf", 0, 2), a("tgt"))
+        ts(a("tgw", 0, 2), a("tgt"), B0 + 511.5, -512.0, OP.is_ge, OP.mult)
         if last:
             tt(a("dm"), a("pp", 64, 96), a("dg2"), OP.mult)
         tt(a("tgc", 0, 2), a("tgf", 0, 2), a("tgw", 0, 2), OP.add)
@@ -794,13 +876,18 @@ def rank_program(g, core, T, topo):
             for h in (0, 1):
                 red(a("avf", h, h + 1), a("dm", h, 32, 2), OP.max)
         cp(a("tg2"), a("tgc", 0, 2))
-        cp(a(xn, ind=a("tg2")), a(l2))
         if not last:
+            cp(a(xn, ind=a("tg2")), a(l2))
             cp(a(xn, ind=a("avl")), a(l3))
         else:
             for h in (0, 1):
                 ts(a("avo", h, h + 1), a("avf", h, h + 1), c(CH[h]), None, OP.max)
-            cp(a("ypb", ind=a("olu")), a(xn, B0, B0 + 512))
+            for lo in range(0, 32, 8):
+                cp(a("ypb", ind=a("olu", lo, lo + 8)), a(xn, B0 + 16 * lo, B0 + 16 * lo + 128))
+            act(a("oc"), a(on, ind=a("tg2")), AF.Copy)
+            conv(a("pm", 0, 2), "zo", "oc", 0, 32)
+            ts(a("ocu"), a("pm", 0, 2), 32.0, None, OP.add)
+            cp(a("ypb", ind=a("ocu")), a(l2))
             cp(a("ypb", ind=a("avo")), a(l3))
             dma("y", "ld7", [(T.ypup[:], a("ypb", 32, 544))])
     issue_all()

@@ -7,7 +7,7 @@ NS0 = 6
 B0 = 48
 LAGV, LAGS = 0.2, 0.0
 HS, HS0 = 128, 384
-QAT, QB = 2, 1
+QAT, QB = 1, 2
 XW = 576
 DW = 8800
 RW = 4240
@@ -18,39 +18,45 @@ WDT = "float16"
 F, I, U, H = "float32", "int32", "uint16", "bfloat16"
 SB = {
     "dicx": (DW, H), "dicy": (DW, H), "pupb": (512, H), "seatb": (32, I), "wtb": (4, I), "seatu": (32, U),
-    "x0": (XW, H), "x1": (XW, H), "o0": (B0 + 512, H), "o1": (B0 + 512, H), "oc": (32, H), "ocu": (2, U), "oio": (512, H), "x2": (752, H), "x2l": (48, U),
+    "x0": (XW, H), "x1": (XW, H), "o0": (XW, H), "o1": (XW, H), "oc": (32, H), "ocu": (2, U), "oio": (512, H), "x2": (752, H), "x2l": (48, U),
     "lt": (ZC + 16, H), "d0": (512, H), "d1": (512, H), "d2": (512, H),
     "ksi": (48, I), "ks": (48, I), "prod": (512, I), "prs": (512, I), "off": (512, U),
     "pw": (512, H), "lns": (32, F), "nsi": (32, I), "roff": (32, U), "rof2": (32, U), "lnn": (32, F), "nni": (32, I),
     "r32": (32, U), "pw0": (256, H), "pw1": (256, H), "ln2": (48, F),
     "pq": (112, F), "dq": (64, F), "zq": (32, F), "wq": (32, F), "tq": (48, F), "sq": (128, F), "st1": (32, F), "st2": (32, F),
     "rq": (128, F), "sc": (128, F), "sd": (128, F), "n15": (32, F), "a15": (32, F), "n2": (32, F), "thn": (32, F),
-    "ex": (RW, F), "eb": (768, H), "cd": (RW, F), "cc": (512, F), "ce": (384, F), "mq": (32, F), "mq2": (32, F), "nq": (32, F), "nq2": (32, F),
+    "ex": (RW, F), "eb": (768, H), "cd": (RW, F), "cc": (512, F), "ce": (384, F), "mq": (32, F), "nm2": (32, F), "nq": (32, F), "nq2": (32, F),
     "f15": (32, F), "m15": (32, F), "u15": (32, F), "nm": (32, F), "nnm": (32, F), "q32": (32, F), "s0": (168, F), "s1": (168, F),
     "y1": (36, F), "y2": (36, F), "wa": (272, H), "v4": (136, WDT), "ap4": (136, WDT), "le2": (6, U), "ch": (40, U), "c1": (48, U), "w": (272, F),
     "mc": (64, H), "kni": (32, I), "kn": (32, I), "kn1": (32, F), "ksq": (32, I), "v0": (32, I), "v1": (32, F),
     "nt": (32, F), "nu": (32, F), "nl": (36, F), "aw": (32, F), "st": (36, F), "apk": (64, WDT), "awq": (32, WDT),
     "yp": (36, F), "idx2": (34, U), "uu": (36, F), "e1": (36, F), "e2": (36, F),
     "srcf": (168, F), "src": (34, U), "srof": (32, F), "sro": (32, U), "g2": (528, H),
-    "dm": (32, F), "avf": (4, F), "avl": (2, U), "avo": (2, U), "olf": (32, F), "olu": (32, U), "awo": (32, WDT),
+    "dm": (32, F), "avf": (4, F), "avg": (4, F), "avp": (4, F), "avl": (2, U), "avo": (2, U), "olf": (32, F), "olu": (32, U), "awo": (32, WDT),
     "xv": (512, H), "sf": (32, F), "vb": (32, F), "vd": (32, F), "vh": (4, F), "vt": (32, F), "cs": (32, F),
     "khi": (32, I), "kh": (32, I), "hp": (32, I), "hs": (32, I), "hw": (32, U), "lt2": (512, H),
     "exd": (96, WDT), "exo": (224, WDT), "cf": (4, F), "tgt": (2, U), "tgf": (4, F), "tgw": (4, F), "tgc": (4, F), "tg2": (2, U),
-    "xg": (B0 + 512, H), "lav": (2, U), "ypb": (544, H), "ysb": (512, F),
+    "xg": (B0 + 512, H), "lav": (2, U), "ypb": (B0 + 512, H), "ysb": (512, F),
     "zo": (144, H), "zw": (144, WDT), "zm": (144, H), "zr": (144, H), "zk": (144, H), "idn": (128, H), "nid": (128, H),
     "nidk": (128, H), "blkb": (128, H), "blkk": (128, H), "g8": (8, H), "dh": (128, H), "dl": (128, H), "ohi": (512, H), "olo": (512, H),
     "io": (144, F), "mg": (128, F), "i16": (48, F), "i8": (32, F), "b32": (32, F),
-    "ie": (256, F), "ia": (256, F), "ic": (384, F), "t1": (256, F), "t2": (256, F), "t3": (256, F),
+    "ie": (256, F), "ia": (256, F), "ic": (384, F), "t1": (208, F), "t4": (96, F), "ti": (512, F), "t2": (256, F), "t3": (256, F),
     "col": (48, F), "ci": (8, I), "q16": (36, F), "qm1": (36, F), "dg": (48, F), "dg2": (32, F), "one": (112, WDT),
     "tm": (232, H), "k7": (32, H), "nio": (16, F),
 }
 for _t in range(RO):
     SB["m1_%d" % _t] = (64, U); SB["l1_%d" % _t] = (64, U)
     for _n in ("m2", "l2", "m3", "l3"):
-        SB["%s_%d" % (_n, _t)] = (32, H)
+        SB["%s_%d" % (_n, _t)] = (32 if _n[1] == "2" else 34, H)
 PS = ["pc", "pa", "pb", "pk", "pm", "pn", "pp", "ph"]
 SCRATCH, HOME = {}, {}
+INSIDE, FILL = {}, 768
+for _k in ("cc", "ti", "ce", "ic", "ia", "ie", "t2", "t3", "t1", "io", "mg", "b32"):
+    INSIDE[_k] = FILL
+    FILL += SB[_k][0]
 for _k, (_w, _d) in SB.items():
+    if _k in INSIDE:
+        continue
     if _w > 64:
         SCRATCH["b_" + _k] = ("sbuf", [128, _w], _d)
         HOME[_k] = (_k, 0)
@@ -60,25 +66,30 @@ for _k, (_w, _d) in SB.items():
         HOME[_k] = ("pool" + _d, _o)
 SCRATCH.update({("b_" + k): ("psum", [128, 512], F) for k in PS})
 SEMAPHORES = ["qv", "qs", "qp", "qg", "sent", "a0", "out0", "out1"] + ["ld%d" % i for i in range(8)] + \
-             ["a%d_%d" % (m, t) for m in (1, 2, 3) for t in range(RO)]
+             ["a%d_%d" % (m, t) for m in (1, 2, 3, 4) for t in range(RO)]
 (CP, CK, CG, CK16, CG15, CW, CM, CJ, CX, CS, CQ, CV, CZ0, CA, CB, CD, CL0, C34, C67, CEF, C16, C24, CE, CY,
  CH0, CH1, CT0) = range(27)
 CZ1 = CT0 + 4
-CTH = CZ1 + 3
+CU, CU2, CK32 = CZ1 + 3, CZ1 + 4, CZ1 + 5
+CTH = CZ1 + 6
 MAG = 1.5 * 2.0 ** 23
-CH = (CK, CK16)
+CH = (CK16, CK32)
 NONE = 4096.0
-CYC, WAKE, HOP, SLACK, AHEAD = 0.92e-3, 0.2, 1.6, 0.03, 400
-PASSES = 2
-EARLY = 16
+CYC, WAKE, HOP, SLACK, AHEAD = 1.0e-3, 0.2, 1.6, 0.03, 400
 SHORT = 0.1
+EARLY = 24
+HV = 20
+LAY = ((0, 10), (10, 14), (14, 32))
+UNSURE = 0.07
 ORDER = []
-LOADED = {"ld3": 5.5, "ld4": 9.5, "ld5": 10.0}
+LOADED = {"ld3": 3.7, "ld4": 6.5, "ld5": 7.0}
 
 
 def a(name, lo=0, hi=None, step=1, ind=None, np_=128):
     if hi is None:
         hi = SB[name][0] if name in SB else 512
+    if name in INSIDE:
+        return ("ex", lo + INSIDE[name], hi + INSIDE[name], step, ind, np_)
     return (name, lo, hi, step, ind, np_)
 
 
@@ -118,36 +129,38 @@ def cost(q, rd, wr):
     n = max(len(range(*x[1:4])) for x in xs)
     if q == "v" and all(x[0] in SB and SB[x[0]][1] in (H, U, WDT) for x in wide):
         n = n / 2
-    if q == "v" and len(wide) == 3 and all(x[0] in SB for x in wide[1:]):
+    if q == "v" and len(rd) == 2 and len(wide) == 3 and all(x[0] in SB for x in wide[1:]):
         n = 2 * n
     return max(64, n) * CYC
 
 
-def lay_out(calls, deps, tail, todo, back):
-    end, free, out = [None] * len(calls), {}, []
-    lead = [x[2] - x[1] if back else 0.0 for x in calls]
+def lay_out(calls, tail):
+    end, free, out, todo = [None] * len(calls), {}, [], list(range(len(calls)))
     while todo:
-        ahead, est, byq = todo[:AHEAD], {}, {}
+        ahead, est, byq, slack = todo[:AHEAD], {}, {}, {}
         for i in ahead:
-            e = free.get(calls[i][0], 0.0) - lead[i]
-            for m, w in deps[i]:
-                e = max(e, (est[m] + calls[m][2] if end[m] is None else end[m]) + w)
+            e, slack[i] = free.get(calls[i][0], 0.0), SLACK
+            for m, w in calls[i][3]:
+                if end[m] is None:
+                    e, slack[i] = max(e, est[m] + calls[m][2] + w), UNSURE
+                else:
+                    e = max(e, end[m] + w)
             est[i] = e
             byq.setdefault(calls[i][0], []).append(i)
         pick = None
         for xs in byq.values():
             xs.sort(key=lambda i: -tail[i])
             for k, i in enumerate(xs):
-                if (pick is None or est[i] + SHORT * calls[i][1] < est[pick] + SHORT * calls[pick][1]) and all(end[m] is not None for m, _ in deps[i]) and all(
-                        est[i] + calls[i][1] + tail[m] <= est[m] + max(tail[m], calls[m][1] + tail[i]) + SLACK for m in xs[:k]):
+                if slack[i] == SLACK and (pick is None or est[i] + SHORT * calls[i][1] < est[pick] + SHORT * calls[pick][1]) and all(
+                        est[i] + calls[i][1] + tail[m] <= est[m] + max(tail[m], calls[m][1] + tail[i]) + slack[m] for m in xs[:k]):
                     pick = i
         if pick is None:
             pick = ahead[0]
         end[pick] = est[pick] + calls[pick][2]
-        free[calls[pick][0]] = est[pick] + lead[pick] + calls[pick][1]
+        free[calls[pick][0]] = est[pick] + calls[pick][1]
         todo.remove(pick)
         out.append(pick)
-    return out, end
+    return out
 
 
 def rank_program(g, core, T, topo):
@@ -241,7 +254,7 @@ def rank_program(g, core, T, topo):
             elif w:
                 lst[:] = [e for e in lst if e[0] & ~m]
             lst.append((m, w, q, n))
-        calls.append((q, busy, done, list(dep.items()), issue))
+        calls.append((q, busy, done, list(dep.items()), issue, None))
         return n
 
     def op(q, rd, wr, fn):
@@ -251,26 +264,18 @@ def rank_program(g, core, T, topo):
             count[s] = count.get(s, 0) + 1
             fn().then_inc(T.sem[s], 1)
             note(use, q, s, count[s])
-        t = cost(q, rd, wr) + (1.3 if len(calls) < 9 and q == "s" else 0.0)
+        t = cost(q, rd, wr) + (1.3 if len(calls) < 7 and q == "s" else 0.0)
         record(q, rd, wr, t, t, issue)
 
     def issue_all():
         if not ORDER:
             n = len(calls)
-            before = [x[3] for x in calls]
-            behind = [[] for _ in calls]
             tail = [0.0] * n
             for i in range(n - 1, -1, -1):
                 tail[i] += calls[i][2]
-                for m, w in before[i]:
+                for m, w in calls[i][3]:
                     tail[m] = max(tail[m], w + tail[i])
-                    behind[m].append((i, w))
-            best = None
-            for _ in range(PASSES):
-                order_, end = lay_out(calls, before, tail, list(range(n)), False)
-                if best is None or max(end) < best:
-                    best, ORDER[:] = max(end), order_
-                tail = lay_out(calls, behind, end, list(range(n - 1, -1, -1)), True)[1]
+            ORDER[:] = lay_out(calls, tail)
         for i in ORDER:
             calls[i][4]()
 
@@ -290,7 +295,7 @@ def rank_program(g, core, T, topo):
         op("v", [i], [o], lambda: g.vector.tensor_reduce(ap(o), ap(i), AX.X, o0, **kw))
 
     def scan(o, d0, d1, first, o0, o1):
-        op("v", [d0, d1], [o], lambda: g.vector.tensor_tensor_scan(ap(o), ap(d0), ap(d1), first, o0, o1))
+        op("v", [d0, d1, first], [o], lambda: g.vector.tensor_tensor_scan(ap(o), ap(d0), ap(d1), first, o0, o1))
 
     def ms(o, v):
         op("v", [], [o], lambda: g.vector.memset(ap(o), v))
@@ -321,6 +326,9 @@ def rank_program(g, core, T, topo):
             op("g", [], [o], lambda: g.iota(ap(o), pat, base, cm))
         else:
             op("g", [], [o], lambda: g.iota(ap(o), pat, base, cm, allow_small_or_imprecise_dtypes=True))
+
+    def fill(o, v):
+        iota(o, [[0, len(range(*o[1:4]))]], v)
 
     def dma(q, s, pairs, also=()):
         (o, i), = pairs
@@ -365,28 +373,40 @@ def rank_program(g, core, T, topo):
     dma("s", "ld2", [(a("wtb", 0, 1), T.wt[:])])
     dma("y", "ld3", [(a("dicx", 0, 4096), T.dic[:, 0:4096])])
     dma("s", "ld4", [(a("dicx", 4096, 8192), T.dic[:, 4096:8192])])
+    ms(a("ln2"), 1.0)
+    in_row[0] = 0
+    act(a("lns", 0, 1), a("ln2", 0, 1), AF.Ln)
     in_row[0] = None
     cp(a("dicx", 8192, DW), a("dicx", 0, DW - 8192))
-    ms(a("ln2"), 1.0)
-    act(a("lns", 0, 1), a("ln2", 0, 1), AF.Ln)
 
+    in_row[0] = "first"
     iota(a("ci", 0, 1), [[0, 1]], 0, 1)
-    iota(a("io"), [[1, 144]], 0)
-    iota(a("mg"), [[16, 8], [0, 16]], 0)
     iota(a("i16"), [[0, 3], [1, 16]], 0)
+    iota(a("io"), [[1, 144]], 0)
     iota(a("b32"), [[256, 2], [1, 16]], 0)
     iota(a("ie"), [[0, 16], [1, 16]], 0)
     iota(a("ia"), [[1, 16], [0, 16]], 0)
     iota(a("ic"), [[64, 24], [1, 16]], 512)
+    for k in range(8):
+        iota(a("ti", 64 * k, 64 * k + 64), [[4224, 2], [256, 2], [1, 16]], 528 * k)
     iota(a("mq"), [[0, 8], [1, 4]], 0)
     iota(a("thn"), [[1, 8], [0, 4]], 0)
+    iota(a("mg"), [[16, 8], [0, 16]], 0)
     iota(a("i8"), [[1, 16], [0, 2]], 0)
-    iota(a("sq", 0, 32), [[0, 8], [1, 4]], int(MAG) - 3)
-    iota(a("st1"), [[0, 8], [1, 4]], int(MAG) - 1026)
-    iota(a("st2"), [[0, 8], [1, 4]], int(MAG) - 1025)
+    fill(a("st1"), int(MAG) - 1023)
+    fill(a("st2"), int(MAG) - 1022)
+    fill(a("sd"), 0)
     iota(a("eb", 512, 768), [[1, 256]], 1)
+    for x in (a("st1", 3, 32, 4), a("st2", 2, 32, 4), a("sq", 96, 128), a("st2", 3, 32, 4)):
+        fill(x, int(MAG) - 8192)
+    fill(a("pq", 96, 112), 0)
+    iota(a("sd", 3, 128, 4), [[0, 8], [1, 4]], -int(MAG) - 3)
+    in_row[0] = None
     for lo in (512, 1024, C2 + 512):
-        iota(a("cd", lo, lo + 512), [[0, 512]], -1)
+        fill(a("cd", lo, lo + 512), 0)
+    for x, v in ((a("lt", ZC, ZC + 16), 0), (a("mc", 32, 64), 2048), (a("s0"), 1), (a("s0", 0, 165, 5), 0), (a("y2", 32, 33), 0), (a("k7"), -7 * 4096),
+                 (a("tm", 96, 128), 1 << 22), (a("tm", 224, 232), 1 << 22), (a("ypb", 0, B0), 0)):
+        fill(x, v)
     for x in ("x0", "x1"):
         ms(a(x, 0, B0), -1.0)
         ms(a(x, B0 + 512, XW), -1.0)
@@ -406,122 +426,99 @@ def rank_program(g, core, T, topo):
     ts(a("t1", 112, 160), a("t1", 64, 112), B0 + 511.5, None, OP.is_le)
     ts(a("dg"), a("i16"), c(CK), None, OP.is_equal)
     tt(a("t1", 160, 208), a("t1", 64, 112), a("t1", 112, 160), OP.mult)
-    ts(a("x2l"), a("t1", 160, 208), 32.0, None, OP.max)
+    cp(a("x2l"), a("t1", 160, 208))
     tt(a("t1", 48, 64), a("t1", 32, 48), a("dg", 0, 16), OP.mult)
     red(c(CM), a("t1", 48, 64), OP.add)
     cp(a("seatu"), a("seatb"))
     ts(c(CX), a("wtb", 0, 1), 2048.0, -4096.0, OP.is_ge, OP.mult)
     tt(c(CW), a("wtb", 0, 1), c(CX), OP.add)
-    cp(a("x0", B0, B0 + 512), a("pupb", ind=a("seatu")))
+    cp(a("x0", B0, B0 + 256), a("pupb", ind=a("seatu", 0, 16)))
     ts(a("zw"), a("zo"), c(CW), None, OP.mult)
 
     def scalar_constants():
-        for j, (m, b) in {CK16: (1, 16), CJ: (1, B0), CV: (-1, B0 - 1), CH0: (2, 0), CH1: (2, 1),
+        for j, (m, b) in {CU: (-512, 7680), CU2: (-512, -512), CK16: (1, 16), CK32: (1, 32), CJ: (1, B0), CV: (-1, 15), CH0: (2, 0), CH1: (2, 1),
                           CT0: (-37, 555), CT0 + 1: (-37, 566), CT0 + 2: (-37, 577), CT0 + 3: (-37, 588)}.items():
             aff(c(j), c(CK), float(m), float(b))
         for n in sorted({NS - 1, NS, NS0 - 1, NS0}):
             ts(c(CQ), c(CK), n - 0.5, -8.5, OP.is_le, OP.mult)
             aff(c(CTH + n), c(CQ), 1.0, 7.5)
-        def sums(j, first, *terms):
-            for f, x in terms:
+        gt, e1, e2, u, add, uns = [a("t4", 16 * n, 16 * n + 16) for n in range(6)]
+        k0 = a("io", 0, 16)
+        ts(gt, k0, c(CK), None, OP.is_lt)
+        ts(u, k0, 528.0, c(CU), OP.mult, OP.add)
+        ts(e1, k0, c(CK), ZC + 1.0, OP.is_equal, OP.mult)
+        ts(e2, k0, c(CK), 2.0, OP.is_equal, OP.mult)
+        ts(uns, k0, c(CK), float(ZC), OP.is_le, OP.mult)
+        tt(add, u, gt, OP.mult)
+        tt(uns, uns, e2, OP.add)
+        tt(add, add, e1, OP.add)
+        tables = [(buf, lo + 64 * (k % 8) + 32 * (k // 8), k) for buf, lo in (("cd", 1536), ("cc", 0)) for k in range(16)]
+
+        def table():
+            buf, w, k = tables.pop()
+            col = lambda x: a(x[0], x[1] + k, x[1] + k + 1)
+            aff(a(buf, w, w + 32), a("b32"), col(gt) if buf == "cc" else 0.0, col(add if buf == "cc" else uns))
+        in_row[0] = 0
+        for n, (j, first, f, x) in enumerate((
+                (C34, row(3), 1, row(4)), (C67, row(6), 1, row(7)), (CEF, row(14), 1, row(15)), (CY, row(11), 1, row(12)),
+                (CE, -60000.0, C2, row(4)), (CD, row(0), E2 + 8, row(1)), (CB, row(0), 8, row(1)), (CA, row(1), 16, row(0)),
+                (C16, c(C34), 1, c(C67)), (CY, c(CY), 1, c(CEF)), (CE, c(CE), C2, row(6)), (CD, c(CD), C2, row(12)),
+                (CZ0, 1.0, -1, row(1)), (None,) * 4,
+                (CE, c(CE), C2, row(14)), (CD, c(CD), C2, row(14)), (CB, c(CB), 1, c(CY)), (CA, c(CA), 64, c(CY)),
+                (C24, c(C16), 1, c(CEF)), (CE, c(CE), -480, c(C67)), (CD, c(CD), 559, c(CEF)), (CL0, 0.0, C2, row(12)),
+                (CE, c(CE), -1008, c(C34)), (CD, c(CD), 60000, c(C16)), (CL0, c(CL0), 512, c(C24)),
+                (CE, c(CE), -1488, c(CEF)), (CD, c(CD), 1, c(CY)))):
+            if j is None:
+                act(a("x0", B0 + 256, B0 + 512), a("pupb", ind=a("seatu", 16, 32)), AF.Copy)
+            else:
                 aff(c(j), x, float(f), first)
-                first = c(j)
-        sums(C34, row(3), (1, row(4)))
-        sums(C67, row(6), (1, row(7)))
-        sums(CEF, row(14), (1, row(15)))
-        sums(CY, row(11), (1, row(12)), (1, c(CEF)))
-        sums(C16, c(C34), (1, c(C67)))
-        sums(C24, c(C16), (1, c(CEF)))
-        sums(CA, row(1), (64, c(CY)), (16, row(0)))
-        sums(CB, c(CY), (8, row(1)), (1, row(0)))
-        sums(CD, c(CB), (E2, row(1)), (559, c(CEF)), (C2, row(12)), (C2, row(14)), (60000, c(C16)))
-        sums(CL0, 0.0, (C2, row(12)), (512, c(C24)))
-        sums(CE, -60000.0, (-480, c(C67)), (-1008, c(C34)), (-1488, c(CEF)), (C2, row(4)), (C2, row(6)), (C2, row(14)))
-        aff(c(CZ0), row(1), -1.0, 1.0)
-        aff(a("t2"), a("ia"), c(CA), c(CD))
+            if n > 18:
+                table()
         aff(a("t3"), a("ie"), c(CB), 0.0)
         for n, j in enumerate((C67, C16, C24)):
             aff(c(CZ1 + n), c(j), c(CE), 60000.0)
+        aff(a("t2"), a("ia"), c(CA), c(CD))
+        for n, j in enumerate((C67, C16, C24)):
             aff(a("ce", 128 * n, 128 * n + 128), a("ic", 128 * n, 128 * n + 128), c(j), c(CZ1 + n))
+        while tables:
+            in_row[0] = 0 if len(tables) > EARLY else None
+            table()
+        in_row[0] = None
 
     def later_constants():
         tt(a("ex", 512, 768), a("t2"), a("t3"), OP.add)
         for i in range(3):
             ts(a("ex", 512 + i, 768, 16), a("ex", 512 + i, 768, 16), c(CZ0), None, OP.mult)
-        J, gt, eq, lt, u = [a("t1", 64 + 16 * n, 80 + 16 * n) for n in range(5)]
-        add, uns, add2, uns2, v = [a("t1", 144 + 16 * n, 160 + 16 * n) for n in range(5)]
-        k0 = a("io", 0, 16)
-        ts(J, k0, -1.0, c(CK), OP.mult, OP.add)
-        ts(v, k0, 16.0, 7680.0, OP.mult, OP.add)
-        ts(gt, J, 0.5, None, OP.is_ge)
-        ts(u, J, -512.0, None, OP.mult)
-        ts(eq, J, 0.0, float(ZC + 2), OP.is_equal, OP.mult)
-        ts(lt, J, -0.5, None, OP.is_le)
-        tt(u, u, v, OP.add)
-        ts(uns, gt, float(ZC + 1), -1.0, OP.mult, OP.add)
-        ts(uns2, lt, float(ZC + 1), -1.0, OP.mult, OP.add)
-        ts(v, u, 1.0, None, OP.add)
-        ts(u, u, -8191.0, None, OP.add)
-        tt(add, v, gt, OP.mult)
-        tt(add2, u, lt, OP.mult)
-        tt(uns, uns, eq, OP.add)
-        tt(add, add, eq, OP.add)
-        ts(add2, add2, -1.0, None, OP.add)
-        ts(eq, eq, 1.0 / (ZC + 2), None, OP.mult)
-        ts(add, add, -1.0, None, OP.add)
-        tt(uns, uns, eq, OP.add)
-        for k in range(15, -1, -1):
-            in_row[0] = 0 if k >= EARLY else None
-            def col(x):
-                return a("t1", x[1] + k, x[1] + k + 1)
-            w = 64 * (k % 8) + 32 * (k // 8)
-            aff(a("cc", w, w + 32), a("b32"), col(gt), col(add))
-            aff(a("cd", 1536 + w, 1568 + w), a("b32"), 0.0, col(uns))
-            aff(a("cd", C2 + 1024 + w, C2 + 1056 + w), a("b32"), col(lt), col(add2))
-            aff(a("cd", C2 + 1536 + w, C2 + 1568 + w), a("b32"), 0.0, col(uns2))
+        act(a("cd", C2 + 1024, C2 + 1536), a("ti"), AF.Relu, c(CU2))
+        ts(c(CQ), c(CK), 512.0, 512.0, OP.mult, OP.add)
+        in_row[0] = 0
+        ts(a("cd", C2 + 1536, C2 + 2048), a("ti"), c(CQ), float(ZC), OP.is_ge, OP.mult)
         in_row[0] = None
-        ms(a("lt", ZC, ZC + 16), 0.0)
         ts(c(CX), c(CK), 14.5, c(CM), OP.is_le, OP.mult)
         ts(a("zm"), a("zo"), c(CX), None, OP.mult)
-        ms(a("st1", 3, 32, 4), MAG - 8192)
-        ms(a("st2", 2, 32, 4), MAG - 8192)
-        ms(a("sq", 96, 128), MAG - 8192)
-        ms(a("pq", 96, 112), 0.0)
-        ms(a("st2", 3, 32, 4), MAG - 8192)
 
     def last_constants():
         return [
-            lambda: ms(a("sd"), 0.0),
             lambda: ts(a("thn"), a("thn"), -6.5, None, OP.add),
-            lambda: ts(a("mq2"), a("mq"), 1.0 / 60, None, OP.mult),
             lambda: ts(a("mq"), a("mq"), 0.25, None, OP.mult),
             lambda: ms(a("v4"), 0.0),
-            lambda: ms(a("sd", 3, 128, 4), -MAG),
             lambda: ts(a("zr"), a("zo"), row(0), None, OP.mult),
             lambda: cp(a("ch", 0, 1), c(CL0)),
             lambda: ts(a("blkb"), a("mg"), c(CG), None, OP.is_equal),
             lambda: ts(a("q16"), a("io", 0, 36), 16.0, c(CJ), OP.mult, OP.add),
             lambda: ts(a("mc", 0, 32), a("io", 0, 32), 0.0, c(CV), OP.mult, OP.add),
             lambda: cp(a("q16", 32, 33), c(CJ)),
-            lambda: ms(a("mc", 32, 64), 2048.0),
             lambda: ts(a("s1", 1, 165, 5), a("q16", 0, 33), -1.0, None, OP.add),
-            lambda: ts(a("q32"), a("q16", 0, 32), 1.0 / 32, None, OP.mult),
-            lambda: ms(a("s0"), 1.0),
-            lambda: ms(a("s0", 0, 165, 5), 0.0),
-            lambda: ms(a("y2", 32, 33), -1.0),
+            lambda: ts(a("q32"), a("q16", 0, 32), -1.0 / NONE, None, OP.mult),
         ]
 
     def visit_constants():
         out = [
             lambda: ts(a("dg2"), a("i8"), c(CK), None, OP.is_equal),
             lambda: ts(a("zk"), a("zo"), NONE, None, OP.mult),
-            lambda: ms(a("k7"), -7 * NONE),
             lambda: ms(a("one"), 1.0),
             lambda: ts(a("blkk"), a("mg"), c(CG), 1024.0, OP.is_equal, OP.mult),
             lambda: ts(a("nidk"), a("io", 0, 128), c(CP), -1024.0, OP.is_equal, OP.mult),
-            lambda: ms(a("tm", 96, 128), 1024 * NONE),
-            lambda: ms(a("tm", 224, 232), 1024 * NONE),
-            lambda: ms(a("ypb", 0, 32), 0.0),
             lambda: ts(a("g8"), a("io", 0, 8), 16.0, c(CG), OP.mult, OP.is_equal),
         ]
         for h in (0, 1):
@@ -537,7 +534,7 @@ def rank_program(g, core, T, topo):
         act(a("oio"), a("pa"), AF.Copy)
         act(a("o0", B0, B0 + 512), a("oio", ind=a("seatu")), AF.Copy)
         for o in ("o0", "o1"):
-            ts(a(o, 0, B0), a("io", 0, B0), -32.0, row(0), OP.add, OP.mult)
+            ts(a(o, 0, B0), a("io", 0, B0), -float(B0), row(0), OP.add, OP.mult)
 
     scalar_constants()
     BIG = float(1 << 20)
@@ -556,20 +553,26 @@ def rank_program(g, core, T, topo):
         ts(a("ks", 0, 47), a("ksi", 0, 47), 4095, None, OP.bitwise_and)
 
         at = lambda j: 64 * (j % 8) + 32 * (j // 8)
-        for js in ([0], [1, 2], [3, 4, 5], [6, 7]):
-            for j in js:
+        def mult(j):
+            tt(a("prod", at(j), at(j) + 32), a("ks", 0, 32), a("ks", j, j + 32), OP.mult)
+
+        def shift(j0, j1):
+            ts(a("prs", at(j0), at(j1) + 64), a("prod", at(j0), at(j1) + 64), 5, 8191, OP.logical_shift_right, OP.bitwise_and)
+
+        def add(j):
+            if t > 0:
+                ts(a("off", at(j), at(j) + 64), a("prs", at(j), at(j) + 64), float((37 * j + 11 * t) % 8), None, OP.add)
+            else:
                 for j2 in (j, j + 8):
-                    tt(a("prod", at(j2), at(j2) + 32), a("ks", 0, 32), a("ks", j2, j2 + 32), OP.mult)
-            lo, hi = at(js[0]), at(js[-1]) + 64
-            ts(a("prs", lo, hi), a("prod", lo, hi), 5, 8191, OP.logical_shift_right, OP.bitwise_and)
-            in_row[0] = t
-            for j in js:
-                if t > 0:
-                    ts(a("off", at(j), at(j) + 64), a("prs", at(j), at(j) + 64), float((37 * j + 11 * t) % 8), None, OP.add)
-                else:
-                    for j2 in (j, j + 8):
-                        ts(a("off", at(j2), at(j2) + 32), a("prs", at(j2), at(j2) + 32), float(37 * j2 % 16), None, OP.add)
-            in_row[0] = None
+                    ts(a("off", at(j2), at(j2) + 32), a("prs", at(j2), at(j2) + 32), float(37 * j2 % 16), None, OP.add)
+
+        in_row[0] = t
+        for f, *js in ((mult, 0), (mult, 8), (mult, 1), (mult, 9), (mult, 2), (mult, 10), (shift, 0, 0), (mult, 7), (mult, 15),
+                       (mult, 6), (add, 0), (mult, 14), (shift, 1, 2), (mult, 3), (mult, 11), (shift, 6, 7), (mult, 4), (add, 1),
+                       (add, 2), (mult, 12), (mult, 5), (mult, 13), (add, 7), (add, 6)):
+            f(*js)
+        later_lists = [lambda: shift(3, 5), lambda: [add(j) for j in (3, 4, 5)]]
+        in_row[0] = None
         if t == 0:
             later_constants()
             for f in last_constants():
@@ -577,8 +580,7 @@ def rank_program(g, core, T, topo):
             send(a(xo, 0, B0 + 512), a("xg"), "a0", host, guest, "out0", [a("dicx", 0, 8192)])
             dma("y", "ld5", [(a("dicy", 0, DW - 8), a("dicx", 8, DW))])
             ms(a("dicy", DW - 8, DW), 0.0)
-            for lo in range(768, E2, 560):
-                iota(a("ex", lo, lo + 560), [[0, 560]], 0)
+            iota(a("ex", FILL, E2 + 32), [[0, E2 + 32 - FILL]], 0)
             iota(a("ex", E2 + 128, RW), [[0, RW - E2 - 128]], 0)
             iota(a("cd", E2, RW), [[0, RW - E2]], 0)
             iota(a("ohi"), [[16, 32], [0, 16]], 0)
@@ -612,7 +614,7 @@ def rank_program(g, core, T, topo):
             yield
             tt(q(4), q(2), q(3), OP.max)
             yield
-            ts(a("sq", 96, 128, 4), q(4), MAG - 1024, None, OP.add)
+            ts(a("sq", 96, 128, 4), q(4), MAG - 1021, None, OP.add)
             yield
 
         ev = []
@@ -620,11 +622,11 @@ def rank_program(g, core, T, topo):
         tv, tsc = (0.0 if t == 0 else 1.7), 0.0
         half = ns - 1
         hs = HS0 if t == 0 else HS
-        ev.append((tv, "vh", half)); tv += 0.72 * (512 - hs) / 512
         for j in range(ns, 15):
             ev.append((tv, "vg", j)); tv += 0.72; ev.append((tv + LAGV, "cnt", j))
             if j >= 15 - QAT:
                 ev.append((tv - 0.01, "quad", j)); tv += 0.12
+        ev.append((tv, "vh", half))
         for j in range(ns + 1):
             if j < ns:
                 ev.append((tsc, "sg", j)); tsc += 0.73; ev.append((tsc, "sub", j))
@@ -640,16 +642,29 @@ def rank_program(g, core, T, topo):
             d, bank = a("d%d" % (j % 3), 0, n), a(("pa", "pb", "ph", "pn", "pm")[j % 5], 0, n)
             in_row[0] = t if kind in ("vg", "vh", "sg", "sign", "quad") else None
             if kind == "vg":
+                if later_lists:
+                    later_lists.pop(0)()
                 tt(ltj(j), word(j), a("x2", 16 * j, 16 * j + 512), OP.is_gt)
             elif kind == "vh":
-                tt(ltj(j, hs, 512), word(j, hs // 16, 32), a("x2", 16 * j + hs, 16 * j + 512), OP.is_gt)
+                for lo, hi in ((hs, 384), (384, 512)):
+                    if lo < hi:
+                        in_row[0] = t
+                        tt(ltj(j, lo, hi), word(j, lo // 16, hi // 16), a("x2", 16 * j + lo, 16 * j + hi), OP.is_gt)
+                        in_row[0] = None
+                        add_mm(a("pc", lo, hi), sel("zo", j), ltj(j, lo, hi), ncnt)
             elif kind == "sg":
                 act(d, word(j, 0, n // 16), AF.Copy)
             elif kind == "sub":
                 mm(bank, a("nid"), a("x2", 16 * j, 16 * j + n), True, False)
                 mm(bank, a("idn"), d, False, True)
-                if j == half - 1:
-                    add_mm(a("pc", hs, 512), sel("zo", half), ltj(half, hs, 512), ncnt)
+            elif kind == "sign" and j == half - 1:
+                for lo in (0, 256):
+                    in_row[0] = t
+                    act(ltj(j, lo, lo + 256), a(bank[0], lo, lo + 256), AF.Sign, -0.5)
+                    in_row[0] = None
+                    add_mm(a("pc", lo, lo + 256), sel("zo", j), ltj(j, lo, lo + 256), ncnt)
+            elif kind == "cnt" and j == half - 1:
+                pass
             elif kind == "sign":
                 act(ltj(j, 0, n), bank, AF.Sign, -0.5)
             elif kind == "quads":
@@ -676,25 +691,30 @@ def rank_program(g, core, T, topo):
         in_row[0] = None
         mm(a("ph"), a("nid"), a("x2", 240, 752), True, False)
         mm(a("ph"), a("idn"), a("d1"), False, True)
-        act(ltj(15), a("ph"), AF.Sign, -0.5)
         for i in list(range(0, 16, 2)) + list(range(1, 16, 2)):
             mm(a("pm", 0, 32), sel("zm", i), a("pw%d" % (i % 2), i // 2, 256, 8), i == 0, i == 15)
         LNB, LNS = math.exp(-15.2), math.exp(-0.2)
+        in_row[0] = t
+        act(ltj(15), a("ph"), AF.Sign, -0.5)
         act(a("ln2", 0, 32), a("pm", 0, 32), AF.Ln, LNB, LNS)
         halves = [(2 * u + h, 16 * h + 8 * u) for h in (0, 1) for u in (0, 1)]
         for m, lo in halves:
             act(a("lns", m, 32, 4), a("pm", lo, lo + 8), AF.Ln, LNB, LNS)
+        aff(a("rq", 0, 128, 4), a("ln2", 0, 32), -1.0, MAG)
+        for lo in range(0, 512, 128):
+            act(a("d0", lo, lo + 128), a("pc", lo, lo + 128), AF.Sign, c(CTH + ns - (lo >= hs)), -1.0)
+            in_row[0] = None
         conv(a("pa", 0, 32), "zo", "lt", 7680, 8192)
         for m, lo in halves:
             act(a("f15", m, 32, 4), a("pa", lo, lo + 8), AF.Relu, 8.0, 8.0)
-        for lo in range(0, 512, 128):
-            act(a("d0", lo, lo + 128), a("pc", lo, lo + 128), AF.Sign, c(CTH + ns - (lo >= hs)), -1.0)
-            act(a("pw", lo, lo + 128), a("d0", lo, lo + 128), AF.Relu)
+        in_row[0] = None
+        for lo in (0, 256):
+            ts(a("pw", lo, lo + 256), a("d0", lo, lo + 256), 0.0, None, OP.max)
         for h in (0, 1):
             for k in range(16):
                 w = 256 * h + 16 * k
                 mm(a("pn", 16 * h, 16 * h + 16), sel("zm", k), a("pw", w, w + 16), k == 0, k == 15)
-        for dl in range(4):
+        for dl in range(1, 4):
             tt(a("rq", dl, 128, 4), a("sq", 32 * dl, 32 * dl + 32), a("ln2", dl, dl + 32), OP.subtract)
         scan(a("sc"), a("rq"), a("sd"), 0.0, OP.max, OP.add)
         ts(a("r32"), a("sc", 3, 128, 4), 16.0, c(CK), OP.mult, OP.add)
@@ -703,12 +723,13 @@ def rank_program(g, core, T, topo):
         tt(a("a15"), a("lns"), a("thn"), OP.is_le)
         tt(a("nm"), a("nsi"), a("mq"), OP.add)
         tt(a("u15"), a("m15"), a("f15"), OP.min)
-        tt(a("nq2"), a("a15"), a("mq2"), OP.add)
+        aff(a("n15"), a("a15"), 15.0, 0.0)
+        tt(a("n2"), a("n15"), a("nsi"), OP.max)
+        tt(a("nm2"), a("n2"), a("mq"), OP.add)
         tt(a("nq"), a("nm"), a("u15"), OP.add)
+        tt(a("nq2"), a("nm2"), a("u15"), OP.add)
         ts(a("roff"), a("nq"), 64.0, c(CK), OP.mult, OP.add)
-        aff(a("n15"), a("nq"), 1.0 / 15, 0.0)
-        tt(a("n2"), a("n15"), a("nq2"), OP.max)
-        ts(a("rof2"), a("n2"), 960.0, c(CK), OP.mult, OP.add)
+        ts(a("rof2"), a("nq2"), 64.0, c(CK), OP.mult, OP.add)
 
         def codes(k):
             w = 64 * (k + 1)
@@ -756,20 +777,20 @@ def rank_program(g, core, T, topo):
         tt(a("ksq"), a("kn"), a("kn"), OP.mult)
         ts(a("v0"), a("ksq"), 5, 511, OP.logical_shift_right, OP.bitwise_and)
         for lo in (0, 3):
-            ts(a("v4", lo, lo + 64, 2), a("v0"), 16.0, None, OP.add)
+            ts(a("v4", lo, lo + 64, 2), a("v0"), float(B0), None, OP.add)
             ts(a("v4", 68 + lo, 68 + lo + 64, 2), a("kn"), -2048.0, None, OP.add)
         if t == 0:
             ts(a("dh"), a("idn"), row(0), None, OP.mult)
             ts(a("dl"), a("idn"), row(1), None, OP.mult)
             for f in visit_constants():
                 f()
-        mm(a("ph", 0, 64), a("idn"), a("mc"), True, False)
+        mm(a("ph", 0, 32), a("idn"), a("mc", 0, 32), True, False)
+        mm(a("pm", 0, 32), a("idn"), a("mc", 32, 64), True, False)
         for lo, hi in ((0, 8), (8, 12), (12, 17)):
-            if hi < 17:
-                act(a("w", 16 * lo, 16 * hi), a("cd", ind=a("ch", lo, hi)), AF.Copy)
-            else:
-                cp(a("w", 16 * lo, 16 * hi), a("cd", ind=a("ch", lo, hi)))
+            act(a("w", 16 * lo, 16 * hi), a("cd", ind=a("ch", lo, hi)), AF.Copy)
+        for lo, hi in ((0, 8), (8, 14)):
             act(a("wa", 16 * lo, 16 * hi), a("cd", ind=a("ch", lo, hi)), AF.Relu, -(ZC + 1.0))
+        ts(a("wa", 224, 272), a("cd", ind=a("ch", 14, 17)), ZC + 1.5, None, OP.is_ge)
         tt(a("y1", 0, 32), a("w", 11, 267, 8), a("w", 23, 272, 8), OP.max)
         tt(a("y1", 32, 33), a("w", 11, 12), a("w", 23, 24), OP.max)
         tt(a("y2", 0, 32), a("w", 4, 260, 8), a("w", 14, 270, 8), OP.max)
@@ -778,57 +799,79 @@ def rank_program(g, core, T, topo):
         y1, y2 = a("y1", 0, 33), a("y2", 0, 33)
         tt(a("yp", 0, 33), y1, y2, OP.max)
         cp(a("idx2", 0, 33), a("yp", 0, 33))
-        for n in (0, 1):
+        for n, bank in enumerate(("ph", "pm")):
             for lo in (0, 3):
-                mm(a("ph", 32 * n, 32 * n + 32), a("blkb"), a("ap4", 68 * n + lo, 68 * n + lo + 63, 2), False, n == 1 and lo == 3)
-        cp(a(m1), a("ph", 0, 64))
-        send(a(m1), a(l1), "a1_%d" % t, host, guest)
-        ts(a("s1", 0, 165, 5), y1, ZC + 0.5, None, OP.is_ge)
+                mm(a(bank, 0, 32), a("blkb"), a("ap4", 68 * n + lo, 68 * n + lo + 63, 2), False, lo == 3)
+            cp(a(m1, 32 * n, 32 * n + 32), a(bank, 0, 32))
+            send(a(m1, 32 * n, 32 * n + 32), a(l1, 32 * n, 32 * n + 32), "a%d_%d" % (1 + 3 * n, t), host, guest)
+        act(a("s1", 0, 165, 5), y1, AF.Relu, -float(ZC))
         ts(a("s1", 2, 165, 5), y1, float(ZC), None, OP.is_equal)
         ts(a("s1", 3, 165, 5), y2, float(ZC), None, OP.is_equal)
-        ts(a("s0", 4, 165, 5), y1, ZC + 1.5, None, OP.is_le)
-        ts(a("s1", 4, 165, 5), y1, ZC + 1.5, 32.0, OP.is_ge, OP.mult)
+        ts(a("s1", 4, 165, 5), y1, ZC + 1.5, -NONE, OP.is_ge, OP.mult)
         scan(a("srcf", 0, 165), a("s0", 0, 165), a("s1", 0, 165), 0.0, OP.mult, OP.add)
         cp(a("src", 0, 33), a("srcf", 4, 165, 5))
         aw = a("s1", 4, 160, 5)
         tt(a("awq"), aw, a("q32"), OP.mult)
         mm(a("pp", 64, 96), a("blkb"), a("awq"))
         tt(a("dm"), a("pp", 64, 96), a("dg2"), OP.mult)
-        for h in (0, 1):
-            red(a("avf", h, h + 1), a("dm", h, 32, 2), OP.max)
         tt(a("srof"), a("srcf", 4, 160, 5), a("awq"), OP.max)
         if t == 0:
             first_numbers()
         thirds = ((0, 10), (10, 22), (22, 33))
+        end_row = "last" if last else None
+        in_row[0] = end_row
+        cp(a("sro"), a("srof"))
         for lo, hi in thirds:
             act(a("g2", 16 * lo, 16 * hi), a("lt", ind=a("idx2", lo, hi)), AF.Relu)
         for lo, hi in thirds:
             tt(a(xn, B0 + 16 * lo, B0 + 16 * hi), a(xo, ind=a("src", lo, hi)), a("g2", 16 * lo, 16 * hi), OP.add)
-            if lo == 0:
-                cp(a("sro"), a("srof"))
         for h in (0, 1):
-            act(a(on, B0 + 256 * h, B0 + 256 * h + 256), a(oo, ind=a("sro", 16 * h, 16 * h + 16)), AF.Copy)
+            act(a(on, B0 + 256 * h, B0 + 256 * h + 256), a(oo, 0, B0 + 512, ind=a("sro", 16 * h, 16 * h + 16)), AF.Copy)
         act(a("xv", 256, 512), a(xn, ind=a(l1, 16, 32)), AF.Copy)
+        in_row[0] = None if last else ("look", t)
+        if not last:
+            cp(a("xv", 0, 256), a(xn, ind=a(l1, 0, 16)))
+        for h in (0, 1):
+            red(a("avf", h, h + 1), a("dm", h, 32, 2), OP.max)
+        in_row[0] = None
         for h in (0, 1):
             ts(a("avl", h, h + 1), a("avf", h, h + 1), c(CH[h]), None, OP.max)
+        if not last:
+            cp(a("avg", 0, 2), a("avl"))
+        act(a(m2), a(xo, ind=a("avl")), AF.Copy)
         if t == 0:
             send(a("avl"), a("lav"), "a2_0", host, guest, "out1")
         else:
-            cp(a(m2), a(xo, ind=a("avl")))
             send(a(m2), a(l2), "a2_%d" % t, host, guest)
-        cp(a("xv", 0, 256), a(xn, ind=a(l1, 0, 16)))
-        conv(a("ph", 0, 32), "zw", "xv", 0, 512)
+        def lay(lo, hi):
+            cp(a("ypb", ind=a("olu", lo, hi)), a(xn, B0 + 16 * lo, B0 + 16 * hi))
+        in_row[0] = end_row
         if last:
             conv(a("pn", 0, 32), "zo", on, B0, B0 + 512)
+            cp(a("xv", 0, 256), a(xn, ind=a(l1, 0, 16)))
+        conv(a("ph", 0, 32), "zw", "xv", 0, 512)
+        in_row[0] = None
+        ts(a("khi"), a("ph", 0, 32), BIG, None, OP.add)
+        if last:
+            ts(a("olu"), a("pn", 0, 32), float(B0), None, OP.add)
+            aff(a("olf"), a("pn", 0, 32), -1.0 / NONE, -B0 / NONE)
+            tt(a("awo"), aw, a("olf"), OP.mult)
+            mm(a("pp", 64, 96), a("blkb"), a("awo"))
+            tt(a("dm"), a("pp", 64, 96), a("dg2"), OP.mult)
+            for h in (0, 1):
+                red(a("avp", h, h + 1), a("dm", h, 32, 2), OP.max)
+            in_row[0] = "lay"
+            for h in (0, 1):
+                ts(a("avg", h, h + 1), a("avp", h, h + 1), c(CH[h]), None, OP.max)
+            in_row[0] = None
             mm(a("pa", np_=8), a("g8"), a(on, B0, B0 + 512))
             act(a("ysb", np_=8), a("pa", np_=8), AF.Copy)
             dma("s", "ld6", [(T.yseat[:], a("ysb", np_=8))])
         if t == 0:
             act(a(l2), a("xg", ind=a("lav")), AF.Copy)
-        act(a(xn, 0, 32), a(l2), AF.Copy)
+        cp(a(xn, ind=a("avl")), a(m2))
         cp(a("sf"), a(l1, 32, 64))
         ts(a("vb"), a(l1, 0, 32), c(CK), None, OP.add)
-        ts(a("khi"), a("ph", 0, 32), BIG, None, OP.add)
         tt(a("vd"), a("vb"), a("dg2"), OP.mult)
         ts(a("kh"), a("khi"), 4095, None, OP.bitwise_and)
         for h in (0, 1):
@@ -839,15 +882,18 @@ def rank_program(g, core, T, topo):
         ts(a("hs"), a("hp"), 5, 8191, OP.logical_shift_right, OP.bitwise_and)
         ts(a("hw"), a("hs"), c(CT0 + t), None, OP.add)
         mm(a("pm", 0, 32), a("idn"), a("k7"), True, False)
-        mm(a("pb", 0, 225), a("idn"), a("tm", 0, 225), True, False)
+        two = ("pb", "pc")
         for h in (0, 1):
-            tt(a("lt2", 256 * h, 256 * h + 256), a("dicx", ind=a("hw", 16 * h, 16 * h + 16)), a("xv", 256 * h, 256 * h + 256), OP.is_gt)
+            mm(a(two[h], 0, 97), a("idn"), a("tm", 128 * h, 128 * h + 97), True, False)
+        act(a("d2", 16 * HV, 512), a("dicx", ind=a("hw", HV, 32)), AF.Copy)
+        for lo, hi in ((0, HV // 2), (HV // 2, HV)):
+            tt(a("lt2", 16 * lo, 16 * hi), a("dicx", ind=a("hw", lo, hi)), a("xv", 16 * lo, 16 * hi), OP.is_gt)
+        in_row[0] = "lay" if last else None
+        tt(a("lt2", 16 * HV, 512), a("d2", 16 * HV, 512), a("xv", 16 * HV, 512), OP.is_gt)
+        if last:
+            lay(*LAY[0])
         for i in range(16):
             mm(a("pm", 0, 32), sel("zk", i), a("lt2", 32 * i, 32 * i + 32), False, i == 15)
-        if last:
-            aff(a("olf"), a("pn", 0, 32), 1.0 / 32, 1.0)
-            ts(a("olu"), a("pn", 0, 32), 32.0, None, OP.add)
-            tt(a("awo"), aw, a("olf"), OP.mult)
         for h in (0, 1):
             scan(a("cs", 16 * h, 16 * h + 16), a("pm", 16 * h, 16 * h + 16), a("vt", 16 * h, 16 * h + 16), NONE, OP.min, OP.max)
         cl = [a("cs", 15, 16), a("cs", 31, 32)]
@@ -855,41 +901,37 @@ def rank_program(g, core, T, topo):
             ts(a("exd", h, 96, 2), a("dg"), cl[h], None, OP.mult)
         for h in (0, 1):
             ts(a("exo", 112 * h, 112 * h + 97), a("one", 0, 97), cl[h], None, OP.mult)
+        in_row[0] = None
         for h in (0, 1):
-            mm(a("pb", 128 * h, 128 * h + 96), a("blkk"), a("exd"), False, False)
+            mm(a(two[h], 0, 96), a("blkk"), a("exd"), False, False)
+            mm(a(two[h], 0, 97), a("nidk"), a("exo", 112 * h, 112 * h + 97), False, True)
+        ts(a("tgt"), a("cs", 15, 32, 16), XW - 1.0, None, OP.min)
+        act(a(m3, 0, 32), a(xn, ind=a("tgt")), AF.Copy)
         for h in (0, 1):
-            mm(a("pb", 128 * h, 128 * h + 97), a("nidk"), a("exo", 112 * h, 112 * h + 97), False, h == 1)
-        if last:
-            mm(a("pp", 64, 96), a("blkb"), a("awo"))
-        for h in (0, 1):
-            red(a("cf", h, h + 1), a("pb", 128 * h, 128 * h + 97), OP.min, apply_absolute_value=True)
-        for h in (0, 1):
-            ts(a("tgt", h, h + 1), a("cf", h, h + 1), c(CH[h]), cl[h], OP.add, OP.min)
-        cp(a(m3), a(xn, ind=a("tgt")))
+            red(a(m3, 32 + h, 33 + h), a(two[h], 0, 97), OP.min, apply_absolute_value=True)
         send(a(m3), a(l3), "a3_%d" % t, guest, host)
-        cp(a("tgf", 0, 2), a("tgt"))
-        ts(a("tgw", 0, 2), a("tgt"), B0 + 511.5, -512.0, OP.is_ge, OP.mult)
-        if last:
-            tt(a("dm"), a("pp", 64, 96), a("dg2"), OP.mult)
-        tt(a("tgc", 0, 2), a("tgf", 0, 2), a("tgw", 0, 2), OP.add)
-        if last:
-            for h in (0, 1):
-                red(a("avf", h, h + 1), a("dm", h, 32, 2), OP.max)
-        cp(a("tg2"), a("tgc", 0, 2))
+        for h in (0, 1):
+            ts(a("tg2" if last else "tgf", h, h + 1), a(m3, 32 + h, 33 + h), c(CH[h]), cl[h], OP.add, OP.min)
+        if not last:
+            ts(a("tgw", 0, 2), a("tgf", 0, 2), B0 + 511.5, -512.0, OP.is_ge, OP.mult)
+            tt(a("tgc", 0, 2), a("tgf", 0, 2), a("tgw", 0, 2), OP.add)
+            cp(a("tg2"), a("tgc", 0, 2))
+        else:
+            act(a(on, B0 + 512, XW), a(on, B0, B0 + 16), AF.Copy)
+            for x in LAY[1:]:
+                lay(*x)
+        for h in (0, 1):
+            ts(a("avo", h, h + 1), a(l3, 32 + h, 33 + h), c(CH[h]), a("avg", h, h + 1), OP.add, OP.min)
         if not last:
             cp(a(xn, ind=a("tg2")), a(l2))
-            cp(a(xn, ind=a("avl")), a(l3))
+            cp(a(xn, ind=a("avo")), a(l3, 0, 32))
         else:
-            for h in (0, 1):
-                ts(a("avo", h, h + 1), a("avf", h, h + 1), c(CH[h]), None, OP.max)
-            for lo in range(0, 32, 8):
-                cp(a("ypb", ind=a("olu", lo, lo + 8)), a(xn, B0 + 16 * lo, B0 + 16 * lo + 128))
             act(a("oc"), a(on, ind=a("tg2")), AF.Copy)
             conv(a("pm", 0, 2), "zo", "oc", 0, 32)
-            ts(a("ocu"), a("pm", 0, 2), 32.0, None, OP.add)
+            ts(a("ocu"), a("pm", 0, 2), float(B0), None, OP.add)
             cp(a("ypb", ind=a("ocu")), a(l2))
-            cp(a("ypb", ind=a("avo")), a(l3))
-            dma("y", "ld7", [(T.ypup[:], a("ypb", 32, 544))])
+            cp(a("ypb", ind=a("avo")), a(l3, 0, 32))
+            dma("y", "ld7", [(T.ypup[:], a("ypb", B0, B0 + 512))])
     issue_all()
     for s in sorted(count):
         if s != "ld7":

@@ -1,15 +1,22 @@
 import math
+import numpy as np
 from concourse.mybir import AluOpType as OP, AxisListType as AX, ActivationFunctionType as AF
 
 RO = 4
 NS = 7
-NS0 = 6
+NS0 = 7
 B0 = 48
 LAGV, LAGS = 0.2, 0.0
-HS, HS0 = 128, 384
-QAT, QB = 1, 2
+HS, HS0 = 256, 128
+CUT = 256
+S1V = (2,)
+ONE = 4
+J15 = 256
+SPLIT, SPLIT0 = (1, 0), (1, 0)
 XW = 576
 DW = 8800
+DY = 1536
+WS = ((0, 8), (8, 12), (12, 17))
 RW = 4240
 E2, C2 = 4096, 2048
 ZC = 8192
@@ -17,47 +24,49 @@ WDT = "float16"
 
 F, I, U, H = "float32", "int32", "uint16", "bfloat16"
 SB = {
-    "dicx": (DW, H), "dicy": (DW, H), "pupb": (512, H), "seatb": (32, I), "wtb": (4, I), "seatu": (32, U),
-    "x0": (XW, H), "x1": (XW, H), "o0": (XW, H), "o1": (XW, H), "oc": (32, H), "ocu": (2, U), "oio": (512, H), "x2": (752, H), "x2l": (48, U),
+    "dicx": (DW, H), "dicy": (DY + DW, H), "pupb": (512, H), "seatb": (32, I), "wtb": (4, I), "seatu": (32, U),
+    "x0": (XW, H), "x1": (XW, H), "o0": (XW, H), "o1": (XW, H), "oc": (32, H), "ocu": (2, U), "oio": (512, H), "x2": (816, H), "x2l": (48, U),
     "lt": (ZC + 16, H), "d0": (512, H), "d1": (512, H), "d2": (512, H),
     "ksi": (48, I), "ks": (48, I), "prod": (512, I), "prs": (512, I), "off": (512, U),
-    "pw": (512, H), "lns": (32, F), "nsi": (32, I), "roff": (32, U), "rof2": (32, U), "lnn": (32, F), "nni": (32, I),
-    "r32": (32, U), "pw0": (256, H), "pw1": (256, H), "ln2": (48, F),
-    "pq": (112, F), "dq": (64, F), "zq": (32, F), "wq": (32, F), "tq": (48, F), "sq": (128, F), "st1": (32, F), "st2": (32, F),
-    "rq": (128, F), "sc": (128, F), "sd": (128, F), "n15": (32, F), "a15": (32, F), "n2": (32, F), "thn": (32, F),
+    "wj": (1, H), "wneg": (32, H), "th15": (32, F), "n8": (32, F), "t15": (32, F), "stp": (36, F), "steps": (2, U),
+    "pw": (512, H), "lns": (32, F), "roff": (32, U), "rof2": (32, U), "lnn": (32, F), "nni": (32, I),
+    "r32": (32, U), "ln2": (48, H),
+    "pq": (112, H), "dq": (64, H), "zq": (32, H), "wq": (32, H), "tq": (48, H), "cq": (384, H), "da": (256, H),
+    "rq": (32, F), "sc": (128, F), "sd": (128, F), "n15": (32, F), "a15": (32, F), "n2": (32, F), "thn": (32, F),
     "ex": (RW, F), "eb": (768, H), "cd": (RW, F), "cc": (512, F), "ce": (384, F), "mq": (32, F), "nm2": (32, F), "nq": (32, F), "nq2": (32, F),
     "f15": (32, F), "m15": (32, F), "u15": (32, F), "nm": (32, F), "nnm": (32, F), "q32": (32, F), "s0": (168, F), "s1": (168, F),
-    "y1": (36, F), "y2": (36, F), "wa": (272, H), "v4": (136, WDT), "ap4": (136, WDT), "le2": (6, U), "ch": (40, U), "c1": (48, U), "w": (272, F),
+    "y1": (36, F), "y2": (36, F), "wa": (272, H), "v4": (544, WDT), "ap4": (544, WDT), "le2": (6, U), "ch": (40, U), "c1": (112, U), "w": (272, F),
     "mc": (64, H), "kni": (32, I), "kn": (32, I), "kn1": (32, F), "ksq": (32, I), "v0": (32, I), "v1": (32, F),
     "nt": (32, F), "nu": (32, F), "nl": (36, F), "aw": (32, F), "st": (36, F), "apk": (64, WDT), "awq": (32, WDT),
     "yp": (36, F), "idx2": (34, U), "uu": (36, F), "e1": (36, F), "e2": (36, F),
     "srcf": (168, F), "src": (34, U), "srof": (32, F), "sro": (32, U), "g2": (528, H),
     "dm": (32, F), "avf": (4, F), "avg": (4, F), "avp": (4, F), "avl": (2, U), "avo": (2, U), "olf": (32, F), "olu": (32, U), "awo": (32, WDT),
-    "xv": (512, H), "sf": (32, F), "vb": (32, F), "vd": (32, F), "vh": (4, F), "vt": (32, F), "cs": (32, F),
-    "khi": (32, I), "kh": (32, I), "hp": (32, I), "hs": (32, I), "hw": (32, U), "lt2": (512, H),
+    "xv": (528, H), "sf": (32, F), "vb": (32, F), "vd": (32, F), "vh": (4, F), "vt": (32, F), "cs": (32, F),
+    "khi": (32, I), "kh": (32, I), "hp": (32, I), "hs": (32, I), "hw": (32, U), "lt2": (528, H),
     "exd": (96, WDT), "exo": (224, WDT), "cf": (4, F), "tgt": (2, U), "tgf": (4, F), "tgw": (4, F), "tgc": (4, F), "tg2": (2, U),
     "xg": (B0 + 512, H), "lav": (2, U), "ypb": (B0 + 512, H), "ysb": (512, F),
     "zo": (144, H), "zw": (144, WDT), "zm": (144, H), "zr": (144, H), "zk": (144, H), "idn": (128, H), "nid": (128, H),
     "nidk": (128, H), "blkb": (128, H), "blkk": (128, H), "g8": (8, H), "dh": (128, H), "dl": (128, H), "ohi": (512, H), "olo": (512, H),
     "io": (144, F), "mg": (128, F), "i16": (48, F), "i8": (32, F), "b32": (32, F),
-    "ie": (256, F), "ia": (256, F), "ic": (384, F), "t1": (208, F), "t4": (96, F), "ti": (512, F), "t2": (256, F), "t3": (256, F),
-    "col": (48, F), "ci": (8, I), "q16": (36, F), "qm1": (36, F), "dg": (48, F), "dg2": (32, F), "one": (112, WDT),
-    "tm": (232, H), "k7": (32, H), "nio": (16, F),
+    "ie": (256, H), "ia": (256, H), "ic": (384, F), "t1": (208, F), "t4": (96, F), "ti": (512, F),
+    "col": (64, F), "ci": (8, I), "q16": (36, F), "qm1": (36, F), "dg": (48, F), "dg2": (32, F), "one": (112, WDT),
+    "tm": (384, H), "k7": (48, H), "rk": (48, H), "nidn": (128, H), "zg": (144, WDT), "cwg": (1, F), "vd2": (48, F), "nsh": (4, F),
+    "vt2": (48, F), "dsc": (48, F), "tot": (64, F), "dm3": (16, F), "am": (48, F), "avs": (4, F), "bb": (48, F), "av2": (4, U),
 }
 for _t in range(RO):
-    SB["m1_%d" % _t] = (64, U); SB["l1_%d" % _t] = (64, U)
+    SB["m1_%d" % _t] = (66, U); SB["l1_%d" % _t] = (66, U)
     for _n in ("m2", "l2", "m3", "l3"):
-        SB["%s_%d" % (_n, _t)] = (32 if _n[1] == "2" else 34, H)
+        SB["%s_%d" % (_n, _t)] = (32, H) if _n[1] == "2" else (34, H) if _t == RO - 1 else (38, F)
 PS = ["pc", "pa", "pb", "pk", "pm", "pn", "pp", "ph"]
 SCRATCH, HOME = {}, {}
 INSIDE, FILL = {}, 768
-for _k in ("cc", "ti", "ce", "ic", "ia", "ie", "t2", "t3", "t1", "io", "mg", "b32"):
+for _k in ("cc", "ti", "ce", "ic", "t1", "io", "mg", "b32", "sd", "t4", "i16", "dg", "thn", "mq", "t15", "i8"):
     INSIDE[_k] = FILL
     FILL += SB[_k][0]
 for _k, (_w, _d) in SB.items():
     if _k in INSIDE:
         continue
-    if _w > 64:
+    if _w > 80:
         SCRATCH["b_" + _k] = ("sbuf", [128, _w], _d)
         HOME[_k] = (_k, 0)
     else:
@@ -71,18 +80,35 @@ SEMAPHORES = ["qv", "qs", "qp", "qg", "sent", "a0", "out0", "out1"] + ["ld%d" % 
  CH0, CH1, CT0) = range(27)
 CZ1 = CT0 + 4
 CU, CU2, CK32 = CZ1 + 3, CZ1 + 4, CZ1 + 5
-CTH = CZ1 + 6
+CN = CZ1 + 6
+CTH = CZ1 + 7 - 5
+CD0, CSP, CH2, CR = 42, 45, 48, 49
+TINY = 2.0 ** -22
 MAG = 1.5 * 2.0 ** 23
 CH = (CK16, CK32)
 NONE = 4096.0
-CYC, WAKE, HOP, SLACK, AHEAD = 1.0e-3, 0.2, 1.6, 0.03, 400
-SHORT = 0.1
+PACES = [{"cycle": c_, "gather": c_ * g_, "scatter": c_ * 3.8, "column": c_ * p_, "wait": w_, "hop": h_, "none": 0.0}
+         for c_, g_, p_, w_, h_ in ((0.95e-3, 1.56, 0.52, 0.17, 1.2), (1.15e-3, 1.9, 0.55, 0.1, 0.7), (0.9e-3, 1.2, 0.6, 0.22, 1.6),
+                                    (1.2e-3, 1.3, 0.6, 0.15, 1.2), (0.9e-3, 1.9, 0.5, 0.2, 0.9))]
+ROWS = 0.7
+STRETCH, SWEEPS, TRIES, NEAR = 160, 12, 1200, 0.15
+HEAT = 0.0003
+LEAD, TURNS = 5, 3
+KEPT = ("loads", "first", 0, 1, 2, 3) + tuple(("steps", t) for t in range(RO))
+FIRM = ("loads", "first")
+LAG = 3
+LROW = 0
+SROW = None
+EXS, EBS = 0, 1
+SOON = {"codes": 1.0, "steps": 1.0}
 EARLY = 24
 HV = 20
 LAY = ((0, 10), (10, 14), (14, 32))
 UNSURE = 0.07
 ORDER = []
-LOADED = {"ld3": 3.7, "ld4": 6.5, "ld5": 7.0}
+LOADED = {"ld3": 2.6, "ld4": 6.5, "ld5": 7.0}
+for _p, _f in zip(PACES, (1.0, 1.15, 0.85, 1.3, 0.9)):
+    _p.update({k: v * _f for k, v in LOADED.items()})
 
 
 def a(name, lo=0, hi=None, step=1, ind=None, np_=128):
@@ -119,48 +145,205 @@ def cost(q, rd, wr):
     xs = [x for x in wr + rd if isinstance(x, tuple)]
     n = len(range(*xs[0][1:4]))
     if q == "p":
-        return max(64, n) * CYC / 2
+        return ("column", 0.0, max(64, n))
     if q == "g":
-        return 0.13 + 2 * n * CYC
+        return ("cycle", 0.13, 2 * n)
     for x in xs:
         if x[4] is not None:
-            return 0.06 + 16 * len(range(*x[4][1:4])) * CYC * (3.8 if x is xs[0] else 1.56)
+            return ("scatter" if x is xs[0] else "gather", 0.06 if q == "v" else 0.075, 16 * len(range(*x[4][1:4])))
     wide = [x for x in xs if len(range(*x[1:4])) > 1]
     n = max(len(range(*x[1:4])) for x in xs)
     if q == "v" and all(x[0] in SB and SB[x[0]][1] in (H, U, WDT) for x in wide):
         n = n / 2
     if q == "v" and len(rd) == 2 and len(wide) == 3 and all(x[0] in SB for x in wide[1:]):
         n = 2 * n
-    return max(64, n) * CYC
+    return ("cycle", 0.0, max(64, n))
 
 
-def lay_out(calls, tail):
-    end, free, out, todo = [None] * len(calls), {}, [], list(range(len(calls)))
-    while todo:
-        ahead, est, byq, slack = todo[:AHEAD], {}, {}, {}
-        for i in ahead:
-            e, slack[i] = free.get(calls[i][0], 0.0), SLACK
-            for m, w in calls[i][3]:
-                if end[m] is None:
-                    e, slack[i] = max(e, est[m] + calls[m][2] + w), UNSURE
-                else:
-                    e = max(e, end[m] + w)
-            est[i] = e
-            byq.setdefault(calls[i][0], []).append(i)
-        pick = None
-        for xs in byq.values():
-            xs.sort(key=lambda i: -tail[i])
-            for k, i in enumerate(xs):
-                if slack[i] == SLACK and (pick is None or est[i] + SHORT * calls[i][1] < est[pick] + SHORT * calls[pick][1]) and all(
-                        est[i] + calls[i][1] + tail[m] <= est[m] + max(tail[m], calls[m][1] + tail[i]) + slack[m] for m in xs[:k]):
-                    pick = i
-        if pick is None:
-            pick = ahead[0]
-        end[pick] = est[pick] + calls[pick][2]
-        free[calls[pick][0]] = est[pick] + calls[pick][1]
-        todo.remove(pick)
-        out.append(pick)
-    return out
+def lay_out(calls):
+    n = len(calls)
+    queue = [x[0] for x in calls]
+    above = [0] * n
+    for i, x in enumerate(calls):
+        far = 0
+        for m, w in x[3]:
+            far |= above[m] if w != "hint" else 0
+        x[3][:] = [(m, w) for m, w in x[3] if not far >> m & 1 or calls[m][2] != 0.0]
+        above[i] = far | sum(1 << m for m, w in x[3] if w != "hint")
+
+    def times(p, hints=True):
+        busy = [x[1][1] + x[1][2] * p[x[1][0]] for x in calls]
+        late = [p.get(x[2], x[2]) for x in calls]
+        before = [[(m, busy[m] + (0.0 if w in ("row", "hint") else late[m] + p[w])) for m, w in x[3] if hints or w != "hint"]
+                  for x in calls]
+        after = [[] for x in calls]
+        for i in range(n):
+            for m, w in before[i]:
+                after[m].append((i, w - busy[m] + busy[i]))
+        return busy, before, after
+
+    def fill(order, busy, edges):
+        at, used = [0.0] * n, {}
+        for i in order:
+            t = max([at[m] + w for m, w in edges[i]] + [0.0])
+            xs = used.setdefault(queue[i], [])
+            k = len(xs)
+            while k > 0 and xs[k - 1][1] > t:
+                k -= 1
+            while k < len(xs) and t + busy[i] > xs[k][0]:
+                t = max(t, xs[k][1])
+                k += 1
+            xs.insert(k, (t, t + busy[i]))
+            at[i] = t
+        return at
+
+    def length(order, busy, before):
+        at, free = [0.0] * n, {}
+        for i in order:
+            at[i] = max([at[m] + w for m, w in before[i]] + [free.get(queue[i], 0.0)])
+            free[queue[i]] = at[i] + busy[i]
+        return max(free.values())
+
+    paces = [times(p) for p in PACES]
+    found = []
+    for busy, before, after in paces[:LEAD]:
+        back = [0.0] * n
+        for i in range(n - 1, -1, -1):
+            back[i] = max([back[m] + w for m, w in after[i]] + [0.0])
+        plain = list(back)
+        for i in range(n - 1, -1, -1):
+            back[i] = max([back[m] + w for m, w in after[i]] + [plain[i] + calls[i][5]])
+        for turn in range(TURNS):
+            at = fill(sorted(range(n), key=lambda i: (round(-back[i] - busy[i], 6), i)), busy, before)
+            order = sorted(range(n), key=lambda i: (round(at[i], 6), i))
+            found.append(([length(order, b, e) for b, e, _ in paces], order))
+            back = fill(sorted(range(n), key=lambda i: (round(-at[i] - busy[i], 6), -i)), busy, after)
+    least = [min(x[0][k] for x in found) for k in range(len(paces))]
+    order = min(found, key=lambda x: sum(t / s for t, s in zip(x[0], least)))[1]
+
+    paces = [times(p, False) for p in PACES]
+    qs = sorted(set(queue))
+    qn = [qs.index(q) for q in queue]
+    draw = np.random.default_rng(0)
+    same = {}
+    for i in range(n):
+        same.setdefault(calls[i][6][1:], {})[calls[i][6][0]] = i
+
+    def borrow(order):
+        best = sum(length(order, b, e) / s for (b, e, _), s in zip(paces, least))
+        for src in range(RO):
+            for dst in range(RO):
+                place = {i: float(k) for k, i in enumerate(order)}
+                pairs = [(x[src], x[dst]) for x in same.values() if src in x and dst in x and src != dst]
+                if pairs:
+                    shift = float(np.median([place[y] - place[x] for x, y in pairs]))
+                    mine = sorted(place[y] for x, y in pairs)
+                    for (x, y), k in zip(sorted(pairs, key=lambda z: place[z[0]]), mine):
+                        place[y] = k
+                    for i in range(n):
+                        place[i] = max([place[m] for m, w in paces[0][1][i]] + [place[i]])
+                    other = sorted(range(n), key=lambda i: (place[i], i))
+                    t = sum(length(other, b, e) / s for (b, e, _), s in zip(paces, least))
+                    if t < best:
+                        best, order = t, other
+        return order
+
+    for lo in list(range(0, n, STRETCH // 2)) * SWEEPS:
+        if lo == 0:
+            order = borrow(order)
+        hi = min(n, lo + STRETCH)
+        inside = set(order[lo:hi])
+        given = []
+        for busy, before, after in paces:
+            at, free, tail, then = [0.0] * n, [0.0] * len(qs), [0.0] * n, [0.0] * len(qs)
+            for i in order[:lo]:
+                at[i] = max([at[m] + w for m, w in before[i]] + [free[qn[i]]])
+                free[qn[i]] = at[i] + busy[i]
+            for i in reversed(order[hi:]):
+                tail[i] = max([tail[m] + w + busy[i] - busy[m] for m, w in after[i]] + [then[qn[i]] + busy[i]])
+                then[qn[i]] = tail[i]
+            out, own = [0.0] * n, [0] * n
+            for i in inside:
+                out[i] = max([tail[m] + w + busy[i] - busy[m] for m, w in after[i] if m not in inside] + [0.0])
+                own[i] = (qn[i], busy[i], max([at[m] + w for m, w in before[i] if m not in inside] + [0.0]),
+                          [x for x in before[i] if x[0] in inside], out[i])
+            given.append((busy, before, after, at, free, tail, then, own))
+
+        def span(xs, g_, u=0):
+            at, free, own, end = g_[3], list(g_[4]), g_[7], 0.0
+            for i in xs[:u]:
+                q, busy, t, before, out = own[i]
+                t = at[i]
+                free[q] = t + busy
+                if t + out > end:
+                    end = t + out
+            for i in xs[u:]:
+                q, busy, t, before, out = own[i]
+                if free[q] > t:
+                    t = free[q]
+                for m, w in before:
+                    if at[m] + w > t:
+                        t = at[m] + w
+                at[i] = t
+                free[q] = t + busy
+                if t + out > end:
+                    end = t + out
+            return max(end, max(x + y for x, y in zip(free, g_[6])))
+
+        def held(xs, g_):
+            busy, before, after, at, free, tail, then, own = g_
+            end, then, found = span(xs, g_), list(then), []
+            for k in range(len(xs) - 1, -1, -1):
+                i = xs[k]
+                tail[i] = max([tail[m] + w + busy[i] - busy[m] for m, w in after[i]] + [then[qn[i]] + busy[i]])
+                then[qn[i]] = tail[i]
+                if at[i] + tail[i] > end - NEAR and at[i] > max([at[m] + w for m, w in before[i]] + [0.0]) + 0.01:
+                    found.append(k)
+            return found
+
+        xs = order[lo:hi]
+        now = [span(xs, g_) / s for g_, s in zip(given, least)]
+        best, places, stale = sum(now), [], [len(xs)] * len(given)
+        kept = (best, xs)
+        for turn in range(TRIES):
+            if not places or turn % 16 == 0:
+                places = held(xs, given[int(draw.integers(len(given)))])
+                if not places:
+                    continue
+            k = places[int(draw.integers(len(places)))]
+            mates = [u for u in range(k - 1, max(-1, k - 60), -1) if qn[xs[u]] == qn[xs[k]]][:int(draw.integers(1, 7))]
+            if not mates:
+                continue
+            u = mates[-1]
+            if draw.random() < 0.5:
+                go = {xs[k]}
+                for i in reversed(xs[u:k + 1]):
+                    if i in go:
+                        go.update(m for m, w in paces[0][1][i])
+                if xs[u] in go:
+                    continue
+                ys = xs[:u] + [i for i in xs[u:k + 1] if i in go] + [i for i in xs[u:k + 1] if i not in go] + xs[k + 1:]
+            else:
+                go = {xs[u]}
+                for i in xs[u:k + 1]:
+                    if i in go:
+                        go.update(m for m, w in paces[0][2][i])
+                if xs[k] in go:
+                    continue
+                ys = xs[:u] + [i for i in xs[u:k + 1] if i not in go] + [i for i in xs[u:k + 1] if i in go] + xs[k + 1:]
+            room, t, new = HEAT * (1.0 - turn / TRIES) * draw.exponential(), best, list(now)
+            for p, g_ in enumerate(given):
+                new[p] = span(ys, g_, min(u, stale[p])) / least[p]
+                stale[p] = u
+                t += new[p] - now[p]
+                if t > best + room + 0.001:
+                    break
+            if t <= best + room:
+                best, xs, places, stale, now = t, ys, places if t > best - 1e-6 else [], [len(xs)] * len(given), new
+                if t < kept[0]:
+                    kept = (t, xs)
+        order[lo:hi] = kept[1]
+    return borrow(order)
 
 
 def rank_program(g, core, T, topo):
@@ -227,23 +410,24 @@ def rank_program(g, core, T, topo):
     calls = []
     seen = {}
     rows = {}
-    in_row = [None]
+    in_row, group, spare = [None], [None], [0]
+    now, met = [0], {}
     in_sum, loose = [False], set()
 
     def record(q, rd, wr, busy, done, issue, after=()):
-        n, dep = len(calls), {m: WAKE for m in after}
+        n, dep = len(calls), {m: "none" for m in after}
         use = uses(rd, wr)
         for name, m, w in use:
             for (m2, w2, q2, n2) in seen.get(name, []):
                 if name in PS and q == q2 == "p":
                     if n2 not in loose or not in_sum[0]:
-                        dep.setdefault(n2, 0.0)
+                        dep.setdefault(n2, "none")
                 elif (name in PS and q2 != q) or ((w or w2) and m & m2):
-                    dep[n2] = WAKE
-        if in_row[0] is not None:
+                    dep[n2] = "wait"
+        if in_row[0] in KEPT:
             key = (in_row[0], q)
             if key in rows:
-                dep.setdefault(rows[key], calls[rows[key]][1] - calls[rows[key]][2])
+                dep.setdefault(rows[key], "row" if in_row[0] in FIRM else "hint")
             rows[key] = n
         for name, m, w in use:
             lst = seen.setdefault(name, [])
@@ -254,7 +438,10 @@ def rank_program(g, core, T, topo):
             elif w:
                 lst[:] = [e for e in lst if e[0] & ~m]
             lst.append((m, w, q, n))
-        calls.append((q, busy, done, list(dep.items()), issue, None))
+        x = [y for y in list(wr) + list(rd) if isinstance(y, tuple) and len(y) == 6 and isinstance(y[0], str)][:1]
+        key = (q, busy) + tuple((y[0].split("_")[0].rstrip("01y").replace("dicx", "dic"),) + y[1:4] for y in x)
+        met[(now[0], key)] = met.get((now[0], key), 0) + 1
+        calls.append((q, busy, done, list(dep.items()), issue, SOON.get(group[0], 0.0), (now[0], key, met[(now[0], key)])))
         return n
 
     def op(q, rd, wr, fn):
@@ -264,18 +451,12 @@ def rank_program(g, core, T, topo):
             count[s] = count.get(s, 0) + 1
             fn().then_inc(T.sem[s], 1)
             note(use, q, s, count[s])
-        t = cost(q, rd, wr) + (1.3 if len(calls) < 7 and q == "s" else 0.0)
-        record(q, rd, wr, t, t, issue)
+        t = ("cycle", 1.4, 0) if len(calls) < 7 and q == "s" else cost(q, rd, wr)
+        record(q, rd, wr, t, 0.0, issue)
 
     def issue_all():
         if not ORDER:
-            n = len(calls)
-            tail = [0.0] * n
-            for i in range(n - 1, -1, -1):
-                tail[i] += calls[i][2]
-                for m, w in calls[i][3]:
-                    tail[m] = max(tail[m], w + tail[i])
-            ORDER[:] = lay_out(calls, tail)
+            ORDER[:] = lay_out(calls)
         for i in ORDER:
             calls[i][4]()
 
@@ -309,8 +490,32 @@ def rank_program(g, core, T, topo):
     def aff(o, i, scale, bias):
         act(o, i, AF.Identity, bias, scale)
 
+    def total(o, i, scale):
+        spare[0] = (spare[0] + 16) % 64
+        x = a("tot", spare[0], spare[0] + len(range(*i[1:4])))
+        op("s", [i], [x, o], lambda: g.scalar.activation(ap(x), ap(i), AF.Identity, scale=scale, accum_out=ap(o)))
+
     def mm(o, l, r, st=True, sp=True):
         op("p", [l, r], [o], lambda: g.tensor.matmul(ap(o), ap(l), ap(r), st, sp))
+
+    def mms(xs, size=8):
+        for k in range(0, len(xs), size):
+            part, n = xs[k:k + size], len(calls)
+            for x in part:
+                mm(*x)
+            mine = calls[n:]
+            del calls[n:]
+            for lst in seen.values():
+                lst[:] = [e if e[3] < n else e[:3] + (n,) for e in lst]
+            for key in rows:
+                rows[key] = min(rows[key], n)
+            dep = {}
+            for x in mine:
+                for m, w in x[3]:
+                    if m < n and dep.get(m) != "wait":
+                        dep[m] = w
+            calls.append(("p", ("column", 0.0, sum(x[1][2] for x in mine)), 0.0, list(dep.items()),
+                          lambda mine=mine: [x[4]() for x in mine], mine[0][5], mine[0][6]))
 
     def add_mm(o, l, r, left):
         def fn():
@@ -339,7 +544,7 @@ def rank_program(g, core, T, topo):
             eng[q].dma_start(ap(o), ap(i)).then_inc(T.sem[s], 16)
             count[s] = 16
             note(use, q, s, 16)
-        record(q, [i] + list(also), [o], 0.1, LOADED.get(s, 1.5), issue)
+        record(q, [i] + list(also), [o], ("cycle", 0.1, 0), s if s in LOADED else 1.7, issue)
 
     def send(src, dst, s, to, frm, loc="sent", also=()):
         def issue():
@@ -354,15 +559,14 @@ def rank_program(g, core, T, topo):
         def landed():
             count[s] = len(topo.engines(T.cores[frm], core))
             note([(dst[0], bits(dst), True)], "remote", s, count[s])
-        n = record("g", [src] + list(also), [], 0.4, HOP, issue)
-        record("landing", [], [dst], 0.0, 0.0, landed, [n])
+        n = record("g", [src] + list(also), [], ("cycle", ROWS, 0), "hop", issue)
+        record("landing", [], [dst], ("cycle", 0.0, 0), 0.0, landed, [n])
 
     def sel(z, i):
         return a(z, 15 - i, 143 - i)
 
     def conv(o, z, buf, lo, hi):
-        for i in range(16):
-            mm(o, sel(z, i), a(buf, lo + i, hi, 16), i == 0, i == 15)
+        mms([(o, sel(z, i), a(buf, lo + i, hi, 16), i == 0, i == 15) for i in range(16)])
 
     def row(r):
         return a("dg", r, r + 1)
@@ -370,9 +574,9 @@ def rank_program(g, core, T, topo):
     in_row[0] = "loads"
     dma("y", "ld0", [(a("pupb"), T.pup[:])])
     dma("s", "ld1", [(a("seatb"), T.seat[:])])
-    dma("s", "ld2", [(a("wtb", 0, 1), T.wt[:])])
-    dma("y", "ld3", [(a("dicx", 0, 4096), T.dic[:, 0:4096])])
-    dma("s", "ld4", [(a("dicx", 4096, 8192), T.dic[:, 4096:8192])])
+    dma("y", "ld2", [(a("wtb", 0, 1), T.wt[:])])
+    dma("y", "ld3", [(a("dicx", 0, 1024), T.dic[:, 0:1024])])
+    dma("y", "ld4", [(a("dicx", 1024, 8192), T.dic[:, 1024:8192])])
     ms(a("ln2"), 1.0)
     in_row[0] = 0
     act(a("lns", 0, 1), a("ln2", 0, 1), AF.Ln)
@@ -387,36 +591,23 @@ def rank_program(g, core, T, topo):
     iota(a("ie"), [[0, 16], [1, 16]], 0)
     iota(a("ia"), [[1, 16], [0, 16]], 0)
     iota(a("ic"), [[64, 24], [1, 16]], 512)
+    iota(a("mg"), [[16, 8], [0, 16]], 0)
+    iota(a("mq"), [[1, 2], [2, 2], [0, 8]], 0)
+    iota(a("thn"), [[0, 4], [1, 8]], 0)
+    iota(a("stp", 0, 16), [[1, 4], [8, 2], [16, 2]], 0)
+    iota(a("i8"), [[1, 16], [0, 2]], 0)
     for k in range(8):
         iota(a("ti", 64 * k, 64 * k + 64), [[4224, 2], [256, 2], [1, 16]], 528 * k)
-    iota(a("mq"), [[0, 8], [1, 4]], 0)
-    iota(a("thn"), [[1, 8], [0, 4]], 0)
-    iota(a("mg"), [[16, 8], [0, 16]], 0)
-    iota(a("i8"), [[1, 16], [0, 2]], 0)
-    fill(a("st1"), int(MAG) - 1023)
-    fill(a("st2"), int(MAG) - 1022)
-    fill(a("sd"), 0)
-    iota(a("eb", 512, 768), [[1, 256]], 1)
-    for x in (a("st1", 3, 32, 4), a("st2", 2, 32, 4), a("sq", 96, 128), a("st2", 3, 32, 4)):
-        fill(x, int(MAG) - 8192)
-    fill(a("pq", 96, 112), 0)
-    iota(a("sd", 3, 128, 4), [[0, 8], [1, 4]], -int(MAG) - 3)
     in_row[0] = None
-    for lo in (512, 1024, C2 + 512):
-        fill(a("cd", lo, lo + 512), 0)
-    for x, v in ((a("lt", ZC, ZC + 16), 0), (a("mc", 32, 64), 2048), (a("s0"), 1), (a("s0", 0, 165, 5), 0), (a("y2", 32, 33), 0), (a("k7"), -7 * 4096),
-                 (a("tm", 96, 128), 1 << 22), (a("tm", 224, 232), 1 << 22), (a("ypb", 0, B0), 0)):
-        fill(x, v)
-    for x in ("x0", "x1"):
-        ms(a(x, 0, B0), -1.0)
-        ms(a(x, B0 + 512, XW), -1.0)
+    ms(a("x0", 0, B0), -1.0)
+    ms(a("x0", B0 + 512, XW), -1.0)
     cp(c(CP), a("ci", 0, 1))
     ts(a("ci", 1, 2), a("ci", 0, 1), 15, None, OP.bitwise_and)
     ts(a("ci", 2, 3), a("ci", 0, 1), 112, None, OP.bitwise_and)
     ms(a("t1", 0, 16), math.exp(-1.0))
     ms(a("t1", 16, 32), 0.0)
     cp(a("col", CK, CG + 1), a("ci", 1, 3))
-    scan(a("t1", 32, 48), a("t1", 0, 16), a("t1", 16, 32), math.e, OP.mult, OP.add)
+    scan(a("t1", 32, 48), a("t1", 0, 16), a("t1", 16, 32), math.exp(0.8), OP.mult, OP.add)
     ts(c(CG15), c(CG), 15.0, None, OP.add)
     ts(c(CS), c(CK), 32.0, float(B0), OP.mult, OP.add)
     ts(a("idn"), a("io", 0, 128), c(CP), None, OP.is_equal)
@@ -458,7 +649,7 @@ def rank_program(g, core, T, topo):
             buf, w, k = tables.pop()
             col = lambda x: a(x[0], x[1] + k, x[1] + k + 1)
             aff(a(buf, w, w + 32), a("b32"), col(gt) if buf == "cc" else 0.0, col(add if buf == "cc" else uns))
-        in_row[0] = 0
+        in_row[0] = SROW
         for n, (j, first, f, x) in enumerate((
                 (C34, row(3), 1, row(4)), (C67, row(6), 1, row(7)), (CEF, row(14), 1, row(15)), (CY, row(11), 1, row(12)),
                 (CE, -60000.0, C2, row(4)), (CD, row(0), E2 + 8, row(1)), (CB, row(0), 8, row(1)), (CA, row(1), 16, row(0)),
@@ -474,58 +665,78 @@ def rank_program(g, core, T, topo):
                 aff(c(j), x, float(f), first)
             if n > 18:
                 table()
-        aff(a("t3"), a("ie"), c(CB), 0.0)
+        for n, (j, x) in enumerate(((CA, "ia"), (CB, "ie"))):
+            aff(a("da", 128 * n, 128 * n + 128), a("idn"), c(j), 0.0)
+            mm(a("pn", 0, 256), a("da", 128 * n, 128 * n + 128), a(x), n == 0, n == 1)
+        aff(a("ex", 512, 768), a("pn", 0, 256), 1.0, c(CD))
+        for i in range(ONE - 1):
+            aff(a("ex", 512 + i, 768, 16), a("ex", 512 + i, 768, 16), c(CZ0), 0.0)
         for n, j in enumerate((C67, C16, C24)):
             aff(c(CZ1 + n), c(j), c(CE), 60000.0)
-        aff(a("t2"), a("ia"), c(CA), c(CD))
         for n, j in enumerate((C67, C16, C24)):
             aff(a("ce", 128 * n, 128 * n + 128), a("ic", 128 * n, 128 * n + 128), c(j), c(CZ1 + n))
         while tables:
-            in_row[0] = 0 if len(tables) > EARLY else None
+            in_row[0] = SROW if len(tables) > EARLY else None
             table()
         in_row[0] = None
 
     def later_constants():
-        tt(a("ex", 512, 768), a("t2"), a("t3"), OP.add)
-        for i in range(3):
-            ts(a("ex", 512 + i, 768, 16), a("ex", 512 + i, 768, 16), c(CZ0), None, OP.mult)
         act(a("cd", C2 + 1024, C2 + 1536), a("ti"), AF.Relu, c(CU2))
         ts(c(CQ), c(CK), 512.0, 512.0, OP.mult, OP.add)
-        in_row[0] = 0
+        in_row[0] = SROW
         ts(a("cd", C2 + 1536, C2 + 2048), a("ti"), c(CQ), float(ZC), OP.is_ge, OP.mult)
         in_row[0] = None
         ts(c(CX), c(CK), 14.5, c(CM), OP.is_le, OP.mult)
-        ts(a("zm"), a("zo"), c(CX), None, OP.mult)
+        ts(a("wj"), c(CX), 3.0, -3.0, OP.add, OP.add)
+        ts(a("zm"), a("zo"), a("wj"), None, OP.mult)
+        ts(a("blkb"), a("mg"), c(CG), None, OP.is_equal)
+        ts(a("wneg"), a("io", 0, 32), 15.5, a("wj"), OP.is_ge, OP.mult)
+        aff(a("wneg"), a("wneg"), -1.0, 0.0)
+        mm(a("pm", 0, 1), a("blkb"), a("wj"))
+        ts(c(CN), a("pm", 0, 1), 0.5, TINY, OP.mult, OP.add)
 
     def last_constants():
         return [
-            lambda: ts(a("thn"), a("thn"), -6.5, None, OP.add),
-            lambda: ts(a("mq"), a("mq"), 0.25, None, OP.mult),
+            lambda: aff(a("thn"), a("thn"), 1.0, -6.5),
+            lambda: aff(a("mq"), a("mq"), 1.0 / 32, 0.0),
+            lambda: aff(a("t15"), a("mq"), 1.0, 15.0 / 8),
+            lambda: tt(a("stp", 16, 32), a("stp", 0, 16), a("dg", 0, 16), OP.mult),
+            lambda: total(a("stp", 32, 33), a("stp", 16, 32), 1.0),
+            lambda: ts(a("steps"), a("io", 0, 8, 4), a("stp", 32, 33), None, OP.add),
             lambda: ms(a("v4"), 0.0),
-            lambda: ts(a("zr"), a("zo"), row(0), None, OP.mult),
+            lambda: aff(a("zr"), a("zo"), row(0), 0.0),
             lambda: cp(a("ch", 0, 1), c(CL0)),
-            lambda: ts(a("blkb"), a("mg"), c(CG), None, OP.is_equal),
-            lambda: ts(a("q16"), a("io", 0, 36), 16.0, c(CJ), OP.mult, OP.add),
-            lambda: ts(a("mc", 0, 32), a("io", 0, 32), 0.0, c(CV), OP.mult, OP.add),
-            lambda: cp(a("q16", 32, 33), c(CJ)),
-            lambda: ts(a("s1", 1, 165, 5), a("q16", 0, 33), -1.0, None, OP.add),
-            lambda: ts(a("q32"), a("q16", 0, 32), -1.0 / NONE, None, OP.mult),
+            lambda: aff(a("q16"), a("io", 0, 36), 16.0, c(CJ)),
+            lambda: aff(a("mc", 0, 32), a("io", 0, 32), 0.0, c(CV)),
+            lambda: aff(a("q16", 32, 33), c(CJ), 1.0, 0.0),
+            lambda: aff(a("s1", 1, 165, 5), a("q16", 0, 33), 1.0, -1.0),
+            lambda: aff(a("q32"), a("q16", 0, 32), 1.0 / NONE, 0.0),
         ]
 
     def visit_constants():
         out = [
             lambda: ts(a("dg2"), a("i8"), c(CK), None, OP.is_equal),
-            lambda: ts(a("zk"), a("zo"), NONE, None, OP.mult),
-            lambda: ms(a("one"), 1.0),
-            lambda: ts(a("blkk"), a("mg"), c(CG), 1024.0, OP.is_equal, OP.mult),
-            lambda: ts(a("nidk"), a("io", 0, 128), c(CP), -1024.0, OP.is_equal, OP.mult),
+            lambda: aff(a("zk"), a("zo"), 2.0 ** 25, 0.0),
+            lambda: aff(a("k7"), a("io", 0, 48), 0.0, -7.5 * 2.0 ** 25),
+            lambda: ts(a("one"), a("io", 0, 112), 96.5, None, OP.is_le),
+            lambda: aff(a("rk"), a("i16"), -2.0 ** 20, 7 * 2.0 ** 20),
+            lambda: aff(c(CX), c(CP), 1.0, -1.0),
+            lambda: ts(a("nidn"), a("io", 0, 128), c(CX), -1024.0, OP.is_equal, OP.mult),
+            lambda: [aff(c(CD0 + h), c(CK), -512.0, -1536.0 - 16 * h) for h in range(3)],
+            lambda: [aff(c(CSP + h), c(CK), 1.0, 768.0 + 16 * h) for h in range(3)],
+            lambda: aff(c(CH2), c(CK), 2.0, 2.0),
+            lambda: aff(a("tm", 353, 354), row(15), -1.0, 1.0),
+            lambda: aff(c(CQ), c(CW), 1.0, 2048.0),
+            lambda: [ts(a("m1_%d" % r, 64, 66), a("io", 0, 2), 0.0, c(CQ), OP.mult, OP.add) for r in range(RO - 1)],
+            lambda: aff(a("blkk"), a("blkb"), 1024.0, 0.0),
+            lambda: aff(a("nidk"), a("idn"), -1024.0, 0.0),
             lambda: ts(a("g8"), a("io", 0, 8), 16.0, c(CG), OP.mult, OP.is_equal),
         ]
-        for h in (0, 1):
-            out.append(lambda h=h: ts(a("tm", 128 * h, 128 * h + 32), a("io", 0, 32), c(CH0 + h), 2.0 ** 23, OP.is_ge, OP.mult))
-        for h in (0, 1):
+        for h in range(3):
+            out.append(lambda h=h: ts(a("tm", 128 * h, 128 * h + 32), a("io", 0, 32), c((CH0, CH1, CH2)[h]), 2.0 ** 23, OP.is_ge, OP.mult))
+        for h in range(3):
             for n, s in ((1, 2.0 ** 19), (2, -2.0 ** 19)):
-                out.append(lambda h=h, n=n, s=s: ts(a("tm", 128 * h + 32 * n, 128 * h + 32 * n + 32), a("tm", 128 * h, 128 * h + 32), s, None, OP.add))
+                out.append(lambda h=h, n=n, s=s: aff(a("tm", 128 * h + 32 * n, 128 * h + 32 * n + 32), a("tm", 128 * h, 128 * h + 32), 1.0, s))
         return out
 
     def first_numbers():
@@ -533,8 +744,7 @@ def rank_program(g, core, T, topo):
         mm(a("pa"), a("dl"), a("olo"), False, True)
         act(a("oio"), a("pa"), AF.Copy)
         act(a("o0", B0, B0 + 512), a("oio", ind=a("seatu")), AF.Copy)
-        for o in ("o0", "o1"):
-            ts(a(o, 0, B0), a("io", 0, B0), -float(B0), row(0), OP.add, OP.mult)
+        ts(a("o0", 0, B0), a("io", 0, B0), -float(B0), row(0), OP.add, OP.mult)
 
     scalar_constants()
     BIG = float(1 << 20)
@@ -544,13 +754,15 @@ def rank_program(g, core, T, topo):
         host = (rank + 1 + t % (N - 1)) % N
         guest = (rank - 1 - t % (N - 1)) % N
         last = t == RO - 1
+        now[0], spare[0] = t, 0
         m1, l1, m2, l2, m3, l3 = ["%s_%d" % (n, t) for n in ("m1", "l1", "m2", "l2", "m3", "l3")]
-        for i in range(16):
-            mm(a("pk", 0, 47), sel("zw", i), a(xo, B0 + 32 * i, B0 + 32 * i + 47), i == 0, i == 15)
-        act(a("x2"), a(xo, ind=a("x2l", 0, 47)), AF.Copy)
-        ts(a("ksi", 0, 47), a("pk", 0, 47), BIG, None, OP.add)
-        conv(a("pk", 64, 96), "zw", xo, B0, B0 + 512)
-        ts(a("ks", 0, 47), a("ksi", 0, 47), 4095, None, OP.bitwise_and)
+        def sums(x):
+            mms([(a("pk", 0, 47), sel("zw", i), a(x, B0 + 32 * i, B0 + 32 * i + 47), i == 0, i == 15) for i in range(16)])
+            act(a("x2", 0, 752), a(x, ind=a("x2l", 0, 47)), AF.Copy)
+        if t == 0:
+            sums(xo)
+            ts(a("ksi", 0, 47), a("pk", 0, 47), BIG, None, OP.add)
+            ts(a("ks", 0, 47), a("ksi", 0, 47), 4095, None, OP.bitwise_and)
 
         at = lambda j: 64 * (j % 8) + 32 * (j // 8)
         def mult(j):
@@ -566,30 +778,47 @@ def rank_program(g, core, T, topo):
                 for j2 in (j, j + 8):
                     ts(a("off", at(j2), at(j2) + 32), a("prs", at(j2), at(j2) + 32), float(37 * j2 % 16), None, OP.add)
 
-        in_row[0] = t
+        in_row[0] = t if LROW else None
         for f, *js in ((mult, 0), (mult, 8), (mult, 1), (mult, 9), (mult, 2), (mult, 10), (shift, 0, 0), (mult, 7), (mult, 15),
                        (mult, 6), (add, 0), (mult, 14), (shift, 1, 2), (mult, 3), (mult, 11), (shift, 6, 7), (mult, 4), (add, 1),
                        (add, 2), (mult, 12), (mult, 5), (mult, 13), (add, 7), (add, 6)):
             f(*js)
         later_lists = [lambda: shift(3, 5), lambda: [add(j) for j in (3, 4, 5)]]
+        while t == 0 and later_lists:
+            later_lists.pop(0)()
         in_row[0] = None
         if t == 0:
             later_constants()
             for f in last_constants():
                 f()
+            in_row[0] = "first"
+            fill(a("pq", 96, 112), 0)
+            fill(a("cq", 0, 128), int(MAG))
+            iota(a("cq", 128, 256), [[0, 32], [1, 4]], 0)
+            fill(a("cq", 256, 384), -1024)
             send(a(xo, 0, B0 + 512), a("xg"), "a0", host, guest, "out0", [a("dicx", 0, 8192)])
-            dma("y", "ld5", [(a("dicy", 0, DW - 8), a("dicx", 8, DW))])
-            ms(a("dicy", DW - 8, DW), 0.0)
-            iota(a("ex", FILL, E2 + 32), [[0, E2 + 32 - FILL]], 0)
-            iota(a("ex", E2 + 128, RW), [[0, RW - E2 - 128]], 0)
-            iota(a("cd", E2, RW), [[0, RW - E2]], 0)
+            dma("y", "ld5", [(a("dicy", DY, DY + DW - 8), a("dicx", 8, DW))])
+            fill(a("cq", 256, 384, 4), 0)
+            for x in (7, 10, 11, 13, 14, 15):
+                fill(a("cq", 256 + x, 384, 16), -8192)
+            fill(a("sd"), 0)
+            iota(a("sd", 3, 128, 4), [[0, 8], [1, 4]], -int(MAG) - 3)
+            for x in (a("cd", 512, 1536), a("cd", C2 + 512, C2 + 1024),
+                      a("ex", FILL, E2 + 8 * ONE), a("ex", E2 + 128, RW), a("cd", E2, RW), a("dicy", 512, DY)):
+                fill(x, 0)
+            for x, v in ((a("dicy", DY + DW - 8, DY + DW), 0), (a("mc", 32, 64), 2048), (a("s0"), 1), (a("s0", 0, 165, 5), 0),
+                         (a("s0", 3, 165, 5), -1), (a("s0", 4, 165, 5), -1), (a("y2", 32, 33), 0), (a("lt", ZC, ZC + 16), 0),
+                         (a("x1", 0, B0), -1), (a("x1", B0 + 512, XW), -1), (a("xv", 512, 528), 0), (a("lt2", 512, 528), 0),
+                         (a("tm", 96, 384, 128), 1 << 22), (a("tm", 97, 256, 128), 1), (a("ypb", 0, B0), 0), (a("o1", 0, B0), 0)):
+                fill(x, v)
             iota(a("ohi"), [[16, 32], [0, 16]], 0)
             iota(a("olo"), [[0, 32], [1, 16]], 0)
+            in_row[0] = None
 
         def word(j, lo=0, hi=32):
             ws = (37 * j + 11 * t) // 16 * 16
             later = t > 0 and (37 * j + 11 * t) % 16 >= 8
-            return a("dicy" if later else "dicx", ws, ws + 8208, ind=a("off", at(j) + lo, at(j) + hi))
+            return a("dicy" if later else "dicx", ws + DY * later, ws + DY * later + 8208, ind=a("off", at(j) + lo, at(j) + hi))
 
         def ltj(j, lo=0, hi=512):
             w = 512 * ((14 - j) % 16)
@@ -599,137 +828,145 @@ def rank_program(g, core, T, topo):
             p0 = lambda lo=0, step=1: a("pq", 64 + lo, 96 + lo if step == 1 else 96, step)
             q = lambda n: a("tq", 8 * n, 8 * n + 8)
             ts(a("pq", 0, 96), a("pp", 0, 96), -1.0, 1024.0, OP.is_le, OP.mult)
-            yield
             tt(a("dq"), a("pq", 0, 64), a("pq", 32, 96), OP.subtract)
             tt(a("zq"), p0(), p0(1), OP.min)
-            tt(a("sq", 32, 64), p0(), a("st1"), OP.add)
-            yield
             tt(a("wq"), a("dq", 32, 64), a("zq"), OP.max)
             tt(q(0), a("dq", 0, 32, 4), p0(0, 4), OP.subtract)
             tt(q(1), a("dq", 32, 64, 4), p0(2, 4), OP.min)
-            yield
             tt(q(2), p0(0, 4), a("wq", 1, 32, 4), OP.min)
             tt(q(3), q(0), q(1), OP.max)
-            tt(a("sq", 64, 96), a("wq"), a("st2"), OP.add)
-            yield
             tt(q(4), q(2), q(3), OP.max)
-            yield
-            ts(a("sq", 96, 128, 4), q(4), MAG - 1021, None, OP.add)
-            yield
+            mms([(a("pp", 128, 256), a("idn"), a("cq", 128 * n, 128 * n + 128), n == 0, False) for n in range(3)])
+            for x, y in ((a("pp", 129, 256, 4), p0()), (a("pp", 130, 256, 4), a("wq")), (a("pp", 131, 256, 16), q(4))):
+                mm(x, a("idn"), y, False, False)
 
-        ev = []
         ns = NS0 if t == 0 else NS
-        tv, tsc = (0.0 if t == 0 else 1.7), 0.0
         half = ns - 1
-        hs = HS0 if t == 0 else HS
-        for j in range(ns, 15):
-            ev.append((tv, "vg", j)); tv += 0.72; ev.append((tv + LAGV, "cnt", j))
-            if j >= 15 - QAT:
-                ev.append((tv - 0.01, "quad", j)); tv += 0.12
-        ev.append((tv, "vh", half))
-        for j in range(ns + 1):
-            if j < ns:
-                ev.append((tsc, "sg", j)); tsc += 0.73; ev.append((tsc, "sub", j))
-            if j > 0:
-                ev.append((tsc + 0.001, "sign", j - 1)); tsc += 0.48; ev.append((tsc + LAGS, "cnt", j - 1))
-                if j == 3:
-                    ev.append((tsc + LAGS + 0.001, "quads", j))
+        hs = 512 - (HS0 if t == 0 else HS)
+        nv, nsc = SPLIT0 if t == 0 else SPLIT
+        up = lambda js, lo=CUT, hi=512: [(j, max(lo, CUT), hi) for j in js if max(lo, CUT) < hi]
+        low = lambda js, lo=0, hi=CUT: [(j, lo, min(hi, CUT)) for j in js if lo < min(hi, CUT)]
+        vs, ss = range(15 - nv, 15), range(half - nsc, half)
+        b15 = up([15], J15) + low([15], J15)
+        byv = [(j, 0, 512) for j in range(ns, 15 - nv)] + up(vs) + up([half], 0, hs) + low(vs) + low([half], 0, hs)
+        bys = [(j, 0, 512) for j in range(half - nsc)] + up(ss) + up([half], hs) + low(ss) + low([half], hs, 512)
+        ev = []
+        tv, tsc = (0.0 if t == 0 else 1.7), 0.0
+        for x in byv:
+            ev.append((tv, "vg", 0, x)); tv += 0.05 + (x[2] - x[1]) * 0.0013; ev.append((tv + LAGV, "cnt", 0, x))
+        for n, x in enumerate(bys + [None]):
+            if x:
+                ev.append((tsc, "sg", n, x)); tsc += 0.06 + (x[2] - x[1]) * 0.0013; ev.append((tsc, "sub", n, x))
+            if n > 0:
+                y = bys[n - 1]
+                ev.append((tsc + 0.001, "sign", n - 1, y)); tsc += 0.05 + (y[2] - y[1]) * 0.0008
+                ev.append((tsc + LAGS, "quads" if y[0] == 2 else "cnt", n - 1, y))
         ev.sort()
-        ncnt, opened = [0], False
-        qs = iter(())
-        for _, kind, j in ev:
-            n = hs if j == half else 512
-            d, bank = a("d%d" % (j % 3), 0, n), a(("pa", "pb", "ph", "pn", "pm")[j % 5], 0, n)
-            in_row[0] = t if kind in ("vg", "vh", "sg", "sign", "quad") else None
+        ncnt = {"pc": [0], "pk": [0]}
+        cnt = lambda lo, hi, step=1: a("pc" if lo >= CUT else "pk", lo, hi, step)
+
+        def exits(q):
+            w = 64 * (q + 1)
+            src = a("ex", w, w + 256, ind=a("r32", 4 * q, 4 * q + 4))
+            if q >= 2:
+                tt(a("ex", w - 64, w), src, a("ce", w - 192, w - 128), OP.min)
+            elif q < EXS:
+                in_row[0] = None
+                act(a("ex", w - 64, w), src, AF.Copy)
+            else:
+                cp(a("ex", w - 64, w), src)
+            in_row[0] = None
+            if q < 4:
+                act(a("eb", w - 64, w), src if q < EBS else a("ex", w - 64, w), AF.Copy)
+                mms([(a("pp", 0, 8 - ONE // 2), sel("zr", cc_), a("eb", 16 * cc_ + ONE, 16 * cc_ + 16, 2), cc_ == 15, cc_ == 0)
+                     for cc_ in range(4 * q + 3, 4 * q - 1, -1)])
+
+        def parts(lo, hi):
+            return [(x, y, c(CTH + ns - (x < hs))) for x, y in ((lo, min(hi, hs)), (max(lo, hs), hi)) if x < y]
+
+        def ends():
+            def words(n):
+                for j, lo, hi in b15[n:n + 1]:
+                    bank = a(("pa", "ph")[n], lo, hi)
+                    in_row[0] = t
+                    act(a("d2", lo, hi), word(j, lo // 16, hi // 16), AF.Copy)
+                    in_row[0] = None
+                    mm(bank, a("nid"), a("x2", 16 * j + lo, 16 * j + hi), True, False)
+                    mm(bank, a("idn"), a("d2", lo, hi), False, True)
+            words(0)
+            for e in (0, 1):
+                in_row[0] = t
+                for x, y, th in parts(0, CUT):
+                    act(a("pw", x + e, y, 2), cnt(x + e, y, 2), AF.Sign, th, -1.0)
+                in_row[0] = None
+                for x, y, th in parts(CUT, 512):
+                    ts(a("pw", x + e, y, 2), cnt(x + e, y, 2), th, 2.0, OP.is_le, OP.mult)
+            mm(a("pm", 0, 32), a("blkb"), a("wneg"), True, False)
+            mms([(a("pm", 0, 32), sel("zm", i), a("pw", i, 512, 16), False, i == 15)
+                 for i in list(range(0, 16, 2)) + list(range(1, 16, 2))])
+            words(1)
+            in_row[0] = t
+            for n, (j, lo, hi) in enumerate(b15):
+                act(ltj(j, lo, hi), a(("pa", "ph")[n], lo, hi), AF.Sign, -0.5)
+                if n == 0:
+                    act(a("ln2", 0, 32), a("pm", 0, 32), AF.Ln, c(CN), 0.5)
+            in_row[0] = None
+            mms([(a("pp", 128 + dl, 256, 4), a("nid"), a("ln2", dl, dl + 32), False, dl == 3) for dl in range(4)])
+            for lo in range(0, J15, 128):
+                tt(ltj(15, lo, lo + 128), word(15, lo // 16, lo // 16 + 8), a("x2", 240 + lo, 368 + lo), OP.is_gt)
+            conv(a("pb", 0, 32), "zo", "lt", 7680, 8192)
+            scan(a("sc"), a("pp", 128, 256), a("sd"), 0.0, OP.max, OP.add)
+            ts(a("r32"), a("sc", 3, 128, 4), 16.0, c(CK), OP.mult, OP.add)
+
+        for _, kind, n, (j, lo, hi) in ev:
+            d, bank = a("d%d" % (n % 3), lo, hi), a(("pa", "pb", "ph", "pn", "pm")[n % 5], lo, hi)
+            in_row[0] = t if kind in ("vg", "sg", "sign") else None
             if kind == "vg":
                 if later_lists:
+                    in_row[0] = t if LROW else None
                     later_lists.pop(0)()
-                tt(ltj(j), word(j), a("x2", 16 * j, 16 * j + 512), OP.is_gt)
-            elif kind == "vh":
-                for lo, hi in ((hs, 384), (384, 512)):
-                    if lo < hi:
-                        in_row[0] = t
-                        tt(ltj(j, lo, hi), word(j, lo // 16, hi // 16), a("x2", 16 * j + lo, 16 * j + hi), OP.is_gt)
-                        in_row[0] = None
-                        add_mm(a("pc", lo, hi), sel("zo", j), ltj(j, lo, hi), ncnt)
-            elif kind == "sg":
-                act(d, word(j, 0, n // 16), AF.Copy)
-            elif kind == "sub":
-                mm(bank, a("nid"), a("x2", 16 * j, 16 * j + n), True, False)
-                mm(bank, a("idn"), d, False, True)
-            elif kind == "sign" and j == half - 1:
-                for lo in (0, 256):
                     in_row[0] = t
-                    act(ltj(j, lo, lo + 256), a(bank[0], lo, lo + 256), AF.Sign, -0.5)
-                    in_row[0] = None
-                    add_mm(a("pc", lo, lo + 256), sel("zo", j), ltj(j, lo, lo + 256), ncnt)
-            elif kind == "cnt" and j == half - 1:
-                pass
+                tt(ltj(j, lo, hi), word(j, lo // 16, hi // 16), a("x2", 16 * j + lo, 16 * j + hi), OP.is_gt)
+            elif kind == "sg":
+                act(d, word(j, lo // 16, hi // 16), AF.Copy)
+            elif kind == "sub":
+                mm(bank, a("nid"), a("x2", 16 * j + lo, 16 * j + hi), True, False)
+                mm(bank, a("idn"), d, False, True)
             elif kind == "sign":
-                act(ltj(j, 0, n), bank, AF.Sign, -0.5)
-            elif kind == "quads":
-                conv(a("pp", 0, 96), "zo", "lt", 6144, 7680)
-                qs = quads()
-            elif kind == "quad":
-                next(qs, None)
-            elif j == half:
-                add_mm(a("pc", 0, hs), sel("zo", j), ltj(j, 0, hs), ncnt)
-            elif opened:
-                add_mm(a("pc"), sel("zo", j), ltj(j), ncnt)
+                act(ltj(j, lo, hi), bank, AF.Sign, -0.5)
             else:
-                mm(a("pc"), sel("zo", j), ltj(j), True, False)
-                opened = True
-        in_row[0] = t
-        for _ in range(QB):
-            next(qs, None)
-        for e in (0, 1):
-            for lo, hi in ((0, hs), (hs, 512)):
-                ts(a("pw%d" % e, lo // 2, hi // 2), a("pc", lo + e, hi, 2), c(CTH + ns - (lo > 0)), None, OP.is_le)
-        for _ in qs:
-            pass
-        act(a("d1"), word(15), AF.Copy)
+                for x, y in ((max(lo, CUT), hi), (lo, min(hi, CUT))):
+                    if x < y:
+                        b = cnt(x, y)[0]
+                        if ncnt[b] == [0]:
+                            mm(cnt(x, y), sel("zo", j), ltj(j, x, y), True, False)
+                            ncnt[b].append("open")
+                        else:
+                            add_mm(cnt(x, y), sel("zo", j), ltj(j, x, y), ncnt[b])
+                if kind == "quads":
+                    group[0] = "quads"
+                    conv(a("pp", 0, 96), "zo", "lt", 6144, 7680)
+                    quads()
+                    group[0] = None
         in_row[0] = None
-        mm(a("ph"), a("nid"), a("x2", 240, 752), True, False)
-        mm(a("ph"), a("idn"), a("d1"), False, True)
-        for i in list(range(0, 16, 2)) + list(range(1, 16, 2)):
-            mm(a("pm", 0, 32), sel("zm", i), a("pw%d" % (i % 2), i // 2, 256, 8), i == 0, i == 15)
-        LNB, LNS = math.exp(-15.2), math.exp(-0.2)
-        in_row[0] = t
-        act(ltj(15), a("ph"), AF.Sign, -0.5)
-        act(a("ln2", 0, 32), a("pm", 0, 32), AF.Ln, LNB, LNS)
-        halves = [(2 * u + h, 16 * h + 8 * u) for h in (0, 1) for u in (0, 1)]
-        for m, lo in halves:
-            act(a("lns", m, 32, 4), a("pm", lo, lo + 8), AF.Ln, LNB, LNS)
-        aff(a("rq", 0, 128, 4), a("ln2", 0, 32), -1.0, MAG)
-        for lo in range(0, 512, 128):
-            act(a("d0", lo, lo + 128), a("pc", lo, lo + 128), AF.Sign, c(CTH + ns - (lo >= hs)), -1.0)
-            in_row[0] = None
-        conv(a("pa", 0, 32), "zo", "lt", 7680, 8192)
-        for m, lo in halves:
-            act(a("f15", m, 32, 4), a("pa", lo, lo + 8), AF.Relu, 8.0, 8.0)
-        in_row[0] = None
-        for lo in (0, 256):
-            ts(a("pw", lo, lo + 256), a("d0", lo, lo + 256), 0.0, None, OP.max)
+        ends()
         for h in (0, 1):
-            for k in range(16):
-                w = 256 * h + 16 * k
-                mm(a("pn", 16 * h, 16 * h + 16), sel("zm", k), a("pw", w, w + 16), k == 0, k == 15)
-        for dl in range(1, 4):
-            tt(a("rq", dl, 128, 4), a("sq", 32 * dl, 32 * dl + 32), a("ln2", dl, dl + 32), OP.subtract)
-        scan(a("sc"), a("rq"), a("sd"), 0.0, OP.max, OP.add)
-        ts(a("r32"), a("sc", 3, 128, 4), 16.0, c(CK), OP.mult, OP.add)
-        ts(a("nsi"), a("lns"), -1.0, None, OP.mult)
-        ts(a("m15"), a("lns"), -14.6, 8.0, OP.is_le, OP.mult)
-        tt(a("a15"), a("lns"), a("thn"), OP.is_le)
-        tt(a("nm"), a("nsi"), a("mq"), OP.add)
-        tt(a("u15"), a("m15"), a("f15"), OP.min)
-        aff(a("n15"), a("a15"), 15.0, 0.0)
-        tt(a("n2"), a("n15"), a("nsi"), OP.max)
-        tt(a("nm2"), a("n2"), a("mq"), OP.add)
+            mms([(a("pm", 16 * h, 16 * h + 16), sel("zm", k), a("pw", 256 * h + 16 * k, 256 * h + 16 * k + 16), k == 0, k == 15)
+                 for k in range(16)])
+        group[0] = "codes"
+        for lo, hi, b in ((0, J15 // 16, 7.5), (J15 // 16, 32, -1.0)):
+            if lo < hi:
+                aff(a("th15", lo, hi), a("ln2", lo, hi), 32.0, b + 32.0 * 15.25)
+        aff(a("rq"), a("ln2", 0, 32), -1.0, MAG)
+        aff(a("n8"), a("rq"), 0.125, -MAG / 8)
+        tt(a("a15"), a("ln2", 0, 32), a("thn"), OP.is_le)
+        tt(a("nm"), a("n8"), a("mq"), OP.add)
+        tt(a("n15"), a("a15"), a("t15"), OP.mult)
+        tt(a("u15"), a("pb", 0, 32), a("th15"), OP.is_ge)
         tt(a("nq"), a("nm"), a("u15"), OP.add)
-        tt(a("nq2"), a("nm2"), a("u15"), OP.add)
-        ts(a("roff"), a("nq"), 64.0, c(CK), OP.mult, OP.add)
-        ts(a("rof2"), a("nq2"), 64.0, c(CK), OP.mult, OP.add)
+        ts(a("roff"), a("nq", ind=a("steps")), 512.0, c(CK), OP.mult, OP.add)
+        tt(a("nq2"), a("nq"), a("n15"), OP.max)
+        ts(a("rof2"), a("nq2", ind=a("steps")), 512.0, c(CK), OP.mult, OP.add)
 
         def codes(k):
             w = 64 * (k + 1)
@@ -739,78 +976,87 @@ def rank_program(g, core, T, topo):
             w = C2 + 64 * (k + 1)
             act(a("cd", w - 64, w), a("cd", w, w + 1536, ind=a("rof2", 4 * k, 4 * k + 4)), AF.Copy)
 
-        def exits(q):
-            w = 64 * (q + 1)
-            src = a("ex", w, w + 256, ind=a("r32", 4 * q, 4 * q + 4))
-            if q >= 2:
-                tt(a("ex", w - 64, w), src, a("ce", w - 192, w - 128), OP.min)
-            else:
-                cp(a("ex", w - 64, w), src)
-            act(a("eb", w - 64, w), a("eb", w, w + 256, ind=a("r32", 4 * q, 4 * q + 4)), AF.Copy)
-            if q < 4:
-                for cc_ in range(4 * q + 3, 4 * q - 1, -1):
-                    mm(a("pp", 0, 6), sel("zr", cc_), a("eb", 16 * cc_ + 4, 16 * cc_ + 16, 2), cc_ == 15, cc_ == 0)
-
         def chain(m):
             cp(a("ch", 2 * m + 1, 2 * m + 17), a("ex", ind=a("ch", 2 * m, 2 * m + 1)))
 
+        def single(s):
+            cp(a("ch", ONE, ONE + 16) if s == ONE - 1 else a("c1", 16 * s, 16 * s + 16),
+               a("ex", 0, E2, ind=a("c1", 16 * s - 16, 16 * s - 15)) if s else a("ex", 64, 320, ind=a("r32", 0, 1)))
+
+        group[0] = "steps"
         for k in range(7, -1, -1):
-            exits(k)
-        for k in range(7, -1, -1):
-            codes(k)
             codes2(k)
-        cp(a("le2"), a("pp", 0, 6))
-        cp(a("ex", E2 + 32, E2 + 128), a("ex", 0, 768, ind=a("le2")))
-        for s in range(4):
-            cp(a("ch", 4, 20) if s == 3 else a("c1", 16 * s, 16 * s + 16),
-               a("ex", 0, E2, ind=a("c1", 16 * s - 16, 16 * s - 15) if s else a("ch", 0, 1)))
-        cp(a("ch", 1, 4), a("c1", 0, 48, 16))
-        for m in range(2, 8):
+        group[0] = None
+        for n in range(8 + max(LAG, ONE)):
+            in_row[0] = ("steps", t)
+            if n < 8:
+                exits(7 - n)
+            in_row[0] = ("steps", t)
+            if n >= 7:
+                single(n - 7) if n - 7 < ONE else None
+            if 0 <= n - LAG < 8:
+                codes(7 - n + LAG)
+        in_row[0] = None
+        cp(a("le2", 0, 8 - ONE // 2), a("pp", 0, 8 - ONE // 2))
+        act(a("ex", E2 + 8 * ONE, E2 + 128), a("ex", 0, 768, ind=a("le2", 0, 8 - ONE // 2)), AF.Copy)
+        cp(a("ch", 1, ONE), a("c1", 0, 16 * ONE - 16, 16))
+        for m in range(ONE // 2, 8):
             chain(m)
         for h in (0, 1):
-            act(a("lnn", h, 32, 2), a("pn", 16 * h, 16 * h + 16), AF.Ln, LNB, LNS)
+            group[0] = "natural"
+            act(a("lnn", h, 32, 2), a("pm", 16 * h, 16 * h + 16), AF.Ln, TINY if h else c(CN), 0.5)
         aff(a("nnm"), a("lnn"), -1.0, MAG)
-        aff(a("s0", 1, 160, 5), a("nnm"), 1.0, 1.0 - MAG)
-        aff(a("s0", 161, 162), a("nnm", 0, 1), 1.0, 1.0 - MAG)
-        ts(a("kni"), a("pk", 64, 96), BIG, None, OP.add)
+        aff(a("s0", 1, 160, 5), a("nnm"), 1.0, -1.0 - MAG)
+        aff(a("s0", 161, 162), a("nnm", 0, 1), 1.0, -1.0 - MAG)
+        group[0] = "keys"
+        conv(a("pn", 0, 32), "zw", xo, B0, B0 + 512)
+        ts(a("kni"), a("pn", 0, 32), BIG, None, OP.add)
         ts(a("kn"), a("kni"), 4095, None, OP.bitwise_and)
         tt(a("ksq"), a("kn"), a("kn"), OP.mult)
         ts(a("v0"), a("ksq"), 5, 511, OP.logical_shift_right, OP.bitwise_and)
-        for lo in (0, 3):
-            ts(a("v4", lo, lo + 64, 2), a("v0"), float(B0), None, OP.add)
-            ts(a("v4", 68 + lo, 68 + lo + 64, 2), a("kn"), -2048.0, None, OP.add)
+        for lo in (11, 23):
+            ts(a("v4", lo, lo + 249, 8), a("v0"), float(B0), None, OP.add)
+            ts(a("v4", 272 + lo, 272 + lo + 249, 8), a("kn"), -2048.0, None, OP.add)
+        group[0] = None
         if t == 0:
-            ts(a("dh"), a("idn"), row(0), None, OP.mult)
-            ts(a("dl"), a("idn"), row(1), None, OP.mult)
+            aff(a("dh"), a("idn"), row(0), 0.0)
+            aff(a("dl"), a("idn"), row(1), 0.0)
             for f in visit_constants():
                 f()
         mm(a("ph", 0, 32), a("idn"), a("mc", 0, 32), True, False)
         mm(a("pm", 0, 32), a("idn"), a("mc", 32, 64), True, False)
-        for lo, hi in ((0, 8), (8, 12), (12, 17)):
+        for lo, hi in WS:
             act(a("w", 16 * lo, 16 * hi), a("cd", ind=a("ch", lo, hi)), AF.Copy)
-        for lo, hi in ((0, 8), (8, 14)):
-            act(a("wa", 16 * lo, 16 * hi), a("cd", ind=a("ch", lo, hi)), AF.Relu, -(ZC + 1.0))
-        ts(a("wa", 224, 272), a("cd", ind=a("ch", 14, 17)), ZC + 1.5, None, OP.is_ge)
+        x = 16 * WS[-1][0]
+        act(a("wa", 11, x, 4), a("w", 11, x, 4), AF.Relu, -(ZC + 1.0))
+        for lo, hi in ((256, 512), (128, 256), (64, 128), (0, 64)):
+            act(a("dicy", lo, hi), a("cd", lo, hi), AF.Relu, -(ZC + 1.0))
+        for n in (0, 1):
+            w = 272 * n
+            tt(a("ap4", w + 11, w + x, 4), a("wa", 11, x, 4), a("v4", w + 11, w + x, 4), OP.mult)
+            in_row[0] = ("steps", t)
+            tt(a("ap4", w + x, w + 272), a("dicy", 0, RW, ind=a("ch", x // 16, 17)), a("v4", w + x, w + 272), OP.mult)
+            in_row[0] = None
         tt(a("y1", 0, 32), a("w", 11, 267, 8), a("w", 23, 272, 8), OP.max)
         tt(a("y1", 32, 33), a("w", 11, 12), a("w", 23, 24), OP.max)
         tt(a("y2", 0, 32), a("w", 4, 260, 8), a("w", 14, 270, 8), OP.max)
-        for n in (0, 1):
-            tt(a("ap4", 68 * n, 68 * n + 66), a("wa", 11, 272, 4), a("v4", 68 * n, 68 * n + 66), OP.mult)
         y1, y2 = a("y1", 0, 33), a("y2", 0, 33)
         tt(a("yp", 0, 33), y1, y2, OP.max)
         cp(a("idx2", 0, 33), a("yp", 0, 33))
         for n, bank in enumerate(("ph", "pm")):
-            for lo in (0, 3):
-                mm(a(bank, 0, 32), a("blkb"), a("ap4", 68 * n + lo, 68 * n + lo + 63, 2), False, lo == 3)
+            for lo in (11, 23):
+                mm(a(bank, 0, 32), a("blkb"), a("ap4", 272 * n + lo, 272 * n + lo + 249, 8), False, lo == 23)
             cp(a(m1, 32 * n, 32 * n + 32), a(bank, 0, 32))
-            send(a(m1, 32 * n, 32 * n + 32), a(l1, 32 * n, 32 * n + 32), "a%d_%d" % (1 + 3 * n, t), host, guest)
-        act(a("s1", 0, 165, 5), y1, AF.Relu, -float(ZC))
-        ts(a("s1", 2, 165, 5), y1, float(ZC), None, OP.is_equal)
-        ts(a("s1", 3, 165, 5), y2, float(ZC), None, OP.is_equal)
-        ts(a("s1", 4, 165, 5), y1, ZC + 1.5, -NONE, OP.is_ge, OP.mult)
+            w = 32 * n + 32 + 2 * (n and not last)
+            send(a(m1, 32 * n, w), a(l1, 32 * n, w), "a%d_%d" % (1 + 3 * n, t), host, guest)
+        for n, (y, low_, f) in enumerate(((y1, ZC, 1.0), None or (None,) * 3, (y1, ZC - 1, 1.0), (y1, ZC + 1, NONE), (y2, ZC - 1, 1.0))):
+            if n in S1V:
+                ts(a("s1", n, 165, 5), y, -float(low_), 0.0, OP.add, OP.max)
+            elif y:
+                act(a("s1", n, 165, 5), y, AF.Relu, -f * low_, f)
         scan(a("srcf", 0, 165), a("s0", 0, 165), a("s1", 0, 165), 0.0, OP.mult, OP.add)
         cp(a("src", 0, 33), a("srcf", 4, 165, 5))
-        aw = a("s1", 4, 160, 5)
+        aw = a("s1", 3, 160, 5)
         tt(a("awq"), aw, a("q32"), OP.mult)
         mm(a("pp", 64, 96), a("blkb"), a("awq"))
         tt(a("dm"), a("pp", 64, 96), a("dg2"), OP.mult)
@@ -832,12 +1078,16 @@ def rank_program(g, core, T, topo):
         if not last:
             cp(a("xv", 0, 256), a(xn, ind=a(l1, 0, 16)))
         for h in (0, 1):
-            red(a("avf", h, h + 1), a("dm", h, 32, 2), OP.max)
+            total(a("avf", h, h + 1), a("dm", h, 32, 2), 1.0)
         in_row[0] = None
         for h in (0, 1):
             ts(a("avl", h, h + 1), a("avf", h, h + 1), c(CH[h]), None, OP.max)
         if not last:
-            cp(a("avg", 0, 2), a("avl"))
+            tt(a("dm3", 0, 15), a("pp", 66, 96, 2), a("dg", 0, 15), OP.mult)
+            total(a("avf", 2, 3), a("dm3", 0, 15), 1.0)
+            for h in range(3):
+                ts(a("am", 16 * h, 16 * h + 16), a("io", 16 * h, 16 * h + 16), c(CS), a("avf", h, h + 1), OP.add, OP.is_equal)
+                aff(a("avs", h, h + 1), a("avf", h, h + 1), 16.0, c(CD0 + h))
         act(a(m2), a(xo, ind=a("avl")), AF.Copy)
         if t == 0:
             send(a("avl"), a("lav"), "a2_0", host, guest, "out1")
@@ -854,16 +1104,12 @@ def rank_program(g, core, T, topo):
         ts(a("khi"), a("ph", 0, 32), BIG, None, OP.add)
         if last:
             ts(a("olu"), a("pn", 0, 32), float(B0), None, OP.add)
-            aff(a("olf"), a("pn", 0, 32), -1.0 / NONE, -B0 / NONE)
+            aff(a("olf"), a("pn", 0, 32), 1.0 / NONE, B0 / NONE)
             tt(a("awo"), aw, a("olf"), OP.mult)
             mm(a("pp", 64, 96), a("blkb"), a("awo"))
             tt(a("dm"), a("pp", 64, 96), a("dg2"), OP.mult)
             for h in (0, 1):
                 red(a("avp", h, h + 1), a("dm", h, 32, 2), OP.max)
-            in_row[0] = "lay"
-            for h in (0, 1):
-                ts(a("avg", h, h + 1), a("avp", h, h + 1), c(CH[h]), None, OP.max)
-            in_row[0] = None
             mm(a("pa", np_=8), a("g8"), a(on, B0, B0 + 512))
             act(a("ysb", np_=8), a("pa", np_=8), AF.Copy)
             dma("s", "ld6", [(T.yseat[:], a("ysb", np_=8))])
@@ -875,16 +1121,27 @@ def rank_program(g, core, T, topo):
         tt(a("vd"), a("vb"), a("dg2"), OP.mult)
         ts(a("kh"), a("khi"), 4095, None, OP.bitwise_and)
         for h in (0, 1):
-            red(a("vh", h, h + 1), a("vd", h, 32, 2), OP.max)
+            total(a("vh", h, h + 1), a("vd", h, 32, 2), 1.0)
         tt(a("hp"), a("kh"), a("sf"), OP.mult)
         for h in (0, 1):
             aff(a("vt", 16 * h, 16 * h + 16), a("io", 0, 16), -1.0, a("vh", h, h + 1))
         ts(a("hs"), a("hp"), 5, 8191, OP.logical_shift_right, OP.bitwise_and)
         ts(a("hw"), a("hs"), c(CT0 + t), None, OP.add)
-        mm(a("pm", 0, 32), a("idn"), a("k7"), True, False)
-        two = ("pb", "pc")
-        for h in (0, 1):
-            mm(a(two[h], 0, 97), a("idn"), a("tm", 128 * h, 128 * h + 97), True, False)
+        nh = 2 if last else 3
+        mm(a("pm", 0, 16 * nh), a("idn"), a("k7", 0, 16 * nh), True, False)
+        two = ("pb", "pc", "pa")[:nh]
+        for h in range(nh):
+            mm(a(two[h], 0, 98), a("idn"), a("tm", 128 * h, 128 * h + 98), True, False)
+        if not last:
+            ts(a("cwg"), a(l1, 64, 65), -2048.0, None, OP.add)
+            ts(a("zg"), a("zo"), a("cwg"), None, OP.mult)
+            mm(a("pn", 0, 48), a("idn"), a("rk"), True, False)
+            mms([(a("pn", 0, 48), sel("zg", i), a("xv", 32 * i, 32 * i + 48), False, i == 15) for i in range(16)])
+            tt(a("vd2", 0, 32), a("sf"), a("dg2"), OP.mult)
+            tt(a("vd2", 32, 47), a("sf", 2, 32, 2), a("dg", 0, 15), OP.mult)
+            for h, x in enumerate((a("vd2", 0, 32, 2), a("vd2", 1, 32, 2), a("vd2", 32, 47))):
+                total(a("nsh", h, h + 1), x, -1.0)
+                aff(a("vt2", 16 * h, 16 * h + 16), a("pn", 16 * h, 16 * h + 16), 1.0, a("nsh", h, h + 1))
         act(a("d2", 16 * HV, 512), a("dicx", ind=a("hw", HV, 32)), AF.Copy)
         for lo, hi in ((0, HV // 2), (HV // 2, HV)):
             tt(a("lt2", 16 * lo, 16 * hi), a("dicx", ind=a("hw", lo, hi)), a("xv", 16 * lo, 16 * hi), OP.is_gt)
@@ -892,38 +1149,53 @@ def rank_program(g, core, T, topo):
         tt(a("lt2", 16 * HV, 512), a("d2", 16 * HV, 512), a("xv", 16 * HV, 512), OP.is_gt)
         if last:
             lay(*LAY[0])
-        for i in range(16):
-            mm(a("pm", 0, 32), sel("zk", i), a("lt2", 32 * i, 32 * i + 32), False, i == 15)
+        for lo, hi in ((0, HV // 4), (HV // 4, HV // 2), (HV // 2, 16)):
+            lo, hi = [x - (0 < x < 16 and not last) for x in (lo, hi)]
+            mms([(a("pm", 0, 16 * nh), sel("zk", i), a("lt2", 32 * i, 32 * i + 16 * nh), False, i == 15) for i in range(lo, hi)])
         for h in (0, 1):
             scan(a("cs", 16 * h, 16 * h + 16), a("pm", 16 * h, 16 * h + 16), a("vt", 16 * h, 16 * h + 16), NONE, OP.min, OP.max)
         cl = [a("cs", 15, 16), a("cs", 31, 32)]
         for h in (0, 1):
             ts(a("exd", h, 96, 2), a("dg"), cl[h], None, OP.mult)
         for h in (0, 1):
-            ts(a("exo", 112 * h, 112 * h + 97), a("one", 0, 97), cl[h], None, OP.mult)
+            ts(a("exo", 112 * h, 112 * h + 98), a("one", 0, 98), cl[h], None, OP.mult)
         in_row[0] = None
-        for h in (0, 1):
+        for h in range(nh):
             mm(a(two[h], 0, 96), a("blkk"), a("exd"), False, False)
-            mm(a(two[h], 0, 97), a("nidk"), a("exo", 112 * h, 112 * h + 97), False, True)
+            mm(a(two[h], 0, 98), a("nidn" if h == 2 else "nidk"), a("exo", 112 * (h % 2), 112 * (h % 2) + 98), False, True)
         ts(a("tgt"), a("cs", 15, 32, 16), XW - 1.0, None, OP.min)
         act(a(m3, 0, 32), a(xn, ind=a("tgt")), AF.Copy)
-        for h in (0, 1):
-            red(a(m3, 32 + h, 33 + h), a(two[h], 0, 97), OP.min, apply_absolute_value=True)
-        send(a(m3), a(l3), "a3_%d" % t, guest, host)
-        for h in (0, 1):
-            ts(a("tg2" if last else "tgf", h, h + 1), a(m3, 32 + h, 33 + h), c(CH[h]), cl[h], OP.add, OP.min)
         if not last:
-            ts(a("tgw", 0, 2), a("tgf", 0, 2), B0 + 511.5, -512.0, OP.is_ge, OP.mult)
-            tt(a("tgc", 0, 2), a("tgf", 0, 2), a("tgw", 0, 2), OP.add)
-            cp(a("tg2"), a("tgc", 0, 2))
-        else:
+            scan(a("dsc"), a("pm", 0, 48), a("vt2"), 0.0, OP.min, OP.max)
+            act(a(m3, 35, 38), a("dsc", 15, 48, 16), AF.Copy)
+            ts(a("tgw", 0, 2), a("cs", 15, 32, 16), B0 + 511.5, -512.0, OP.is_ge, OP.mult)
+            tt(a("tgc", 0, 2), a("cs", 15, 32, 16), a("tgw", 0, 2), OP.add)
+            cl = [a("tgc", 0, 1), a("tgc", 1, 2)]
+        for h in range(nh):
+            red(a(m3, 32 + h, 33 + h), a(two[h], 0, 98), OP.min, apply_absolute_value=True)
+        send(a(m3, 0, 34 if last else 38), a(l3, 0, 34 if last else 38), "a3_%d" % t, guest, host)
+        for h in (0, 1):
+            ts(a("tg2", h, h + 1), a(m3, 32 + h, 33 + h), cl[h], c(CH[h]), OP.mult, OP.max)
+        if last:
             act(a(on, B0 + 512, XW), a(on, B0, B0 + 16), AF.Copy)
             for x in LAY[1:]:
                 lay(*x)
-        for h in (0, 1):
-            ts(a("avo", h, h + 1), a(l3, 32 + h, 33 + h), c(CH[h]), a("avg", h, h + 1), OP.add, OP.min)
-        if not last:
+        else:
             cp(a(xn, ind=a("tg2")), a(l2))
+            sums(xn)
+            in_row[0] = t + 1 if LROW else None
+            for h in range(3):
+                ts(a("bb", 16 * h, 16 * h + 16), a("am", 16 * h, 16 * h + 16), a(l3, 32 + h, 33 + h), a(l3, 35 + h, 36 + h), OP.mult, OP.mult)
+            for h in range(3):
+                ts(a("av2", h, h + 1), a(l3, 32 + h, 33 + h), a("avs", h, h + 1), c(CSP + h), OP.mult, OP.add)
+            tt(a("ksi", 0, 47), a("pk", 0, 47), a("bb", 0, 47), OP.add)
+            cp(a("x2", ind=a("av2", 0, 2)), a(l3, 0, 32))
+            ts(a("ks", 0, 47), a("ksi", 0, 47), 4095, None, OP.bitwise_and)
+            cp(a("x2", ind=a("av2", 2, 3)), a(l3, 1, 17))
+            in_row[0] = None
+        for h in (0, 1):
+            ts(a("avo", h, h + 1), a(l3, 32 + h, 33 + h), a("avp" if last else "avf", h, h + 1), c(CH[h]), OP.mult, OP.max)
+        if not last:
             cp(a(xn, ind=a("avo")), a(l3, 0, 32))
         else:
             act(a("oc"), a(on, ind=a("tg2")), AF.Copy)

import math
import numpy as np
from concourse.mybir import AluOpType as OP, AxisListType as AX, ActivationFunctionType as AF

RO = 4
NS = 7
NS0 = 7
B0 = 48
LAGV, LAGS = 0.2, 0.0
HS, HS0 = 256, 128
CUT = 256
S1V = (2,)
ONE = 4
J15 = 256
SPLIT, SPLIT0 = (1, 0), (1, 0)
XW = 576
DW = 8800
DY = 1536
WS = ((0, 8), (8, 12), (12, 17))
RW = 4240
E2, C2 = 4096, 2048
ZC = 8192
WDT = "float16"

F, I, U, H = "float32", "int32", "uint16", "bfloat16"
SB = {
    "dicx": (DW, H), "dicy": (DY + DW, H), "pupb": (512, H), "seatb": (32, I), "wtb": (4, I), "seatu": (32, U),
    "x0": (XW, H), "x1": (XW, H), "o0": (XW, H), "o1": (XW, H), "oc": (32, H), "ocu": (2, U), "oio": (512, H), "x2": (816, H), "x2l": (48, U),
    "lt": (ZC + 16, H), "d0": (512, H), "d1": (512, H), "d2": (512, H),
    "ksi": (48, I), "ks": (48, I), "prod": (512, I), "prs": (512, I), "off": (512, U),
    "wj": (1, H), "wneg": (32, H), "th15": (32, F), "n8": (32, F), "t15": (32, F), "stp": (36, F), "steps": (2, U),
    "pw": (512, H), "lns": (32, F), "roff": (32, U), "rof2": (32, U), "lnn": (32, F), "nni": (32, I),
    "r32": (32, U), "ln2": (48, H),
    "pq": (112, H), "dq": (64, H), "zq": (32, H), "wq": (32, H), "tq": (48, H), "cq": (384, H), "da": (256, H),
    "rq": (32, F), "sc": (128, F), "sd": (128, F), "n15": (32, F), "a15": (32, F), "n2": (32, F), "thn": (32, F),
    "ex": (RW, F), "eb": (768, H), "cd": (RW, F), "cc": (512, F), "ce": (384, F), "mq": (32, F), "nm2": (32, F), "nq": (32, F), "nq2": (32, F),
    "f15": (32, F), "m15": (32, F), "u15": (32, F), "nm": (32, F), "nnm": (32, F), "q32": (32, F), "s0": (168, F), "s1": (168, F),
    "y1": (36, F), "y2": (36, F), "wa": (272, H), "v4": (544, WDT), "ap4": (544, WDT), "le2": (6, U), "ch": (40, U), "c1": (112, U), "w": (272, F),
    "mc": (64, H), "kni": (32, I), "kn": (32, I), "kn1": (32, F), "ksq": (32, I), "v0": (32, I), "v1": (32, F),
    "nt": (32, F), "nu": (32, F), "nl": (36, F), "aw": (32, F), "st": (36, F), "apk": (64, WDT), "awq": (32, WDT),
    "yp": (36, F), "idx2": (34, U), "uu": (36, F), "e1": (36, F), "e2": (36, F),
    "srcf": (168, F), "src": (34, U), "srof": (32, F), "sro": (32, U), "g2": (528, H),
    "dm": (32, F), "avf": (4, F), "avg": (4, F), "avp": (4, F), "avl": (2, U), "avo": (2, U), "olf": (32, F), "olu": (32, U), "awo": (32, WDT),
    "xv": (528, H), "sf": (32, F), "vb": (32, F), "vd": (32, F), "vh": (4, F), "vt": (32, F), "cs": (32, F),
    "khi": (32, I), "kh": (32, I), "hp": (32, I), "hs": (32, I), "hw": (32, U), "lt2": (528, H),
    "exd": (96, WDT), "exo": (224, WDT), "cf": (4, F), "tgt": (2, U), "tgf": (4, F), "tgw": (4, F), "tgc": (4, F), "tg2": (2, U),
    "xg": (B0 + 512, H), "lav": (2, U), "ypb": (B0 + 512, H), "ysb": (512, F),
    "zo": (144, H), "zw": (144, WDT), "zm": (144, H), "zr": (144, H), "zk": (144, H), "idn": (128, H), "nid": (128, H),
    "nidk": (128, H), "blkb": (128, H), "blkk": (128, H), "g8": (8, H), "dh": (128, H), "dl": (128, H), "ohi": (512, H), "olo": (512, H),
    "io": (144, F), "mg": (128, F), "i16": (48, F), "i8": (32, F), "b32": (32, F),
    "ie": (256, H), "ia": (256, H), "ic": (384, F), "t1": (208, F), "t4": (96, F), "ti": (512, F),
    "col": (64, F), "ci": (8, I), "q16": (36, F), "qm1": (36, F), "dg": (48, F), "dg2": (32, F), "one": (112, WDT),
    "tm": (384, H), "k7": (48, H), "rk": (48, H), "nidn": (128, H), "zg": (144, WDT), "cwg": (1, F), "vd2": (48, F), "nsh": (4, F),
    "vt2": (48, F), "dsc": (48, F), "tot": (64, F), "dm3": (16, F), "am": (48, F), "avs": (4, F), "bb": (48, F), "av2": (4, U),
}
for _t in range(RO):
    SB["m1_%d" % _t] = (66, U); SB["l1_%d" % _t] = (66, U)
    for _n in ("m2", "l2", "m3", "l3"):
        SB["%s_%d" % (_n, _t)] = (32, H) if _n[1] == "2" else (34, H) if _t == RO - 1 else (38, F)
PS = ["pc", "pa", "pb", "pk", "pm", "pn", "pp", "ph"]
SCRATCH, HOME = {}, {}
INSIDE, FILL = {}, 768
for _k in ("cc", "ti", "ce", "ic", "t1", "io", "mg", "b32", "sd", "t4", "i16", "dg", "thn", "mq", "t15", "i8"):
    INSIDE[_k] = FILL
    FILL += SB[_k][0]
for _k, (_w, _d) in SB.items():
    if _k in INSIDE:
        continue
    if _w > 80:
        SCRATCH["b_" + _k] = ("sbuf", [128, _w], _d)
        HOME[_k] = (_k, 0)
    else:
        _o = SCRATCH.get("b_pool" + _d, (0, [128, 0]))[1][1]
        SCRATCH["b_pool" + _d] = ("sbuf", [128, _o + (_w + 15) // 16 * 16], _d)
        HOME[_k] = ("pool" + _d, _o)
SCRATCH.update({("b_" + k): ("psum", [128, 512], F) for k in PS})
SEMAPHORES = ["qv", "qs", "qp", "qg", "sent", "a0", "out0", "out1"] + ["ld%d" % i for i in range(8)] + \
             ["a%d_%d" % (m, t) for m in (1, 2, 3, 4) for t in range(RO)]
(CP, CK, CG, CK16, CG15, CW, CM, CJ, CX, CS, CQ, CV, CZ0, CA, CB, CD, CL0, C34, C67, CEF, C16, C24, CE, CY,
 CH0, CH1, CT0) = range(27)
CZ1 = CT0 + 4
CU, CU2, CK32 = CZ1 + 3, CZ1 + 4, CZ1 + 5
CN = CZ1 + 6
CTH = CZ1 + 7 - 5
CD0, CSP, CH2, CR = 42, 45, 48, 49
TINY = 2.0 ** -22
MAG = 1.5 * 2.0 ** 23
CH = (CK16, CK32)
NONE = 4096.0
PACES = [{"cycle": c_, "gather": c_ * g_, "scatter": c_ * 3.8, "column": c_ * p_, "wait": w_, "hop": h_, "none": 0.0}
         for c_, g_, p_, w_, h_ in ((0.95e-3, 1.56, 0.52, 0.17, 1.2), (1.15e-3, 1.9, 0.55, 0.1, 0.7), (0.9e-3, 1.2, 0.6, 0.22, 1.6),
                                    (1.2e-3, 1.3, 0.6, 0.15, 1.2), (0.9e-3, 1.9, 0.5, 0.2, 0.9))]
ROWS = 0.7
STRETCH, SWEEPS, TRIES, NEAR = 160, 12, 1200, 0.15
HEAT = 0.0003
LEAD, TURNS = 5, 3
KEPT = ("loads", "first", 0, 1, 2, 3) + tuple(("steps", t) for t in range(RO))
FIRM = ("loads", "first")
LAG = 3
LROW = 0
SROW = None
EXS, EBS = 0, 1
SOON = {"codes": 1.0, "steps": 1.0}
EARLY = 24
HV = 20
LAY = ((0, 10), (10, 14), (14, 32))
UNSURE = 0.07
ORDER = []
LOADED = {"ld3": 2.6, "ld4": 6.5, "ld5": 7.0}
for _p, _f in zip(PACES, (1.0, 1.15, 0.85, 1.3, 0.9)):
    _p.update({k: v * _f for k, v in LOADED.items()})


def a(name, lo=0, hi=None, step=1, ind=None, np_=128):
    if hi is None:
        hi = SB[name][0] if name in SB else 512
    if name in INSIDE:
        return ("ex", lo + INSIDE[name], hi + INSIDE[name], step, ind, np_)
    return (name, lo, hi, step, ind, np_)


def c(j):
    return a("col", j, j + 1)


def bits(x):
    lo, hi, step = x[1], x[2], x[3]
    if step == 1:
        return ((1 << (hi - lo)) - 1) << lo
    return sum(1 << j for j in range(lo, hi, step))


def uses(rd, wr):
    use = []
    for w, xs in ((False, rd), (True, wr)):
        for x in xs:
            if isinstance(x, tuple):
                use.append((x[0], bits(x), w))
                if x[4] is not None:
                    use.append((x[4][0], bits(x[4]), False))
    return use


def cost(q, rd, wr):
    xs = [x for x in wr + rd if isinstance(x, tuple)]
    n = len(range(*xs[0][1:4]))
    if q == "p":
        return ("column", 0.0, max(64, n))
    if q == "g":
        return ("cycle", 0.13, 2 * n)
    for x in xs:
        if x[4] is not None:
            return ("scatter" if x is xs[0] else "gather", 0.06 if q == "v" else 0.075, 16 * len(range(*x[4][1:4])))
    wide = [x for x in xs if len(range(*x[1:4])) > 1]
    n = max(len(range(*x[1:4])) for x in xs)
    if q == "v" and all(x[0] in SB and SB[x[0]][1] in (H, U, WDT) for x in wide):
        n = n / 2
    if q == "v" and len(rd) == 2 and len(wide) == 3 and all(x[0] in SB for x in wide[1:]):
        n = 2 * n
    return ("cycle", 0.0, max(64, n))


def lay_out(calls):
    n = len(calls)
    queue = [x[0] for x in calls]
    above = [0] * n
    for i, x in enumerate(calls):
        far = 0
        for m, w in x[3]:
            far |= above[m] if w != "hint" else 0
        x[3][:] = [(m, w) for m, w in x[3] if not far >> m & 1 or calls[m][2] != 0.0]
        above[i] = far | sum(1 << m for m, w in x[3] if w != "hint")

    def times(p, hints=True):
        busy = [x[1][1] + x[1][2] * p[x[1][0]] for x in calls]
        late = [p.get(x[2], x[2]) for x in calls]
        before = [[(m, busy[m] + (0.0 if w in ("row", "hint") else late[m] + p[w])) for m, w in x[3] if hints or w != "hint"]
                  for x in calls]
        after = [[] for x in calls]
        for i in range(n):
            for m, w in before[i]:
                after[m].append((i, w - busy[m] + busy[i]))
        return busy, before, after

    def fill(order, busy, edges):
        at, used = [0.0] * n, {}
        for i in order:
            t = max([at[m] + w for m, w in edges[i]] + [0.0])
            xs = used.setdefault(queue[i], [])
            k = len(xs)
            while k > 0 and xs[k - 1][1] > t:
                k -= 1
            while k < len(xs) and t + busy[i] > xs[k][0]:
                t = max(t, xs[k][1])
                k += 1
            xs.insert(k, (t, t + busy[i]))
            at[i] = t
        return at

    def length(order, busy, before):
        at, free = [0.0] * n, {}
        for i in order:
            at[i] = max([at[m] + w for m, w in before[i]] + [free.get(queue[i], 0.0)])
            free[queue[i]] = at[i] + busy[i]
        return max(free.values())

    paces = [times(p) for p in PACES]
    found = []
    for busy, before, after in paces[:LEAD]:
        back = [0.0] * n
        for i in range(n - 1, -1, -1):
            back[i] = max([back[m] + w for m, w in after[i]] + [0.0])
        plain = list(back)
        for i in range(n - 1, -1, -1):
            back[i] = max([back[m] + w for m, w in after[i]] + [plain[i] + calls[i][5]])
        for turn in range(TURNS):
            at = fill(sorted(range(n), key=lambda i: (round(-back[i] - busy[i], 6), i)), busy, before)
            order = sorted(range(n), key=lambda i: (round(at[i], 6), i))
            found.append(([length(order, b, e) for b, e, _ in paces], order))
            back = fill(sorted(range(n), key=lambda i: (round(-at[i] - busy[i], 6), -i)), busy, after)
    least = [min(x[0][k] for x in found) for k in range(len(paces))]
    order = min(found, key=lambda x: sum(t / s for t, s in zip(x[0], least)))[1]

    paces = [times(p, False) for p in PACES]
    qs = sorted(set(queue))
    qn = [qs.index(q) for q in queue]
    draw = np.random.default_rng(0)
    same = {}
    for i in range(n):
        same.setdefault(calls[i][6][1:], {})[calls[i][6][0]] = i

    def borrow(order):
        best = sum(length(order, b, e) / s for (b, e, _), s in zip(paces, least))
        for src in range(RO):
            for dst in range(RO):
                place = {i: float(k) for k, i in enumerate(order)}
                pairs = [(x[src], x[dst]) for x in same.values() if src in x and dst in x and src != dst]
                if pairs:
                    shift = float(np.median([place[y] - place[x] for x, y in pairs]))
                    mine = sorted(place[y] for x, y in pairs)
                    for (x, y), k in zip(sorted(pairs, key=lambda z: place[z[0]]), mine):
                        place[y] = k
                    for i in range(n):
                        place[i] = max([place[m] for m, w in paces[0][1][i]] + [place[i]])
                    other = sorted(range(n), key=lambda i: (place[i], i))
                    t = sum(length(other, b, e) / s for (b, e, _), s in zip(paces, least))
                    if t < best:
                        best, order = t, other
        return order

    for lo in list(range(0, n, STRETCH // 2)) * SWEEPS:
        if lo == 0:
            order = borrow(order)
        hi = min(n, lo + STRETCH)
        inside = set(order[lo:hi])
        given = []
        for busy, before, after in paces:
            at, free, tail, then = [0.0] * n, [0.0] * len(qs), [0.0] * n, [0.0] * len(qs)
            for i in order[:lo]:
                at[i] = max([at[m] + w for m, w in before[i]] + [free[qn[i]]])
                free[qn[i]] = at[i] + busy[i]
            for i in reversed(order[hi:]):
                tail[i] = max([tail[m] + w + busy[i] - busy[m] for m, w in after[i]] + [then[qn[i]] + busy[i]])
                then[qn[i]] = tail[i]
            out, own = [0.0] * n, [0] * n
            for i in inside:
                out[i] = max([tail[m] + w + busy[i] - busy[m] for m, w in after[i] if m not in inside] + [0.0])
                own[i] = (qn[i], busy[i], max([at[m] + w for m, w in before[i] if m not in inside] + [0.0]),
                          [x for x in before[i] if x[0] in inside], out[i])
            given.append((busy, before, after, at, free, tail, then, own))

        def span(xs, g_, u=0):
            at, free, own, end = g_[3], list(g_[4]), g_[7], 0.0
            for i in xs[:u]:
                q, busy, t, before, out = own[i]
                t = at[i]
                free[q] = t + busy
                if t + out > end:
                    end = t + out
            for i in xs[u:]:
                q, busy, t, before, out = own[i]
                if free[q] > t:
                    t = free[q]
                for m, w in before:
                    if at[m] + w > t:
                        t = at[m] + w
                at[i] = t
                free[q] = t + busy
                if t + out > end:
                    end = t + out
            return max(end, max(x + y for x, y in zip(free, g_[6])))

        def held(xs, g_):
            busy, before, after, at, free, tail, then, own = g_
            end, then, found = span(xs, g_), list(then), []
            for k in range(len(xs) - 1, -1, -1):
                i = xs[k]
                tail[i] = max([tail[m] + w + busy[i] - busy[m] for m, w in after[i]] + [then[qn[i]] + busy[i]])
                then[qn[i]] = tail[i]
                if at[i] + tail[i] > end - NEAR and at[i] > max([at[m] + w for m, w in before[i]] + [0.0]) + 0.01:
                    found.append(k)
            return found

        xs = order[lo:hi]
        now = [span(xs, g_) / s for g_, s in zip(given, least)]
        best, places, stale = sum(now), [], [len(xs)] * len(given)
        kept = (best, xs)
        for turn in range(TRIES):
            if not places or turn % 16 == 0:
                places = held(xs, given[int(draw.integers(len(given)))])
                if not places:
                    continue
            k = places[int(draw.integers(len(places)))]
            mates = [u for u in range(k - 1, max(-1, k - 60), -1) if qn[xs[u]] == qn[xs[k]]][:int(draw.integers(1, 7))]
            if not mates:
                continue
            u = mates[-1]
            if draw.random() < 0.5:
                go = {xs[k]}
                for i in reversed(xs[u:k + 1]):
                    if i in go:
                        go.update(m for m, w in paces[0][1][i])
                if xs[u] in go:
                    continue
                ys = xs[:u] + [i for i in xs[u:k + 1] if i in go] + [i for i in xs[u:k + 1] if i not in go] + xs[k + 1:]
            else:
                go = {xs[u]}
                for i in xs[u:k + 1]:
                    if i in go:
                        go.update(m for m, w in paces[0][2][i])
                if xs[k] in go:
                    continue
                ys = xs[:u] + [i for i in xs[u:k + 1] if i not in go] + [i for i in xs[u:k + 1] if i in go] + xs[k + 1:]
            room, t, new = HEAT * (1.0 - turn / TRIES) * draw.exponential(), best, list(now)
            for p, g_ in enumerate(given):
                new[p] = span(ys, g_, min(u, stale[p])) / least[p]
                stale[p] = u
                t += new[p] - now[p]
                if t > best + room + 0.001:
                    break
            if t <= best + room:
                best, xs, places, stale, now = t, ys, places if t > best - 1e-6 else [], [len(xs)] * len(given), new
                if t < kept[0]:
                    kept = (t, xs)
        order[lo:hi] = kept[1]
    return borrow(order)


def rank_program(g, core, T, topo):
    rank = T.rank_of(core)
    if rank is None:
        return
    N = len(T.cores)
    eng = {"v": g.vector, "s": g.scalar, "p": g.tensor, "g": g, "y": g.sync}
    qsem = {"v": "qv", "s": "qs", "p": "qp", "g": "qg"}
    count = {}
    known = {q: {} for q in eng}
    snap = {}
    acc = {}

    def ap(x):
        if not isinstance(x, tuple):
            return x
        name, lo, hi, step, ind, np_ = x
        home, base = HOME.get(name, (name, 0))
        t, lo, hi = T["b_" + home], lo + base, hi + base
        r = t[0:np_, lo:hi:step] if step != 1 else t[0:np_, lo:hi]
        return r.indirect(ap(ind)) if ind is not None else r

    def wait(q, s, v):
        if known[q].get(s, 0) >= v:
            return
        eng[q].wait_ge(T.sem[s], v)
        k = known[q]
        for s2, v2 in snap.get((s, v), {s: v}).items():
            if k.get(s2, 0) < v2:
                k[s2] = v2

    def order(q, rd, wr):
        use = uses(rd, wr)
        need = {}
        for name, m, w in use:
            for (m2, w2, q2, s2, v2) in acc.get(name, []):
                if name in PS and q2 != q:
                    hit = True
                elif name in PS and q == "p":
                    hit = False
                else:
                    hit = (w or w2) and (m & m2) != 0
                if hit and need.get(s2, 0) < v2:
                    need[s2] = v2
        for s2 in sorted(need, key=lambda s: s == qsem.get(q)):
            wait(q, s2, need[s2])
        return use

    def note(use, q, s, v):
        sn = dict(known[q]) if q in known else {}
        sn[s] = v
        snap[(s, v)] = sn
        for name, m, w in use:
            lst = acc.setdefault(name, [])
            if name in PS:
                lst[:] = [e for e in lst if e[2] == q]
            if w:
                lst[:] = [e for e in lst if e[0] & ~m]
            else:
                lst[:] = [e for e in lst if not (e[3] == s and not e[1] and not e[0] & ~m)]
            lst.append((m, w, q, s, v))

    calls = []
    seen = {}
    rows = {}
    in_row, group, spare = [None], [None], [0]
    now, met = [0], {}
    in_sum, loose = [False], set()

    def record(q, rd, wr, busy, done, issue, after=()):
        n, dep = len(calls), {m: "none" for m in after}
        use = uses(rd, wr)
        for name, m, w in use:
            for (m2, w2, q2, n2) in seen.get(name, []):
                if name in PS and q == q2 == "p":
                    if n2 not in loose or not in_sum[0]:
                        dep.setdefault(n2, "none")
                elif (name in PS and q2 != q) or ((w or w2) and m & m2):
                    dep[n2] = "wait"
        if in_row[0] in KEPT:
            key = (in_row[0], q)
            if key in rows:
                dep.setdefault(rows[key], "row" if in_row[0] in FIRM else "hint")
            rows[key] = n
        for name, m, w in use:
            lst = seen.setdefault(name, [])
            if name in PS and in_sum[0]:
                loose.add(n)
            elif name in PS and q == "p":
                lst[:] = []
            elif w:
                lst[:] = [e for e in lst if e[0] & ~m]
            lst.append((m, w, q, n))
        x = [y for y in list(wr) + list(rd) if isinstance(y, tuple) and len(y) == 6 and isinstance(y[0], str)][:1]
        key = (q, busy) + tuple((y[0].split("_")[0].rstrip("01y").replace("dicx", "dic"),) + y[1:4] for y in x)
        met[(now[0], key)] = met.get((now[0], key), 0) + 1
        calls.append((q, busy, done, list(dep.items()), issue, SOON.get(group[0], 0.0), (now[0], key, met[(now[0], key)])))
        return n

    def op(q, rd, wr, fn):
        def issue():
            use = order(q, rd, wr)
            s = qsem[q]
            count[s] = count.get(s, 0) + 1
            fn().then_inc(T.sem[s], 1)
            note(use, q, s, count[s])
        t = ("cycle", 1.4, 0) if len(calls) < 7 and q == "s" else cost(q, rd, wr)
        record(q, rd, wr, t, 0.0, issue)

    def issue_all():
        if not ORDER:
            ORDER[:] = lay_out(calls)
        for i in ORDER:
            calls[i][4]()

    def ts(o, i, s1, s2, o0, o1=None):
        if o1 is None:
            op("v", [i, s1], [o], lambda: g.vector.tensor_scalar(ap(o), ap(i), ap(s1), None, o0))
        else:
            op("v", [i, s1, s2], [o], lambda: g.vector.tensor_scalar(ap(o), ap(i), ap(s1), ap(s2), o0, o1))

    def tt(o, i0, i1, o0):
        op("v", [i0, i1], [o], lambda: g.vector.tensor_tensor(ap(o), ap(i0), ap(i1), o0))

    def cp(o, i):
        op("v", [i], [o], lambda: g.vector.tensor_copy(ap(o), ap(i)))

    def red(o, i, o0, **kw):
        op("v", [i], [o], lambda: g.vector.tensor_reduce(ap(o), ap(i), AX.X, o0, **kw))

    def scan(o, d0, d1, first, o0, o1):
        op("v", [d0, d1, first], [o], lambda: g.vector.tensor_tensor_scan(ap(o), ap(d0), ap(d1), first, o0, o1))

    def ms(o, v):
        op("v", [], [o], lambda: g.vector.memset(ap(o), v))

    def act(o, i, f, bias=None, scale=1.0):
        if bias is None:
            op("s", [i], [o], lambda: g.scalar.activation(ap(o), ap(i), f))
        else:
            op("s", [i, bias, scale], [o], lambda: g.scalar.activation(ap(o), ap(i), f, bias=ap(bias), scale=ap(scale)))

    def aff(o, i, scale, bias):
        act(o, i, AF.Identity, bias, scale)

    def total(o, i, scale):
        spare[0] = (spare[0] + 16) % 64
        x = a("tot", spare[0], spare[0] + len(range(*i[1:4])))
        op("s", [i], [x, o], lambda: g.scalar.activation(ap(x), ap(i), AF.Identity, scale=scale, accum_out=ap(o)))

    def mm(o, l, r, st=True, sp=True):
        op("p", [l, r], [o], lambda: g.tensor.matmul(ap(o), ap(l), ap(r), st, sp))

    def mms(xs, size=8):
        for k in range(0, len(xs), size):
            part, n = xs[k:k + size], len(calls)
            for x in part:
                mm(*x)
            mine = calls[n:]
            del calls[n:]
            for lst in seen.values():
                lst[:] = [e if e[3] < n else e[:3] + (n,) for e in lst]
            for key in rows:
                rows[key] = min(rows[key], n)
            dep = {}
            for x in mine:
                for m, w in x[3]:
                    if m < n and dep.get(m) != "wait":
                        dep[m] = w
            calls.append(("p", ("column", 0.0, sum(x[1][2] for x in mine)), 0.0, list(dep.items()),
                          lambda mine=mine: [x[4]() for x in mine], mine[0][5], mine[0][6]))

    def add_mm(o, l, r, left):
        def fn():
            left[0] -= 1
            return g.tensor.matmul(ap(o), ap(l), ap(r), False, left[0] == 0)
        left[0] += 1
        in_sum[0] = True
        op("p", [l, r], [o], fn)
        in_sum[0] = False

    def iota(o, pat, base, cm=0):
        if SB[o[0]][1] == I:
            op("g", [], [o], lambda: g.iota(ap(o), pat, base, cm))
        else:
            op("g", [], [o], lambda: g.iota(ap(o), pat, base, cm, allow_small_or_imprecise_dtypes=True))

    def fill(o, v):
        iota(o, [[0, len(range(*o[1:4]))]], v)

    def dma(q, s, pairs, also=()):
        (o, i), = pairs

        def issue():
            order(q, list(also), [])
            use = order(q, [i], [o])
            eng[q].dma_start(ap(o), ap(i)).then_inc(T.sem[s], 16)
            count[s] = 16
            note(use, q, s, 16)
        record(q, [i] + list(also), [o], ("cycle", 0.1, 0), s if s in LOADED else 1.7, issue)

    def send(src, dst, s, to, frm, loc="sent", also=()):
        def issue():
            order("g", [src] + list(also), [])
            d = T.cores[to]
            rid, pid, _ = topo.addr(d)
            g.remote_dma(ap(dst), ap(src), T.sem[s], T.sem[loc], pid, rid, topo.mask(core, d))
            count[loc] = count.get(loc, 0) + len(topo.engines(core, d))
            if loc != "sent":
                note([(src[0], bits(src), False)], "remote", loc, count[loc])

        def landed():
            count[s] = len(topo.engines(T.cores[frm], core))
            note([(dst[0], bits(dst), True)], "remote", s, count[s])
        n = record("g", [src] + list(also), [], ("cycle", ROWS, 0), "hop", issue)
        record("landing", [], [dst], ("cycle", 0.0, 0), 0.0, landed, [n])

    def sel(z, i):
        return a(z, 15 - i, 143 - i)

    def conv(o, z, buf, lo, hi):
        mms([(o, sel(z, i), a(buf, lo + i, hi, 16), i == 0, i == 15) for i in range(16)])

    def row(r):
        return a("dg", r, r + 1)

    in_row[0] = "loads"
    dma("y", "ld0", [(a("pupb"), T.pup[:])])
    dma("s", "ld1", [(a("seatb"), T.seat[:])])
    dma("y", "ld2", [(a("wtb", 0, 1), T.wt[:])])
    dma("y", "ld3", [(a("dicx", 0, 1024), T.dic[:, 0:1024])])
    dma("y", "ld4", [(a("dicx", 1024, 8192), T.dic[:, 1024:8192])])
    ms(a("ln2"), 1.0)
    in_row[0] = 0
    act(a("lns", 0, 1), a("ln2", 0, 1), AF.Ln)
    in_row[0] = None
    cp(a("dicx", 8192, DW), a("dicx", 0, DW - 8192))

    in_row[0] = "first"
    iota(a("ci", 0, 1), [[0, 1]], 0, 1)
    iota(a("i16"), [[0, 3], [1, 16]], 0)
    iota(a("io"), [[1, 144]], 0)
    iota(a("b32"), [[256, 2], [1, 16]], 0)
    iota(a("ie"), [[0, 16], [1, 16]], 0)
    iota(a("ia"), [[1, 16], [0, 16]], 0)
    iota(a("ic"), [[64, 24], [1, 16]], 512)
    iota(a("mg"), [[16, 8], [0, 16]], 0)
    iota(a("mq"), [[1, 2], [2, 2], [0, 8]], 0)
    iota(a("thn"), [[0, 4], [1, 8]], 0)
    iota(a("stp", 0, 16), [[1, 4], [8, 2], [16, 2]], 0)
    iota(a("i8"), [[1, 16], [0, 2]], 0)
    for k in range(8):
        iota(a("ti", 64 * k, 64 * k + 64), [[4224, 2], [256, 2], [1, 16]], 528 * k)
    in_row[0] = None
    ms(a("x0", 0, B0), -1.0)
    ms(a("x0", B0 + 512, XW), -1.0)
    cp(c(CP), a("ci", 0, 1))
    ts(a("ci", 1, 2), a("ci", 0, 1), 15, None, OP.bitwise_and)
    ts(a("ci", 2, 3), a("ci", 0, 1), 112, None, OP.bitwise_and)
    ms(a("t1", 0, 16), math.exp(-1.0))
    ms(a("t1", 16, 32), 0.0)
    cp(a("col", CK, CG + 1), a("ci", 1, 3))
    scan(a("t1", 32, 48), a("t1", 0, 16), a("t1", 16, 32), math.exp(0.8), OP.mult, OP.add)
    ts(c(CG15), c(CG), 15.0, None, OP.add)
    ts(c(CS), c(CK), 32.0, float(B0), OP.mult, OP.add)
    ts(a("idn"), a("io", 0, 128), c(CP), None, OP.is_equal)
    ts(a("zo"), a("io"), c(CG15), None, OP.is_equal)
    ts(a("t1", 64, 112), a("io", 0, 48), c(CS), None, OP.add)
    ts(a("nid"), a("io", 0, 128), c(CP), -1.0, OP.is_equal, OP.mult)
    ts(a("t1", 112, 160), a("t1", 64, 112), B0 + 511.5, None, OP.is_le)
    ts(a("dg"), a("i16"), c(CK), None, OP.is_equal)
    tt(a("t1", 160, 208), a("t1", 64, 112), a("t1", 112, 160), OP.mult)
    cp(a("x2l"), a("t1", 160, 208))
    tt(a("t1", 48, 64), a("t1", 32, 48), a("dg", 0, 16), OP.mult)
    red(c(CM), a("t1", 48, 64), OP.add)
    cp(a("seatu"), a("seatb"))
    ts(c(CX), a("wtb", 0, 1), 2048.0, -4096.0, OP.is_ge, OP.mult)
    tt(c(CW), a("wtb", 0, 1), c(CX), OP.add)
    cp(a("x0", B0, B0 + 256), a("pupb", ind=a("seatu", 0, 16)))
    ts(a("zw"), a("zo"), c(CW), None, OP.mult)

    def scalar_constants():
        for j, (m, b) in {CU: (-512, 7680), CU2: (-512, -512), CK16: (1, 16), CK32: (1, 32), CJ: (1, B0), CV: (-1, 15), CH0: (2, 0), CH1: (2, 1),
                          CT0: (-37, 555), CT0 + 1: (-37, 566), CT0 + 2: (-37, 577), CT0 + 3: (-37, 588)}.items():
            aff(c(j), c(CK), float(m), float(b))
        for n in sorted({NS - 1, NS, NS0 - 1, NS0}):
            ts(c(CQ), c(CK), n - 0.5, -8.5, OP.is_le, OP.mult)
            aff(c(CTH + n), c(CQ), 1.0, 7.5)
        gt, e1, e2, u, add, uns = [a("t4", 16 * n, 16 * n + 16) for n in range(6)]
        k0 = a("io", 0, 16)
        ts(gt, k0, c(CK), None, OP.is_lt)
        ts(u, k0, 528.0, c(CU), OP.mult, OP.add)
        ts(e1, k0, c(CK), ZC + 1.0, OP.is_equal, OP.mult)
        ts(e2, k0, c(CK), 2.0, OP.is_equal, OP.mult)
        ts(uns, k0, c(CK), float(ZC), OP.is_le, OP.mult)
        tt(add, u, gt, OP.mult)
        tt(uns, uns, e2, OP.add)
        tt(add, add, e1, OP.add)
        tables = [(buf, lo + 64 * (k % 8) + 32 * (k // 8), k) for buf, lo in (("cd", 1536), ("cc", 0)) for k in range(16)]

        def table():
            buf, w, k = tables.pop()
            col = lambda x: a(x[0], x[1] + k, x[1] + k + 1)
            aff(a(buf, w, w + 32), a("b32"), col(gt) if buf == "cc" else 0.0, col(add if buf == "cc" else uns))
        in_row[0] = SROW
        for n, (j, first, f, x) in enumerate((
                (C34, row(3), 1, row(4)), (C67, row(6), 1, row(7)), (CEF, row(14), 1, row(15)), (CY, row(11), 1, row(12)),
                (CE, -60000.0, C2, row(4)), (CD, row(0), E2 + 8, row(1)), (CB, row(0), 8, row(1)), (CA, row(1), 16, row(0)),
                (C16, c(C34), 1, c(C67)), (CY, c(CY), 1, c(CEF)), (CE, c(CE), C2, row(6)), (CD, c(CD), C2, row(12)),
                (CZ0, 1.0, -1, row(1)), (None,) * 4,
                (CE, c(CE), C2, row(14)), (CD, c(CD), C2, row(14)), (CB, c(CB), 1, c(CY)), (CA, c(CA), 64, c(CY)),
                (C24, c(C16), 1, c(CEF)), (CE, c(CE), -480, c(C67)), (CD, c(CD), 559, c(CEF)), (CL0, 0.0, C2, row(12)),
                (CE, c(CE), -1008, c(C34)), (CD, c(CD), 60000, c(C16)), (CL0, c(CL0), 512, c(C24)),
                (CE, c(CE), -1488, c(CEF)), (CD, c(CD), 1, c(CY)))):
            if j is None:
                act(a("x0", B0 + 256, B0 + 512), a("pupb", ind=a("seatu", 16, 32)), AF.Copy)
            else:
                aff(c(j), x, float(f), first)
            if n > 18:
                table()
        for n, (j, x) in enumerate(((CA, "ia"), (CB, "ie"))):
            aff(a("da", 128 * n, 128 * n + 128), a("idn"), c(j), 0.0)
            mm(a("pn", 0, 256), a("da", 128 * n, 128 * n + 128), a(x), n == 0, n == 1)
        aff(a("ex", 512, 768), a("pn", 0, 256), 1.0, c(CD))
        for i in range(ONE - 1):
            aff(a("ex", 512 + i, 768, 16), a("ex", 512 + i, 768, 16), c(CZ0), 0.0)
        for n, j in enumerate((C67, C16, C24)):
            aff(c(CZ1 + n), c(j), c(CE), 60000.0)
        for n, j in enumerate((C67, C16, C24)):
            aff(a("ce", 128 * n, 128 * n + 128), a("ic", 128 * n, 128 * n + 128), c(j), c(CZ1 + n))
        while tables:
            in_row[0] = SROW if len(tables) > EARLY else None
            table()
        in_row[0] = None

    def later_constants():
        act(a("cd", C2 + 1024, C2 + 1536), a("ti"), AF.Relu, c(CU2))
        ts(c(CQ), c(CK), 512.0, 512.0, OP.mult, OP.add)
        in_row[0] = SROW
        ts(a("cd", C2 + 1536, C2 + 2048), a("ti"), c(CQ), float(ZC), OP.is_ge, OP.mult)
        in_row[0] = None
        ts(c(CX), c(CK), 14.5, c(CM), OP.is_le, OP.mult)
        ts(a("wj"), c(CX), 3.0, -3.0, OP.add, OP.add)
        ts(a("zm"), a("zo"), a("wj"), None, OP.mult)
        ts(a("blkb"), a("mg"), c(CG), None, OP.is_equal)
        ts(a("wneg"), a("io", 0, 32), 15.5, a("wj"), OP.is_ge, OP.mult)
        aff(a("wneg"), a("wneg"), -1.0, 0.0)
        mm(a("pm", 0, 1), a("blkb"), a("wj"))
        ts(c(CN), a("pm", 0, 1), 0.5, TINY, OP.mult, OP.add)

    def last_constants():
        return [
            lambda: aff(a("thn"), a("thn"), 1.0, -6.5),
            lambda: aff(a("mq"), a("mq"), 1.0 / 32, 0.0),
            lambda: aff(a("t15"), a("mq"), 1.0, 15.0 / 8),
            lambda: tt(a("stp", 16, 32), a("stp", 0, 16), a("dg", 0, 16), OP.mult),
            lambda: total(a("stp", 32, 33), a("stp", 16, 32), 1.0),
            lambda: ts(a("steps"), a("io", 0, 8, 4), a("stp", 32, 33), None, OP.add),
            lambda: ms(a("v4"), 0.0),
            lambda: aff(a("zr"), a("zo"), row(0), 0.0),
            lambda: cp(a("ch", 0, 1), c(CL0)),
            lambda: aff(a("q16"), a("io", 0, 36), 16.0, c(CJ)),
            lambda: aff(a("mc", 0, 32), a("io", 0, 32), 0.0, c(CV)),
            lambda: aff(a("q16", 32, 33), c(CJ), 1.0, 0.0),
            lambda: aff(a("s1", 1, 165, 5), a("q16", 0, 33), 1.0, -1.0),
            lambda: aff(a("q32"), a("q16", 0, 32), 1.0 / NONE, 0.0),
        ]

    def visit_constants():
        out = [
            lambda: ts(a("dg2"), a("i8"), c(CK), None, OP.is_equal),
            lambda: aff(a("zk"), a("zo"), 2.0 ** 25, 0.0),
            lambda: aff(a("k7"), a("io", 0, 48), 0.0, -7.5 * 2.0 ** 25),
            lambda: ts(a("one"), a("io", 0, 112), 96.5, None, OP.is_le),
            lambda: aff(a("rk"), a("i16"), -2.0 ** 20, 7 * 2.0 ** 20),
            lambda: aff(c(CX), c(CP), 1.0, -1.0),
            lambda: ts(a("nidn"), a("io", 0, 128), c(CX), -1024.0, OP.is_equal, OP.mult),
            lambda: [aff(c(CD0 + h), c(CK), -512.0, -1536.0 - 16 * h) for h in range(3)],
            lambda: [aff(c(CSP + h), c(CK), 1.0, 768.0 + 16 * h) for h in range(3)],
            lambda: aff(c(CH2), c(CK), 2.0, 2.0),
            lambda: aff(a("tm", 353, 354), row(15), -1.0, 1.0),
            lambda: aff(c(CQ), c(CW), 1.0, 2048.0),
            lambda: [ts(a("m1_%d" % r, 64, 66), a("io", 0, 2), 0.0, c(CQ), OP.mult, OP.add) for r in range(RO - 1)],
            lambda: aff(a("blkk"), a("blkb"), 1024.0, 0.0),
            lambda: aff(a("nidk"), a("idn"), -1024.0, 0.0),
            lambda: ts(a("g8"), a("io", 0, 8), 16.0, c(CG), OP.mult, OP.is_equal),
        ]
        for h in range(3):
            out.append(lambda h=h: ts(a("tm", 128 * h, 128 * h + 32), a("io", 0, 32), c((CH0, CH1, CH2)[h]), 2.0 ** 23, OP.is_ge, OP.mult))
        for h in range(3):
            for n, s in ((1, 2.0 ** 19), (2, -2.0 ** 19)):
                out.append(lambda h=h, n=n, s=s: aff(a("tm", 128 * h + 32 * n, 128 * h + 32 * n + 32), a("tm", 128 * h, 128 * h + 32), 1.0, s))
        return out

    def first_numbers():
        mm(a("pa"), a("dh"), a("ohi"), True, False)
        mm(a("pa"), a("dl"), a("olo"), False, True)
        act(a("oio"), a("pa"), AF.Copy)
        act(a("o0", B0, B0 + 512), a("oio", ind=a("seatu")), AF.Copy)
        ts(a("o0", 0, B0), a("io", 0, B0), -float(B0), row(0), OP.add, OP.mult)

    scalar_constants()
    BIG = float(1 << 20)
    for t in range(RO):
        xo, xn = ("x0", "x1") if t % 2 == 0 else ("x1", "x0")
        oo, on = ("o0", "o1") if t % 2 == 0 else ("o1", "o0")
        host = (rank + 1 + t % (N - 1)) % N
        guest = (rank - 1 - t % (N - 1)) % N
        last = t == RO - 1
        now[0], spare[0] = t, 0
        m1, l1, m2, l2, m3, l3 = ["%s_%d" % (n, t) for n in ("m1", "l1", "m2", "l2", "m3", "l3")]
        def sums(x):
            mms([(a("pk", 0, 47), sel("zw", i), a(x, B0 + 32 * i, B0 + 32 * i + 47), i == 0, i == 15) for i in range(16)])
            act(a("x2", 0, 752), a(x, ind=a("x2l", 0, 47)), AF.Copy)
        if t == 0:
            sums(xo)
            ts(a("ksi", 0, 47), a("pk", 0, 47), BIG, None, OP.add)
            ts(a("ks", 0, 47), a("ksi", 0, 47), 4095, None, OP.bitwise_and)

        at = lambda j: 64 * (j % 8) + 32 * (j // 8)
        def mult(j):
            tt(a("prod", at(j), at(j) + 32), a("ks", 0, 32), a("ks", j, j + 32), OP.mult)

        def shift(j0, j1):
            ts(a("prs", at(j0), at(j1) + 64), a("prod", at(j0), at(j1) + 64), 5, 8191, OP.logical_shift_right, OP.bitwise_and)

        def add(j):
            if t > 0:
                ts(a("off", at(j), at(j) + 64), a("prs", at(j), at(j) + 64), float((37 * j + 11 * t) % 8), None, OP.add)
            else:
                for j2 in (j, j + 8):
                    ts(a("off", at(j2), at(j2) + 32), a("prs", at(j2), at(j2) + 32), float(37 * j2 % 16), None, OP.add)

        in_row[0] = t if LROW else None
        for f, *js in ((mult, 0), (mult, 8), (mult, 1), (mult, 9), (mult, 2), (mult, 10), (shift, 0, 0), (mult, 7), (mult, 15),
                       (mult, 6), (add, 0), (mult, 14), (shift, 1, 2), (mult, 3), (mult, 11), (shift, 6, 7), (mult, 4), (add, 1),
                       (add, 2), (mult, 12), (mult, 5), (mult, 13), (add, 7), (add, 6)):
            f(*js)
        later_lists = [lambda: shift(3, 5), lambda: [add(j) for j in (3, 4, 5)]]
        while t == 0 and later_lists:
            later_lists.pop(0)()
        in_row[0] = None
        if t == 0:
            later_constants()
            for f in last_constants():
                f()
            in_row[0] = "first"
            fill(a("pq", 96, 112), 0)
            fill(a("cq", 0, 128), int(MAG))
            iota(a("cq", 128, 256), [[0, 32], [1, 4]], 0)
            fill(a("cq", 256, 384), -1024)
            send(a(xo, 0, B0 + 512), a("xg"), "a0", host, guest, "out0", [a("dicx", 0, 8192)])
            dma("y", "ld5", [(a("dicy", DY, DY + DW - 8), a("dicx", 8, DW))])
            fill(a("cq", 256, 384, 4), 0)
            for x in (7, 10, 11, 13, 14, 15):
                fill(a("cq", 256 + x, 384, 16), -8192)
            fill(a("sd"), 0)
            iota(a("sd", 3, 128, 4), [[0, 8], [1, 4]], -int(MAG) - 3)
            for x in (a("cd", 512, 1536), a("cd", C2 + 512, C2 + 1024),
                      a("ex", FILL, E2 + 8 * ONE), a("ex", E2 + 128, RW), a("cd", E2, RW), a("dicy", 512, DY)):
                fill(x, 0)
            for x, v in ((a("dicy", DY + DW - 8, DY + DW), 0), (a("mc", 32, 64), 2048), (a("s0"), 1), (a("s0", 0, 165, 5), 0),
                         (a("s0", 3, 165, 5), -1), (a("s0", 4, 165, 5), -1), (a("y2", 32, 33), 0), (a("lt", ZC, ZC + 16), 0),
                         (a("x1", 0, B0), -1), (a("x1", B0 + 512, XW), -1), (a("xv", 512, 528), 0), (a("lt2", 512, 528), 0),
                         (a("tm", 96, 384, 128), 1 << 22), (a("tm", 97, 256, 128), 1), (a("ypb", 0, B0), 0), (a("o1", 0, B0), 0)):
                fill(x, v)
            iota(a("ohi"), [[16, 32], [0, 16]], 0)
            iota(a("olo"), [[0, 32], [1, 16]], 0)
            in_row[0] = None

        def word(j, lo=0, hi=32):
            ws = (37 * j + 11 * t) // 16 * 16
            later = t > 0 and (37 * j + 11 * t) % 16 >= 8
            return a("dicy" if later else "dicx", ws + DY * later, ws + DY * later + 8208, ind=a("off", at(j) + lo, at(j) + hi))

        def ltj(j, lo=0, hi=512):
            w = 512 * ((14 - j) % 16)
            return a("lt", w + lo, w + hi)

        def quads():
            p0 = lambda lo=0, step=1: a("pq", 64 + lo, 96 + lo if step == 1 else 96, step)
            q = lambda n: a("tq", 8 * n, 8 * n + 8)
            ts(a("pq", 0, 96), a("pp", 0, 96), -1.0, 1024.0, OP.is_le, OP.mult)
            tt(a("dq"), a("pq", 0, 64), a("pq", 32, 96), OP.subtract)
            tt(a("zq"), p0(), p0(1), OP.min)
            tt(a("wq"), a("dq", 32, 64), a("zq"), OP.max)
            tt(q(0), a("dq", 0, 32, 4), p0(0, 4), OP.subtract)
            tt(q(1), a("dq", 32, 64, 4), p0(2, 4), OP.min)
            tt(q(2), p0(0, 4), a("wq", 1, 32, 4), OP.min)
            tt(q(3), q(0), q(1), OP.max)
            tt(q(4), q(2), q(3), OP.max)
            mms([(a("pp", 128, 256), a("idn"), a("cq", 128 * n, 128 * n + 128), n == 0, False) for n in range(3)])
            for x, y in ((a("pp", 129, 256, 4), p0()), (a("pp", 130, 256, 4), a("wq")), (a("pp", 131, 256, 16), q(4))):
                mm(x, a("idn"), y, False, False)

        ns = NS0 if t == 0 else NS
        half = ns - 1
        hs = 512 - (HS0 if t == 0 else HS)
        nv, nsc = SPLIT0 if t == 0 else SPLIT
        up = lambda js, lo=CUT, hi=512: [(j, max(lo, CUT), hi) for j in js if max(lo, CUT) < hi]
        low = lambda js, lo=0, hi=CUT: [(j, lo, min(hi, CUT)) for j in js if lo < min(hi, CUT)]
        vs, ss = range(15 - nv, 15), range(half - nsc, half)
        b15 = up([15], J15) + low([15], J15)
        byv = [(j, 0, 512) for j in range(ns, 15 - nv)] + up(vs) + up([half], 0, hs) + low(vs) + low([half], 0, hs)
        bys = [(j, 0, 512) for j in range(half - nsc)] + up(ss) + up([half], hs) + low(ss) + low([half], hs, 512)
        ev = []
        tv, tsc = (0.0 if t == 0 else 1.7), 0.0
        for x in byv:
            ev.append((tv, "vg", 0, x)); tv += 0.05 + (x[2] - x[1]) * 0.0013; ev.append((tv + LAGV, "cnt", 0, x))
        for n, x in enumerate(bys + [None]):
            if x:
                ev.append((tsc, "sg", n, x)); tsc += 0.06 + (x[2] - x[1]) * 0.0013; ev.append((tsc, "sub", n, x))
            if n > 0:
                y = bys[n - 1]
                ev.append((tsc + 0.001, "sign", n - 1, y)); tsc += 0.05 + (y[2] - y[1]) * 0.0008
                ev.append((tsc + LAGS, "quads" if y[0] == 2 else "cnt", n - 1, y))
        ev.sort()
        ncnt = {"pc": [0], "pk": [0]}
        cnt = lambda lo, hi, step=1: a("pc" if lo >= CUT else "pk", lo, hi, step)

        def exits(q):
            w = 64 * (q + 1)
            src = a("ex", w, w + 256, ind=a("r32", 4 * q, 4 * q + 4))
            if q >= 2:
                tt(a("ex", w - 64, w), src, a("ce", w - 192, w - 128), OP.min)
            elif q < EXS:
                in_row[0] = None
                act(a("ex", w - 64, w), src, AF.Copy)
            else:
                cp(a("ex", w - 64, w), src)
            in_row[0] = None
            if q < 4:
                act(a("eb", w - 64, w), src if q < EBS else a("ex", w - 64, w), AF.Copy)
                mms([(a("pp", 0, 8 - ONE // 2), sel("zr", cc_), a("eb", 16 * cc_ + ONE, 16 * cc_ + 16, 2), cc_ == 15, cc_ == 0)
                     for cc_ in range(4 * q + 3, 4 * q - 1, -1)])

        def parts(lo, hi):
            return [(x, y, c(CTH + ns - (x < hs))) for x, y in ((lo, min(hi, hs)), (max(lo, hs), hi)) if x < y]

        def ends():
            def words(n):
                for j, lo, hi in b15[n:n + 1]:
                    bank = a(("pa", "ph")[n], lo, hi)
                    in_row[0] = t
                    act(a("d2", lo, hi), word(j, lo // 16, hi // 16), AF.Copy)
                    in_row[0] = None
                    mm(bank, a("nid"), a("x2", 16 * j + lo, 16 * j + hi), True, False)
                    mm(bank, a("idn"), a("d2", lo, hi), False, True)
            words(0)
            for e in (0, 1):
                in_row[0] = t
                for x, y, th in parts(0, CUT):
                    act(a("pw", x + e, y, 2), cnt(x + e, y, 2), AF.Sign, th, -1.0)
                in_row[0] = None
                for x, y, th in parts(CUT, 512):
                    ts(a("pw", x + e, y, 2), cnt(x + e, y, 2), th, 2.0, OP.is_le, OP.mult)
            mm(a("pm", 0, 32), a("blkb"), a("wneg"), True, False)
            mms([(a("pm", 0, 32), sel("zm", i), a("pw", i, 512, 16), False, i == 15)
                 for i in list(range(0, 16, 2)) + list(range(1, 16, 2))])
            words(1)
            in_row[0] = t
            for n, (j, lo, hi) in enumerate(b15):
                act(ltj(j, lo, hi), a(("pa", "ph")[n], lo, hi), AF.Sign, -0.5)
                if n == 0:
                    act(a("ln2", 0, 32), a("pm", 0, 32), AF.Ln, c(CN), 0.5)
            in_row[0] = None
            mms([(a("pp", 128 + dl, 256, 4), a("nid"), a("ln2", dl, dl + 32), False, dl == 3) for dl in range(4)])
            for lo in range(0, J15, 128):
                tt(ltj(15, lo, lo + 128), word(15, lo // 16, lo // 16 + 8), a("x2", 240 + lo, 368 + lo), OP.is_gt)
            conv(a("pb", 0, 32), "zo", "lt", 7680, 8192)
            scan(a("sc"), a("pp", 128, 256), a("sd"), 0.0, OP.max, OP.add)
            ts(a("r32"), a("sc", 3, 128, 4), 16.0, c(CK), OP.mult, OP.add)

        for _, kind, n, (j, lo, hi) in ev:
            d, bank = a("d%d" % (n % 3), lo, hi), a(("pa", "pb", "ph", "pn", "pm")[n % 5], lo, hi)
            in_row[0] = t if kind in ("vg", "sg", "sign") else None
            if kind == "vg":
                if later_lists:
                    in_row[0] = t if LROW else None
                    later_lists.pop(0)()
                    in_row[0] = t
                tt(ltj(j, lo, hi), word(j, lo // 16, hi // 16), a("x2", 16 * j + lo, 16 * j + hi), OP.is_gt)
            elif kind == "sg":
                act(d, word(j, lo // 16, hi // 16), AF.Copy)
            elif kind == "sub":
                mm(bank, a("nid"), a("x2", 16 * j + lo, 16 * j + hi), True, False)
                mm(bank, a("idn"), d, False, True)
            elif kind == "sign":
                act(ltj(j, lo, hi), bank, AF.Sign, -0.5)
            else:
                for x, y in ((max(lo, CUT), hi), (lo, min(hi, CUT))):
                    if x < y:
                        b = cnt(x, y)[0]
                        if ncnt[b] == [0]:
                            mm(cnt(x, y), sel("zo", j), ltj(j, x, y), True, False)
                            ncnt[b].append("open")
                        else:
                            add_mm(cnt(x, y), sel("zo", j), ltj(j, x, y), ncnt[b])
                if kind == "quads":
                    group[0] = "quads"
                    conv(a("pp", 0, 96), "zo", "lt", 6144, 7680)
                    quads()
                    group[0] = None
        in_row[0] = None
        ends()
        for h in (0, 1):
            mms([(a("pm", 16 * h, 16 * h + 16), sel("zm", k), a("pw", 256 * h + 16 * k, 256 * h + 16 * k + 16), k == 0, k == 15)
                 for k in range(16)])
        group[0] = "codes"
        for lo, hi, b in ((0, J15 // 16, 7.5), (J15 // 16, 32, -1.0)):
            if lo < hi:
                aff(a("th15", lo, hi), a("ln2", lo, hi), 32.0, b + 32.0 * 15.25)
        aff(a("rq"), a("ln2", 0, 32), -1.0, MAG)
        aff(a("n8"), a("rq"), 0.125, -MAG / 8)
        tt(a("a15"), a("ln2", 0, 32), a("thn"), OP.is_le)
        tt(a("nm"), a("n8"), a("mq"), OP.add)
        tt(a("n15"), a("a15"), a("t15"), OP.mult)
        tt(a("u15"), a("pb", 0, 32), a("th15"), OP.is_ge)
        tt(a("nq"), a("nm"), a("u15"), OP.add)
        ts(a("roff"), a("nq", ind=a("steps")), 512.0, c(CK), OP.mult, OP.add)
        tt(a("nq2"), a("nq"), a("n15"), OP.max)
        ts(a("rof2"), a("nq2", ind=a("steps")), 512.0, c(CK), OP.mult, OP.add)

        def codes(k):
            w = 64 * (k + 1)
            tt(a("cd", w - 64, w), a("cd", w, w + 1536, ind=a("roff", 4 * k, 4 * k + 4)), a("cc", w - 64, w), OP.max)

        def codes2(k):
            w = C2 + 64 * (k + 1)
            act(a("cd", w - 64, w), a("cd", w, w + 1536, ind=a("rof2", 4 * k, 4 * k + 4)), AF.Copy)

        def chain(m):
            cp(a("ch", 2 * m + 1, 2 * m + 17), a("ex", ind=a("ch", 2 * m, 2 * m + 1)))

        def single(s):
            cp(a("ch", ONE, ONE + 16) if s == ONE - 1 else a("c1", 16 * s, 16 * s + 16),
               a("ex", 0, E2, ind=a("c1", 16 * s - 16, 16 * s - 15)) if s else a("ex", 64, 320, ind=a("r32", 0, 1)))

        group[0] = "steps"
        for k in range(7, -1, -1):
            codes2(k)
        group[0] = None
        for n in range(8 + max(LAG, ONE)):
            in_row[0] = ("steps", t)
            if n < 8:
                exits(7 - n)
            in_row[0] = ("steps", t)
            if n >= 7:
                single(n - 7) if n - 7 < ONE else None
            if 0 <= n - LAG < 8:
                codes(7 - n + LAG)
        in_row[0] = None
        cp(a("le2", 0, 8 - ONE // 2), a("pp", 0, 8 - ONE // 2))
        act(a("ex", E2 + 8 * ONE, E2 + 128), a("ex", 0, 768, ind=a("le2", 0, 8 - ONE // 2)), AF.Copy)
        cp(a("ch", 1, ONE), a("c1", 0, 16 * ONE - 16, 16))
        for m in range(ONE // 2, 8):
            chain(m)
        for h in (0, 1):
            group[0] = "natural"
            act(a("lnn", h, 32, 2), a("pm", 16 * h, 16 * h + 16), AF.Ln, TINY if h else c(CN), 0.5)
        aff(a("nnm"), a("lnn"), -1.0, MAG)
        aff(a("s0", 1, 160, 5), a("nnm"), 1.0, -1.0 - MAG)
        aff(a("s0", 161, 162), a("nnm", 0, 1), 1.0, -1.0 - MAG)
        group[0] = "keys"
        conv(a("pn", 0, 32), "zw", xo, B0, B0 + 512)
        ts(a("kni"), a("pn", 0, 32), BIG, None, OP.add)
        ts(a("kn"), a("kni"), 4095, None, OP.bitwise_and)
        tt(a("ksq"), a("kn"), a("kn"), OP.mult)
        ts(a("v0"), a("ksq"), 5, 511, OP.logical_shift_right, OP.bitwise_and)
        for lo in (11, 23):
            ts(a("v4", lo, lo + 249, 8), a("v0"), float(B0), None, OP.add)
            ts(a("v4", 272 + lo, 272 + lo + 249, 8), a("kn"), -2048.0, None, OP.add)
        group[0] = None
        if t == 0:
            aff(a("dh"), a("idn"), row(0), 0.0)
            aff(a("dl"), a("idn"), row(1), 0.0)
            for f in visit_constants():
                f()
        mm(a("ph", 0, 32), a("idn"), a("mc", 0, 32), True, False)
        mm(a("pm", 0, 32), a("idn"), a("mc", 32, 64), True, False)
        for lo, hi in WS:
            act(a("w", 16 * lo, 16 * hi), a("cd", ind=a("ch", lo, hi)), AF.Copy)
        x = 16 * WS[-1][0]
        act(a("wa", 11, x, 4), a("w", 11, x, 4), AF.Relu, -(ZC + 1.0))
        for lo, hi in ((256, 512), (128, 256), (64, 128), (0, 64)):
            act(a("dicy", lo, hi), a("cd", lo, hi), AF.Relu, -(ZC + 1.0))
        for n in (0, 1):
            w = 272 * n
            tt(a("ap4", w + 11, w + x, 4), a("wa", 11, x, 4), a("v4", w + 11, w + x, 4), OP.mult)
            in_row[0] = ("steps", t)
            tt(a("ap4", w + x, w + 272), a("dicy", 0, RW, ind=a("ch", x // 16, 17)), a("v4", w + x, w + 272), OP.mult)
            in_row[0] = None
        tt(a("y1", 0, 32), a("w", 11, 267, 8), a("w", 23, 272, 8), OP.max)
        tt(a("y1", 32, 33), a("w", 11, 12), a("w", 23, 24), OP.max)
        tt(a("y2", 0, 32), a("w", 4, 260, 8), a("w", 14, 270, 8), OP.max)
        y1, y2 = a("y1", 0, 33), a("y2", 0, 33)
        tt(a("yp", 0, 33), y1, y2, OP.max)
        cp(a("idx2", 0, 33), a("yp", 0, 33))
        for n, bank in enumerate(("ph", "pm")):
            for lo in (11, 23):
                mm(a(bank, 0, 32), a("blkb"), a("ap4", 272 * n + lo, 272 * n + lo + 249, 8), False, lo == 23)
            cp(a(m1, 32 * n, 32 * n + 32), a(bank, 0, 32))
            w = 32 * n + 32 + 2 * (n and not last)
            send(a(m1, 32 * n, w), a(l1, 32 * n, w), "a%d_%d" % (1 + 3 * n, t), host, guest)
        for n, (y, low_, f) in enumerate(((y1, ZC, 1.0), None or (None,) * 3, (y1, ZC - 1, 1.0), (y1, ZC + 1, NONE), (y2, ZC - 1, 1.0))):
            if n in S1V:
                ts(a("s1", n, 165, 5), y, -float(low_), 0.0, OP.add, OP.max)
            elif y:
                act(a("s1", n, 165, 5), y, AF.Relu, -f * low_, f)
        scan(a("srcf", 0, 165), a("s0", 0, 165), a("s1", 0, 165), 0.0, OP.mult, OP.add)
        cp(a("src", 0, 33), a("srcf", 4, 165, 5))
        aw = a("s1", 3, 160, 5)
        tt(a("awq"), aw, a("q32"), OP.mult)
        mm(a("pp", 64, 96), a("blkb"), a("awq"))
        tt(a("dm"), a("pp", 64, 96), a("dg2"), OP.mult)
        tt(a("srof"), a("srcf", 4, 160, 5), a("awq"), OP.max)
        if t == 0:
            first_numbers()
        thirds = ((0, 10), (10, 22), (22, 33))
        end_row = "last" if last else None
        in_row[0] = end_row
        cp(a("sro"), a("srof"))
        for lo, hi in thirds:
            act(a("g2", 16 * lo, 16 * hi), a("lt", ind=a("idx2", lo, hi)), AF.Relu)
        for lo, hi in thirds:
            tt(a(xn, B0 + 16 * lo, B0 + 16 * hi), a(xo, ind=a("src", lo, hi)), a("g2", 16 * lo, 16 * hi), OP.add)
        for h in (0, 1):
            act(a(on, B0 + 256 * h, B0 + 256 * h + 256), a(oo, 0, B0 + 512, ind=a("sro", 16 * h, 16 * h + 16)), AF.Copy)
        act(a("xv", 256, 512), a(xn, ind=a(l1, 16, 32)), AF.Copy)
        in_row[0] = None if last else ("look", t)
        if not last:
            cp(a("xv", 0, 256), a(xn, ind=a(l1, 0, 16)))
        for h in (0, 1):
            total(a("avf", h, h + 1), a("dm", h, 32, 2), 1.0)
        in_row[0] = None
        for h in (0, 1):
            ts(a("avl", h, h + 1), a("avf", h, h + 1), c(CH[h]), None, OP.max)
        if not last:
            tt(a("dm3", 0, 15), a("pp", 66, 96, 2), a("dg", 0, 15), OP.mult)
            total(a("avf", 2, 3), a("dm3", 0, 15), 1.0)
            for h in range(3):
                ts(a("am", 16 * h, 16 * h + 16), a("io", 16 * h, 16 * h + 16), c(CS), a("avf", h, h + 1), OP.add, OP.is_equal)
                aff(a("avs", h, h + 1), a("avf", h, h + 1), 16.0, c(CD0 + h))
        act(a(m2), a(xo, ind=a("avl")), AF.Copy)
        if t == 0:
            send(a("avl"), a("lav"), "a2_0", host, guest, "out1")
        else:
            send(a(m2), a(l2), "a2_%d" % t, host, guest)
        def lay(lo, hi):
            cp(a("ypb", ind=a("olu", lo, hi)), a(xn, B0 + 16 * lo, B0 + 16 * hi))
        in_row[0] = end_row
        if last:
            conv(a("pn", 0, 32), "zo", on, B0, B0 + 512)
            cp(a("xv", 0, 256), a(xn, ind=a(l1, 0, 16)))
        conv(a("ph", 0, 32), "zw", "xv", 0, 512)
        in_row[0] = None
        ts(a("khi"), a("ph", 0, 32), BIG, None, OP.add)
        if last:
            ts(a("olu"), a("pn", 0, 32), float(B0), None, OP.add)
            aff(a("olf"), a("pn", 0, 32), 1.0 / NONE, B0 / NONE)
            tt(a("awo"), aw, a("olf"), OP.mult)
            mm(a("pp", 64, 96), a("blkb"), a("awo"))
            tt(a("dm"), a("pp", 64, 96), a("dg2"), OP.mult)
            for h in (0, 1):
                red(a("avp", h, h + 1), a("dm", h, 32, 2), OP.max)
            mm(a("pa", np_=8), a("g8"), a(on, B0, B0 + 512))
            act(a("ysb", np_=8), a("pa", np_=8), AF.Copy)
            dma("s", "ld6", [(T.yseat[:], a("ysb", np_=8))])
        if t == 0:
            act(a(l2), a("xg", ind=a("lav")), AF.Copy)
        cp(a(xn, ind=a("avl")), a(m2))
        cp(a("sf"), a(l1, 32, 64))
        ts(a("vb"), a(l1, 0, 32), c(CK), None, OP.add)
        tt(a("vd"), a("vb"), a("dg2"), OP.mult)
        ts(a("kh"), a("khi"), 4095, None, OP.bitwise_and)
        for h in (0, 1):
            total(a("vh", h, h + 1), a("vd", h, 32, 2), 1.0)
        tt(a("hp"), a("kh"), a("sf"), OP.mult)
        for h in (0, 1):
            aff(a("vt", 16 * h, 16 * h + 16), a("io", 0, 16), -1.0, a("vh", h, h + 1))
        ts(a("hs"), a("hp"), 5, 8191, OP.logical_shift_right, OP.bitwise_and)
        ts(a("hw"), a("hs"), c(CT0 + t), None, OP.add)
        nh = 2 if last else 3
        mm(a("pm", 0, 16 * nh), a("idn"), a("k7", 0, 16 * nh), True, False)
        two = ("pb", "pc", "pa")[:nh]
        for h in range(nh):
            mm(a(two[h], 0, 98), a("idn"), a("tm", 128 * h, 128 * h + 98), True, False)
        if not last:
            ts(a("cwg"), a(l1, 64, 65), -2048.0, None, OP.add)
            ts(a("zg"), a("zo"), a("cwg"), None, OP.mult)
            mm(a("pn", 0, 48), a("idn"), a("rk"), True, False)
            mms([(a("pn", 0, 48), sel("zg", i), a("xv", 32 * i, 32 * i + 48), False, i == 15) for i in range(16)])
            tt(a("vd2", 0, 32), a("sf"), a("dg2"), OP.mult)
            tt(a("vd2", 32, 47), a("sf", 2, 32, 2), a("dg", 0, 15), OP.mult)
            for h, x in enumerate((a("vd2", 0, 32, 2), a("vd2", 1, 32, 2), a("vd2", 32, 47))):
                total(a("nsh", h, h + 1), x, -1.0)
                aff(a("vt2", 16 * h, 16 * h + 16), a("pn", 16 * h, 16 * h + 16), 1.0, a("nsh", h, h + 1))
        act(a("d2", 16 * HV, 512), a("dicx", ind=a("hw", HV, 32)), AF.Copy)
        for lo, hi in ((0, HV // 2), (HV // 2, HV)):
            tt(a("lt2", 16 * lo, 16 * hi), a("dicx", ind=a("hw", lo, hi)), a("xv", 16 * lo, 16 * hi), OP.is_gt)
        in_row[0] = "lay" if last else None
        tt(a("lt2", 16 * HV, 512), a("d2", 16 * HV, 512), a("xv", 16 * HV, 512), OP.is_gt)
        if last:
            lay(*LAY[0])
        for lo, hi in ((0, HV // 4), (HV // 4, HV // 2), (HV // 2, 16)):
            lo, hi = [x - (0 < x < 16 and not last) for x in (lo, hi)]
            mms([(a("pm", 0, 16 * nh), sel("zk", i), a("lt2", 32 * i, 32 * i + 16 * nh), False, i == 15) for i in range(lo, hi)])
        for h in (0, 1):
            scan(a("cs", 16 * h, 16 * h + 16), a("pm", 16 * h, 16 * h + 16), a("vt", 16 * h, 16 * h + 16), NONE, OP.min, OP.max)
        cl = [a("cs", 15, 16), a("cs", 31, 32)]
        for h in (0, 1):
            ts(a("exd", h, 96, 2), a("dg"), cl[h], None, OP.mult)
        for h in (0, 1):
            ts(a("exo", 112 * h, 112 * h + 98), a("one", 0, 98), cl[h], None, OP.mult)
        in_row[0] = None
        for h in range(nh):
            mm(a(two[h], 0, 96), a("blkk"), a("exd"), False, False)
            mm(a(two[h], 0, 98), a("nidn" if h == 2 else "nidk"), a("exo", 112 * (h % 2), 112 * (h % 2) + 98), False, True)
        ts(a("tgt"), a("cs", 15, 32, 16), XW - 1.0, None, OP.min)
        act(a(m3, 0, 32), a(xn, ind=a("tgt")), AF.Copy)
        if not last:
            scan(a("dsc"), a("pm", 0, 48), a("vt2"), 0.0, OP.min, OP.max)
            act(a(m3, 35, 38), a("dsc", 15, 48, 16), AF.Copy)
            ts(a("tgw", 0, 2), a("cs", 15, 32, 16), B0 + 511.5, -512.0, OP.is_ge, OP.mult)
            tt(a("tgc", 0, 2), a("cs", 15, 32, 16), a("tgw", 0, 2), OP.add)
            cl = [a("tgc", 0, 1), a("tgc", 1, 2)]
        for h in range(nh):
            red(a(m3, 32 + h, 33 + h), a(two[h], 0, 98), OP.min, apply_absolute_value=True)
        send(a(m3, 0, 34 if last else 38), a(l3, 0, 34 if last else 38), "a3_%d" % t, guest, host)
        for h in (0, 1):
            ts(a("tg2", h, h + 1), a(m3, 32 + h, 33 + h), cl[h], c(CH[h]), OP.mult, OP.max)
        if last:
            act(a(on, B0 + 512, XW), a(on, B0, B0 + 16), AF.Copy)
            for x in LAY[1:]:
                lay(*x)
        else:
            cp(a(xn, ind=a("tg2")), a(l2))
            sums(xn)
            in_row[0] = t + 1 if LROW else None
            for h in range(3):
                ts(a("bb", 16 * h, 16 * h + 16), a("am", 16 * h, 16 * h + 16), a(l3, 32 + h, 33 + h), a(l3, 35 + h, 36 + h), OP.mult, OP.mult)
            for h in range(3):
                ts(a("av2", h, h + 1), a(l3, 32 + h, 33 + h), a("avs", h, h + 1), c(CSP + h), OP.mult, OP.add)
            tt(a("ksi", 0, 47), a("pk", 0, 47), a("bb", 0, 47), OP.add)
            cp(a("x2", ind=a("av2", 0, 2)), a(l3, 0, 32))
            ts(a("ks", 0, 47), a("ksi", 0, 47), 4095, None, OP.bitwise_and)
            cp(a("x2", ind=a("av2", 2, 3)), a(l3, 1, 17))
            in_row[0] = None
        for h in (0, 1):
            ts(a("avo", h, h + 1), a(l3, 32 + h, 33 + h), a("avp" if last else "avf", h, h + 1), c(CH[h]), OP.mult, OP.max)
        if not last:
            cp(a(xn, ind=a("avo")), a(l3, 0, 32))
        else:
            act(a("oc"), a(on, ind=a("tg2")), AF.Copy)
            conv(a("pm", 0, 2), "zo", "oc", 0, 32)
            ts(a("ocu"), a("pm", 0, 2), float(B0), None, OP.add)
            cp(a("ypb", ind=a("ocu")), a(l2))
            cp(a("ypb", ind=a("avo")), a(l3, 0, 32))
            dma("y", "ld7", [(T.ypup[:], a("ypb", B0, B0 + 512))])
    issue_all()
    for s in sorted(count):
        if s != "ld7":
            g.wait_ge(T.sem[s], count[s])
    g.wait_ge(T.sem.ld7, 16)
